import numpy as np
import ml_dtypes


def mxq(x, axis, fmt="e4m3"):
    dtype, down = {"e4m3": (ml_dtypes.float8_e4m3fn, 7), "e5m2": (ml_dtypes.float8_e5m2, 14)}[fmt]
    v = np.moveaxis(np.asarray(x, np.float32).astype(ml_dtypes.bfloat16).astype(np.float64), axis, -1)
    blocks = v.reshape(v.shape[:-1] + (-1, 32))
    amax = np.abs(blocks).max(-1, keepdims=True)
    byte = np.maximum(np.where(amax > 0, np.frexp(amax)[1] - 1 + 127, 0) - down, 1)
    scale = np.exp2(byte - 127.0)
    codes = (blocks / scale).astype(np.float32).astype(dtype).astype(np.float64)
    return np.moveaxis((codes * scale).reshape(v.shape), -1, axis)


WIDE = False


def mx_kscale(k):
    if not WIDE:
        return np.ones(k)
    levels = np.array([18, -18])
    if k % 512:
        return np.exp2(np.random.permutation(np.resize(levels, k // 32))).repeat(32)
    a = np.empty((k // 512, 16))
    for p in range(k // 512):
        a[p, :8] = np.random.permutation(np.resize(levels, 8))
        for g in range(8):
            far = levels[np.abs(levels - a[p, g]) >= 10]
            a[p, g + 8] = far[np.random.randint(len(far))]
    return np.exp2(a.ravel()).repeat(32)


def f64(x):
    return np.asarray(x).astype(np.float64)


def striped(idx):
    return np.tile(np.asarray(idx).reshape(-1, 16).T, (8, 1)).astype(np.uint16)


def unstriped(offs):
    return offs[:16].T.reshape(-1).astype(np.int64)


T, C, D, DV = 2048, 1024, 256, 512
BETA = 0.25


def setup_inputs():
    n = np.random.standard_normal
    grid = lambda v: np.clip(np.round(v * 16) / 16, -4, 4)
    u = mx_kscale(T)
    return {
        "zT": (grid(n((DV, T)))).astype(np.float32),
        "cb": (grid(n((DV, C)))).astype(np.float32),
        "cb2": (grid(0.5 * n((DV, C)))).astype(np.float32),
        "tw": np.tile(np.random.randint(8, 33, T) / 16.0 * u, (128, 1)).astype(np.float32),
        "xT": (n((D, T)) / np.sqrt(T) / u).astype(np.float32),
        "offs": striped(np.random.randint(0, C, T)),
        "offs2": striped(np.random.randint(0, C, T)),
    }


def reference(zT, cb, cb2, tw, xT, offs, offs2):
    e = f64(zT) - f64(cb)[:, unstriped(offs)] - f64(cb2)[:, unstriped(offs2)]
    g = f64(tw)[:1] * (BETA * e)
    return mxq(f64(xT), 1, "e4m3") @ mxq(g, 1, "e5m2").T

@@ -1,0 +1,238 @@
+from contextlib import ExitStack
+
+import concourse.mybir as mybir
+from concourse.masks import make_identity
+
+T, C, D, DV = 2048, 1024, 256, 512
+BETA = 0.25
+FLOPS = 2 * T * D * DV
+BYTES = 4 * (DV * T + 2 * DV * C + T + D * T + D * DV) + 2 * 2 * 128 * (T // 16)
+
+F32 = mybir.dt.float32
+BF16 = mybir.dt.bfloat16
+U32 = mybir.dt.uint32
+U16 = mybir.dt.uint16
+U8 = mybir.dt.uint8
+E4M3 = mybir.dt.float8_e4m3fn_x4
+E5M2 = mybir.dt.float8_e5m2_x4
+COPY = mybir.ActivationFunctionType.Copy
+MULT = mybir.AluOpType.mult
+
+P = 128
+SLOTS = 4
+RUN = 8
+K_PASS = P * SLOTS
+PASSES = T // K_PASS
+NB = DV // P
+DB = D // P
+EARLY = PASSES - 1
+T_EARLY = EARLY * K_PASS
+WINDOW = 2 * C
+
+
+def tile_attend_gvq_rw_w_kernel(tc, zT, cb, cb2, tw, xT, offs, offs2, out):
+    nc = tc.nc
+    with ExitStack() as ctx:
+        keep = ctx.enter_context(tc.tile_pool(name="keep", bufs=1))
+        ring = ctx.enter_context(tc.tile_pool(name="ring", bufs=4))
+        psum_acc = ctx.enter_context(tc.psum_pool(name="psum_acc", bufs=1))
+        psum_e = ctx.enter_context(tc.psum_pool(name="psum_e", bufs=4))
+        psum_x = ctx.enter_context(tc.psum_pool(name="psum_x", bufs=2))
+
+        lists = [keep.tile([P, T // 16], U16, name=f"list{b}") for b in range(2)]
+        books = [keep.tile([P, (NB + 1) * C], F32, name=f"book{b}") for b in range(2)]
+        z_early = [keep.tile([P, T_EARLY], F32, name=f"z_early{nb}") for nb in range(NB)]
+        z_late = keep.tile([P, NB, K_PASS], F32)
+        neg_z = [keep.tile([P, SLOTS, T // SLOTS], F32, name=f"neg_z{nb}") for nb in range(NB)]
+        x_raw = [keep.tile([P, T], F32, name=f"x_raw{db}") for db in range(DB)]
+        x_pairs = [keep.tile([P, 2, T // 2], BF16, name=f"x_pairs{db}") for db in range(DB)]
+        x_turned = keep.tile([P, PASSES, D * SLOTS], BF16, align_bytes=64)
+        x_codes = keep.tile([P, PASSES, D], U32, align_bytes=64)
+        x_scales = keep.tile([P, PASSES, D], U8, align_bytes=64)
+        g_turned = keep.tile([P, PASSES, DV * SLOTS], BF16, align_bytes=64)
+        g_codes = keep.tile([P, PASSES, DV], U32, align_bytes=64)
+        g_scales = keep.tile([P, PASSES, DV], U8, align_bytes=64)
+        ident = keep.tile([P, P], F32)
+        tw_rows = keep.tile([P, T // SLOTS], F32)
+        neg_w = keep.tile([P, PASSES, SLOTS], F32)
+        acc = [psum_acc.tile([P, DV], F32, name=f"acc{db}") for db in range(DB)]
+
+        def book_start(nb):
+            return (NB - 1 - nb) * C
+
+        nc.gpsimd.memset(books[0][:, NB * C :], 0.0)
+        nc.gpsimd.memset(tw_rows[:], 0.0)
+        make_identity(nc, ident[:])
+        nc.gpsimd.memset(books[1][:, NB * C :], 0.0)
+
+        def load_book(b, nb):
+            src = (cb, cb2)[b]
+            nc.sync.dma_start(out=books[b][:, book_start(nb) : book_start(nb) + C], in_=src[nb * P : (nb + 1) * P, :])
+
+        def load_z_early(nb):
+            nc.sync.dma_start(out=z_early[nb][:], in_=zT[nb * P : (nb + 1) * P, :T_EARLY])
+
+        def load_x(db):
+            nc.sync.dma_start(out=x_raw[db][:], in_=xT[db * P : (db + 1) * P, :])
+
+        load_book(0, 0)
+        nc.sync.dma_start(lists[0][:], offs)
+        nc.sync.dma_start(lists[1][:], offs2)
+        nc.scalar.dma_start(
+            out=tw_rows[0:SLOTS, :].rearrange("j (q r) -> j q r", r=RUN),
+            in_=tw[0:1, :].rearrange("o (q j r) -> (o j) q r", j=SLOTS, r=RUN),
+        )
+        load_z_early(0)
+        load_book(1, 0)
+        for nb in range(1, NB):
+            if nb <= DB:
+                load_x(nb - 1)
+            load_book(0, nb)
+            load_z_early(nb)
+            load_book(1, nb)
+        nc.sync.dma_start(out=z_late[:], in_=zT[:, T_EARLY:].rearrange("(b p) t -> p b t", p=P))
+
+        w_bank = psum_x.tile([P, PASSES, P], F32, tag="small", name="w_bank")
+        for k in range(PASSES):
+            nc.tensor.transpose(w_bank[:, k, :], tw_rows[:, k * P : (k + 1) * P], ident[:])
+        nc.scalar.activation(neg_w[:], w_bank[:, :, 0:SLOTS], COPY, scale=-BETA)
+
+        def negate_z(nb, src, first, count):
+            cols = slice(first // SLOTS, (first + count) // SLOTS)
+            nc.scalar.activation(
+                neg_z[nb][:, :, cols].rearrange("p j (q r) -> p j q r", r=RUN),
+                src.rearrange("p (q j r) -> p j q r", j=SLOTS, r=RUN),
+                COPY,
+                scale=-1.0,
+            )
+
+        def gather(b, nb, first, count):
+            picked = ring.tile([P, SLOTS, count // SLOTS], F32, tag=f"picked{count}", name=f"picked{b}_{nb}_{first}")
+            window = books[b][:, book_start(nb) : book_start(nb) + WINDOW].bitcast(U32)
+            nc.vector.tensor_copy(
+                picked[:].bitcast(U32).rearrange("p j (q r) -> p q j r", r=RUN),
+                window.indirect(lists[b][:, first // 16 : (first + count) // 16]),
+            )
+            return picked
+
+        def turn(bank, src, col, start, stop):
+            for j in range(SLOTS):
+                nc.tensor.matmul(
+                    bank[:, j, :],
+                    src[:, j, col : col + P],
+                    ident[:],
+                    start=(start and j == 0),
+                    stop=(stop and j == SLOTS - 1),
+                    is_transpose=True,
+                )
+
+        def g_cols(k, nb):
+            return g_turned[:, k, nb * K_PASS : (nb + 1) * K_PASS].rearrange("p (n j) -> p n j", j=SLOTS)
+
+        def weigh_on_scalar(bank, k, nb):
+            planes = ring.tile([P, SLOTS, P], BF16, tag="planes", name=f"planes{k}_{nb}")
+            for j in range(SLOTS):
+                nc.scalar.activation(planes[:, j, :], bank[:, j, :], COPY, scale=neg_w[:, k, j : j + 1])
+            nc.scalar.copy(
+                g_cols(k, nb).rearrange("p (c i) j -> p c j i", i=4),
+                planes[:].rearrange("p j (c i) -> p c j i", i=4),
+            )
+
+        def weigh_on_vector(bank, k, nb):
+            nc.vector.tensor_tensor(
+                g_cols(k, nb),
+                bank[:].rearrange("p j n -> p n j"),
+                neg_w[:, k : k + 1, :].to_broadcast([P, P, SLOTS]),
+                MULT,
+            )
+
+        def cast_x(db):
+            src = x_raw[db][:].rearrange("p (q u e r) -> p u q r e", u=2, e=2, r=RUN)
+            for u in range(2):
+                nc.scalar.copy(x_pairs[db][:, u, :].rearrange("p (q r e) -> p q r e", r=RUN, e=2), src[:, u])
+
+        def turn_x(k):
+            bank = psum_x.tile([P, DB, 2, P], F32, tag="small", name=f"x_bank{k}")
+            for db in range(DB):
+                for u in range(2):
+                    words = x_pairs[db][:, u, :].bitcast(F32)
+                    nc.tensor.transpose(bank[:, db, u, :], words[:, k * P : (k + 1) * P], ident[:])
+            nc.scalar.copy(
+                x_turned[:, k, :].bitcast(F32).rearrange("p (b d u) -> p b d u", b=DB, u=2),
+                bank[:].rearrange("p b u d -> p b d u"),
+            )
+
+        def quantize_x(k0, k1):
+            nc.vector.quantize_mx(
+                out=x_codes[:, k0:k1, :].rearrange("p k d -> p (k d)").bitcast(E4M3),
+                scales=x_scales[:, k0:k1, :].rearrange("p k d -> p (k d)"),
+                in_=x_turned[:, k0:k1, :].rearrange("p k c -> p (k c)"),
+            )
+
+        def quantize_g(k, nb0, nb1):
+            nc.vector.quantize_mx(
+                out=g_codes[:, k, nb0 * P : nb1 * P].bitcast(E5M2),
+                scales=g_scales[:, k, nb0 * P : nb1 * P],
+                in_=g_turned[:, k, nb0 * K_PASS : nb1 * K_PASS],
+            )
+
+        def multiply(k):
+            for db in range(DB):
+                nc.tensor.matmul_mx(
+                    out=acc[db][:],
+                    lhsT=x_codes[:, k, db * P : (db + 1) * P].bitcast(E4M3),
+                    lhsT_scale=x_scales[:, k, db * P : (db + 1) * P],
+                    rhs=g_codes[:, k, :].bitcast(E5M2),
+                    rhs_scale=g_scales[:, k, :],
+                    start=(k == 0),
+                    stop=(k == PASSES - 1),
+                )
+
+        for nb in range(NB):
+            negate_z(nb, z_early[nb][:], 0, T_EARLY)
+            first = gather(0, nb, 0, T_EARLY)
+            banks = [psum_e.tile([P, SLOTS, P], F32, tag="e", name=f"e{k}_{nb}") for k in range(EARLY)]
+            for k in range(EARLY):
+                turn(banks[k], neg_z[nb], k * P, True, False)
+                turn(banks[k], first, k * P, False, False)
+            second = gather(1, nb, 0, T_EARLY)
+            if nb == NB - 1:
+                quantize_x(0, 2)
+                quantize_x(2, 4)
+            for k in range(EARLY):
+                turn(banks[k], second, k * P, False, True)
+                weigh_on_scalar(banks[k], k, nb)
+            if nb < DB:
+                cast_x(nb)
+            if nb == DB - 1:
+                for k in range(PASSES):
+                    turn_x(k)
+            if nb >= DB:
+                for late in (2 * (nb - DB), 2 * (nb - DB) + 1):
+                    negate_z(late, z_late[:, late, :], T_EARLY, K_PASS)
+
+        last = PASSES - 1
+        for nb in range(NB):
+            first = gather(0, nb, T_EARLY, K_PASS)
+            bank = psum_e.tile([P, SLOTS, P], F32, tag="e", name=f"e{last}_{nb}")
+            turn(bank, neg_z[nb], last * P, True, False)
+            turn(bank, first, 0, False, False)
+            second = gather(1, nb, T_EARLY, K_PASS)
+            turn(bank, second, 0, False, True)
+            if nb >= 1:
+                quantize_g(nb - 1, 0, NB)
+                multiply(nb - 1)
+            if nb < NB - 1:
+                weigh_on_scalar(bank, last, nb)
+            else:
+                quantize_g(last, 0, 2)
+                weigh_on_vector(bank, last, nb)
+                quantize_g(last, 2, 3)
+                quantize_g(last, 3, 4)
+        multiply(last)
+
+        result = [keep.tile([P, DV], F32, name=f"result{db}") for db in range(DB)]
+        nc.vector.tensor_copy(result[0][:], acc[0][:])
+        nc.sync.dma_start(out=out[0:P, :], in_=result[0][:])
+        nc.scalar.copy(result[1][:], acc[1][:])
+        nc.scalar.dma_start(out=out[P : 2 * P, :], in_=result[1][:])

@@ -35,9 +35,7 @@ def tile_attend_gvq_rw_w_kernel(tc, zT, cb, cb2, tw, xT, offs, offs2, out):
     with ExitStack() as ctx:
         keep = ctx.enter_context(tc.tile_pool(name="keep", bufs=1))
         ring = ctx.enter_context(tc.tile_pool(name="ring", bufs=4))
-        psum_acc = ctx.enter_context(tc.psum_pool(name="psum_acc", bufs=1))
-        psum_e = ctx.enter_context(tc.psum_pool(name="psum_e", bufs=4))
-        psum_x = ctx.enter_context(tc.psum_pool(name="psum_x", bufs=2))
+        psum = ctx.enter_context(tc.psum_pool(name="psum", bufs=8))
 
         lists = [keep.tile([P, T // 16], U16, name=f"list{b}") for b in range(2)]
         books = [keep.tile([P, (NB + 1) * C], F32, name=f"book{b}") for b in range(2)]
@@ -53,17 +51,16 @@ def tile_attend_gvq_rw_w_kernel(tc, zT, cb, cb2, tw, xT, offs, offs2, out):
         g_codes = keep.tile([P, PASSES, DV], U32, align_bytes=64)
         g_scales = keep.tile([P, PASSES, DV], U8, align_bytes=64)
         ident = keep.tile([P, P], F32)
-        tw_rows = keep.tile([P, T // SLOTS], F32)
+        tw_rows = keep.tile([P, K_PASS], F32)
+        tw_planes = keep.tile([P, SLOTS, P], F32)
         neg_w = keep.tile([P, PASSES, SLOTS], F32)
-        acc = [psum_acc.tile([P, DV], F32, name=f"acc{db}") for db in range(DB)]
 
         def book_start(nb):
             return (NB - 1 - nb) * C
 
-        nc.gpsimd.memset(books[0][:, NB * C :], 0.0)
-        nc.gpsimd.memset(tw_rows[:], 0.0)
+        for b in range(2):
+            nc.vector.memset(books[b][:, NB * C :], 0.0)
         make_identity(nc, ident[:])
-        nc.gpsimd.memset(books[1][:, NB * C :], 0.0)
 
         def load_book(b, nb):
             src = (cb, cb2)[b]
@@ -72,30 +69,44 @@ def tile_attend_gvq_rw_w_kernel(tc, zT, cb, cb2, tw, xT, offs, offs2, out):
         def load_z_early(nb):
             nc.sync.dma_start(out=z_early[nb][:], in_=zT[nb * P : (nb + 1) * P, :T_EARLY])
 
-        def load_x(db):
-            nc.sync.dma_start(out=x_raw[db][:], in_=xT[db * P : (db + 1) * P, :])
+        def load_x(db, half):
+            cols = slice(half * T // 2, (half + 1) * T // 2)
+            nc.sync.dma_start(out=x_raw[db][:, cols], in_=xT[db * P : (db + 1) * P, cols])
 
         load_book(0, 0)
         nc.sync.dma_start(lists[0][:], offs)
-        nc.sync.dma_start(lists[1][:], offs2)
-        nc.scalar.dma_start(
-            out=tw_rows[0:SLOTS, :].rearrange("j (q r) -> j q r", r=RUN),
-            in_=tw[0:1, :].rearrange("o (q j r) -> (o j) q r", j=SLOTS, r=RUN),
-        )
         load_z_early(0)
         load_book(1, 0)
-        for nb in range(1, NB):
-            if nb <= DB:
-                load_x(nb - 1)
-            load_book(0, nb)
-            load_z_early(nb)
-            load_book(1, nb)
+        nc.sync.dma_start(lists[1][:], offs2)
+        load_x(0, 0)
+        nc.sync.dma_start(
+            out=tw_rows[:], in_=tw[0 : P // PASSES, :].rearrange("a (k t) -> (a k) t", k=PASSES)
+        )
+        load_book(0, 1)
+        load_z_early(1)
+        load_book(1, 1)
+        load_x(0, 1)
+        load_x(1, 0)
+        load_book(0, 2)
+        load_z_early(2)
+        load_book(1, 2)
+        load_x(1, 1)
+        load_book(0, 3)
+        load_z_early(3)
+        load_book(1, 3)
         nc.sync.dma_start(out=z_late[:], in_=zT[:, T_EARLY:].rearrange("(b p) t -> p b t", p=P))
 
-        w_bank = psum_x.tile([P, PASSES, P], F32, tag="small", name="w_bank")
-        for k in range(PASSES):
-            nc.tensor.transpose(w_bank[:, k, :], tw_rows[:, k * P : (k + 1) * P], ident[:])
-        nc.scalar.activation(neg_w[:], w_bank[:, :, 0:SLOTS], COPY, scale=-BETA)
+        def turn_weights():
+            nc.scalar.activation(
+                tw_planes[:].rearrange("p j (q r) -> p j q r", r=RUN),
+                tw_rows[:].rearrange("p (q j r) -> p j q r", j=SLOTS, r=RUN),
+                COPY,
+                scale=-BETA,
+            )
+            bank = psum.tile([P, SLOTS, P], F32, tag="bank", name="w_bank")
+            for j in range(SLOTS):
+                nc.tensor.transpose(bank[:, j, :], tw_planes[:, j, :], ident[:])
+            nc.scalar.copy(neg_w[:], bank[:, :, 0:PASSES].rearrange("p j k -> p k j"))
 
         def negate_z(nb, src, first, count):
             cols = slice(first // SLOTS, (first + count) // SLOTS)
@@ -146,13 +157,15 @@ def tile_attend_gvq_rw_w_kernel(tc, zT, cb, cb2, tw, xT, offs, offs2, out):
                 MULT,
             )
 
-        def cast_x(db):
-            src = x_raw[db][:].rearrange("p (q u e r) -> p u q r e", u=2, e=2, r=RUN)
+        def cast_x(db, half):
+            cols = slice(half * T // 2, (half + 1) * T // 2)
+            src = x_raw[db][:, cols].rearrange("p (q u e r) -> p u q r e", u=2, e=2, r=RUN)
             for u in range(2):
-                nc.scalar.copy(x_pairs[db][:, u, :].rearrange("p (q r e) -> p q r e", r=RUN, e=2), src[:, u])
+                dst = x_pairs[db][:, u, half * T // 4 : (half + 1) * T // 4]
+                nc.scalar.copy(dst.rearrange("p (q r e) -> p q r e", r=RUN, e=2), src[:, u])
 
         def turn_x(k):
-            bank = psum_x.tile([P, DB, 2, P], F32, tag="small", name=f"x_bank{k}")
+            bank = psum.tile([P, DB, 2, P], F32, tag="bank", name=f"x_bank{k}")
             for db in range(DB):
                 for u in range(2):
                     words = x_pairs[db][:, u, :].bitcast(F32)
@@ -176,7 +189,7 @@ def tile_attend_gvq_rw_w_kernel(tc, zT, cb, cb2, tw, xT, offs, offs2, out):
                 in_=g_turned[:, k, nb0 * K_PASS : nb1 * K_PASS],
             )
 
-        def multiply(k):
+        def multiply(acc, k):
             for db in range(DB):
                 nc.tensor.matmul_mx(
                     out=acc[db][:],
@@ -188,48 +201,61 @@ def tile_attend_gvq_rw_w_kernel(tc, zT, cb, cb2, tw, xT, offs, offs2, out):
                     stop=(k == PASSES - 1),
                 )
 
+        negate_z(0, z_early[0][:], 0, T_EARLY)
+        cast_x(0, 0)
+        turn_weights()
         for nb in range(NB):
-            negate_z(nb, z_early[nb][:], 0, T_EARLY)
             first = gather(0, nb, 0, T_EARLY)
-            banks = [psum_e.tile([P, SLOTS, P], F32, tag="e", name=f"e{k}_{nb}") for k in range(EARLY)]
+            banks = [psum.tile([P, SLOTS, P], F32, tag="bank", name=f"e{k}_{nb}") for k in range(EARLY)]
             for k in range(EARLY):
                 turn(banks[k], neg_z[nb], k * P, True, False)
                 turn(banks[k], first, k * P, False, False)
             second = gather(1, nb, 0, T_EARLY)
-            if nb == NB - 1:
-                quantize_x(0, 2)
-                quantize_x(2, 4)
+            if nb + 1 < NB:
+                negate_z(nb + 1, z_early[nb + 1][:], 0, T_EARLY)
             for k in range(EARLY):
                 turn(banks[k], second, k * P, False, True)
                 weigh_on_scalar(banks[k], k, nb)
-            if nb < DB:
-                cast_x(nb)
-            if nb == DB - 1:
-                for k in range(PASSES):
-                    turn_x(k)
-            if nb >= DB:
-                for late in (2 * (nb - DB), 2 * (nb - DB) + 1):
+            if nb == 0:
+                cast_x(0, 1)
+            if nb == 1:
+                cast_x(1, 0)
+                turn_x(0)
+                turn_x(1)
+            if nb == 2:
+                cast_x(1, 1)
+                turn_x(2)
+                turn_x(3)
+                for late in range(NB):
                     negate_z(late, z_late[:, late, :], T_EARLY, K_PASS)
 
         last = PASSES - 1
+        acc = [psum.tile([P, DV], F32, tag="bank", name=f"acc{db}") for db in range(DB)]
         for nb in range(NB):
             first = gather(0, nb, T_EARLY, K_PASS)
-            bank = psum_e.tile([P, SLOTS, P], F32, tag="e", name=f"e{last}_{nb}")
+            bank = psum.tile([P, SLOTS, P], F32, tag="bank", name=f"e{last}_{nb}")
             turn(bank, neg_z[nb], last * P, True, False)
             turn(bank, first, 0, False, False)
+            if nb == NB - 1:
+                quantize_g(1, 0, NB)
+                multiply(acc, 1)
             second = gather(1, nb, T_EARLY, K_PASS)
             turn(bank, second, 0, False, True)
-            if nb >= 1:
-                quantize_g(nb - 1, 0, NB)
-                multiply(nb - 1)
+            if nb == 0:
+                quantize_x(0, PASSES)
+            if nb == NB - 2:
+                quantize_g(0, 0, NB)
+                multiply(acc, 0)
             if nb < NB - 1:
                 weigh_on_scalar(bank, last, nb)
             else:
+                quantize_g(2, 0, NB)
+                multiply(acc, 2)
                 quantize_g(last, 0, 2)
                 weigh_on_vector(bank, last, nb)
                 quantize_g(last, 2, 3)
                 quantize_g(last, 3, 4)
-        multiply(last)
+        multiply(acc, last)
 
         result = [keep.tile([P, DV], F32, name=f"result{db}") for db in range(DB)]
         nc.vector.tensor_copy(result[0][:], acc[0][:])

@@ -17,6 +17,7 @@ E4M3 = mybir.dt.float8_e4m3fn_x4
 E5M2 = mybir.dt.float8_e5m2_x4
 COPY = mybir.ActivationFunctionType.Copy
 MULT = mybir.AluOpType.mult
+SUBTRACT = mybir.AluOpType.subtract
 
 P = 128
 SLOTS = 4
@@ -41,7 +42,7 @@ def tile_attend_gvq_rw_w_kernel(tc, zT, cb, cb2, tw, xT, offs, offs2, out):
         books = [keep.tile([P, (NB + 1) * C], F32, name=f"book{b}") for b in range(2)]
         z_early = [keep.tile([P, T_EARLY], F32, name=f"z_early{nb}") for nb in range(NB)]
         z_late = keep.tile([P, NB, K_PASS], F32)
-        neg_z = [keep.tile([P, SLOTS, T // SLOTS], F32, name=f"neg_z{nb}") for nb in range(NB)]
+        neg_z_late = [keep.tile([P, SLOTS, P], F32, name=f"neg_z{nb}") for nb in range(NB)]
         x_raw = [keep.tile([P, T], F32, name=f"x_raw{db}") for db in range(DB)]
         x_pairs = [keep.tile([P, 2, T // 2], BF16, name=f"x_pairs{db}") for db in range(DB)]
         x_turned = keep.tile([P, PASSES, D * SLOTS], BF16, align_bytes=64)
@@ -50,6 +51,7 @@ def tile_attend_gvq_rw_w_kernel(tc, zT, cb, cb2, tw, xT, offs, offs2, out):
         g_turned = keep.tile([P, PASSES, DV * SLOTS], BF16, align_bytes=64)
         g_codes = keep.tile([P, PASSES, DV], U32, align_bytes=64)
         g_scales = keep.tile([P, PASSES, DV], U8, align_bytes=64)
+        rooms = [keep.tile([P, T_EARLY], F32, name=f"room{i}") for i in range(6)]
         ident = keep.tile([P, P], F32)
         tw_rows = keep.tile([P, K_PASS], F32)
         tw_planes = keep.tile([P, SLOTS, P], F32)
@@ -75,25 +77,25 @@ def tile_attend_gvq_rw_w_kernel(tc, zT, cb, cb2, tw, xT, offs, offs2, out):
 
         load_book(0, 0)
         nc.sync.dma_start(lists[0][:], offs)
-        load_z_early(0)
         load_book(1, 0)
         nc.sync.dma_start(lists[1][:], offs2)
+        load_z_early(0)
+        load_book(0, 1)
         load_x(0, 0)
         nc.sync.dma_start(
             out=tw_rows[:], in_=tw[0 : P // PASSES, :].rearrange("a (k t) -> (a k) t", k=PASSES)
         )
-        load_book(0, 1)
-        load_z_early(1)
         load_book(1, 1)
-        load_x(0, 1)
-        load_x(1, 0)
+        load_z_early(1)
         load_book(0, 2)
-        load_z_early(2)
+        load_x(1, 0)
         load_book(1, 2)
-        load_x(1, 1)
+        load_z_early(2)
         load_book(0, 3)
-        load_z_early(3)
+        load_x(0, 1)
         load_book(1, 3)
+        load_z_early(3)
+        load_x(1, 1)
         nc.sync.dma_start(out=z_late[:], in_=zT[:, T_EARLY:].rearrange("(b p) t -> p b t", p=P))
 
         def turn_weights():
@@ -108,23 +110,40 @@ def tile_attend_gvq_rw_w_kernel(tc, zT, cb, cb2, tw, xT, offs, offs2, out):
                 nc.tensor.transpose(bank[:, j, :], tw_planes[:, j, :], ident[:])
             nc.scalar.copy(neg_w[:], bank[:, :, 0:PASSES].rearrange("p j k -> p k j"))
 
-        def negate_z(nb, src, first, count):
-            cols = slice(first // SLOTS, (first + count) // SLOTS)
+        def negate_z_late(nb):
             nc.scalar.activation(
-                neg_z[nb][:, :, cols].rearrange("p j (q r) -> p j q r", r=RUN),
-                src.rearrange("p (q j r) -> p j q r", j=SLOTS, r=RUN),
+                neg_z_late[nb][:].rearrange("p j (q r) -> p j q r", r=RUN),
+                z_late[:, nb, :].rearrange("p (q j r) -> p j q r", j=SLOTS, r=RUN),
                 COPY,
                 scale=-1.0,
             )
 
-        def gather(b, nb, first, count):
-            picked = ring.tile([P, SLOTS, count // SLOTS], F32, tag=f"picked{count}", name=f"picked{b}_{nb}_{first}")
+        def minus_z_early(first, nb, k):
+            diff = ring.tile([P, SLOTS, P], F32, tag="diff", name=f"diff{k}_{nb}")
+            nc.gpsimd.tensor_tensor(
+                diff[:].rearrange("p j (q r) -> p j q r", r=RUN),
+                first[:, :, k * P : (k + 1) * P].rearrange("p j (q r) -> p j q r", r=RUN),
+                z_early[nb][:, k * K_PASS : (k + 1) * K_PASS].rearrange("p (q j r) -> p j q r", j=SLOTS, r=RUN),
+                SUBTRACT,
+            )
+            return diff
+
+        def gather(b, nb, first, room):
+            count = room.shape[1]
+            picked = room.rearrange("p (j c) -> p j c", j=SLOTS)
             window = books[b][:, book_start(nb) : book_start(nb) + WINDOW].bitcast(U32)
             nc.vector.tensor_copy(
-                picked[:].bitcast(U32).rearrange("p j (q r) -> p q j r", r=RUN),
+                picked.bitcast(U32).rearrange("p j (q r) -> p q j r", r=RUN),
                 window.indirect(lists[b][:, first // 16 : (first + count) // 16]),
             )
             return picked
+
+        def early_room(b, nb):
+            return rooms[(2 * nb + b) % len(rooms)][:]
+
+        def late_room(b, nb):
+            start = (nb % EARLY) * K_PASS
+            return early_room(b, NB - 2)[:, start : start + K_PASS]
 
         def turn(bank, src, col, start, stop):
             for j in range(SLOTS):
@@ -144,10 +163,10 @@ def tile_attend_gvq_rw_w_kernel(tc, zT, cb, cb2, tw, xT, offs, offs2, out):
             planes = ring.tile([P, SLOTS, P], BF16, tag="planes", name=f"planes{k}_{nb}")
             for j in range(SLOTS):
                 nc.scalar.activation(planes[:, j, :], bank[:, j, :], COPY, scale=neg_w[:, k, j : j + 1])
-            nc.scalar.copy(
-                g_cols(k, nb).rearrange("p (c i) j -> p c j i", i=4),
-                planes[:].rearrange("p j (c i) -> p c j i", i=4),
-            )
+            return planes
+
+        def interleave(planes, k, nb):
+            nc.scalar.copy(g_cols(k, nb), planes[:].rearrange("p j n -> p n j"))
 
         def weigh_on_vector(bank, k, nb):
             nc.vector.tensor_tensor(
@@ -201,45 +220,43 @@ def tile_attend_gvq_rw_w_kernel(tc, zT, cb, cb2, tw, xT, offs, offs2, out):
                     stop=(k == PASSES - 1),
                 )
 
-        negate_z(0, z_early[0][:], 0, T_EARLY)
         cast_x(0, 0)
         turn_weights()
         for nb in range(NB):
-            first = gather(0, nb, 0, T_EARLY)
+            first = gather(0, nb, 0, early_room(0, nb))
             banks = [psum.tile([P, SLOTS, P], F32, tag="bank", name=f"e{k}_{nb}") for k in range(EARLY)]
             for k in range(EARLY):
-                turn(banks[k], neg_z[nb], k * P, True, False)
-                turn(banks[k], first, k * P, False, False)
-            second = gather(1, nb, 0, T_EARLY)
-            if nb + 1 < NB:
-                negate_z(nb + 1, z_early[nb + 1][:], 0, T_EARLY)
+                turn(banks[k], minus_z_early(first, nb, k), 0, True, False)
+            second = gather(1, nb, 0, early_room(1, nb))
+            weighed = []
             for k in range(EARLY):
                 turn(banks[k], second, k * P, False, True)
-                weigh_on_scalar(banks[k], k, nb)
-            if nb == 0:
-                cast_x(0, 1)
+                weighed.append(weigh_on_scalar(banks[k], k, nb))
+            for k in range(EARLY):
+                interleave(weighed[k], k, nb)
             if nb == 1:
                 cast_x(1, 0)
                 turn_x(0)
                 turn_x(1)
+                cast_x(0, 1)
             if nb == 2:
                 cast_x(1, 1)
                 turn_x(2)
                 turn_x(3)
                 for late in range(NB):
-                    negate_z(late, z_late[:, late, :], T_EARLY, K_PASS)
+                    negate_z_late(late)
 
         last = PASSES - 1
         acc = [psum.tile([P, DV], F32, tag="bank", name=f"acc{db}") for db in range(DB)]
         for nb in range(NB):
-            first = gather(0, nb, T_EARLY, K_PASS)
+            first = gather(0, nb, T_EARLY, late_room(0, nb))
             bank = psum.tile([P, SLOTS, P], F32, tag="bank", name=f"e{last}_{nb}")
-            turn(bank, neg_z[nb], last * P, True, False)
+            turn(bank, neg_z_late[nb], 0, True, False)
             turn(bank, first, 0, False, False)
             if nb == NB - 1:
                 quantize_g(1, 0, NB)
                 multiply(acc, 1)
-            second = gather(1, nb, T_EARLY, K_PASS)
+            second = gather(1, nb, T_EARLY, late_room(1, nb))
             turn(bank, second, 0, False, True)
             if nb == 0:
                 quantize_x(0, PASSES)
@@ -247,7 +264,7 @@ def tile_attend_gvq_rw_w_kernel(tc, zT, cb, cb2, tw, xT, offs, offs2, out):
                 quantize_g(0, 0, NB)
                 multiply(acc, 0)
             if nb < NB - 1:
-                weigh_on_scalar(bank, last, nb)
+                interleave(weigh_on_scalar(bank, last, nb), last, nb)
             else:
                 quantize_g(2, 0, NB)
                 multiply(acc, 2)

@@ -79,24 +79,24 @@ def tile_attend_gvq_rw_w_kernel(tc, zT, cb, cb2, tw, xT, offs, offs2, out):
         nc.sync.dma_start(lists[0][:], offs)
         load_book(1, 0)
         nc.sync.dma_start(lists[1][:], offs2)
-        load_z_early(0)
-        load_book(0, 1)
-        load_x(0, 0)
         nc.sync.dma_start(
             out=tw_rows[:], in_=tw[0 : P // PASSES, :].rearrange("a (k t) -> (a k) t", k=PASSES)
         )
+        load_z_early(0)
+        load_book(0, 1)
         load_book(1, 1)
-        load_z_early(1)
+        load_x(0, 0)
         load_book(0, 2)
-        load_x(1, 0)
+        load_z_early(1)
         load_book(1, 2)
-        load_z_early(2)
         load_book(0, 3)
-        load_x(0, 1)
         load_book(1, 3)
+        load_x(1, 0)
+        load_z_early(2)
         load_z_early(3)
-        load_x(1, 1)
         nc.sync.dma_start(out=z_late[:], in_=zT[:, T_EARLY:].rearrange("(b p) t -> p b t", p=P))
+        load_x(0, 1)
+        load_x(1, 1)
 
         def turn_weights():
             nc.scalar.activation(
@@ -122,11 +122,16 @@ def tile_attend_gvq_rw_w_kernel(tc, zT, cb, cb2, tw, xT, offs, offs2, out):
             diff = ring.tile([P, SLOTS, P], F32, tag="diff", name=f"diff{k}_{nb}")
             nc.gpsimd.tensor_tensor(
                 diff[:].rearrange("p j (q r) -> p j q r", r=RUN),
-                first[:, :, k * P : (k + 1) * P].rearrange("p j (q r) -> p j q r", r=RUN),
+                first[:, k * K_PASS : (k + 1) * K_PASS].rearrange("p (q j r) -> p j q r", j=SLOTS, r=RUN),
                 z_early[nb][:, k * K_PASS : (k + 1) * K_PASS].rearrange("p (q j r) -> p j q r", j=SLOTS, r=RUN),
                 SUBTRACT,
             )
             return diff
+
+        def gather_plain(b, nb, room):
+            window = books[b][:, book_start(nb) : book_start(nb) + WINDOW].bitcast(U32)
+            nc.vector.tensor_copy(room.bitcast(U32), window.indirect(lists[b][:, 0 : T_EARLY // 16]))
+            return room
 
         def gather(b, nb, first, room):
             count = room.shape[1]
@@ -220,10 +225,9 @@ def tile_attend_gvq_rw_w_kernel(tc, zT, cb, cb2, tw, xT, offs, offs2, out):
                     stop=(k == PASSES - 1),
                 )
 
-        cast_x(0, 0)
         turn_weights()
         for nb in range(NB):
-            first = gather(0, nb, 0, early_room(0, nb))
+            first = gather_plain(0, nb, early_room(0, nb))
             banks = [psum.tile([P, SLOTS, P], F32, tag="bank", name=f"e{k}_{nb}") for k in range(EARLY)]
             for k in range(EARLY):
                 turn(banks[k], minus_z_early(first, nb, k), 0, True, False)
@@ -234,17 +238,19 @@ def tile_attend_gvq_rw_w_kernel(tc, zT, cb, cb2, tw, xT, offs, offs2, out):
                 weighed.append(weigh_on_scalar(banks[k], k, nb))
             for k in range(EARLY):
                 interleave(weighed[k], k, nb)
+            if nb == 0:
+                cast_x(0, 0)
             if nb == 1:
                 cast_x(1, 0)
                 turn_x(0)
                 turn_x(1)
-                cast_x(0, 1)
             if nb == 2:
+                for late in range(NB):
+                    negate_z_late(late)
+                cast_x(0, 1)
                 cast_x(1, 1)
                 turn_x(2)
                 turn_x(3)
-                for late in range(NB):
-                    negate_z_late(late)
 
         last = PASSES - 1
         acc = [psum.tile([P, DV], F32, tag="bank", name=f"acc{db}") for db in range(DB)]
@@ -259,10 +265,11 @@ def tile_attend_gvq_rw_w_kernel(tc, zT, cb, cb2, tw, xT, offs, offs2, out):
             second = gather(1, nb, T_EARLY, late_room(1, nb))
             turn(bank, second, 0, False, True)
             if nb == 0:
-                quantize_x(0, PASSES)
+                quantize_x(0, 2)
             if nb == NB - 2:
                 quantize_g(0, 0, NB)
                 multiply(acc, 0)
+                quantize_x(2, 4)
             if nb < NB - 1:
                 interleave(weigh_on_scalar(bank, last, nb), last, nb)
             else:
@@ -275,7 +282,11 @@ def tile_attend_gvq_rw_w_kernel(tc, zT, cb, cb2, tw, xT, offs, offs2, out):
         multiply(acc, last)
 
         result = [keep.tile([P, DV], F32, name=f"result{db}") for db in range(DB)]
-        nc.vector.tensor_copy(result[0][:], acc[0][:])
-        nc.sync.dma_start(out=out[0:P, :], in_=result[0][:])
-        nc.scalar.copy(result[1][:], acc[1][:])
-        nc.scalar.dma_start(out=out[P : 2 * P, :], in_=result[1][:])
+        for half in range(2):
+            cols = slice(half * DV // 2, (half + 1) * DV // 2)
+            nc.vector.tensor_copy(result[0][:, cols], acc[0][:, cols])
+            nc.sync.dma_start(out=out[0:P, cols], in_=result[0][:, cols])
+        for half in range(2):
+            cols = slice(half * DV // 2, (half + 1) * DV // 2)
+            nc.scalar.copy(result[1][:, cols], acc[1][:, cols])
+            nc.sync.dma_start(out=out[P : 2 * P, cols], in_=result[1][:, cols])

@@ -17,6 +17,7 @@ E4M3 = mybir.dt.float8_e4m3fn_x4
 E5M2 = mybir.dt.float8_e5m2_x4
 COPY = mybir.ActivationFunctionType.Copy
 MULT = mybir.AluOpType.mult
+ADD = mybir.AluOpType.add
 SUBTRACT = mybir.AluOpType.subtract
 
 P = 128
@@ -26,9 +27,9 @@ K_PASS = P * SLOTS
 PASSES = T // K_PASS
 NB = DV // P
 DB = D // P
-EARLY = PASSES - 1
-T_EARLY = EARLY * K_PASS
-WINDOW = 2 * C
+PADS = 2
+LAST_NB = NB - 1
+LAST_K = PASSES - 1
 
 
 def tile_attend_gvq_rw_w_kernel(tc, zT, cb, cb2, tw, xT, offs, offs2, out):
@@ -36,22 +37,31 @@ def tile_attend_gvq_rw_w_kernel(tc, zT, cb, cb2, tw, xT, offs, offs2, out):
     with ExitStack() as ctx:
         keep = ctx.enter_context(tc.tile_pool(name="keep", bufs=1))
         ring = ctx.enter_context(tc.tile_pool(name="ring", bufs=4))
-        psum = ctx.enter_context(tc.psum_pool(name="psum", bufs=8))
+        ends = ctx.enter_context(tc.tile_pool(name="ends", bufs=1))
+        psum = ctx.enter_context(tc.psum_pool(name="psum", bufs=1))
+
+        def shared(tag, name, shape, dtype):
+            return keep.tile(shape, dtype, tag=tag, name=name, align_bytes=64)
+
+        def bank_tile(i, name, shape):
+            return psum.tile(shape, F32, tag=f"bank{i}", name=name)
 
         lists = [keep.tile([P, T // 16], U16, name=f"list{b}") for b in range(2)]
-        books = [keep.tile([P, (NB + 1) * C], F32, name=f"book{b}") for b in range(2)]
-        z_early = [keep.tile([P, T_EARLY], F32, name=f"z_early{nb}") for nb in range(NB)]
-        z_late = keep.tile([P, NB, K_PASS], F32)
-        neg_z_late = [keep.tile([P, SLOTS, P], F32, name=f"neg_z{nb}") for nb in range(NB)]
+        books = [keep.tile([P, (NB + PADS) * C], F32, name=f"book{b}") for b in range(2)]
+        z = [shared(f"z{nb}", f"z{nb}", [P, T], F32) for nb in range(NB)]
+        neg_z = keep.tile([P, SLOTS, T // SLOTS], F32)
         x_raw = [keep.tile([P, T], F32, name=f"x_raw{db}") for db in range(DB)]
         x_pairs = [keep.tile([P, 2, T // 2], BF16, name=f"x_pairs{db}") for db in range(DB)]
         x_turned = keep.tile([P, PASSES, D * SLOTS], BF16, align_bytes=64)
-        x_codes = keep.tile([P, PASSES, D], U32, align_bytes=64)
         x_scales = keep.tile([P, PASSES, D], U8, align_bytes=64)
-        g_turned = keep.tile([P, PASSES, DV * SLOTS], BF16, align_bytes=64)
-        g_codes = keep.tile([P, PASSES, DV], U32, align_bytes=64)
         g_scales = keep.tile([P, PASSES, DV], U8, align_bytes=64)
-        rooms = [keep.tile([P, T_EARLY], F32, name=f"room{i}") for i in range(6)]
+        g_low = [shared(f"low{k}", f"g_low{k}", [P, 2 * K_PASS], BF16) for k in range(PASSES)]
+        g_high = [
+            shared("high0", "g_high0", [P, 2 * K_PASS], BF16),
+            ends.tile([P, 2 * K_PASS], BF16, name="g_high1", align_bytes=64, offset=1024),
+            shared("high2", "g_high2", [P, 2 * K_PASS], BF16),
+        ]
+        g_third = shared("third", "g_third", [P, K_PASS], BF16)
         ident = keep.tile([P, P], F32)
         tw_rows = keep.tile([P, K_PASS], F32)
         tw_planes = keep.tile([P, SLOTS, P], F32)
@@ -60,16 +70,21 @@ def tile_attend_gvq_rw_w_kernel(tc, zT, cb, cb2, tw, xT, offs, offs2, out):
         def book_start(nb):
             return (NB - 1 - nb) * C
 
-        for b in range(2):
-            nc.vector.memset(books[b][:, NB * C :], 0.0)
+        def clear_pad(b, i):
+            nc.gpsimd.memset(books[b][:, (NB + i) * C : (NB + i + 1) * C], 0.0)
+
+        clear_pad(0, 0)
         make_identity(nc, ident[:])
+        clear_pad(1, 0)
+        clear_pad(0, 1)
+        clear_pad(1, 1)
 
         def load_book(b, nb):
             src = (cb, cb2)[b]
             nc.sync.dma_start(out=books[b][:, book_start(nb) : book_start(nb) + C], in_=src[nb * P : (nb + 1) * P, :])
 
-        def load_z_early(nb):
-            nc.sync.dma_start(out=z_early[nb][:], in_=zT[nb * P : (nb + 1) * P, :T_EARLY])
+        def load_z(nb, c0, c1):
+            nc.sync.dma_start(out=z[nb][:, c0:c1], in_=zT[nb * P : (nb + 1) * P, c0:c1])
 
         def load_x(db, half):
             cols = slice(half * T // 2, (half + 1) * T // 2)
@@ -77,26 +92,26 @@ def tile_attend_gvq_rw_w_kernel(tc, zT, cb, cb2, tw, xT, offs, offs2, out):
 
         load_book(0, 0)
         nc.sync.dma_start(lists[0][:], offs)
+        load_x(0, 0)
+        load_x(1, 0)
         load_book(1, 0)
         nc.sync.dma_start(lists[1][:], offs2)
+        load_z(0, 0, T // 2)
         nc.sync.dma_start(
             out=tw_rows[:], in_=tw[0 : P // PASSES, :].rearrange("a (k t) -> (a k) t", k=PASSES)
         )
-        load_z_early(0)
+        load_z(0, T // 2, T)
         load_book(0, 1)
-        load_book(1, 1)
-        load_x(0, 0)
-        load_book(0, 2)
-        load_z_early(1)
-        load_book(1, 2)
-        load_book(0, 3)
-        load_book(1, 3)
-        load_x(1, 0)
-        load_z_early(2)
-        load_z_early(3)
-        nc.sync.dma_start(out=z_late[:], in_=zT[:, T_EARLY:].rearrange("(b p) t -> p b t", p=P))
         load_x(0, 1)
         load_x(1, 1)
+        load_book(1, 1)
+        load_z(1, 0, T)
+        load_book(0, 2)
+        load_book(1, 2)
+        load_z(3, 0, T)
+        load_book(0, 3)
+        load_z(2, 0, T)
+        load_book(1, 3)
 
         def turn_weights():
             nc.scalar.activation(
@@ -105,50 +120,43 @@ def tile_attend_gvq_rw_w_kernel(tc, zT, cb, cb2, tw, xT, offs, offs2, out):
                 COPY,
                 scale=-BETA,
             )
-            bank = psum.tile([P, SLOTS, P], F32, tag="bank", name="w_bank")
+            bank = bank_tile(0, "w_bank", [P, SLOTS, P])
             for j in range(SLOTS):
                 nc.tensor.transpose(bank[:, j, :], tw_planes[:, j, :], ident[:])
             nc.scalar.copy(neg_w[:], bank[:, :, 0:PASSES].rearrange("p j k -> p k j"))
 
-        def negate_z_late(nb):
-            nc.scalar.activation(
-                neg_z_late[nb][:].rearrange("p j (q r) -> p j q r", r=RUN),
-                z_late[:, nb, :].rearrange("p (q j r) -> p j q r", j=SLOTS, r=RUN),
-                COPY,
-                scale=-1.0,
+        def negate_z():
+            nc.gpsimd.tensor_scalar(
+                neg_z[:].rearrange("p j (m r) -> p j m r", r=RUN),
+                z[LAST_NB][:].rearrange("p (m j r) -> p j m r", j=SLOTS, r=RUN),
+                -1.0,
+                0.0,
+                MULT,
+                ADD,
             )
 
-        def minus_z_early(first, nb, k):
+        def minus_z(first, nb, k):
             diff = ring.tile([P, SLOTS, P], F32, tag="diff", name=f"diff{k}_{nb}")
             nc.gpsimd.tensor_tensor(
                 diff[:].rearrange("p j (q r) -> p j q r", r=RUN),
                 first[:, k * K_PASS : (k + 1) * K_PASS].rearrange("p (q j r) -> p j q r", j=SLOTS, r=RUN),
-                z_early[nb][:, k * K_PASS : (k + 1) * K_PASS].rearrange("p (q j r) -> p j q r", j=SLOTS, r=RUN),
+                z[nb][:, k * K_PASS : (k + 1) * K_PASS].rearrange("p (q j r) -> p j q r", j=SLOTS, r=RUN),
                 SUBTRACT,
             )
             return diff
 
-        def gather_plain(b, nb, room):
-            window = books[b][:, book_start(nb) : book_start(nb) + WINDOW].bitcast(U32)
-            nc.vector.tensor_copy(room.bitcast(U32), window.indirect(lists[b][:, 0 : T_EARLY // 16]))
-            return room
+        def looked_up(b, nb, k0, k1):
+            columns = {1: C, 3: 2 * C, 4: 4 * C}[k1 - k0]
+            window = books[b][:, book_start(nb) : book_start(nb) + columns].bitcast(U32)
+            return window.indirect(lists[b][:, k0 * K_PASS // 16 : k1 * K_PASS // 16])
 
-        def gather(b, nb, first, room):
-            count = room.shape[1]
-            picked = room.rearrange("p (j c) -> p j c", j=SLOTS)
-            window = books[b][:, book_start(nb) : book_start(nb) + WINDOW].bitcast(U32)
+        def gather_plain(nb, k0, k1, room):
+            nc.vector.tensor_copy(room[:, k0 * K_PASS : k1 * K_PASS].bitcast(U32), looked_up(0, nb, k0, k1))
+
+        def gather_planes(b, nb, k0, k1, planes):
             nc.vector.tensor_copy(
-                picked.bitcast(U32).rearrange("p j (q r) -> p q j r", r=RUN),
-                window.indirect(lists[b][:, first // 16 : (first + count) // 16]),
+                planes.bitcast(U32).rearrange("p j (m r) -> p m j r", r=RUN), looked_up(b, nb, k0, k1)
             )
-            return picked
-
-        def early_room(b, nb):
-            return rooms[(2 * nb + b) % len(rooms)][:]
-
-        def late_room(b, nb):
-            start = (nb % EARLY) * K_PASS
-            return early_room(b, NB - 2)[:, start : start + K_PASS]
 
         def turn(bank, src, col, start, stop):
             for j in range(SLOTS):
@@ -161,25 +169,18 @@ def tile_attend_gvq_rw_w_kernel(tc, zT, cb, cb2, tw, xT, offs, offs2, out):
                     is_transpose=True,
                 )
 
-        def g_cols(k, nb):
-            return g_turned[:, k, nb * K_PASS : (nb + 1) * K_PASS].rearrange("p (n j) -> p n j", j=SLOTS)
+        def g_place(k, nb):
+            if nb < 2:
+                return g_low[k][:, nb * K_PASS : (nb + 1) * K_PASS]
+            if k < LAST_K:
+                return g_high[k][:, (nb - 2) * K_PASS : (nb - 1) * K_PASS]
+            return g_third[:]
 
         def weigh_on_scalar(bank, k, nb):
             planes = ring.tile([P, SLOTS, P], BF16, tag="planes", name=f"planes{k}_{nb}")
             for j in range(SLOTS):
                 nc.scalar.activation(planes[:, j, :], bank[:, j, :], COPY, scale=neg_w[:, k, j : j + 1])
-            return planes
-
-        def interleave(planes, k, nb):
-            nc.scalar.copy(g_cols(k, nb), planes[:].rearrange("p j n -> p n j"))
-
-        def weigh_on_vector(bank, k, nb):
-            nc.vector.tensor_tensor(
-                g_cols(k, nb),
-                bank[:].rearrange("p j n -> p n j"),
-                neg_w[:, k : k + 1, :].to_broadcast([P, P, SLOTS]),
-                MULT,
-            )
+            nc.scalar.copy(g_place(k, nb).rearrange("p (n j) -> p n j", j=SLOTS), planes[:].rearrange("p j n -> p n j"))
 
         def cast_x(db, half):
             cols = slice(half * T // 2, (half + 1) * T // 2)
@@ -189,7 +190,7 @@ def tile_attend_gvq_rw_w_kernel(tc, zT, cb, cb2, tw, xT, offs, offs2, out):
                 nc.scalar.copy(dst.rearrange("p (q r e) -> p q r e", r=RUN, e=2), src[:, u])
 
         def turn_x(k):
-            bank = psum.tile([P, DB, 2, P], F32, tag="bank", name=f"x_bank{k}")
+            bank = bank_tile(PASSES + k, f"x_bank{k}", [P, DB, 2, P])
             for db in range(DB):
                 for u in range(2):
                     words = x_pairs[db][:, u, :].bitcast(F32)
@@ -199,6 +200,36 @@ def tile_attend_gvq_rw_w_kernel(tc, zT, cb, cb2, tw, xT, offs, offs2, out):
                 bank[:].rearrange("p b u d -> p b d u"),
             )
 
+        for half in range(2):
+            for db in range(DB):
+                cast_x(db, half)
+            turn_x(2 * half)
+            turn_x(2 * half + 1)
+            if half == 0:
+                turn_weights()
+
+        for nb in range(LAST_NB):
+            pieces = [(0, 1), (1, PASSES)] if nb == 0 else [(0, PASSES)]
+            first = shared(f"first{nb % 2}", f"first{nb}", [P, T], F32)
+            for k0, k1 in pieces:
+                gather_plain(nb, k0, k1, first)
+            banks = [bank_tile(PASSES * (nb % 2) + k, f"e{k}_{nb}", [P, SLOTS, P]) for k in range(PASSES)]
+            for k in range(PASSES):
+                turn(banks[k], minus_z(first, nb, k), 0, True, False)
+            second = shared(f"second{nb % 2}", f"second{nb}", [P, SLOTS, T // SLOTS], F32)
+            for k0, k1 in pieces:
+                gather_planes(1, nb, k0, k1, second[:, :, k0 * P : k1 * P])
+            for k in range(PASSES):
+                turn(banks[k], second, k * P, False, True)
+                weigh_on_scalar(banks[k], k, nb)
+            if nb == 1:
+                negate_z()
+
+        x_codes = shared("first0", "x_codes", [P, PASSES, D], U32)
+        early_codes = shared(f"z{LAST_NB - 1}", "early_codes", [P, LAST_K, DV], U32)
+        last_codes = ends.tile([P, DV], U32, name="last_codes", align_bytes=64, offset=2048)
+        g_codes = [early_codes[:, k, :] for k in range(LAST_K)] + [last_codes[:]]
+
         def quantize_x(k0, k1):
             nc.vector.quantize_mx(
                 out=x_codes[:, k0:k1, :].rearrange("p k d -> p (k d)").bitcast(E4M3),
@@ -206,80 +237,65 @@ def tile_attend_gvq_rw_w_kernel(tc, zT, cb, cb2, tw, xT, offs, offs2, out):
                 in_=x_turned[:, k0:k1, :].rearrange("p k c -> p (k c)"),
             )
 
-        def quantize_g(k, nb0, nb1):
+        def quantize_g(k, nb0, nb1, turned):
             nc.vector.quantize_mx(
-                out=g_codes[:, k, nb0 * P : nb1 * P].bitcast(E5M2),
+                out=g_codes[k][:, nb0 * P : nb1 * P].bitcast(E5M2),
                 scales=g_scales[:, k, nb0 * P : nb1 * P],
-                in_=g_turned[:, k, nb0 * K_PASS : nb1 * K_PASS],
+                in_=turned,
             )
 
-        def multiply(acc, k):
+        def multiply(k):
             for db in range(DB):
                 nc.tensor.matmul_mx(
                     out=acc[db][:],
                     lhsT=x_codes[:, k, db * P : (db + 1) * P].bitcast(E4M3),
                     lhsT_scale=x_scales[:, k, db * P : (db + 1) * P],
-                    rhs=g_codes[:, k, :].bitcast(E5M2),
+                    rhs=g_codes[k].bitcast(E5M2),
                     rhs_scale=g_scales[:, k, :],
                     start=(k == 0),
-                    stop=(k == PASSES - 1),
+                    stop=(k == LAST_K),
                 )
 
-        turn_weights()
-        for nb in range(NB):
-            first = gather_plain(0, nb, early_room(0, nb))
-            banks = [psum.tile([P, SLOTS, P], F32, tag="bank", name=f"e{k}_{nb}") for k in range(EARLY)]
-            for k in range(EARLY):
-                turn(banks[k], minus_z_early(first, nb, k), 0, True, False)
-            second = gather(1, nb, 0, early_room(1, nb))
-            weighed = []
-            for k in range(EARLY):
-                turn(banks[k], second, k * P, False, True)
-                weighed.append(weigh_on_scalar(banks[k], k, nb))
-            for k in range(EARLY):
-                interleave(weighed[k], k, nb)
-            if nb == 0:
-                cast_x(0, 0)
-            if nb == 1:
-                cast_x(1, 0)
-                turn_x(0)
-                turn_x(1)
-            if nb == 2:
-                for late in range(NB):
-                    negate_z_late(late)
-                cast_x(0, 1)
-                cast_x(1, 1)
-                turn_x(2)
-                turn_x(3)
+        nb = LAST_NB
+        banks = [bank_tile(PASSES + k, f"e{k}_{nb}", [P, SLOTS, P]) for k in range(PASSES)]
+        acc = [bank_tile(db, f"acc{db}", [P, DV]) for db in range(DB)]
+        first = shared("first1", "first3", [P, SLOTS, LAST_K * P], F32)
+        second = shared("second1", "second3", [P, LAST_K, SLOTS, P], F32)
+        gather_planes(0, nb, 0, LAST_K, first[:])
+        for k in range(PASSES):
+            turn(banks[k], neg_z, k * P, True, False)
+        for k in range(LAST_K):
+            turn(banks[k], first, k * P, False, False)
+        for k in range(LAST_K):
+            gather_planes(1, nb, k, k + 1, second[:, k])
+            turn(banks[k], second[:, k], 0, False, True)
+            weigh_on_scalar(banks[k], k, nb)
+        quantize_x(0, PASSES)
+        for k in range(LAST_K):
+            quantize_g(k, 0, 2, g_low[k][:])
 
-        last = PASSES - 1
-        acc = [psum.tile([P, DV], F32, tag="bank", name=f"acc{db}") for db in range(DB)]
-        for nb in range(NB):
-            first = gather(0, nb, T_EARLY, late_room(0, nb))
-            bank = psum.tile([P, SLOTS, P], F32, tag="bank", name=f"e{last}_{nb}")
-            turn(bank, neg_z_late[nb], 0, True, False)
-            turn(bank, first, 0, False, False)
-            if nb == NB - 1:
-                quantize_g(1, 0, NB)
-                multiply(acc, 1)
-            second = gather(1, nb, T_EARLY, late_room(1, nb))
-            turn(bank, second, 0, False, True)
-            if nb == 0:
-                quantize_x(0, 2)
-            if nb == NB - 2:
-                quantize_g(0, 0, NB)
-                multiply(acc, 0)
-                quantize_x(2, 4)
-            if nb < NB - 1:
-                interleave(weigh_on_scalar(bank, last, nb), last, nb)
+        for b in range(2):
+            quantize_g(b, 2, NB, g_high[b][:])
+            multiply(b)
+            if b == 0:
+                room = shared("high0", "last_room0", [P, SLOTS, P], F32)
             else:
-                quantize_g(2, 0, NB)
-                multiply(acc, 2)
-                quantize_g(last, 0, 2)
-                weigh_on_vector(bank, last, nb)
-                quantize_g(last, 2, 3)
-                quantize_g(last, 3, 4)
-        multiply(acc, last)
+                room = ends.tile([P, SLOTS, P], F32, name="last_room1", align_bytes=64, offset=0)
+            gather_planes(b, nb, LAST_K, PASSES, room[:])
+            turn(banks[LAST_K], room, 0, False, b == 1)
+        quantize_g(LAST_K, 0, 2, g_low[LAST_K][:])
+        quantize_g(LAST_K, 2, 3, g_third[:])
+        quantize_g(2, 2, NB, g_high[2][:])
+        multiply(2)
+        g_last = shared("high2", "g_last", [P, K_PASS], BF16)
+        nc.vector.tensor_tensor(
+            g_last[:].rearrange("p (n j) -> p n j", j=SLOTS),
+            banks[LAST_K][:].rearrange("p j n -> p n j"),
+            neg_w[:, LAST_K:PASSES, :].to_broadcast([P, P, SLOTS]),
+            MULT,
+        )
+        quantize_g(LAST_K, LAST_NB, NB, g_last[:])
+        multiply(LAST_K)
 
         result = [keep.tile([P, DV], F32, name=f"result{db}") for db in range(DB)]
         for half in range(2):

@@ -48,7 +48,8 @@ def tile_attend_gvq_rw_w_kernel(tc, zT, cb, cb2, tw, xT, offs, offs2, out):
 
         lists = [keep.tile([P, T // 16], U16, name=f"list{b}") for b in range(2)]
         books = [keep.tile([P, (NB + PADS) * C], F32, name=f"book{b}") for b in range(2)]
-        z = [shared(f"z{nb}", f"z{nb}", [P, T], F32) for nb in range(NB)]
+        z = [[shared(f"z{nb}_{h}", f"z{nb}_{h}", [P, T // 2], F32) for h in range(2)] for nb in range(LAST_NB)]
+        z_last = keep.tile([P, T], F32)
         neg_z = keep.tile([P, SLOTS, T // SLOTS], F32)
         x_raw = [keep.tile([P, T], F32, name=f"x_raw{db}") for db in range(DB)]
         x_pairs = [keep.tile([P, 2, T // 2], BF16, name=f"x_pairs{db}") for db in range(DB)]
@@ -57,8 +58,8 @@ def tile_attend_gvq_rw_w_kernel(tc, zT, cb, cb2, tw, xT, offs, offs2, out):
         g_scales = keep.tile([P, PASSES, DV], U8, align_bytes=64)
         g_low = [shared(f"low{k}", f"g_low{k}", [P, 2 * K_PASS], BF16) for k in range(PASSES)]
         g_high = [
-            shared("high0", "g_high0", [P, 2 * K_PASS], BF16),
-            ends.tile([P, 2 * K_PASS], BF16, name="g_high1", align_bytes=64, offset=1024),
+            ends.tile([P, 2 * K_PASS], BF16, name="g_high0", align_bytes=64, offset=3072),
+            shared("high1", "g_high1", [P, 2 * K_PASS], BF16),
             shared("high2", "g_high2", [P, 2 * K_PASS], BF16),
         ]
         g_third = shared("third", "g_third", [P, K_PASS], BF16)
@@ -83,8 +84,9 @@ def tile_attend_gvq_rw_w_kernel(tc, zT, cb, cb2, tw, xT, offs, offs2, out):
             src = (cb, cb2)[b]
             nc.sync.dma_start(out=books[b][:, book_start(nb) : book_start(nb) + C], in_=src[nb * P : (nb + 1) * P, :])
 
-        def load_z(nb, c0, c1):
-            nc.sync.dma_start(out=z[nb][:, c0:c1], in_=zT[nb * P : (nb + 1) * P, c0:c1])
+        def load_z(nb, half):
+            cols = slice(half * T // 2, (half + 1) * T // 2)
+            nc.sync.dma_start(out=z[nb][half][:], in_=zT[nb * P : (nb + 1) * P, cols])
 
         def load_x(db, half):
             cols = slice(half * T // 2, (half + 1) * T // 2)
@@ -96,21 +98,23 @@ def tile_attend_gvq_rw_w_kernel(tc, zT, cb, cb2, tw, xT, offs, offs2, out):
         load_x(1, 0)
         load_book(1, 0)
         nc.sync.dma_start(lists[1][:], offs2)
-        load_z(0, 0, T // 2)
+        load_z(0, 0)
         nc.sync.dma_start(
             out=tw_rows[:], in_=tw[0 : P // PASSES, :].rearrange("a (k t) -> (a k) t", k=PASSES)
         )
-        load_z(0, T // 2, T)
+        load_z(0, 1)
         load_book(0, 1)
         load_x(0, 1)
         load_x(1, 1)
         load_book(1, 1)
-        load_z(1, 0, T)
+        load_z(1, 0)
+        load_z(1, 1)
+        nc.sync.dma_start(out=z_last[:], in_=zT[LAST_NB * P :, :])
         load_book(0, 2)
         load_book(1, 2)
-        load_z(3, 0, T)
         load_book(0, 3)
-        load_z(2, 0, T)
+        load_z(2, 0)
+        load_z(2, 1)
         load_book(1, 3)
 
         def turn_weights():
@@ -128,25 +132,26 @@ def tile_attend_gvq_rw_w_kernel(tc, zT, cb, cb2, tw, xT, offs, offs2, out):
         def negate_z():
             nc.gpsimd.tensor_scalar(
                 neg_z[:].rearrange("p j (m r) -> p j m r", r=RUN),
-                z[LAST_NB][:].rearrange("p (m j r) -> p j m r", j=SLOTS, r=RUN),
+                z_last[:].rearrange("p (m j r) -> p j m r", j=SLOTS, r=RUN),
                 -1.0,
                 0.0,
                 MULT,
                 ADD,
             )
 
-        def minus_z(first, nb, k):
-            diff = ring.tile([P, SLOTS, P], F32, tag="diff", name=f"diff{k}_{nb}")
+        def minus_z(first, nb, half):
+            cols = slice(half * T // 2, (half + 1) * T // 2)
+            diff = ring.tile([P, SLOTS, 2 * P], F32, tag="diff", name=f"diff{half}_{nb}")
             nc.gpsimd.tensor_tensor(
-                diff[:].rearrange("p j (q r) -> p j q r", r=RUN),
-                first[:, k * K_PASS : (k + 1) * K_PASS].rearrange("p (q j r) -> p j q r", j=SLOTS, r=RUN),
-                z[nb][:, k * K_PASS : (k + 1) * K_PASS].rearrange("p (q j r) -> p j q r", j=SLOTS, r=RUN),
+                diff[:].rearrange("p j (m r) -> p j m r", r=RUN),
+                first[:, cols].rearrange("p (m j r) -> p j m r", j=SLOTS, r=RUN),
+                z[nb][half][:].rearrange("p (m j r) -> p j m r", j=SLOTS, r=RUN),
                 SUBTRACT,
             )
             return diff
 
         def looked_up(b, nb, k0, k1):
-            columns = {1: C, 3: 2 * C, 4: 4 * C}[k1 - k0]
+            columns = {1: C, 2: 2 * C, 3: 2 * C, 4: 4 * C}[k1 - k0]
             window = books[b][:, book_start(nb) : book_start(nb) + columns].bitcast(U32)
             return window.indirect(lists[b][:, k0 * K_PASS // 16 : k1 * K_PASS // 16])
 
@@ -213,26 +218,30 @@ def tile_attend_gvq_rw_w_kernel(tc, zT, cb, cb2, tw, xT, offs, offs2, out):
             first = shared(f"first{nb % 2}", f"first{nb}", [P, T], F32)
             for k0, k1 in pieces:
                 gather_plain(nb, k0, k1, first)
-            banks = [bank_tile(PASSES * (nb % 2) + k, f"e{k}_{nb}", [P, SLOTS, P]) for k in range(PASSES)]
-            for k in range(PASSES):
-                turn(banks[k], minus_z(first, nb, k), 0, True, False)
             second = shared(f"second{nb % 2}", f"second{nb}", [P, SLOTS, T // SLOTS], F32)
+            if nb == LAST_NB - 1:
+                pieces = [(0, 2), (2, PASSES)]
             for k0, k1 in pieces:
                 gather_planes(1, nb, k0, k1, second[:, :, k0 * P : k1 * P])
-            for k in range(PASSES):
-                turn(banks[k], second, k * P, False, True)
-                weigh_on_scalar(banks[k], k, nb)
+            for half in range(2):
+                diff = minus_z(first, nb, half)
+                for k in (2 * half, 2 * half + 1):
+                    bank = bank_tile(PASSES * (nb % 2) + k, f"e{k}_{nb}", [P, SLOTS, P])
+                    turn(bank, diff, (k % 2) * P, True, False)
+                    turn(bank, second, k * P, False, True)
+                    weigh_on_scalar(bank, k, nb)
             if nb == 1:
                 negate_z()
 
-        x_codes = shared("first0", "x_codes", [P, PASSES, D], U32)
-        early_codes = shared(f"z{LAST_NB - 1}", "early_codes", [P, LAST_K, DV], U32)
-        last_codes = ends.tile([P, DV], U32, name="last_codes", align_bytes=64, offset=2048)
-        g_codes = [early_codes[:, k, :] for k in range(LAST_K)] + [last_codes[:]]
+        early_codes = shared(f"z{LAST_NB - 1}_1", "early_codes", [P, 2 * D + DV], U32)
+        late_codes = ends.tile([P, 2 * D + LAST_K * DV], U32, name="late_codes", align_bytes=64, offset=4096)
+        x_codes = [early_codes[:, : 2 * D], late_codes[:, : 2 * D]]
+        g_codes = [early_codes[:, 2 * D :]] + [late_codes[:, 2 * D + i * DV : 2 * D + (i + 1) * DV] for i in range(LAST_K)]
 
-        def quantize_x(k0, k1):
+        def quantize_x(half):
+            k0, k1 = 2 * half, 2 * half + 2
             nc.vector.quantize_mx(
-                out=x_codes[:, k0:k1, :].rearrange("p k d -> p (k d)").bitcast(E4M3),
+                out=x_codes[half].bitcast(E4M3),
                 scales=x_scales[:, k0:k1, :].rearrange("p k d -> p (k d)"),
                 in_=x_turned[:, k0:k1, :].rearrange("p k c -> p (k c)"),
             )
@@ -248,7 +257,7 @@ def tile_attend_gvq_rw_w_kernel(tc, zT, cb, cb2, tw, xT, offs, offs2, out):
             for db in range(DB):
                 nc.tensor.matmul_mx(
                     out=acc[db][:],
-                    lhsT=x_codes[:, k, db * P : (db + 1) * P].bitcast(E4M3),
+                    lhsT=x_codes[k // 2][:, (k % 2) * D + db * P : (k % 2) * D + (db + 1) * P].bitcast(E4M3),
                     lhsT_scale=x_scales[:, k, db * P : (db + 1) * P],
                     rhs=g_codes[k].bitcast(E5M2),
                     rhs_scale=g_scales[:, k, :],
@@ -257,43 +266,51 @@ def tile_attend_gvq_rw_w_kernel(tc, zT, cb, cb2, tw, xT, offs, offs2, out):
                 )
 
         nb = LAST_NB
-        banks = [bank_tile(PASSES + k, f"e{k}_{nb}", [P, SLOTS, P]) for k in range(PASSES)]
         acc = [bank_tile(db, f"acc{db}", [P, DV]) for db in range(DB)]
-        first = shared("first1", "first3", [P, SLOTS, LAST_K * P], F32)
-        second = shared("second1", "second3", [P, LAST_K, SLOTS, P], F32)
-        gather_planes(0, nb, 0, LAST_K, first[:])
-        for k in range(PASSES):
-            turn(banks[k], neg_z, k * P, True, False)
-        for k in range(LAST_K):
-            turn(banks[k], first, k * P, False, False)
+        slot_banks = [bank_tile(PASSES + j, f"last{j}", [P, P]) for j in range(SLOTS)]
+        both = shared(f"z{LAST_NB - 1}_0", "both3", [P, 2 * LAST_K * K_PASS], F32)
+        first = both[:, : LAST_K * K_PASS].rearrange("p (j c) -> p j c", j=SLOTS)
+        second = both[:, LAST_K * K_PASS :].rearrange("p (k j c) -> p k j c", k=LAST_K, j=SLOTS)
+        gather_planes(0, nb, 0, LAST_K, first)
         for k in range(LAST_K):
             gather_planes(1, nb, k, k + 1, second[:, k])
-            turn(banks[k], second[:, k], 0, False, True)
-            weigh_on_scalar(banks[k], k, nb)
-        quantize_x(0, PASSES)
-        for k in range(LAST_K):
-            quantize_g(k, 0, 2, g_low[k][:])
+            bank = bank_tile(2 + k % 2, f"e{k}_{nb}", [P, SLOTS, P])
+            turn(bank, neg_z, k * P, True, False)
+            turn(bank, first, k * P, False, False)
+            turn(bank, second[:, k], 0, False, True)
+            weigh_on_scalar(bank, k, nb)
+        quantize_x(0)
+        quantize_g(0, 0, 2, g_low[0][:])
+        quantize_g(0, 2, NB, g_high[0][:])
+        multiply(0)
 
+        rooms = ends.tile([P, 2, SLOTS, P], F32, name="last_rooms", align_bytes=64, offset=0)
+
+        def turn_slots(src, col, start, stop):
+            for j in range(SLOTS):
+                nc.tensor.matmul(
+                    slot_banks[j][:], src[:, j, col : col + P], ident[:], start=start, stop=stop, is_transpose=True
+                )
+
+        turn_slots(neg_z, LAST_K * P, True, False)
         for b in range(2):
-            quantize_g(b, 2, NB, g_high[b][:])
-            multiply(b)
-            if b == 0:
-                room = shared("high0", "last_room0", [P, SLOTS, P], F32)
-            else:
-                room = ends.tile([P, SLOTS, P], F32, name="last_room1", align_bytes=64, offset=0)
-            gather_planes(b, nb, LAST_K, PASSES, room[:])
-            turn(banks[LAST_K], room, 0, False, b == 1)
-        quantize_g(LAST_K, 0, 2, g_low[LAST_K][:])
-        quantize_g(LAST_K, 2, 3, g_third[:])
+            gather_planes(b, nb, LAST_K, PASSES, rooms[:, b])
+            turn_slots(rooms[:, b], 0, False, b == 1)
+        planes = ring.tile([P, SLOTS, P], BF16, tag="planes", name="last_planes")
+        for j in range(SLOTS):
+            nc.scalar.activation(planes[:, j, :], slot_banks[j][:], COPY, scale=neg_w[:, LAST_K, j : j + 1])
+        g_last = keep.tile([P, K_PASS], BF16, align_bytes=64)
+        nc.scalar.copy(g_last[:].rearrange("p (n j) -> p n j", j=SLOTS), planes[:].rearrange("p j n -> p n j"))
+
+        quantize_g(1, 0, 2, g_low[1][:])
+        quantize_g(1, 2, NB, g_high[1][:])
+        multiply(1)
+        quantize_x(1)
+        quantize_g(2, 0, 2, g_low[2][:])
         quantize_g(2, 2, NB, g_high[2][:])
         multiply(2)
-        g_last = shared("high2", "g_last", [P, K_PASS], BF16)
-        nc.vector.tensor_tensor(
-            g_last[:].rearrange("p (n j) -> p n j", j=SLOTS),
-            banks[LAST_K][:].rearrange("p j n -> p n j"),
-            neg_w[:, LAST_K:PASSES, :].to_broadcast([P, P, SLOTS]),
-            MULT,
-        )
+        quantize_g(LAST_K, 0, 2, g_low[LAST_K][:])
+        quantize_g(LAST_K, 2, 3, g_third[:])
         quantize_g(LAST_K, LAST_NB, NB, g_last[:])
         multiply(LAST_K)
 

@@ -37,7 +37,6 @@ def tile_attend_gvq_rw_w_kernel(tc, zT, cb, cb2, tw, xT, offs, offs2, out):
     with ExitStack() as ctx:
         keep = ctx.enter_context(tc.tile_pool(name="keep", bufs=1))
         ring = ctx.enter_context(tc.tile_pool(name="ring", bufs=4))
-        ends = ctx.enter_context(tc.tile_pool(name="ends", bufs=1))
         psum = ctx.enter_context(tc.psum_pool(name="psum", bufs=1))
 
         def shared(tag, name, shape, dtype):
@@ -56,13 +55,7 @@ def tile_attend_gvq_rw_w_kernel(tc, zT, cb, cb2, tw, xT, offs, offs2, out):
         x_turned = keep.tile([P, PASSES, D * SLOTS], BF16, align_bytes=64)
         x_scales = keep.tile([P, PASSES, D], U8, align_bytes=64)
         g_scales = keep.tile([P, PASSES, DV], U8, align_bytes=64)
-        g_low = [shared(f"low{k}", f"g_low{k}", [P, 2 * K_PASS], BF16) for k in range(PASSES)]
-        g_high = [
-            ends.tile([P, 2 * K_PASS], BF16, name="g_high0", align_bytes=64, offset=3072),
-            shared("high1", "g_high1", [P, 2 * K_PASS], BF16),
-            shared("high2", "g_high2", [P, 2 * K_PASS], BF16),
-        ]
-        g_third = shared("third", "g_third", [P, K_PASS], BF16)
+        g_turned = [shared(f"g{k}", f"g_turned{k}", [P, NB * K_PASS], BF16) for k in range(PASSES)]
         ident = keep.tile([P, P], F32)
         tw_rows = keep.tile([P, K_PASS], F32)
         tw_planes = keep.tile([P, SLOTS, P], F32)
@@ -94,28 +87,28 @@ def tile_attend_gvq_rw_w_kernel(tc, zT, cb, cb2, tw, xT, offs, offs2, out):
 
         load_book(0, 0)
         nc.sync.dma_start(lists[0][:], offs)
-        load_x(0, 0)
-        load_x(1, 0)
         load_book(1, 0)
         nc.sync.dma_start(lists[1][:], offs2)
+        load_x(0, 0)
+        load_x(1, 0)
         load_z(0, 0)
         nc.sync.dma_start(
             out=tw_rows[:], in_=tw[0 : P // PASSES, :].rearrange("a (k t) -> (a k) t", k=PASSES)
         )
-        load_z(0, 1)
         load_book(0, 1)
+        load_z(0, 1)
+        load_book(1, 1)
         load_x(0, 1)
         load_x(1, 1)
-        load_book(1, 1)
         load_z(1, 0)
         load_z(1, 1)
-        nc.sync.dma_start(out=z_last[:], in_=zT[LAST_NB * P :, :])
         load_book(0, 2)
+        nc.sync.dma_start(out=z_last[:], in_=zT[LAST_NB * P :, :])
         load_book(1, 2)
         load_book(0, 3)
+        load_book(1, 3)
         load_z(2, 0)
         load_z(2, 1)
-        load_book(1, 3)
 
         def turn_weights():
             nc.scalar.activation(
@@ -175,11 +168,7 @@ def tile_attend_gvq_rw_w_kernel(tc, zT, cb, cb2, tw, xT, offs, offs2, out):
                 )
 
         def g_place(k, nb):
-            if nb < 2:
-                return g_low[k][:, nb * K_PASS : (nb + 1) * K_PASS]
-            if k < LAST_K:
-                return g_high[k][:, (nb - 2) * K_PASS : (nb - 1) * K_PASS]
-            return g_third[:]
+            return g_turned[k][:, nb * K_PASS : (nb + 1) * K_PASS]
 
         def weigh_on_scalar(bank, k, nb):
             planes = ring.tile([P, SLOTS, P], BF16, tag="planes", name=f"planes{k}_{nb}")
@@ -233,10 +222,11 @@ def tile_attend_gvq_rw_w_kernel(tc, zT, cb, cb2, tw, xT, offs, offs2, out):
             if nb == 1:
                 negate_z()
 
-        early_codes = shared(f"z{LAST_NB - 1}_1", "early_codes", [P, 2 * D + DV], U32)
-        late_codes = ends.tile([P, 2 * D + LAST_K * DV], U32, name="late_codes", align_bytes=64, offset=4096)
-        x_codes = [early_codes[:, : 2 * D], late_codes[:, : 2 * D]]
-        g_codes = [early_codes[:, 2 * D :]] + [late_codes[:, 2 * D + i * DV : 2 * D + (i + 1) * DV] for i in range(LAST_K)]
+        codes_a = shared("second0", "codes_a", [P, 2 * D + 2 * DV], U32)
+        codes_b = shared("g1", "codes_b", [P, 2 * D + DV], U32)
+        codes_c = shared("g2", "codes_c", [P, DV], U32)
+        x_codes = [codes_a[:, : 2 * D], codes_b[:, : 2 * D]]
+        g_codes = [codes_a[:, 2 * D : 2 * D + DV], codes_a[:, 2 * D + DV :], codes_b[:, 2 * D :], codes_c[:]]
 
         def quantize_x(half):
             k0, k1 = 2 * half, 2 * half + 2
@@ -246,11 +236,11 @@ def tile_attend_gvq_rw_w_kernel(tc, zT, cb, cb2, tw, xT, offs, offs2, out):
                 in_=x_turned[:, k0:k1, :].rearrange("p k c -> p (k c)"),
             )
 
-        def quantize_g(k, nb0, nb1, turned):
+        def quantize_g(k, nb0, nb1):
             nc.vector.quantize_mx(
                 out=g_codes[k][:, nb0 * P : nb1 * P].bitcast(E5M2),
                 scales=g_scales[:, k, nb0 * P : nb1 * P],
-                in_=turned,
+                in_=g_turned[k][:, nb0 * K_PASS : nb1 * K_PASS],
             )
 
         def multiply(k):
@@ -267,51 +257,33 @@ def tile_attend_gvq_rw_w_kernel(tc, zT, cb, cb2, tw, xT, offs, offs2, out):
 
         nb = LAST_NB
         acc = [bank_tile(db, f"acc{db}", [P, DV]) for db in range(DB)]
-        slot_banks = [bank_tile(PASSES + j, f"last{j}", [P, P]) for j in range(SLOTS)]
-        both = shared(f"z{LAST_NB - 1}_0", "both3", [P, 2 * LAST_K * K_PASS], F32)
+        both = shared(f"z{LAST_NB - 1}_0", "both3", [P, 2 * T], F32)
         first = both[:, : LAST_K * K_PASS].rearrange("p (j c) -> p j c", j=SLOTS)
-        second = both[:, LAST_K * K_PASS :].rearrange("p (k j c) -> p k j c", k=LAST_K, j=SLOTS)
+        rooms = both[:, LAST_K * K_PASS :].rearrange("p (k j c) -> p k j c", k=PASSES + 1, j=SLOTS)
         gather_planes(0, nb, 0, LAST_K, first)
         for k in range(LAST_K):
-            gather_planes(1, nb, k, k + 1, second[:, k])
+            gather_planes(1, nb, k, k + 1, rooms[:, k])
             bank = bank_tile(2 + k % 2, f"e{k}_{nb}", [P, SLOTS, P])
             turn(bank, neg_z, k * P, True, False)
             turn(bank, first, k * P, False, False)
-            turn(bank, second[:, k], 0, False, True)
+            turn(bank, rooms[:, k], 0, False, True)
             weigh_on_scalar(bank, k, nb)
-        quantize_x(0)
-        quantize_g(0, 0, 2, g_low[0][:])
-        quantize_g(0, 2, NB, g_high[0][:])
-        multiply(0)
 
-        rooms = ends.tile([P, 2, SLOTS, P], F32, name="last_rooms", align_bytes=64, offset=0)
-
-        def turn_slots(src, col, start, stop):
-            for j in range(SLOTS):
-                nc.tensor.matmul(
-                    slot_banks[j][:], src[:, j, col : col + P], ident[:], start=start, stop=stop, is_transpose=True
-                )
-
-        turn_slots(neg_z, LAST_K * P, True, False)
+        bank = bank_tile(2 + LAST_K % 2, f"e{LAST_K}_{nb}", [P, SLOTS, P])
+        turn(bank, neg_z, LAST_K * P, True, False)
         for b in range(2):
-            gather_planes(b, nb, LAST_K, PASSES, rooms[:, b])
-            turn_slots(rooms[:, b], 0, False, b == 1)
-        planes = ring.tile([P, SLOTS, P], BF16, tag="planes", name="last_planes")
-        for j in range(SLOTS):
-            nc.scalar.activation(planes[:, j, :], slot_banks[j][:], COPY, scale=neg_w[:, LAST_K, j : j + 1])
-        g_last = keep.tile([P, K_PASS], BF16, align_bytes=64)
-        nc.scalar.copy(g_last[:].rearrange("p (n j) -> p n j", j=SLOTS), planes[:].rearrange("p j n -> p n j"))
+            gather_planes(b, nb, LAST_K, PASSES, rooms[:, LAST_K + b])
+            turn(bank, rooms[:, LAST_K + b], 0, False, b == 1)
+        weigh_on_scalar(bank, LAST_K, nb)
 
-        quantize_g(1, 0, 2, g_low[1][:])
-        quantize_g(1, 2, NB, g_high[1][:])
-        multiply(1)
-        quantize_x(1)
-        quantize_g(2, 0, 2, g_low[2][:])
-        quantize_g(2, 2, NB, g_high[2][:])
-        multiply(2)
-        quantize_g(LAST_K, 0, 2, g_low[LAST_K][:])
-        quantize_g(LAST_K, 2, 3, g_third[:])
-        quantize_g(LAST_K, LAST_NB, NB, g_last[:])
+        for k in range(LAST_K):
+            if k % 2 == 0:
+                quantize_x(k // 2)
+            quantize_g(k, 0, NB)
+            multiply(k)
+        quantize_g(LAST_K, 0, 2)
+        quantize_g(LAST_K, 2, 3)
+        quantize_g(LAST_K, 3, NB)
         multiply(LAST_K)
 
         result = [keep.tile([P, DV], F32, name=f"result{db}") for db in range(DB)]

@@ -203,13 +203,11 @@ def tile_attend_gvq_rw_w_kernel(tc, zT, cb, cb2, tw, xT, offs, offs2, out):
                 turn_weights()
 
         for nb in range(LAST_NB):
-            pieces = [(0, 1), (1, PASSES)] if nb == 0 else [(0, PASSES)]
+            pieces = [[(0, 1), (1, PASSES)], [(0, PASSES)], [(0, 2), (2, PASSES)]][nb]
             first = shared(f"first{nb % 2}", f"first{nb}", [P, T], F32)
             for k0, k1 in pieces:
                 gather_plain(nb, k0, k1, first)
             second = shared(f"second{nb % 2}", f"second{nb}", [P, SLOTS, T // SLOTS], F32)
-            if nb == LAST_NB - 1:
-                pieces = [(0, 2), (2, PASSES)]
             for k0, k1 in pieces:
                 gather_planes(1, nb, k0, k1, second[:, :, k0 * P : k1 * P])
             for half in range(2):
@@ -257,19 +255,19 @@ def tile_attend_gvq_rw_w_kernel(tc, zT, cb, cb2, tw, xT, offs, offs2, out):
 
         nb = LAST_NB
         acc = [bank_tile(db, f"acc{db}", [P, DV]) for db in range(DB)]
-        both = shared(f"z{LAST_NB - 1}_0", "both3", [P, 2 * T], F32)
+        both = shared(f"z{LAST_NB - 1}_1", "both3", [P, 2 * T], F32)
         first = both[:, : LAST_K * K_PASS].rearrange("p (j c) -> p j c", j=SLOTS)
         rooms = both[:, LAST_K * K_PASS :].rearrange("p (k j c) -> p k j c", k=PASSES + 1, j=SLOTS)
         gather_planes(0, nb, 0, LAST_K, first)
         for k in range(LAST_K):
             gather_planes(1, nb, k, k + 1, rooms[:, k])
-            bank = bank_tile(2 + k % 2, f"e{k}_{nb}", [P, SLOTS, P])
+            bank = bank_tile(PASSES + k, f"e{k}_{nb}", [P, SLOTS, P])
             turn(bank, neg_z, k * P, True, False)
             turn(bank, first, k * P, False, False)
             turn(bank, rooms[:, k], 0, False, True)
             weigh_on_scalar(bank, k, nb)
 
-        bank = bank_tile(2 + LAST_K % 2, f"e{LAST_K}_{nb}", [P, SLOTS, P])
+        bank = bank_tile(PASSES + LAST_K, f"e{LAST_K}_{nb}", [P, SLOTS, P])
         turn(bank, neg_z, LAST_K * P, True, False)
         for b in range(2):
             gather_planes(b, nb, LAST_K, PASSES, rooms[:, LAST_K + b])

@@ -27,16 +27,24 @@ K_PASS = P * SLOTS
 PASSES = T // K_PASS
 NB = DV // P
 DB = D // P
-PADS = 2
+LIST_ROWS = 16
 LAST_NB = NB - 1
 LAST_K = PASSES - 1
+RING = 4
+
+WINDOW_BLOCKS = {1: 1, 2: 2, 3: 2, 4: 4}
+PADS = (2, 3)
+WHOLE = [(0, PASSES)]
+HALVES = [(0, 2), (2, PASSES)]
+FIRST_PIECES = [[(0, 1), (1, PASSES)], WHOLE, HALVES, [(0, 2), (2, 3), (3, PASSES)]]
+SECOND_PIECES = [WHOLE, WHOLE, HALVES]
 
 
 def tile_attend_gvq_rw_w_kernel(tc, zT, cb, cb2, tw, xT, offs, offs2, out):
     nc = tc.nc
     with ExitStack() as ctx:
         keep = ctx.enter_context(tc.tile_pool(name="keep", bufs=1))
-        ring = ctx.enter_context(tc.tile_pool(name="ring", bufs=4))
+        ring = ctx.enter_context(tc.tile_pool(name="ring", bufs=RING))
         psum = ctx.enter_context(tc.psum_pool(name="psum", bufs=1))
 
         def shared(tag, name, shape, dtype):
@@ -45,8 +53,8 @@ def tile_attend_gvq_rw_w_kernel(tc, zT, cb, cb2, tw, xT, offs, offs2, out):
         def bank_tile(i, name, shape):
             return psum.tile(shape, F32, tag=f"bank{i}", name=name)
 
-        lists = [keep.tile([P, T // 16], U16, name=f"list{b}") for b in range(2)]
-        books = [keep.tile([P, (NB + PADS) * C], F32, name=f"book{b}") for b in range(2)]
+        lists = [keep.tile([P, T // LIST_ROWS], U16, name=f"list{b}") for b in range(2)]
+        books = [keep.tile([P, (NB + PADS[b]) * C], F32, name=f"book{b}") for b in range(2)]
         z = [[shared(f"z{nb}_{h}", f"z{nb}_{h}", [P, T // 2], F32) for h in range(2)] for nb in range(LAST_NB)]
         z_last = keep.tile([P, T], F32)
         neg_z = keep.tile([P, SLOTS, T // SLOTS], F32)
@@ -69,9 +77,10 @@ def tile_attend_gvq_rw_w_kernel(tc, zT, cb, cb2, tw, xT, offs, offs2, out):
 
         clear_pad(0, 0)
         make_identity(nc, ident[:])
-        clear_pad(1, 0)
+        for i in range(PADS[1]):
+            clear_pad(1, i)
         clear_pad(0, 1)
-        clear_pad(1, 1)
+        nc.vector.memset(tw_rows[:], 0.0)
 
         def load_book(b, nb):
             src = (cb, cb2)[b]
@@ -92,9 +101,7 @@ def tile_attend_gvq_rw_w_kernel(tc, zT, cb, cb2, tw, xT, offs, offs2, out):
         load_x(0, 0)
         load_x(1, 0)
         load_z(0, 0)
-        nc.sync.dma_start(
-            out=tw_rows[:], in_=tw[0 : P // PASSES, :].rearrange("a (k t) -> (a k) t", k=PASSES)
-        )
+        nc.sync.dma_start(out=tw_rows[0:PASSES, :], in_=tw[0:1, :].rearrange("a (k t) -> (a k) t", k=PASSES))
         load_book(0, 1)
         load_z(0, 1)
         load_book(1, 1)
@@ -144,37 +151,37 @@ def tile_attend_gvq_rw_w_kernel(tc, zT, cb, cb2, tw, xT, offs, offs2, out):
             return diff
 
         def looked_up(b, nb, k0, k1):
-            columns = {1: C, 2: 2 * C, 3: 2 * C, 4: 4 * C}[k1 - k0]
+            columns = WINDOW_BLOCKS[k1 - k0] * C
             window = books[b][:, book_start(nb) : book_start(nb) + columns].bitcast(U32)
-            return window.indirect(lists[b][:, k0 * K_PASS // 16 : k1 * K_PASS // 16])
+            return window.indirect(lists[b][:, k0 * K_PASS // LIST_ROWS : k1 * K_PASS // LIST_ROWS])
 
-        def gather_plain(nb, k0, k1, room):
-            nc.vector.tensor_copy(room[:, k0 * K_PASS : k1 * K_PASS].bitcast(U32), looked_up(0, nb, k0, k1))
+        def gather_in_token_order(nb, k0, k1, first):
+            nc.vector.tensor_copy(first[:, k0 * K_PASS : k1 * K_PASS].bitcast(U32), looked_up(0, nb, k0, k1))
 
-        def gather_planes(b, nb, k0, k1, planes):
-            nc.vector.tensor_copy(
-                planes.bitcast(U32).rearrange("p j (m r) -> p m j r", r=RUN), looked_up(b, nb, k0, k1)
-            )
+        def gather_into_planes(b, nb, k0, k1, planes):
+            picked = planes[:, :, k0 * P : k1 * P].bitcast(U32)
+            nc.vector.tensor_copy(picked.rearrange("p j (m r) -> p m j r", r=RUN), looked_up(b, nb, k0, k1))
 
-        def turn(bank, src, col, start, stop):
+        def turn(bank, planes, col, start, stop):
             for j in range(SLOTS):
                 nc.tensor.matmul(
                     bank[:, j, :],
-                    src[:, j, col : col + P],
+                    planes[:, j, col : col + P],
                     ident[:],
                     start=(start and j == 0),
                     stop=(stop and j == SLOTS - 1),
                     is_transpose=True,
                 )
 
-        def g_place(k, nb):
-            return g_turned[k][:, nb * K_PASS : (nb + 1) * K_PASS]
-
-        def weigh_on_scalar(bank, k, nb):
-            planes = ring.tile([P, SLOTS, P], BF16, tag="planes", name=f"planes{k}_{nb}")
+        def weigh(sums, k, nb):
+            if nb == LAST_NB and k >= 1:
+                staged = shared("last_staged", f"staged{k}_{nb}", [P, SLOTS, P], BF16)
+            else:
+                staged = ring.tile([P, SLOTS, P], BF16, tag="staged", name=f"staged{k}_{nb}")
             for j in range(SLOTS):
-                nc.scalar.activation(planes[:, j, :], bank[:, j, :], COPY, scale=neg_w[:, k, j : j + 1])
-            nc.scalar.copy(g_place(k, nb).rearrange("p (n j) -> p n j", j=SLOTS), planes[:].rearrange("p j n -> p n j"))
+                nc.scalar.activation(staged[:, j, :], sums[j], COPY, scale=neg_w[:, k, j : j + 1])
+            words = g_turned[k][:, nb * K_PASS : (nb + 1) * K_PASS]
+            nc.scalar.copy(words.rearrange("p (n j) -> p n j", j=SLOTS), staged[:].rearrange("p j n -> p n j"))
 
         def cast_x(db, half):
             cols = slice(half * T // 2, (half + 1) * T // 2)
@@ -203,33 +210,31 @@ def tile_attend_gvq_rw_w_kernel(tc, zT, cb, cb2, tw, xT, offs, offs2, out):
                 turn_weights()
 
         for nb in range(LAST_NB):
-            pieces = [[(0, 1), (1, PASSES)], [(0, PASSES)], [(0, 2), (2, PASSES)]][nb]
             first = shared(f"first{nb % 2}", f"first{nb}", [P, T], F32)
-            for k0, k1 in pieces:
-                gather_plain(nb, k0, k1, first)
-            second = shared(f"second{nb % 2}", f"second{nb}", [P, SLOTS, T // SLOTS], F32)
-            for k0, k1 in pieces:
-                gather_planes(1, nb, k0, k1, second[:, :, k0 * P : k1 * P])
+            for k0, k1 in FIRST_PIECES[nb]:
+                gather_in_token_order(nb, k0, k1, first)
+            second = shared("z0_0" if nb == 1 else "second", f"second{nb}", [P, SLOTS, T // SLOTS], F32)
+            for k0, k1 in SECOND_PIECES[nb]:
+                gather_into_planes(1, nb, k0, k1, second)
             for half in range(2):
                 diff = minus_z(first, nb, half)
                 for k in (2 * half, 2 * half + 1):
                     bank = bank_tile(PASSES * (nb % 2) + k, f"e{k}_{nb}", [P, SLOTS, P])
                     turn(bank, diff, (k % 2) * P, True, False)
                     turn(bank, second, k * P, False, True)
-                    weigh_on_scalar(bank, k, nb)
-            if nb == 1:
+                    weigh([bank[:, j, :] for j in range(SLOTS)], k, nb)
+            if nb == LAST_NB - 2:
                 negate_z()
 
-        codes_a = shared("second0", "codes_a", [P, 2 * D + 2 * DV], U32)
-        codes_b = shared("g1", "codes_b", [P, 2 * D + DV], U32)
-        codes_c = shared("g2", "codes_c", [P, DV], U32)
-        x_codes = [codes_a[:, : 2 * D], codes_b[:, : 2 * D]]
-        g_codes = [codes_a[:, 2 * D : 2 * D + DV], codes_a[:, 2 * D + DV :], codes_b[:, 2 * D :], codes_c[:]]
+        codes_01 = shared("second", "codes_01", [P, 2 * D + 2 * DV], U32)
+        codes_2 = shared("g1", "codes_2", [P, D + DV], U32)
+        codes_3 = shared("g2", "codes_3", [P, D + DV], U32)
+        x_codes = [codes_01[:, :D], codes_01[:, D : 2 * D], codes_2[:, :D], codes_3[:, :D]]
+        g_codes = [codes_01[:, 2 * D : 2 * D + DV], codes_01[:, 2 * D + DV :], codes_2[:, D:], codes_3[:, D:]]
 
-        def quantize_x(half):
-            k0, k1 = 2 * half, 2 * half + 2
+        def quantize_x(k0, k1, codes):
             nc.vector.quantize_mx(
-                out=x_codes[half].bitcast(E4M3),
+                out=codes.bitcast(E4M3),
                 scales=x_scales[:, k0:k1, :].rearrange("p k d -> p (k d)"),
                 in_=x_turned[:, k0:k1, :].rearrange("p k c -> p (k c)"),
             )
@@ -245,7 +250,7 @@ def tile_attend_gvq_rw_w_kernel(tc, zT, cb, cb2, tw, xT, offs, offs2, out):
             for db in range(DB):
                 nc.tensor.matmul_mx(
                     out=acc[db][:],
-                    lhsT=x_codes[k // 2][:, (k % 2) * D + db * P : (k % 2) * D + (db + 1) * P].bitcast(E4M3),
+                    lhsT=x_codes[k][:, db * P : (db + 1) * P].bitcast(E4M3),
                     lhsT_scale=x_scales[:, k, db * P : (db + 1) * P],
                     rhs=g_codes[k].bitcast(E5M2),
                     rhs_scale=g_scales[:, k, :],
@@ -253,35 +258,47 @@ def tile_attend_gvq_rw_w_kernel(tc, zT, cb, cb2, tw, xT, offs, offs2, out):
                     stop=(k == LAST_K),
                 )
 
-        nb = LAST_NB
         acc = [bank_tile(db, f"acc{db}", [P, DV]) for db in range(DB)]
-        both = shared(f"z{LAST_NB - 1}_1", "both3", [P, 2 * T], F32)
-        first = both[:, : LAST_K * K_PASS].rearrange("p (j c) -> p j c", j=SLOTS)
-        rooms = both[:, LAST_K * K_PASS :].rearrange("p (k j c) -> p k j c", k=PASSES + 1, j=SLOTS)
-        gather_planes(0, nb, 0, LAST_K, first)
-        for k in range(LAST_K):
-            gather_planes(1, nb, k, k + 1, rooms[:, k])
-            bank = bank_tile(PASSES + k, f"e{k}_{nb}", [P, SLOTS, P])
-            turn(bank, neg_z, k * P, True, False)
-            turn(bank, first, k * P, False, False)
-            turn(bank, rooms[:, k], 0, False, True)
-            weigh_on_scalar(bank, k, nb)
+        both = shared(f"z{LAST_NB - 1}_1", "both_last", [P, 2 * T], F32)
+        first = both[:, :T].rearrange("p (j c) -> p j c", j=SLOTS)
+        second = both[:, T:].rearrange("p (j c) -> p j c", j=SLOTS)
+        for k in range(PASSES):
+            for k0, k1 in FIRST_PIECES[LAST_NB]:
+                if k0 == k:
+                    gather_into_planes(0, LAST_NB, k0, k1, first)
+            gather_into_planes(1, LAST_NB, k, k + 1, second)
+            if k < LAST_K:
+                bank = bank_tile(PASSES + k, f"e{k}_{LAST_NB}", [P, SLOTS, P])
+                turn(bank, neg_z, k * P, True, False)
+                turn(bank, first, k * P, False, False)
+                turn(bank, second, k * P, False, True)
+                weigh([bank[:, j, :] for j in range(SLOTS)], k, LAST_NB)
+            else:
+                free_banks = (PASSES + k, DB, DB + 1, PASSES)
+                sums = [bank_tile(i, f"last{i}", [P, P]) for i in free_banks]
+                terms = (neg_z, first, second)
+                for i, planes in enumerate(terms):
+                    for j in range(SLOTS):
+                        nc.tensor.matmul(
+                            sums[j][:],
+                            planes[:, j, k * P : (k + 1) * P],
+                            ident[:],
+                            start=(i == 0),
+                            stop=(i == len(terms) - 1),
+                            is_transpose=True,
+                        )
+                weigh([slot_sum[:] for slot_sum in sums], k, LAST_NB)
 
-        bank = bank_tile(PASSES + LAST_K, f"e{LAST_K}_{nb}", [P, SLOTS, P])
-        turn(bank, neg_z, LAST_K * P, True, False)
-        for b in range(2):
-            gather_planes(b, nb, LAST_K, PASSES, rooms[:, LAST_K + b])
-            turn(bank, rooms[:, LAST_K + b], 0, False, b == 1)
-        weigh_on_scalar(bank, LAST_K, nb)
-
-        for k in range(LAST_K):
-            if k % 2 == 0:
-                quantize_x(k // 2)
+        quantize_x(0, 2, codes_01[:, : 2 * D])
+        for k in range(2):
             quantize_g(k, 0, NB)
             multiply(k)
-        quantize_g(LAST_K, 0, 2)
-        quantize_g(LAST_K, 2, 3)
-        quantize_g(LAST_K, 3, NB)
+        quantize_x(2, 3, x_codes[2])
+        quantize_g(2, 0, NB)
+        multiply(2)
+        quantize_x(LAST_K, PASSES, x_codes[LAST_K])
+        quantize_g(LAST_K, 0, NB // 2)
+        quantize_g(LAST_K, NB // 2, NB)
         multiply(LAST_K)
 
         result = [keep.tile([P, DV], F32, name=f"result{db}") for db in range(DB)]

@@ -75,7 +75,7 @@ def tile_attend_gvq_rw_w_kernel(tc, zT, cb, cb2, tw, xT, offs, offs2, out):
         def clear_pad(b, i):
             nc.gpsimd.memset(books[b][:, (NB + i) * C : (NB + i + 1) * C], 0.0)
 
-        clear_pad(0, 0)
+        nc.vector.memset(books[0][:, NB * C : (NB + 1) * C], 0.0)
         make_identity(nc, ident[:])
         for i in range(PADS[1]):
             clear_pad(1, i)
@@ -107,10 +107,10 @@ def tile_attend_gvq_rw_w_kernel(tc, zT, cb, cb2, tw, xT, offs, offs2, out):
         load_book(1, 1)
         load_x(0, 1)
         load_x(1, 1)
+        nc.sync.dma_start(out=z_last[:], in_=zT[LAST_NB * P :, :])
         load_z(1, 0)
         load_z(1, 1)
         load_book(0, 2)
-        nc.sync.dma_start(out=z_last[:], in_=zT[LAST_NB * P :, :])
         load_book(1, 2)
         load_book(0, 3)
         load_book(1, 3)
@@ -223,7 +223,7 @@ def tile_attend_gvq_rw_w_kernel(tc, zT, cb, cb2, tw, xT, offs, offs2, out):
                     turn(bank, diff, (k % 2) * P, True, False)
                     turn(bank, second, k * P, False, True)
                     weigh([bank[:, j, :] for j in range(SLOTS)], k, nb)
-            if nb == LAST_NB - 2:
+            if nb == 0:
                 negate_z()
 
         codes_01 = shared("second", "codes_01", [P, 2 * D + 2 * DV], U32)
@@ -239,6 +239,13 @@ def tile_attend_gvq_rw_w_kernel(tc, zT, cb, cb2, tw, xT, offs, offs2, out):
                 in_=x_turned[:, k0:k1, :].rearrange("p k c -> p (k c)"),
             )
 
+        def quantize_last_x(db, codes):
+            nc.vector.quantize_mx(
+                out=codes.bitcast(E4M3),
+                scales=x_scales[:, LAST_K, db * P : (db + 1) * P],
+                in_=x_turned[:, LAST_K, db * K_PASS : (db + 1) * K_PASS],
+            )
+
         def quantize_g(k, nb0, nb1):
             nc.vector.quantize_mx(
                 out=g_codes[k][:, nb0 * P : nb1 * P].bitcast(E5M2),
@@ -246,11 +253,16 @@ def tile_attend_gvq_rw_w_kernel(tc, zT, cb, cb2, tw, xT, offs, offs2, out):
                 in_=g_turned[k][:, nb0 * K_PASS : nb1 * K_PASS],
             )
 
+        def stationary(k, db):
+            if k == LAST_K and db == DB - 1:
+                return last_codes[:]
+            return x_codes[k][:, db * P : (db + 1) * P]
+
         def multiply(k):
             for db in range(DB):
                 nc.tensor.matmul_mx(
                     out=acc[db][:],
-                    lhsT=x_codes[k][:, db * P : (db + 1) * P].bitcast(E4M3),
+                    lhsT=stationary(k, db).bitcast(E4M3),
                     lhsT_scale=x_scales[:, k, db * P : (db + 1) * P],
                     rhs=g_codes[k].bitcast(E5M2),
                     rhs_scale=g_scales[:, k, :],
@@ -289,6 +301,7 @@ def tile_attend_gvq_rw_w_kernel(tc, zT, cb, cb2, tw, xT, offs, offs2, out):
                         )
                 weigh([slot_sum[:] for slot_sum in sums], k, LAST_NB)
 
+        last_codes = shared(f"g{LAST_K}", "last_codes", [P, P], U32)
         quantize_x(0, 2, codes_01[:, : 2 * D])
         for k in range(2):
             quantize_g(k, 0, NB)
@@ -296,9 +309,10 @@ def tile_attend_gvq_rw_w_kernel(tc, zT, cb, cb2, tw, xT, offs, offs2, out):
         quantize_x(2, 3, x_codes[2])
         quantize_g(2, 0, NB)
         multiply(2)
-        quantize_x(LAST_K, PASSES, x_codes[LAST_K])
+        quantize_last_x(0, x_codes[LAST_K][:, :P])
         quantize_g(LAST_K, 0, NB // 2)
         quantize_g(LAST_K, NB // 2, NB)
+        quantize_last_x(1, last_codes[:])
         multiply(LAST_K)
 
         result = [keep.tile([P, DV], F32, name=f"result{db}") for db in range(DB)]

@@ -38,6 +38,7 @@ WHOLE = [(0, PASSES)]
 HALVES = [(0, 2), (2, PASSES)]
 FIRST_PIECES = [[(0, 1), (1, PASSES)], WHOLE, HALVES, [(0, 2), (2, 3), (3, PASSES)]]
 SECOND_PIECES = [WHOLE, WHOLE, HALVES]
+STAGED_ROOM = {1: K_PASS + 2 * D + 2 * (P + DV), 2: K_PASS + 2 * (P + DV), 3: K_PASS}
 
 
 def tile_attend_gvq_rw_w_kernel(tc, zT, cb, cb2, tw, xT, offs, offs2, out):
@@ -45,6 +46,7 @@ def tile_attend_gvq_rw_w_kernel(tc, zT, cb, cb2, tw, xT, offs, offs2, out):
     with ExitStack() as ctx:
         keep = ctx.enter_context(tc.tile_pool(name="keep", bufs=1))
         ring = ctx.enter_context(tc.tile_pool(name="ring", bufs=RING))
+        late = ctx.enter_context(tc.tile_pool(name="late", bufs=1))
         psum = ctx.enter_context(tc.psum_pool(name="psum", bufs=1))
 
         def shared(tag, name, shape, dtype):
@@ -175,7 +177,8 @@ def tile_attend_gvq_rw_w_kernel(tc, zT, cb, cb2, tw, xT, offs, offs2, out):
 
         def weigh(sums, k, nb):
             if nb == LAST_NB and k >= 1:
-                staged = shared("last_staged", f"staged{k}_{nb}", [P, SLOTS, P], BF16)
+                room = late.tile([P, STAGED_ROOM[k]], BF16, offset=0, align_bytes=64, name=f"staged{k}_{nb}")
+                staged = room[:, :K_PASS].rearrange("p (j n) -> p j n", j=SLOTS)
             else:
                 staged = ring.tile([P, SLOTS, P], BF16, tag="staged", name=f"staged{k}_{nb}")
             for j in range(SLOTS):
@@ -226,11 +229,8 @@ def tile_attend_gvq_rw_w_kernel(tc, zT, cb, cb2, tw, xT, offs, offs2, out):
             if nb == 0:
                 negate_z()
 
-        codes_01 = shared("second", "codes_01", [P, 2 * D + 2 * DV], U32)
-        codes_2 = shared("g1", "codes_2", [P, D + DV], U32)
-        codes_3 = shared("g2", "codes_3", [P, D + DV], U32)
-        x_codes = [codes_01[:, :D], codes_01[:, D : 2 * D], codes_2[:, :D], codes_3[:, :D]]
-        g_codes = [codes_01[:, 2 * D : 2 * D + DV], codes_01[:, 2 * D + DV :], codes_2[:, D:], codes_3[:, D:]]
+        x_codes_01 = shared("second", "x_codes_01", [P, 2 * D], U32)
+        g_codes_012 = keep.tile([P, LAST_K, DV], U32, align_bytes=64)
 
         def quantize_x(k0, k1, codes):
             nc.vector.quantize_mx(
@@ -301,15 +301,19 @@ def tile_attend_gvq_rw_w_kernel(tc, zT, cb, cb2, tw, xT, offs, offs2, out):
                         )
                 weigh([slot_sum[:] for slot_sum in sums], k, LAST_NB)
 
-        last_codes = shared(f"g{LAST_K}", "last_codes", [P, P], U32)
-        quantize_x(0, 2, codes_01[:, : 2 * D])
+        x_codes_2 = late.tile([P, D], U32, offset=2 * K_PASS + 4 * (P + DV), align_bytes=64)
+        codes_3 = late.tile([P, P + DV], U32, offset=2 * K_PASS, align_bytes=64)
+        last_codes = late.tile([P, P], U32, offset=0, align_bytes=64)
+        x_codes = [x_codes_01[:, :D], x_codes_01[:, D:], x_codes_2[:], codes_3[:, :P]]
+        g_codes = [g_codes_012[:, k, :] for k in range(LAST_K)] + [codes_3[:, P:]]
+        quantize_x(0, 2, x_codes_01[:])
         for k in range(2):
             quantize_g(k, 0, NB)
             multiply(k)
         quantize_x(2, 3, x_codes[2])
         quantize_g(2, 0, NB)
         multiply(2)
-        quantize_last_x(0, x_codes[LAST_K][:, :P])
+        quantize_last_x(0, x_codes[LAST_K])
         quantize_g(LAST_K, 0, NB // 2)
         quantize_g(LAST_K, NB // 2, NB)
         quantize_last_x(1, last_codes[:])

@@ -36,9 +36,9 @@ WINDOW_BLOCKS = {1: 1, 2: 2, 3: 2, 4: 4}
 PADS = (2, 3)
 WHOLE = [(0, PASSES)]
 HALVES = [(0, 2), (2, PASSES)]
-FIRST_PIECES = [[(0, 1), (1, PASSES)], WHOLE, HALVES, [(0, 2), (2, 3), (3, PASSES)]]
+FIRST_PIECES = [[(0, 1), (1, PASSES)], WHOLE, HALVES, HALVES]
 SECOND_PIECES = [WHOLE, WHOLE, HALVES]
-STAGED_ROOM = {1: K_PASS + 2 * D + 2 * (P + DV), 2: K_PASS + 2 * (P + DV), 3: K_PASS}
+STAGED_ROOM = [K_PASS + 2 * (P + DV) + 6 * D, K_PASS + 2 * (P + DV) + 4 * D, K_PASS + 2 * (P + DV), K_PASS]
 
 
 def tile_attend_gvq_rw_w_kernel(tc, zT, cb, cb2, tw, xT, offs, offs2, out):
@@ -176,14 +176,23 @@ def tile_attend_gvq_rw_w_kernel(tc, zT, cb, cb2, tw, xT, offs, offs2, out):
                 )
 
         def weigh(sums, k, nb):
-            if nb == LAST_NB and k >= 1:
+            if nb == LAST_NB:
                 room = late.tile([P, STAGED_ROOM[k]], BF16, offset=0, align_bytes=64, name=f"staged{k}_{nb}")
                 staged = room[:, :K_PASS].rearrange("p (j n) -> p j n", j=SLOTS)
             else:
                 staged = ring.tile([P, SLOTS, P], BF16, tag="staged", name=f"staged{k}_{nb}")
+            words = g_turned[k][:, nb * K_PASS : (nb + 1) * K_PASS]
+            if nb == LAST_NB and k == LAST_K:
+                pairs = room[:, :K_PASS].rearrange("p (u n e) -> p u e n", u=2, e=2)
+                for j in range(SLOTS):
+                    nc.scalar.activation(pairs[:, j // 2, j % 2, :], sums[j], COPY, scale=neg_w[:, k, j : j + 1])
+                nc.scalar.copy(
+                    words.bitcast(F32).rearrange("p (n u) -> p n u", u=2),
+                    room[:, :K_PASS].bitcast(F32).rearrange("p (u n) -> p n u", u=2),
+                )
+                return
             for j in range(SLOTS):
                 nc.scalar.activation(staged[:, j, :], sums[j], COPY, scale=neg_w[:, k, j : j + 1])
-            words = g_turned[k][:, nb * K_PASS : (nb + 1) * K_PASS]
             nc.scalar.copy(words.rearrange("p (n j) -> p n j", j=SLOTS), staged[:].rearrange("p j n -> p n j"))
 
         def cast_x(db, half):
@@ -229,8 +238,13 @@ def tile_attend_gvq_rw_w_kernel(tc, zT, cb, cb2, tw, xT, offs, offs2, out):
             if nb == 0:
                 negate_z()
 
-        x_codes_01 = shared("second", "x_codes_01", [P, 2 * D], U32)
+        x_codes_0 = late.tile([P, D], U32, offset=2 * K_PASS + 4 * (P + DV) + 8 * D, align_bytes=64)
+        x_codes_12 = late.tile([P, 2 * D], U32, offset=2 * K_PASS + 4 * (P + DV), align_bytes=64)
+        codes_3 = late.tile([P, P + DV], U32, offset=2 * K_PASS, align_bytes=64)
+        last_codes = late.tile([P, P], U32, offset=0, align_bytes=64)
         g_codes_012 = keep.tile([P, LAST_K, DV], U32, align_bytes=64)
+        x_codes = [x_codes_0[:], x_codes_12[:, :D], x_codes_12[:, D:], codes_3[:, :P]]
+        g_codes = [g_codes_012[:, k, :] for k in range(LAST_K)] + [codes_3[:, P:]]
 
         def quantize_x(k0, k1, codes):
             nc.vector.quantize_mx(
@@ -278,7 +292,15 @@ def tile_attend_gvq_rw_w_kernel(tc, zT, cb, cb2, tw, xT, offs, offs2, out):
             for k0, k1 in FIRST_PIECES[LAST_NB]:
                 if k0 == k:
                     gather_into_planes(0, LAST_NB, k0, k1, first)
-            gather_into_planes(1, LAST_NB, k, k + 1, second)
+            if k == LAST_K:
+                quantize_g(0, 0, NB)
+                quantize_x(0, 1, x_codes[0])
+                multiply(0)
+                last_planes = shared("g0", "last_planes", [P, SLOTS, P], F32)
+                picked = last_planes[:].bitcast(U32).rearrange("p j (m r) -> p m j r", r=RUN)
+                nc.vector.tensor_copy(picked, looked_up(1, LAST_NB, k, k + 1))
+            else:
+                gather_into_planes(1, LAST_NB, k, k + 1, second)
             if k < LAST_K:
                 bank = bank_tile(PASSES + k, f"e{k}_{LAST_NB}", [P, SLOTS, P])
                 turn(bank, neg_z, k * P, True, False)
@@ -288,12 +310,12 @@ def tile_attend_gvq_rw_w_kernel(tc, zT, cb, cb2, tw, xT, offs, offs2, out):
             else:
                 free_banks = (PASSES + k, DB, DB + 1, PASSES)
                 sums = [bank_tile(i, f"last{i}", [P, P]) for i in free_banks]
-                terms = (neg_z, first, second)
+                terms = (neg_z[:, :, k * P :], first[:, :, k * P :], last_planes[:])
                 for i, planes in enumerate(terms):
                     for j in range(SLOTS):
                         nc.tensor.matmul(
                             sums[j][:],
-                            planes[:, j, k * P : (k + 1) * P],
+                            planes[:, j, :],
                             ident[:],
                             start=(i == 0),
                             stop=(i == len(terms) - 1),
@@ -301,21 +323,14 @@ def tile_attend_gvq_rw_w_kernel(tc, zT, cb, cb2, tw, xT, offs, offs2, out):
                         )
                 weigh([slot_sum[:] for slot_sum in sums], k, LAST_NB)
 
-        x_codes_2 = late.tile([P, D], U32, offset=2 * K_PASS + 4 * (P + DV), align_bytes=64)
-        codes_3 = late.tile([P, P + DV], U32, offset=2 * K_PASS, align_bytes=64)
-        last_codes = late.tile([P, P], U32, offset=0, align_bytes=64)
-        x_codes = [x_codes_01[:, :D], x_codes_01[:, D:], x_codes_2[:], codes_3[:, :P]]
-        g_codes = [g_codes_012[:, k, :] for k in range(LAST_K)] + [codes_3[:, P:]]
-        quantize_x(0, 2, x_codes_01[:])
-        for k in range(2):
+        quantize_x(1, LAST_K, x_codes_12[:])
+        for k in range(1, LAST_K):
             quantize_g(k, 0, NB)
             multiply(k)
-        quantize_x(2, 3, x_codes[2])
-        quantize_g(2, 0, NB)
-        multiply(2)
         quantize_last_x(0, x_codes[LAST_K])
         quantize_g(LAST_K, 0, NB // 2)
-        quantize_g(LAST_K, NB // 2, NB)
+        quantize_g(LAST_K, NB // 2, LAST_NB)
+        quantize_g(LAST_K, LAST_NB, NB)
         quantize_last_x(1, last_codes[:])
         multiply(LAST_K)
 

@@ -36,9 +36,15 @@ WINDOW_BLOCKS = {1: 1, 2: 2, 3: 2, 4: 4}
 PADS = (2, 3)
 WHOLE = [(0, PASSES)]
 HALVES = [(0, 2), (2, PASSES)]
-FIRST_PIECES = [[(0, 1), (1, PASSES)], WHOLE, HALVES, HALVES]
+FIRST_PIECES = [[(0, 1), (1, PASSES)], WHOLE, HALVES, [(0, 2), (2, 3), (3, PASSES)]]
 SECOND_PIECES = [WHOLE, WHOLE, HALVES]
-STAGED_ROOM = [K_PASS + 2 * (P + DV) + 6 * D, K_PASS + 2 * (P + DV) + 4 * D, K_PASS + 2 * (P + DV), K_PASS]
+SPLIT_K = 2
+SPLIT_WIDTH = DV + DV // 2
+AT_CODES_3 = 2 * K_PASS
+AT_SPLIT_SCALES = AT_CODES_3 + 4 * (P + DV)
+AT_X_SPLIT = AT_SPLIT_SCALES + SPLIT_WIDTH
+AT_X_01 = AT_X_SPLIT + 4 * D
+STAGED_ROOM = [(AT_X_01 + 8 * D) // 2, K_PASS, AT_SPLIT_SCALES // 2, K_PASS]
 
 
 def tile_attend_gvq_rw_w_kernel(tc, zT, cb, cb2, tw, xT, offs, offs2, out):
@@ -62,10 +68,14 @@ def tile_attend_gvq_rw_w_kernel(tc, zT, cb, cb2, tw, xT, offs, offs2, out):
         neg_z = keep.tile([P, SLOTS, T // SLOTS], F32)
         x_raw = [keep.tile([P, T], F32, name=f"x_raw{db}") for db in range(DB)]
         x_pairs = [keep.tile([P, 2, T // 2], BF16, name=f"x_pairs{db}") for db in range(DB)]
-        x_turned = keep.tile([P, PASSES, D * SLOTS], BF16, align_bytes=64)
+        x_turned_01 = keep.tile([P, 2 * D * SLOTS], BF16, align_bytes=64)
+        x_turned_2 = shared("x2", "x_turned_2", [P, D * SLOTS], BF16)
+        x_turned_3 = keep.tile([P, D * SLOTS], BF16, align_bytes=64)
+        x_turned = [x_turned_01[:, : D * SLOTS], x_turned_01[:, D * SLOTS :], x_turned_2[:], x_turned_3[:]]
         x_scales = keep.tile([P, PASSES, D], U8, align_bytes=64)
         g_scales = keep.tile([P, PASSES, DV], U8, align_bytes=64)
         g_turned = [shared(f"g{k}", f"g_turned{k}", [P, NB * K_PASS], BF16) for k in range(PASSES)]
+        split_codes = keep.tile([P, SPLIT_WIDTH], U32, align_bytes=64)
         ident = keep.tile([P, P], F32)
         tw_rows = keep.tile([P, K_PASS], F32)
         tw_planes = keep.tile([P, SLOTS, P], F32)
@@ -82,6 +92,7 @@ def tile_attend_gvq_rw_w_kernel(tc, zT, cb, cb2, tw, xT, offs, offs2, out):
         for i in range(PADS[1]):
             clear_pad(1, i)
         clear_pad(0, 1)
+        nc.gpsimd.memset(split_codes[:, DV // 2 : DV], 0)
         nc.vector.memset(tw_rows[:], 0.0)
 
         def load_book(b, nb):
@@ -209,7 +220,7 @@ def tile_attend_gvq_rw_w_kernel(tc, zT, cb, cb2, tw, xT, offs, offs2, out):
                     words = x_pairs[db][:, u, :].bitcast(F32)
                     nc.tensor.transpose(bank[:, db, u, :], words[:, k * P : (k + 1) * P], ident[:])
             nc.scalar.copy(
-                x_turned[:, k, :].bitcast(F32).rearrange("p (b d u) -> p b d u", b=DB, u=2),
+                x_turned[k].bitcast(F32).rearrange("p (b d u) -> p b d u", b=DB, u=2),
                 bank[:].rearrange("p b u d -> p b d u"),
             )
 
@@ -238,51 +249,48 @@ def tile_attend_gvq_rw_w_kernel(tc, zT, cb, cb2, tw, xT, offs, offs2, out):
             if nb == 0:
                 negate_z()
 
-        x_codes_0 = late.tile([P, D], U32, offset=2 * K_PASS + 4 * (P + DV) + 8 * D, align_bytes=64)
-        x_codes_12 = late.tile([P, 2 * D], U32, offset=2 * K_PASS + 4 * (P + DV), align_bytes=64)
-        codes_3 = late.tile([P, P + DV], U32, offset=2 * K_PASS, align_bytes=64)
+        codes_3 = late.tile([P, P + DV], U32, offset=AT_CODES_3, align_bytes=64)
+        split_scales = late.tile([P, SPLIT_WIDTH], U8, offset=AT_SPLIT_SCALES, align_bytes=64)
+        x_codes_2 = late.tile([P, D], U32, offset=AT_X_SPLIT, align_bytes=64)
+        x_codes_01 = late.tile([P, 2 * D], U32, offset=AT_X_01, align_bytes=64)
         last_codes = late.tile([P, P], U32, offset=0, align_bytes=64)
-        g_codes_012 = keep.tile([P, LAST_K, DV], U32, align_bytes=64)
-        x_codes = [x_codes_0[:], x_codes_12[:, :D], x_codes_12[:, D:], codes_3[:, :P]]
-        g_codes = [g_codes_012[:, k, :] for k in range(LAST_K)] + [codes_3[:, P:]]
+        g_codes_01 = keep.tile([P, 2, DV], U32, align_bytes=64)
+        x_codes = [x_codes_01[:, :D], x_codes_01[:, D:], x_codes_2[:], codes_3[:, :P]]
 
-        def quantize_x(k0, k1, codes):
-            nc.vector.quantize_mx(
-                out=codes.bitcast(E4M3),
-                scales=x_scales[:, k0:k1, :].rearrange("p k d -> p (k d)"),
-                in_=x_turned[:, k0:k1, :].rearrange("p k c -> p (k c)"),
-            )
+        def quantize(fmt, codes, scales, values):
+            nc.vector.quantize_mx(out=codes.bitcast(fmt), scales=scales, in_=values)
 
         def quantize_last_x(db, codes):
-            nc.vector.quantize_mx(
-                out=codes.bitcast(E4M3),
-                scales=x_scales[:, LAST_K, db * P : (db + 1) * P],
-                in_=x_turned[:, LAST_K, db * K_PASS : (db + 1) * K_PASS],
-            )
+            quantize(E4M3, codes, x_scales[:, LAST_K, db * P : (db + 1) * P], x_turned[LAST_K][:, db * K_PASS : (db + 1) * K_PASS])
 
-        def quantize_g(k, nb0, nb1):
-            nc.vector.quantize_mx(
-                out=g_codes[k][:, nb0 * P : nb1 * P].bitcast(E5M2),
-                scales=g_scales[:, k, nb0 * P : nb1 * P],
-                in_=g_turned[k][:, nb0 * K_PASS : nb1 * K_PASS],
-            )
+        def quantize_last_g(nb0, nb1):
+            cols = slice(nb0 * P, nb1 * P)
+            quantize(E5M2, codes_3[:, P:][:, cols], g_scales[:, LAST_K, cols], g_turned[LAST_K][:, nb0 * K_PASS : nb1 * K_PASS])
+
+        def quantize_split(half):
+            cols = slice(half * DV, half * DV + DV // 2)
+            quantize(E5M2, split_codes[:, cols], split_scales[:, cols], g_turned[SPLIT_K][:, half * 2 * K_PASS : (half + 1) * 2 * K_PASS])
 
         def stationary(k, db):
             if k == LAST_K and db == DB - 1:
                 return last_codes[:]
             return x_codes[k][:, db * P : (db + 1) * P]
 
-        def multiply(k):
+        def multiply(k, codes, scales, start, stop):
             for db in range(DB):
                 nc.tensor.matmul_mx(
                     out=acc[db][:],
                     lhsT=stationary(k, db).bitcast(E4M3),
                     lhsT_scale=x_scales[:, k, db * P : (db + 1) * P],
-                    rhs=g_codes[k].bitcast(E5M2),
-                    rhs_scale=g_scales[:, k, :],
-                    start=(k == 0),
-                    stop=(k == LAST_K),
+                    rhs=codes.bitcast(E5M2),
+                    rhs_scale=scales,
+                    start=start,
+                    stop=stop,
                 )
+
+        def multiply_split(half):
+            cols = slice(half * DV // 2, half * DV // 2 + DV)
+            multiply(SPLIT_K, split_codes[:, cols], split_scales[:, cols], half == 0, False)
 
         acc = [bank_tile(db, f"acc{db}", [P, DV]) for db in range(DB)]
         both = shared(f"z{LAST_NB - 1}_1", "both_last", [P, 2 * T], F32)
@@ -293,10 +301,11 @@ def tile_attend_gvq_rw_w_kernel(tc, zT, cb, cb2, tw, xT, offs, offs2, out):
                 if k0 == k:
                     gather_into_planes(0, LAST_NB, k0, k1, first)
             if k == LAST_K:
-                quantize_g(0, 0, NB)
-                quantize_x(0, 1, x_codes[0])
-                multiply(0)
-                last_planes = shared("g0", "last_planes", [P, SLOTS, P], F32)
+                nc.gpsimd.memset(split_scales[:, DV // 2 : DV].bitcast(U32), 0)
+                quantize(E4M3, x_codes[SPLIT_K], x_scales[:, SPLIT_K, :], x_turned[SPLIT_K])
+                quantize_split(0)
+                multiply_split(0)
+                last_planes = shared("x2", "last_planes", [P, SLOTS, P], F32)
                 picked = last_planes[:].bitcast(U32).rearrange("p j (m r) -> p m j r", r=RUN)
                 nc.vector.tensor_copy(picked, looked_up(1, LAST_NB, k, k + 1))
             else:
@@ -323,16 +332,18 @@ def tile_attend_gvq_rw_w_kernel(tc, zT, cb, cb2, tw, xT, offs, offs2, out):
                         )
                 weigh([slot_sum[:] for slot_sum in sums], k, LAST_NB)
 
-        quantize_x(1, LAST_K, x_codes_12[:])
-        for k in range(1, LAST_K):
-            quantize_g(k, 0, NB)
-            multiply(k)
+        quantize(E4M3, x_codes_01[:], x_scales[:, 0:2, :].rearrange("p k d -> p (k d)"), x_turned_01[:])
+        for k in range(2):
+            quantize(E5M2, g_codes_01[:, k, :], g_scales[:, k, :], g_turned[k][:])
+            multiply(k, g_codes_01[:, k, :], g_scales[:, k, :], False, False)
+        quantize_split(1)
+        multiply_split(1)
         quantize_last_x(0, x_codes[LAST_K])
-        quantize_g(LAST_K, 0, NB // 2)
-        quantize_g(LAST_K, NB // 2, LAST_NB)
-        quantize_g(LAST_K, LAST_NB, NB)
+        quantize_last_g(0, NB // 2)
+        quantize_last_g(NB // 2, LAST_NB)
+        quantize_last_g(LAST_NB, NB)
         quantize_last_x(1, last_codes[:])
-        multiply(LAST_K)
+        multiply(LAST_K, codes_3[:, P:], g_scales[:, LAST_K, :], False, True)
 
         result = [keep.tile([P, DV], F32, name=f"result{db}") for db in range(DB)]
         for half in range(2):

@@ -38,13 +38,13 @@ WHOLE = [(0, PASSES)]
 HALVES = [(0, 2), (2, PASSES)]
 FIRST_PIECES = [[(0, 1), (1, PASSES)], WHOLE, HALVES, [(0, 2), (2, 3), (3, PASSES)]]
 SECOND_PIECES = [WHOLE, WHOLE, HALVES]
-SPLIT_K = 2
+SPLIT_K = 0
 SPLIT_WIDTH = DV + DV // 2
 AT_CODES_3 = 2 * K_PASS
 AT_SPLIT_SCALES = AT_CODES_3 + 4 * (P + DV)
 AT_X_SPLIT = AT_SPLIT_SCALES + SPLIT_WIDTH
-AT_X_01 = AT_X_SPLIT + 4 * D
-STAGED_ROOM = [(AT_X_01 + 8 * D) // 2, K_PASS, AT_SPLIT_SCALES // 2, K_PASS]
+AT_X_12 = AT_X_SPLIT + 4 * D
+STAGED_ROOM = [(AT_X_12 + 8 * D) // 2, K_PASS, AT_SPLIT_SCALES // 2, K_PASS]
 
 
 def tile_attend_gvq_rw_w_kernel(tc, zT, cb, cb2, tw, xT, offs, offs2, out):
@@ -68,10 +68,10 @@ def tile_attend_gvq_rw_w_kernel(tc, zT, cb, cb2, tw, xT, offs, offs2, out):
         neg_z = keep.tile([P, SLOTS, T // SLOTS], F32)
         x_raw = [keep.tile([P, T], F32, name=f"x_raw{db}") for db in range(DB)]
         x_pairs = [keep.tile([P, 2, T // 2], BF16, name=f"x_pairs{db}") for db in range(DB)]
-        x_turned_01 = keep.tile([P, 2 * D * SLOTS], BF16, align_bytes=64)
-        x_turned_2 = shared("x2", "x_turned_2", [P, D * SLOTS], BF16)
+        x_turned_12 = keep.tile([P, 2 * D * SLOTS], BF16, align_bytes=64)
+        x_turned_0 = shared("x0", "x_turned_0", [P, D * SLOTS], BF16)
         x_turned_3 = keep.tile([P, D * SLOTS], BF16, align_bytes=64)
-        x_turned = [x_turned_01[:, : D * SLOTS], x_turned_01[:, D * SLOTS :], x_turned_2[:], x_turned_3[:]]
+        x_turned = [x_turned_0[:], x_turned_12[:, : D * SLOTS], x_turned_12[:, D * SLOTS :], x_turned_3[:]]
         x_scales = keep.tile([P, PASSES, D], U8, align_bytes=64)
         g_scales = keep.tile([P, PASSES, DV], U8, align_bytes=64)
         g_turned = [shared(f"g{k}", f"g_turned{k}", [P, NB * K_PASS], BF16) for k in range(PASSES)]
@@ -251,11 +251,11 @@ def tile_attend_gvq_rw_w_kernel(tc, zT, cb, cb2, tw, xT, offs, offs2, out):
 
         codes_3 = late.tile([P, P + DV], U32, offset=AT_CODES_3, align_bytes=64)
         split_scales = late.tile([P, SPLIT_WIDTH], U8, offset=AT_SPLIT_SCALES, align_bytes=64)
-        x_codes_2 = late.tile([P, D], U32, offset=AT_X_SPLIT, align_bytes=64)
-        x_codes_01 = late.tile([P, 2 * D], U32, offset=AT_X_01, align_bytes=64)
+        x_codes_0 = late.tile([P, D], U32, offset=AT_X_SPLIT, align_bytes=64)
+        x_codes_12 = late.tile([P, 2 * D], U32, offset=AT_X_12, align_bytes=64)
         last_codes = late.tile([P, P], U32, offset=0, align_bytes=64)
-        g_codes_01 = keep.tile([P, 2, DV], U32, align_bytes=64)
-        x_codes = [x_codes_01[:, :D], x_codes_01[:, D:], x_codes_2[:], codes_3[:, :P]]
+        g_codes_12 = keep.tile([P, 2, DV], U32, align_bytes=64)
+        x_codes = [x_codes_0[:], x_codes_12[:, :D], x_codes_12[:, D:], codes_3[:, :P]]
 
         def quantize(fmt, codes, scales, values):
             nc.vector.quantize_mx(out=codes.bitcast(fmt), scales=scales, in_=values)
@@ -305,7 +305,7 @@ def tile_attend_gvq_rw_w_kernel(tc, zT, cb, cb2, tw, xT, offs, offs2, out):
                 quantize(E4M3, x_codes[SPLIT_K], x_scales[:, SPLIT_K, :], x_turned[SPLIT_K])
                 quantize_split(0)
                 multiply_split(0)
-                last_planes = shared("x2", "last_planes", [P, SLOTS, P], F32)
+                last_planes = shared("x0", "last_planes", [P, SLOTS, P], F32)
                 picked = last_planes[:].bitcast(U32).rearrange("p j (m r) -> p m j r", r=RUN)
                 nc.vector.tensor_copy(picked, looked_up(1, LAST_NB, k, k + 1))
             else:
@@ -332,12 +332,12 @@ def tile_attend_gvq_rw_w_kernel(tc, zT, cb, cb2, tw, xT, offs, offs2, out):
                         )
                 weigh([slot_sum[:] for slot_sum in sums], k, LAST_NB)
 
-        quantize(E4M3, x_codes_01[:], x_scales[:, 0:2, :].rearrange("p k d -> p (k d)"), x_turned_01[:])
-        for k in range(2):
-            quantize(E5M2, g_codes_01[:, k, :], g_scales[:, k, :], g_turned[k][:])
-            multiply(k, g_codes_01[:, k, :], g_scales[:, k, :], False, False)
         quantize_split(1)
         multiply_split(1)
+        quantize(E4M3, x_codes_12[:], x_scales[:, 1:LAST_K, :].rearrange("p k d -> p (k d)"), x_turned_12[:])
+        for k in range(1, LAST_K):
+            quantize(E5M2, g_codes_12[:, k - 1, :], g_scales[:, k, :], g_turned[k][:])
+            multiply(k, g_codes_12[:, k - 1, :], g_scales[:, k, :], False, False)
         quantize_last_x(0, x_codes[LAST_K])
         quantize_last_g(0, NB // 2)
         quantize_last_g(NB // 2, LAST_NB)
@@ -353,4 +353,5 @@ def tile_attend_gvq_rw_w_kernel(tc, zT, cb, cb2, tw, xT, offs, offs2, out):
         for half in range(2):
             cols = slice(half * DV // 2, (half + 1) * DV // 2)
             nc.scalar.copy(result[1][:, cols], acc[1][:, cols])
-            nc.sync.dma_start(out=out[P : 2 * P, cols], in_=result[1][:, cols])
+            queue = nc.scalar if half == 1 else nc.sync
+            queue.dma_start(out=out[P : 2 * P, cols], in_=result[1][:, cols])

@@ -38,13 +38,13 @@ WHOLE = [(0, PASSES)]
 HALVES = [(0, 2), (2, PASSES)]
 FIRST_PIECES = [[(0, 1), (1, PASSES)], WHOLE, HALVES, [(0, 2), (2, 3), (3, PASSES)]]
 SECOND_PIECES = [WHOLE, WHOLE, HALVES]
-SPLIT_K = 0
-SPLIT_WIDTH = DV + DV // 2
+SPLIT_WIDTH = 2 * DV - P
 AT_CODES_3 = 2 * K_PASS
 AT_SPLIT_SCALES = AT_CODES_3 + 4 * (P + DV)
-AT_X_SPLIT = AT_SPLIT_SCALES + SPLIT_WIDTH
-AT_X_12 = AT_X_SPLIT + 4 * D
-STAGED_ROOM = [(AT_X_12 + 8 * D) // 2, K_PASS, AT_SPLIT_SCALES // 2, K_PASS]
+AT_X_0 = AT_SPLIT_SCALES + SPLIT_WIDTH
+AT_X_12 = AT_X_0 + 4 * D
+LATE_END = AT_X_12 + 8 * D
+STAGING_SPAN = [LATE_END, AT_CODES_3, AT_SPLIT_SCALES, AT_CODES_3]
 
 
 def tile_attend_gvq_rw_w_kernel(tc, zT, cb, cb2, tw, xT, offs, offs2, out):
@@ -68,13 +68,11 @@ def tile_attend_gvq_rw_w_kernel(tc, zT, cb, cb2, tw, xT, offs, offs2, out):
         neg_z = keep.tile([P, SLOTS, T // SLOTS], F32)
         x_raw = [keep.tile([P, T], F32, name=f"x_raw{db}") for db in range(DB)]
         x_pairs = [keep.tile([P, 2, T // 2], BF16, name=f"x_pairs{db}") for db in range(DB)]
-        x_turned_12 = keep.tile([P, 2 * D * SLOTS], BF16, align_bytes=64)
-        x_turned_0 = shared("x0", "x_turned_0", [P, D * SLOTS], BF16)
-        x_turned_3 = keep.tile([P, D * SLOTS], BF16, align_bytes=64)
-        x_turned = [x_turned_0[:], x_turned_12[:, : D * SLOTS], x_turned_12[:, D * SLOTS :], x_turned_3[:]]
+        x_turned = keep.tile([P, PASSES, D * SLOTS], BF16, align_bytes=64)
         x_scales = keep.tile([P, PASSES, D], U8, align_bytes=64)
-        g_scales = keep.tile([P, PASSES, DV], U8, align_bytes=64)
-        g_turned = [shared(f"g{k}", f"g_turned{k}", [P, NB * K_PASS], BF16) for k in range(PASSES)]
+        g_scales = keep.tile([P, LAST_K, DV], U8, align_bytes=64)
+        g_early = shared("g_early", "g_early", [P, K_PASS], BF16)
+        g_turned = [keep.tile([P, NB * K_PASS], BF16, align_bytes=64, name=f"g_turned{k}") for k in range(PASSES)]
         split_codes = keep.tile([P, SPLIT_WIDTH], U32, align_bytes=64)
         ident = keep.tile([P, P], F32)
         tw_rows = keep.tile([P, K_PASS], F32)
@@ -92,7 +90,7 @@ def tile_attend_gvq_rw_w_kernel(tc, zT, cb, cb2, tw, xT, offs, offs2, out):
         for i in range(PADS[1]):
             clear_pad(1, i)
         clear_pad(0, 1)
-        nc.gpsimd.memset(split_codes[:, DV // 2 : DV], 0)
+        nc.gpsimd.memset(split_codes[:, P:DV], 0)
         nc.vector.memset(tw_rows[:], 0.0)
 
         def load_book(b, nb):
@@ -172,8 +170,8 @@ def tile_attend_gvq_rw_w_kernel(tc, zT, cb, cb2, tw, xT, offs, offs2, out):
             nc.vector.tensor_copy(first[:, k0 * K_PASS : k1 * K_PASS].bitcast(U32), looked_up(0, nb, k0, k1))
 
         def gather_into_planes(b, nb, k0, k1, planes):
-            picked = planes[:, :, k0 * P : k1 * P].bitcast(U32)
-            nc.vector.tensor_copy(picked.rearrange("p j (m r) -> p m j r", r=RUN), looked_up(b, nb, k0, k1))
+            picked = planes.bitcast(U32).rearrange("p j (m r) -> p m j r", r=RUN)
+            nc.vector.tensor_copy(picked, looked_up(b, nb, k0, k1))
 
         def turn(bank, planes, col, start, stop):
             for j in range(SLOTS):
@@ -186,25 +184,32 @@ def tile_attend_gvq_rw_w_kernel(tc, zT, cb, cb2, tw, xT, offs, offs2, out):
                     is_transpose=True,
                 )
 
+        def g_words(k, nb0, nb1):
+            if k == 0 and nb0 == 0:
+                return g_early[:]
+            return g_turned[k][:, nb0 * K_PASS : nb1 * K_PASS]
+
+        def staging(k, nb):
+            if nb < LAST_NB:
+                return ring.tile([P, K_PASS], BF16, tag="staged", name=f"staged{k}_{nb}")[:]
+            span = late.tile([P, STAGING_SPAN[k] // 2], BF16, offset=0, align_bytes=64, name=f"staged{k}_{nb}")
+            return span[:, :K_PASS]
+
         def weigh(sums, k, nb):
-            if nb == LAST_NB:
-                room = late.tile([P, STAGED_ROOM[k]], BF16, offset=0, align_bytes=64, name=f"staged{k}_{nb}")
-                staged = room[:, :K_PASS].rearrange("p (j n) -> p j n", j=SLOTS)
-            else:
-                staged = ring.tile([P, SLOTS, P], BF16, tag="staged", name=f"staged{k}_{nb}")
-            words = g_turned[k][:, nb * K_PASS : (nb + 1) * K_PASS]
-            if nb == LAST_NB and k == LAST_K:
-                pairs = room[:, :K_PASS].rearrange("p (u n e) -> p u e n", u=2, e=2)
-                for j in range(SLOTS):
-                    nc.scalar.activation(pairs[:, j // 2, j % 2, :], sums[j], COPY, scale=neg_w[:, k, j : j + 1])
-                nc.scalar.copy(
-                    words.bitcast(F32).rearrange("p (n u) -> p n u", u=2),
-                    room[:, :K_PASS].bitcast(F32).rearrange("p (u n) -> p n u", u=2),
-                )
-                return
+            staged = staging(k, nb).rearrange("p (j n) -> p j n", j=SLOTS)
             for j in range(SLOTS):
                 nc.scalar.activation(staged[:, j, :], sums[j], COPY, scale=neg_w[:, k, j : j + 1])
-            nc.scalar.copy(words.rearrange("p (n j) -> p n j", j=SLOTS), staged[:].rearrange("p j n -> p n j"))
+            nc.scalar.copy(g_words(k, nb, nb + 1).rearrange("p (n j) -> p n j", j=SLOTS), staged.rearrange("p j n -> p n j"))
+
+        def weigh_in_pairs(sums, k, nb):
+            staged = staging(k, nb)
+            pairs = staged.rearrange("p (u n e) -> p u e n", u=2, e=2)
+            for j in range(SLOTS):
+                nc.scalar.activation(pairs[:, j // 2, j % 2, :], sums[j], COPY, scale=neg_w[:, k, j : j + 1])
+            nc.scalar.copy(
+                g_words(k, nb, nb + 1).bitcast(F32).rearrange("p (n u) -> p n u", u=2),
+                staged.bitcast(F32).rearrange("p (u n) -> p n u", u=2),
+            )
 
         def cast_x(db, half):
             cols = slice(half * T // 2, (half + 1) * T // 2)
@@ -220,7 +225,7 @@ def tile_attend_gvq_rw_w_kernel(tc, zT, cb, cb2, tw, xT, offs, offs2, out):
                     words = x_pairs[db][:, u, :].bitcast(F32)
                     nc.tensor.transpose(bank[:, db, u, :], words[:, k * P : (k + 1) * P], ident[:])
             nc.scalar.copy(
-                x_turned[k].bitcast(F32).rearrange("p (b d u) -> p b d u", b=DB, u=2),
+                x_turned[:, k, :].bitcast(F32).rearrange("p (b d u) -> p b d u", b=DB, u=2),
                 bank[:].rearrange("p b u d -> p b d u"),
             )
 
@@ -238,7 +243,7 @@ def tile_attend_gvq_rw_w_kernel(tc, zT, cb, cb2, tw, xT, offs, offs2, out):
                 gather_in_token_order(nb, k0, k1, first)
             second = shared("z0_0" if nb == 1 else "second", f"second{nb}", [P, SLOTS, T // SLOTS], F32)
             for k0, k1 in SECOND_PIECES[nb]:
-                gather_into_planes(1, nb, k0, k1, second)
+                gather_into_planes(1, nb, k0, k1, second[:, :, k0 * P : k1 * P])
             for half in range(2):
                 diff = minus_z(first, nb, half)
                 for k in (2 * half, 2 * half + 1):
@@ -251,36 +256,41 @@ def tile_attend_gvq_rw_w_kernel(tc, zT, cb, cb2, tw, xT, offs, offs2, out):
 
         codes_3 = late.tile([P, P + DV], U32, offset=AT_CODES_3, align_bytes=64)
         split_scales = late.tile([P, SPLIT_WIDTH], U8, offset=AT_SPLIT_SCALES, align_bytes=64)
-        x_codes_0 = late.tile([P, D], U32, offset=AT_X_SPLIT, align_bytes=64)
+        x_codes_0 = late.tile([P, D], U32, offset=AT_X_0, align_bytes=64)
         x_codes_12 = late.tile([P, 2 * D], U32, offset=AT_X_12, align_bytes=64)
-        last_codes = late.tile([P, P], U32, offset=0, align_bytes=64)
+        last_x_codes = late.tile([P, P], U32, offset=0, align_bytes=64)
         g_codes_12 = keep.tile([P, 2, DV], U32, align_bytes=64)
-        x_codes = [x_codes_0[:], x_codes_12[:, :D], x_codes_12[:, D:], codes_3[:, :P]]
+        x_codes = [
+            [x_codes_0[:, :P], x_codes_0[:, P:]],
+            [x_codes_12[:, :P], x_codes_12[:, P:D]],
+            [x_codes_12[:, D : D + P], x_codes_12[:, D + P :]],
+            [codes_3[:, :P], last_x_codes[:]],
+        ]
+        g_codes_3 = codes_3[:, P:]
 
-        def quantize(fmt, codes, scales, values):
-            nc.vector.quantize_mx(out=codes.bitcast(fmt), scales=scales, in_=values)
+        def quantize_x(k0, k1, codes):
+            nc.vector.quantize_mx(
+                out=codes.bitcast(E4M3),
+                scales=x_scales[:, k0:k1, :].rearrange("p k d -> p (k d)"),
+                in_=x_turned[:, k0:k1, :].rearrange("p k c -> p (k c)"),
+            )
 
-        def quantize_last_x(db, codes):
-            quantize(E4M3, codes, x_scales[:, LAST_K, db * P : (db + 1) * P], x_turned[LAST_K][:, db * K_PASS : (db + 1) * K_PASS])
+        def quantize_last_x(db):
+            nc.vector.quantize_mx(
+                out=x_codes[LAST_K][db].bitcast(E4M3),
+                scales=x_scales[:, LAST_K, db * P : (db + 1) * P],
+                in_=x_turned[:, LAST_K, db * K_PASS : (db + 1) * K_PASS],
+            )
 
-        def quantize_last_g(nb0, nb1):
+        def quantize_g(k, nb0, nb1, codes, scales):
             cols = slice(nb0 * P, nb1 * P)
-            quantize(E5M2, codes_3[:, P:][:, cols], g_scales[:, LAST_K, cols], g_turned[LAST_K][:, nb0 * K_PASS : nb1 * K_PASS])
-
-        def quantize_split(half):
-            cols = slice(half * DV, half * DV + DV // 2)
-            quantize(E5M2, split_codes[:, cols], split_scales[:, cols], g_turned[SPLIT_K][:, half * 2 * K_PASS : (half + 1) * 2 * K_PASS])
-
-        def stationary(k, db):
-            if k == LAST_K and db == DB - 1:
-                return last_codes[:]
-            return x_codes[k][:, db * P : (db + 1) * P]
+            nc.vector.quantize_mx(out=codes[:, cols].bitcast(E5M2), scales=scales[:, cols], in_=g_words(k, nb0, nb1))
 
         def multiply(k, codes, scales, start, stop):
             for db in range(DB):
                 nc.tensor.matmul_mx(
                     out=acc[db][:],
-                    lhsT=stationary(k, db).bitcast(E4M3),
+                    lhsT=x_codes[k][db].bitcast(E4M3),
                     lhsT_scale=x_scales[:, k, db * P : (db + 1) * P],
                     rhs=codes.bitcast(E5M2),
                     rhs_scale=scales,
@@ -288,9 +298,8 @@ def tile_attend_gvq_rw_w_kernel(tc, zT, cb, cb2, tw, xT, offs, offs2, out):
                     stop=stop,
                 )
 
-        def multiply_split(half):
-            cols = slice(half * DV // 2, half * DV // 2 + DV)
-            multiply(SPLIT_K, split_codes[:, cols], split_scales[:, cols], half == 0, False)
+        early_part = (split_codes[:, :DV], split_scales[:, :DV])
+        late_part = (split_codes[:, SPLIT_WIDTH - DV :], split_scales[:, SPLIT_WIDTH - DV :])
 
         acc = [bank_tile(db, f"acc{db}", [P, DV]) for db in range(DB)]
         both = shared(f"z{LAST_NB - 1}_1", "both_last", [P, 2 * T], F32)
@@ -299,59 +308,58 @@ def tile_attend_gvq_rw_w_kernel(tc, zT, cb, cb2, tw, xT, offs, offs2, out):
         for k in range(PASSES):
             for k0, k1 in FIRST_PIECES[LAST_NB]:
                 if k0 == k:
-                    gather_into_planes(0, LAST_NB, k0, k1, first)
-            if k == LAST_K:
-                nc.gpsimd.memset(split_scales[:, DV // 2 : DV].bitcast(U32), 0)
-                quantize(E4M3, x_codes[SPLIT_K], x_scales[:, SPLIT_K, :], x_turned[SPLIT_K])
-                quantize_split(0)
-                multiply_split(0)
-                last_planes = shared("x0", "last_planes", [P, SLOTS, P], F32)
-                picked = last_planes[:].bitcast(U32).rearrange("p j (m r) -> p m j r", r=RUN)
-                nc.vector.tensor_copy(picked, looked_up(1, LAST_NB, k, k + 1))
-            else:
-                gather_into_planes(1, LAST_NB, k, k + 1, second)
+                    gather_into_planes(0, LAST_NB, k0, k1, first[:, :, k0 * P : k1 * P])
             if k < LAST_K:
+                gather_into_planes(1, LAST_NB, k, k + 1, second[:, :, k * P : (k + 1) * P])
                 bank = bank_tile(PASSES + k, f"e{k}_{LAST_NB}", [P, SLOTS, P])
                 turn(bank, neg_z, k * P, True, False)
                 turn(bank, first, k * P, False, False)
                 turn(bank, second, k * P, False, True)
                 weigh([bank[:, j, :] for j in range(SLOTS)], k, LAST_NB)
-            else:
-                free_banks = (PASSES + k, DB, DB + 1, PASSES)
-                sums = [bank_tile(i, f"last{i}", [P, P]) for i in free_banks]
-                terms = (neg_z[:, :, k * P :], first[:, :, k * P :], last_planes[:])
-                for i, planes in enumerate(terms):
-                    for j in range(SLOTS):
-                        nc.tensor.matmul(
-                            sums[j][:],
-                            planes[:, j, :],
-                            ident[:],
-                            start=(i == 0),
-                            stop=(i == len(terms) - 1),
-                            is_transpose=True,
-                        )
-                weigh([slot_sum[:] for slot_sum in sums], k, LAST_NB)
 
-        quantize_split(1)
-        multiply_split(1)
-        quantize(E4M3, x_codes_12[:], x_scales[:, 1:LAST_K, :].rearrange("p k d -> p (k d)"), x_turned_12[:])
+        nc.gpsimd.memset(split_scales[:, P:DV].bitcast(U32), 0)
+        quantize_g(0, 0, 1, *early_part)
+        quantize_x(0, 1, x_codes_0[:])
+        multiply(0, *early_part, True, False)
+
+        last_planes = shared("g_early", "last_planes", [P, SLOTS, P], F32)
+        gather_into_planes(1, LAST_NB, LAST_K, PASSES, last_planes[:])
+        free_banks = (PASSES + LAST_K, DB, DB + 1, PASSES)
+        sums = [bank_tile(i, f"last{i}", [P, P]) for i in free_banks]
+        terms = (neg_z[:, :, LAST_K * P :], first[:, :, LAST_K * P :], last_planes[:])
+        for i, planes in enumerate(terms):
+            for j in range(SLOTS):
+                nc.tensor.matmul(
+                    sums[j][:],
+                    planes[:, j, :],
+                    ident[:],
+                    start=(i == 0),
+                    stop=(i == len(terms) - 1),
+                    is_transpose=True,
+                )
+        weigh_in_pairs([slot_sum[:] for slot_sum in sums], LAST_K, LAST_NB)
+
+        quantize_g(0, 1, 2, *late_part)
+        quantize_g(0, 2, NB, *late_part)
+        multiply(0, *late_part, False, False)
+        quantize_x(1, LAST_K, x_codes_12[:])
         for k in range(1, LAST_K):
-            quantize(E5M2, g_codes_12[:, k - 1, :], g_scales[:, k, :], g_turned[k][:])
-            multiply(k, g_codes_12[:, k - 1, :], g_scales[:, k, :], False, False)
-        quantize_last_x(0, x_codes[LAST_K])
-        quantize_last_g(0, NB // 2)
-        quantize_last_g(NB // 2, LAST_NB)
-        quantize_last_g(LAST_NB, NB)
-        quantize_last_x(1, last_codes[:])
-        multiply(LAST_K, codes_3[:, P:], g_scales[:, LAST_K, :], False, True)
+            quantize_g(k, 0, NB, g_codes_12[:, k - 1, :], g_scales[:, k - 1, :])
+            multiply(k, g_codes_12[:, k - 1, :], g_scales[:, k - 1, :], False, False)
+        last_scales = g_scales[:, LAST_K - 1, :]
+        quantize_last_x(0)
+        quantize_g(LAST_K, 0, 2, g_codes_3, last_scales)
+        quantize_g(LAST_K, 2, LAST_NB, g_codes_3, last_scales)
+        quantize_g(LAST_K, LAST_NB, NB, g_codes_3, last_scales)
+        quantize_last_x(1)
+        multiply(LAST_K, g_codes_3, last_scales, False, True)
 
         result = [keep.tile([P, DV], F32, name=f"result{db}") for db in range(DB)]
         for half in range(2):
             cols = slice(half * DV // 2, (half + 1) * DV // 2)
             nc.vector.tensor_copy(result[0][:, cols], acc[0][:, cols])
             nc.sync.dma_start(out=out[0:P, cols], in_=result[0][:, cols])
-        for half in range(2):
+        for half, queue in enumerate((nc.sync, nc.scalar)):
             cols = slice(half * DV // 2, (half + 1) * DV // 2)
             nc.scalar.copy(result[1][:, cols], acc[1][:, cols])
-            queue = nc.scalar if half == 1 else nc.sync
             queue.dma_start(out=out[P : 2 * P, cols], in_=result[1][:, cols])

@@ -36,7 +36,7 @@ WINDOW_BLOCKS = {1: 1, 2: 2, 3: 2, 4: 4}
 PADS = (2, 3)
 WHOLE = [(0, PASSES)]
 HALVES = [(0, 2), (2, PASSES)]
-FIRST_PIECES = [[(0, 1), (1, PASSES)], WHOLE, HALVES, [(0, 2), (2, 3), (3, PASSES)]]
+FIRST_PIECES = [[(0, 1), (1, PASSES)], WHOLE, HALVES]
 SECOND_PIECES = [WHOLE, WHOLE, HALVES]
 SPLIT_WIDTH = 2 * DV - P
 AT_CODES_3 = 2 * K_PASS
@@ -71,7 +71,7 @@ def tile_attend_gvq_rw_w_kernel(tc, zT, cb, cb2, tw, xT, offs, offs2, out):
         x_turned = keep.tile([P, PASSES, D * SLOTS], BF16, align_bytes=64)
         x_scales = keep.tile([P, PASSES, D], U8, align_bytes=64)
         g_scales = keep.tile([P, LAST_K, DV], U8, align_bytes=64)
-        g_early = shared("g_early", "g_early", [P, K_PASS], BF16)
+        g_early = [shared(f"g_early{nb}", f"g_early{nb}", [P, K_PASS], BF16) for nb in range(2)]
         g_turned = [keep.tile([P, NB * K_PASS], BF16, align_bytes=64, name=f"g_turned{k}") for k in range(PASSES)]
         split_codes = keep.tile([P, SPLIT_WIDTH], U32, align_bytes=64)
         ident = keep.tile([P, P], F32)
@@ -185,8 +185,8 @@ def tile_attend_gvq_rw_w_kernel(tc, zT, cb, cb2, tw, xT, offs, offs2, out):
                 )
 
         def g_words(k, nb0, nb1):
-            if k == 0 and nb0 == 0:
-                return g_early[:]
+            if k == 0 and nb0 < 2:
+                return g_early[nb0][:]
             return g_turned[k][:, nb0 * K_PASS : nb1 * K_PASS]
 
         def staging(k, nb):
@@ -305,43 +305,40 @@ def tile_attend_gvq_rw_w_kernel(tc, zT, cb, cb2, tw, xT, offs, offs2, out):
         both = shared(f"z{LAST_NB - 1}_1", "both_last", [P, 2 * T], F32)
         first = both[:, :T].rearrange("p (j c) -> p j c", j=SLOTS)
         second = both[:, T:].rearrange("p (j c) -> p j c", j=SLOTS)
-        for k in range(PASSES):
-            for k0, k1 in FIRST_PIECES[LAST_NB]:
-                if k0 == k:
-                    gather_into_planes(0, LAST_NB, k0, k1, first[:, :, k0 * P : k1 * P])
-            if k < LAST_K:
-                gather_into_planes(1, LAST_NB, k, k + 1, second[:, :, k * P : (k + 1) * P])
-                bank = bank_tile(PASSES + k, f"e{k}_{LAST_NB}", [P, SLOTS, P])
-                turn(bank, neg_z, k * P, True, False)
-                turn(bank, first, k * P, False, False)
-                turn(bank, second, k * P, False, True)
-                weigh([bank[:, j, :] for j in range(SLOTS)], k, LAST_NB)
+        for k in range(LAST_K):
+            gather_into_planes(0, LAST_NB, k, k + 1, first[:, :, k * P : (k + 1) * P])
+            gather_into_planes(1, LAST_NB, k, k + 1, second[:, :, k * P : (k + 1) * P])
+            bank = bank_tile(PASSES + k, f"e{k}_{LAST_NB}", [P, SLOTS, P])
+            turn(bank, neg_z, k * P, True, False)
+            turn(bank, first, k * P, False, False)
+            turn(bank, second, k * P, False, True)
+            weigh([bank[:, j, :] for j in range(SLOTS)], k, LAST_NB)
+
+        free_banks = (PASSES + LAST_K, DB, DB + 1, PASSES)
+        sums = [bank_tile(i, f"last{i}", [P, P]) for i in free_banks]
+
+        def turn_last(planes, start, stop):
+            for j in range(SLOTS):
+                nc.tensor.matmul(sums[j][:], planes[:, j, :], ident[:], start=start, stop=stop, is_transpose=True)
+
+        turn_last(neg_z[:, :, LAST_K * P :], True, False)
 
         nc.gpsimd.memset(split_scales[:, P:DV].bitcast(U32), 0)
         quantize_g(0, 0, 1, *early_part)
         quantize_x(0, 1, x_codes_0[:])
         multiply(0, *early_part, True, False)
 
-        last_planes = shared("g_early", "last_planes", [P, SLOTS, P], F32)
-        gather_into_planes(1, LAST_NB, LAST_K, PASSES, last_planes[:])
-        free_banks = (PASSES + LAST_K, DB, DB + 1, PASSES)
-        sums = [bank_tile(i, f"last{i}", [P, P]) for i in free_banks]
-        terms = (neg_z[:, :, LAST_K * P :], first[:, :, LAST_K * P :], last_planes[:])
-        for i, planes in enumerate(terms):
-            for j in range(SLOTS):
-                nc.tensor.matmul(
-                    sums[j][:],
-                    planes[:, j, :],
-                    ident[:],
-                    start=(i == 0),
-                    stop=(i == len(terms) - 1),
-                    is_transpose=True,
-                )
-        weigh_in_pairs([slot_sum[:] for slot_sum in sums], LAST_K, LAST_NB)
-
+        last_first = shared("g_early0", "last_first", [P, SLOTS, P], F32)
+        gather_into_planes(0, LAST_NB, LAST_K, PASSES, last_first[:])
+        turn_last(last_first, False, False)
         quantize_g(0, 1, 2, *late_part)
         quantize_g(0, 2, NB, *late_part)
         multiply(0, *late_part, False, False)
+        last_planes = shared("g_early1", "last_planes", [P, SLOTS, P], F32)
+        gather_into_planes(1, LAST_NB, LAST_K, PASSES, last_planes[:])
+        turn_last(last_planes, False, True)
+        weigh_in_pairs([slot_sum[:] for slot_sum in sums], LAST_K, LAST_NB)
+
         quantize_x(1, LAST_K, x_codes_12[:])
         for k in range(1, LAST_K):
             quantize_g(k, 0, NB, g_codes_12[:, k - 1, :], g_scales[:, k - 1, :])

@@ -33,18 +33,17 @@ LAST_K = PASSES - 1
 RING = 4
 
 WINDOW_BLOCKS = {1: 1, 2: 2, 3: 2, 4: 4}
-PADS = (2, 3)
-WHOLE = [(0, PASSES)]
-HALVES = [(0, 2), (2, PASSES)]
-FIRST_PIECES = [[(0, 1), (1, PASSES)], WHOLE, HALVES]
-SECOND_PIECES = [WHOLE, WHOLE, HALVES]
-SPLIT_WIDTH = 2 * DV - P
-AT_CODES_3 = 2 * K_PASS
-AT_SPLIT_SCALES = AT_CODES_3 + 4 * (P + DV)
+PADS = (3, 3)
+DIFF_BLOCKS = 2
+SPLIT_WIDTH = DV + DV // 2
+AT_G_3 = 2 * K_PASS
+AT_X_LATE = AT_G_3 + 4 * DV
+AT_LAST_PLANES = AT_X_LATE + 4 * (2 * D + P)
+AT_PLANES_2 = AT_LAST_PLANES + 4 * K_PASS
+AT_SPLIT_SCALES = AT_PLANES_2 + 4 * K_PASS
 AT_X_0 = AT_SPLIT_SCALES + SPLIT_WIDTH
-AT_X_12 = AT_X_0 + 4 * D
-LATE_END = AT_X_12 + 8 * D
-STAGING_SPAN = [LATE_END, AT_CODES_3, AT_SPLIT_SCALES, AT_CODES_3]
+LATE_END = AT_X_0 + 4 * D
+STAGING_SPAN = {(1, 2): LATE_END, (0, 3): AT_PLANES_2, (1, 3): AT_G_3, (2, 3): AT_X_LATE, (3, 3): AT_G_3}
 
 
 def tile_attend_gvq_rw_w_kernel(tc, zT, cb, cb2, tw, xT, offs, offs2, out):
@@ -63,15 +62,13 @@ def tile_attend_gvq_rw_w_kernel(tc, zT, cb, cb2, tw, xT, offs, offs2, out):
 
         lists = [keep.tile([P, T // LIST_ROWS], U16, name=f"list{b}") for b in range(2)]
         books = [keep.tile([P, (NB + PADS[b]) * C], F32, name=f"book{b}") for b in range(2)]
-        z = [[shared(f"z{nb}_{h}", f"z{nb}_{h}", [P, T // 2], F32) for h in range(2)] for nb in range(LAST_NB)]
-        z_last = keep.tile([P, T], F32)
-        neg_z = keep.tile([P, SLOTS, T // SLOTS], F32)
-        x_raw = [keep.tile([P, T], F32, name=f"x_raw{db}") for db in range(DB)]
+        z = [[shared(f"z{nb}_{h}", f"z{nb}_{h}", [P, T // 2], F32) for h in range(2)] for nb in range(DIFF_BLOCKS)]
+        z_late = {nb: shared(f"z{nb}", f"z{nb}", [P, T], F32) for nb in range(DIFF_BLOCKS, NB)}
+        x_raw = [shared(f"x_raw{db}", f"x_raw{db}", [P, T], F32) for db in range(DB)]
         x_pairs = [keep.tile([P, 2, T // 2], BF16, name=f"x_pairs{db}") for db in range(DB)]
         x_turned = keep.tile([P, PASSES, D * SLOTS], BF16, align_bytes=64)
         x_scales = keep.tile([P, PASSES, D], U8, align_bytes=64)
         g_scales = keep.tile([P, LAST_K, DV], U8, align_bytes=64)
-        g_early = [shared(f"g_early{nb}", f"g_early{nb}", [P, K_PASS], BF16) for nb in range(2)]
         g_turned = [keep.tile([P, NB * K_PASS], BF16, align_bytes=64, name=f"g_turned{k}") for k in range(PASSES)]
         split_codes = keep.tile([P, SPLIT_WIDTH], U32, align_bytes=64)
         ident = keep.tile([P, P], F32)
@@ -82,16 +79,12 @@ def tile_attend_gvq_rw_w_kernel(tc, zT, cb, cb2, tw, xT, offs, offs2, out):
         def book_start(nb):
             return (NB - 1 - nb) * C
 
-        def clear_pad(b, i):
-            nc.gpsimd.memset(books[b][:, (NB + i) * C : (NB + i + 1) * C], 0.0)
-
-        nc.vector.memset(books[0][:, NB * C : (NB + 1) * C], 0.0)
+        nc.vector.memset(books[0][:, NB * C : (NB + 2) * C].bitcast(U32), 0)
+        nc.gpsimd.memset(books[0][:, (NB + 2) * C :], 0.0)
         make_identity(nc, ident[:])
-        for i in range(PADS[1]):
-            clear_pad(1, i)
-        clear_pad(0, 1)
-        nc.gpsimd.memset(split_codes[:, P:DV], 0)
-        nc.vector.memset(tw_rows[:], 0.0)
+        nc.gpsimd.memset(tw_rows[:], 0.0)
+        nc.gpsimd.memset(books[1][:, NB * C :], 0.0)
+        nc.gpsimd.memset(split_codes[:, DV // 2 : DV], 0)
 
         def load_book(b, nb):
             src = (cb, cb2)[b]
@@ -100,6 +93,9 @@ def tile_attend_gvq_rw_w_kernel(tc, zT, cb, cb2, tw, xT, offs, offs2, out):
         def load_z(nb, half):
             cols = slice(half * T // 2, (half + 1) * T // 2)
             nc.sync.dma_start(out=z[nb][half][:], in_=zT[nb * P : (nb + 1) * P, cols])
+
+        def load_late_z(nb):
+            nc.sync.dma_start(out=z_late[nb][:], in_=zT[nb * P : (nb + 1) * P, :])
 
         def load_x(db, half):
             cols = slice(half * T // 2, (half + 1) * T // 2)
@@ -118,15 +114,14 @@ def tile_attend_gvq_rw_w_kernel(tc, zT, cb, cb2, tw, xT, offs, offs2, out):
         load_book(1, 1)
         load_x(0, 1)
         load_x(1, 1)
-        nc.sync.dma_start(out=z_last[:], in_=zT[LAST_NB * P :, :])
+        load_late_z(3)
         load_z(1, 0)
         load_z(1, 1)
         load_book(0, 2)
         load_book(1, 2)
         load_book(0, 3)
         load_book(1, 3)
-        load_z(2, 0)
-        load_z(2, 1)
+        load_late_z(2)
 
         def turn_weights():
             nc.scalar.activation(
@@ -140,15 +135,17 @@ def tile_attend_gvq_rw_w_kernel(tc, zT, cb, cb2, tw, xT, offs, offs2, out):
                 nc.tensor.transpose(bank[:, j, :], tw_planes[:, j, :], ident[:])
             nc.scalar.copy(neg_w[:], bank[:, :, 0:PASSES].rearrange("p j k -> p k j"))
 
-        def negate_z():
+        def negate_z(nb):
+            neg_z = shared(f"x_raw{nb % DB}", f"neg_z{nb}", [P, SLOTS, T // SLOTS], F32)
             nc.gpsimd.tensor_scalar(
                 neg_z[:].rearrange("p j (m r) -> p j m r", r=RUN),
-                z_last[:].rearrange("p (m j r) -> p j m r", j=SLOTS, r=RUN),
+                z_late[nb][:].rearrange("p (m j r) -> p j m r", j=SLOTS, r=RUN),
                 -1.0,
                 0.0,
                 MULT,
                 ADD,
             )
+            return neg_z
 
         def minus_z(first, nb, half):
             cols = slice(half * T // 2, (half + 1) * T // 2)
@@ -185,14 +182,12 @@ def tile_attend_gvq_rw_w_kernel(tc, zT, cb, cb2, tw, xT, offs, offs2, out):
                 )
 
         def g_words(k, nb0, nb1):
-            if k == 0 and nb0 < 2:
-                return g_early[nb0][:]
             return g_turned[k][:, nb0 * K_PASS : nb1 * K_PASS]
 
         def staging(k, nb):
-            if nb < LAST_NB:
+            if (k, nb) not in STAGING_SPAN:
                 return ring.tile([P, K_PASS], BF16, tag="staged", name=f"staged{k}_{nb}")[:]
-            span = late.tile([P, STAGING_SPAN[k] // 2], BF16, offset=0, align_bytes=64, name=f"staged{k}_{nb}")
+            span = late.tile([P, STAGING_SPAN[k, nb] // 2], BF16, offset=0, align_bytes=64, name=f"staged{k}_{nb}")
             return span[:, :K_PASS]
 
         def weigh(sums, k, nb):
@@ -237,36 +232,58 @@ def tile_attend_gvq_rw_w_kernel(tc, zT, cb, cb2, tw, xT, offs, offs2, out):
             if half == 0:
                 turn_weights()
 
-        for nb in range(LAST_NB):
-            first = shared(f"first{nb % 2}", f"first{nb}", [P, T], F32)
-            for k0, k1 in FIRST_PIECES[nb]:
-                gather_in_token_order(nb, k0, k1, first)
-            second = shared("z0_0" if nb == 1 else "second", f"second{nb}", [P, SLOTS, T // SLOTS], F32)
-            for k0, k1 in SECOND_PIECES[nb]:
-                gather_into_planes(1, nb, k0, k1, second[:, :, k0 * P : k1 * P])
+        neg_z = {}
+        for nb in range(DIFF_BLOCKS):
+            first = shared("z0_0" if nb == 1 else "first", f"first{nb}", [P, T], F32)
+            gather_in_token_order(nb, 0, PASSES, first)
+            second = shared("z0_1" if nb == 1 else "second", f"second{nb}", [P, SLOTS, T // SLOTS], F32)
+            gather_into_planes(1, nb, 0, PASSES, second[:])
             for half in range(2):
                 diff = minus_z(first, nb, half)
                 for k in (2 * half, 2 * half + 1):
-                    bank = bank_tile(PASSES * (nb % 2) + k, f"e{k}_{nb}", [P, SLOTS, P])
+                    bank = bank_tile(PASSES * nb + k, f"e{k}_{nb}", [P, SLOTS, P])
                     turn(bank, diff, (k % 2) * P, True, False)
                     turn(bank, second, k * P, False, True)
                     weigh([bank[:, j, :] for j in range(SLOTS)], k, nb)
-            if nb == 0:
-                negate_z()
+            neg_z[LAST_NB - nb] = negate_z(LAST_NB - nb)
 
-        codes_3 = late.tile([P, P + DV], U32, offset=AT_CODES_3, align_bytes=64)
+        def unit(k, nb, first, second):
+            bank = bank_tile(PASSES * (nb % 2) + k, f"e{k}_{nb}", [P, SLOTS, P])
+            turn(bank, neg_z[nb], k * P, True, False)
+            turn(bank, first, k * P, False, False)
+            turn(bank, second, k * P, False, True)
+            weigh([bank[:, j, :] for j in range(SLOTS)], k, nb)
+
+        first = shared("first", "first2", [P, SLOTS, T // SLOTS], F32)
+        second = shared("second", "second2", [P, SLOTS, T // SLOTS], F32)
+        gather_into_planes(0, 2, 0, PASSES, first[:])
+        gather_into_planes(1, 2, 0, PASSES, second[:])
+        for k in range(PASSES):
+            unit(k, 2, first, second)
+
+        both = shared("z2", "both_last", [P, T + T // 2], F32)
+        first = both[:, :T].rearrange("p (j c) -> p j c", j=SLOTS)
+        second = both[:, T:].rearrange("p (j c) -> p j c", j=SLOTS)
+        gather_into_planes(0, LAST_NB, 0, 2, first[:, :, : 2 * P])
+        gather_into_planes(1, LAST_NB, 0, 2, second)
+        gather_into_planes(0, LAST_NB, 2, PASSES, first[:, :, 2 * P :])
+        for k in range(2):
+            unit(k, LAST_NB, first, second)
+
         split_scales = late.tile([P, SPLIT_WIDTH], U8, offset=AT_SPLIT_SCALES, align_bytes=64)
         x_codes_0 = late.tile([P, D], U32, offset=AT_X_0, align_bytes=64)
-        x_codes_12 = late.tile([P, 2 * D], U32, offset=AT_X_12, align_bytes=64)
+        x_codes_late = late.tile([P, 2 * D + P], U32, offset=AT_X_LATE, align_bytes=64)
+        g_codes_3 = late.tile([P, DV], U32, offset=AT_G_3, align_bytes=64)
         last_x_codes = late.tile([P, P], U32, offset=0, align_bytes=64)
+        planes_2 = late.tile([P, SLOTS, P], F32, offset=AT_PLANES_2, align_bytes=64)
+        last_planes = late.tile([P, SLOTS, P], F32, offset=AT_LAST_PLANES, align_bytes=64)
         g_codes_12 = keep.tile([P, 2, DV], U32, align_bytes=64)
         x_codes = [
             [x_codes_0[:, :P], x_codes_0[:, P:]],
-            [x_codes_12[:, :P], x_codes_12[:, P:D]],
-            [x_codes_12[:, D : D + P], x_codes_12[:, D + P :]],
-            [codes_3[:, :P], last_x_codes[:]],
+            [x_codes_late[:, :P], x_codes_late[:, P:D]],
+            [x_codes_late[:, D : D + P], x_codes_late[:, D + P : 2 * D]],
+            [x_codes_late[:, 2 * D :], last_x_codes[:]],
         ]
-        g_codes_3 = codes_3[:, P:]
 
         def quantize_x(k0, k1, codes):
             nc.vector.quantize_mx(
@@ -300,19 +317,11 @@ def tile_attend_gvq_rw_w_kernel(tc, zT, cb, cb2, tw, xT, offs, offs2, out):
 
         early_part = (split_codes[:, :DV], split_scales[:, :DV])
         late_part = (split_codes[:, SPLIT_WIDTH - DV :], split_scales[:, SPLIT_WIDTH - DV :])
-
         acc = [bank_tile(db, f"acc{db}", [P, DV]) for db in range(DB)]
-        both = shared(f"z{LAST_NB - 1}_1", "both_last", [P, 2 * T], F32)
-        first = both[:, :T].rearrange("p (j c) -> p j c", j=SLOTS)
-        second = both[:, T:].rearrange("p (j c) -> p j c", j=SLOTS)
-        for k in range(LAST_K):
-            gather_into_planes(0, LAST_NB, k, k + 1, first[:, :, k * P : (k + 1) * P])
-            gather_into_planes(1, LAST_NB, k, k + 1, second[:, :, k * P : (k + 1) * P])
-            bank = bank_tile(PASSES + k, f"e{k}_{LAST_NB}", [P, SLOTS, P])
-            turn(bank, neg_z, k * P, True, False)
-            turn(bank, first, k * P, False, False)
-            turn(bank, second, k * P, False, True)
-            weigh([bank[:, j, :] for j in range(SLOTS)], k, LAST_NB)
+
+        bank_2 = bank_tile(PASSES + 2, "e2_last", [P, SLOTS, P])
+        turn(bank_2, neg_z[LAST_NB], 2 * P, True, False)
+        turn(bank_2, first, 2 * P, False, False)
 
         free_banks = (PASSES + LAST_K, DB, DB + 1, PASSES)
         sums = [bank_tile(i, f"last{i}", [P, P]) for i in free_banks]
@@ -321,35 +330,33 @@ def tile_attend_gvq_rw_w_kernel(tc, zT, cb, cb2, tw, xT, offs, offs2, out):
             for j in range(SLOTS):
                 nc.tensor.matmul(sums[j][:], planes[:, j, :], ident[:], start=start, stop=stop, is_transpose=True)
 
-        turn_last(neg_z[:, :, LAST_K * P :], True, False)
-
-        nc.gpsimd.memset(split_scales[:, P:DV].bitcast(U32), 0)
-        quantize_g(0, 0, 1, *early_part)
+        nc.gpsimd.memset(split_scales[:, DV // 2 : DV].bitcast(U32), 0)
+        quantize_g(0, 0, 2, *early_part)
         quantize_x(0, 1, x_codes_0[:])
         multiply(0, *early_part, True, False)
 
-        last_first = shared("g_early0", "last_first", [P, SLOTS, P], F32)
-        gather_into_planes(0, LAST_NB, LAST_K, PASSES, last_first[:])
-        turn_last(last_first, False, False)
-        quantize_g(0, 1, 2, *late_part)
+        gather_into_planes(1, LAST_NB, 2, LAST_K, planes_2[:])
+        turn_last(neg_z[LAST_NB][:, :, LAST_K * P :], True, False)
+        turn_last(first[:, :, LAST_K * P :], False, False)
+        turn(bank_2, planes_2, 0, False, True)
+        weigh([bank_2[:, j, :] for j in range(SLOTS)], 2, LAST_NB)
         quantize_g(0, 2, NB, *late_part)
         multiply(0, *late_part, False, False)
-        last_planes = shared("g_early1", "last_planes", [P, SLOTS, P], F32)
         gather_into_planes(1, LAST_NB, LAST_K, PASSES, last_planes[:])
         turn_last(last_planes, False, True)
         weigh_in_pairs([slot_sum[:] for slot_sum in sums], LAST_K, LAST_NB)
 
-        quantize_x(1, LAST_K, x_codes_12[:])
+        quantize_x(1, LAST_K, x_codes_late[:, : 2 * D])
+        quantize_last_x(0)
         for k in range(1, LAST_K):
             quantize_g(k, 0, NB, g_codes_12[:, k - 1, :], g_scales[:, k - 1, :])
             multiply(k, g_codes_12[:, k - 1, :], g_scales[:, k - 1, :], False, False)
         last_scales = g_scales[:, LAST_K - 1, :]
-        quantize_last_x(0)
-        quantize_g(LAST_K, 0, 2, g_codes_3, last_scales)
-        quantize_g(LAST_K, 2, LAST_NB, g_codes_3, last_scales)
-        quantize_g(LAST_K, LAST_NB, NB, g_codes_3, last_scales)
+        quantize_g(LAST_K, 0, 2, g_codes_3[:], last_scales)
+        quantize_g(LAST_K, 2, LAST_NB, g_codes_3[:], last_scales)
+        quantize_g(LAST_K, LAST_NB, NB, g_codes_3[:], last_scales)
         quantize_last_x(1)
-        multiply(LAST_K, g_codes_3, last_scales, False, True)
+        multiply(LAST_K, g_codes_3[:], last_scales, False, True)
 
         result = [keep.tile([P, DV], F32, name=f"result{db}") for db in range(DB)]
         for half in range(2):

@@ -33,17 +33,18 @@ LAST_K = PASSES - 1
 RING = 4
 
 WINDOW_BLOCKS = {1: 1, 2: 2, 3: 2, 4: 4}
-PADS = (3, 3)
+PADS = (2, 3)
+FIRST_PIECES = [[(0, 1), (1, PASSES)], [(0, PASSES)]]
 DIFF_BLOCKS = 2
 SPLIT_WIDTH = DV + DV // 2
 AT_G_3 = 2 * K_PASS
 AT_X_LATE = AT_G_3 + 4 * DV
 AT_LAST_PLANES = AT_X_LATE + 4 * (2 * D + P)
-AT_PLANES_2 = AT_LAST_PLANES + 4 * K_PASS
-AT_SPLIT_SCALES = AT_PLANES_2 + 4 * K_PASS
+AT_LAST_FIRST = AT_LAST_PLANES + 4 * K_PASS
+AT_SPLIT_SCALES = AT_LAST_FIRST + 4 * K_PASS
 AT_X_0 = AT_SPLIT_SCALES + SPLIT_WIDTH
 LATE_END = AT_X_0 + 4 * D
-STAGING_SPAN = {(1, 2): LATE_END, (0, 3): AT_PLANES_2, (1, 3): AT_G_3, (2, 3): AT_X_LATE, (3, 3): AT_G_3}
+STAGING_SPAN = {(1, 2): LATE_END, (0, 3): AT_LAST_FIRST, (1, 3): AT_G_3, (2, 3): AT_X_LATE, (3, 3): AT_G_3}
 
 
 def tile_attend_gvq_rw_w_kernel(tc, zT, cb, cb2, tw, xT, offs, offs2, out):
@@ -79,12 +80,16 @@ def tile_attend_gvq_rw_w_kernel(tc, zT, cb, cb2, tw, xT, offs, offs2, out):
         def book_start(nb):
             return (NB - 1 - nb) * C
 
-        nc.vector.memset(books[0][:, NB * C : (NB + 2) * C].bitcast(U32), 0)
-        nc.gpsimd.memset(books[0][:, (NB + 2) * C :], 0.0)
+        def clear_pad(b, i):
+            nc.gpsimd.memset(books[b][:, (NB + i) * C : (NB + i + 1) * C], 0.0)
+
+        nc.vector.memset(books[0][:, NB * C : (NB + 1) * C], 0.0)
         make_identity(nc, ident[:])
-        nc.gpsimd.memset(tw_rows[:], 0.0)
-        nc.gpsimd.memset(books[1][:, NB * C :], 0.0)
+        for i in range(PADS[1]):
+            clear_pad(1, i)
+        clear_pad(0, 1)
         nc.gpsimd.memset(split_codes[:, DV // 2 : DV], 0)
+        nc.vector.memset(tw_rows[:], 0.0)
 
         def load_book(b, nb):
             src = (cb, cb2)[b]
@@ -119,9 +124,9 @@ def tile_attend_gvq_rw_w_kernel(tc, zT, cb, cb2, tw, xT, offs, offs2, out):
         load_z(1, 1)
         load_book(0, 2)
         load_book(1, 2)
+        load_late_z(2)
         load_book(0, 3)
         load_book(1, 3)
-        load_late_z(2)
 
         def turn_weights():
             nc.scalar.activation(
@@ -235,7 +240,8 @@ def tile_attend_gvq_rw_w_kernel(tc, zT, cb, cb2, tw, xT, offs, offs2, out):
         neg_z = {}
         for nb in range(DIFF_BLOCKS):
             first = shared("z0_0" if nb == 1 else "first", f"first{nb}", [P, T], F32)
-            gather_in_token_order(nb, 0, PASSES, first)
+            for k0, k1 in FIRST_PIECES[nb]:
+                gather_in_token_order(nb, k0, k1, first)
             second = shared("z0_1" if nb == 1 else "second", f"second{nb}", [P, SLOTS, T // SLOTS], F32)
             gather_into_planes(1, nb, 0, PASSES, second[:])
             for half in range(2):
@@ -247,35 +253,39 @@ def tile_attend_gvq_rw_w_kernel(tc, zT, cb, cb2, tw, xT, offs, offs2, out):
                     weigh([bank[:, j, :] for j in range(SLOTS)], k, nb)
             neg_z[LAST_NB - nb] = negate_z(LAST_NB - nb)
 
-        def unit(k, nb, first, second):
-            bank = bank_tile(PASSES * (nb % 2) + k, f"e{k}_{nb}", [P, SLOTS, P])
-            turn(bank, neg_z[nb], k * P, True, False)
-            turn(bank, first, k * P, False, False)
-            turn(bank, second, k * P, False, True)
-            weigh([bank[:, j, :] for j in range(SLOTS)], k, nb)
-
         first = shared("first", "first2", [P, SLOTS, T // SLOTS], F32)
         second = shared("second", "second2", [P, SLOTS, T // SLOTS], F32)
         gather_into_planes(0, 2, 0, PASSES, first[:])
         gather_into_planes(1, 2, 0, PASSES, second[:])
+        banks = [bank_tile(k, f"e{k}_2", [P, SLOTS, P]) for k in range(PASSES)]
         for k in range(PASSES):
-            unit(k, 2, first, second)
+            turn(banks[k], first, k * P, True, False)
+        for k in range(PASSES):
+            turn(banks[k], neg_z[2], k * P, False, False)
+        for k in range(PASSES):
+            turn(banks[k], second, k * P, False, True)
+            weigh([banks[k][:, j, :] for j in range(SLOTS)], k, 2)
 
-        both = shared("z2", "both_last", [P, T + T // 2], F32)
-        first = both[:, :T].rearrange("p (j c) -> p j c", j=SLOTS)
-        second = both[:, T:].rearrange("p (j c) -> p j c", j=SLOTS)
-        gather_into_planes(0, LAST_NB, 0, 2, first[:, :, : 2 * P])
-        gather_into_planes(1, LAST_NB, 0, 2, second)
-        gather_into_planes(0, LAST_NB, 2, PASSES, first[:, :, 2 * P :])
-        for k in range(2):
-            unit(k, LAST_NB, first, second)
+        both = shared("z2", "both_last", [P, 2, SLOTS, LAST_K * P], F32)
+        first, second = both[:, 0], both[:, 1]
+        banks = [bank_tile(PASSES + k, f"e{k}_{LAST_NB}", [P, SLOTS, P]) for k in range(LAST_K)]
+        for k in range(LAST_K):
+            turn(banks[k], neg_z[LAST_NB], k * P, True, False)
+        for k0, k1 in ((0, 2), (2, LAST_K)):
+            gather_into_planes(0, LAST_NB, k0, k1, first[:, :, k0 * P : k1 * P])
+            gather_into_planes(1, LAST_NB, k0, k1, second[:, :, k0 * P : k1 * P])
+            for k in range(k0, k1):
+                turn(banks[k], first, k * P, False, False)
+            for k in range(k0, k1):
+                turn(banks[k], second, k * P, False, True)
+                weigh([banks[k][:, j, :] for j in range(SLOTS)], k, LAST_NB)
 
         split_scales = late.tile([P, SPLIT_WIDTH], U8, offset=AT_SPLIT_SCALES, align_bytes=64)
         x_codes_0 = late.tile([P, D], U32, offset=AT_X_0, align_bytes=64)
         x_codes_late = late.tile([P, 2 * D + P], U32, offset=AT_X_LATE, align_bytes=64)
         g_codes_3 = late.tile([P, DV], U32, offset=AT_G_3, align_bytes=64)
         last_x_codes = late.tile([P, P], U32, offset=0, align_bytes=64)
-        planes_2 = late.tile([P, SLOTS, P], F32, offset=AT_PLANES_2, align_bytes=64)
+        last_first = late.tile([P, SLOTS, P], F32, offset=AT_LAST_FIRST, align_bytes=64)
         last_planes = late.tile([P, SLOTS, P], F32, offset=AT_LAST_PLANES, align_bytes=64)
         g_codes_12 = keep.tile([P, 2, DV], U32, align_bytes=64)
         x_codes = [
@@ -319,10 +329,6 @@ def tile_attend_gvq_rw_w_kernel(tc, zT, cb, cb2, tw, xT, offs, offs2, out):
         late_part = (split_codes[:, SPLIT_WIDTH - DV :], split_scales[:, SPLIT_WIDTH - DV :])
         acc = [bank_tile(db, f"acc{db}", [P, DV]) for db in range(DB)]
 
-        bank_2 = bank_tile(PASSES + 2, "e2_last", [P, SLOTS, P])
-        turn(bank_2, neg_z[LAST_NB], 2 * P, True, False)
-        turn(bank_2, first, 2 * P, False, False)
-
         free_banks = (PASSES + LAST_K, DB, DB + 1, PASSES)
         sums = [bank_tile(i, f"last{i}", [P, P]) for i in free_banks]
 
@@ -330,16 +336,15 @@ def tile_attend_gvq_rw_w_kernel(tc, zT, cb, cb2, tw, xT, offs, offs2, out):
             for j in range(SLOTS):
                 nc.tensor.matmul(sums[j][:], planes[:, j, :], ident[:], start=start, stop=stop, is_transpose=True)
 
+        turn_last(neg_z[LAST_NB][:, :, LAST_K * P :], True, False)
+
         nc.gpsimd.memset(split_scales[:, DV // 2 : DV].bitcast(U32), 0)
         quantize_g(0, 0, 2, *early_part)
         quantize_x(0, 1, x_codes_0[:])
         multiply(0, *early_part, True, False)
 
-        gather_into_planes(1, LAST_NB, 2, LAST_K, planes_2[:])
-        turn_last(neg_z[LAST_NB][:, :, LAST_K * P :], True, False)
-        turn_last(first[:, :, LAST_K * P :], False, False)
-        turn(bank_2, planes_2, 0, False, True)
-        weigh([bank_2[:, j, :] for j in range(SLOTS)], 2, LAST_NB)
+        gather_into_planes(0, LAST_NB, LAST_K, PASSES, last_first[:])
+        turn_last(last_first, False, False)
         quantize_g(0, 2, NB, *late_part)
         multiply(0, *late_part, False, False)
         gather_into_planes(1, LAST_NB, LAST_K, PASSES, last_planes[:])

@@ -34,8 +34,10 @@ RING = 4
 
 WINDOW_BLOCKS = {1: 1, 2: 2, 3: 2, 4: 4}
 PADS = (2, 3)
-FIRST_PIECES = [[(0, 1), (1, PASSES)], [(0, PASSES)]]
-DIFF_BLOCKS = 2
+WHOLE = [(0, PASSES)]
+HALVES = [(0, 2), (2, PASSES)]
+FIRST_PIECES = [[(0, 1), (1, PASSES)], WHOLE, HALVES]
+SECOND_PIECES = [WHOLE, WHOLE, HALVES]
 SPLIT_WIDTH = DV + DV // 2
 AT_G_3 = 2 * K_PASS
 AT_X_LATE = AT_G_3 + 4 * DV
@@ -44,7 +46,7 @@ AT_LAST_FIRST = AT_LAST_PLANES + 4 * K_PASS
 AT_SPLIT_SCALES = AT_LAST_FIRST + 4 * K_PASS
 AT_X_0 = AT_SPLIT_SCALES + SPLIT_WIDTH
 LATE_END = AT_X_0 + 4 * D
-STAGING_SPAN = {(1, 2): LATE_END, (0, 3): AT_LAST_FIRST, (1, 3): AT_G_3, (2, 3): AT_X_LATE, (3, 3): AT_G_3}
+STAGING_SPAN = {(3, 2): LATE_END, (0, 3): AT_LAST_FIRST, (1, 3): AT_G_3, (2, 3): AT_X_LATE, (3, 3): AT_G_3}
 
 
 def tile_attend_gvq_rw_w_kernel(tc, zT, cb, cb2, tw, xT, offs, offs2, out):
@@ -63,9 +65,10 @@ def tile_attend_gvq_rw_w_kernel(tc, zT, cb, cb2, tw, xT, offs, offs2, out):
 
         lists = [keep.tile([P, T // LIST_ROWS], U16, name=f"list{b}") for b in range(2)]
         books = [keep.tile([P, (NB + PADS[b]) * C], F32, name=f"book{b}") for b in range(2)]
-        z = [[shared(f"z{nb}_{h}", f"z{nb}_{h}", [P, T // 2], F32) for h in range(2)] for nb in range(DIFF_BLOCKS)]
-        z_late = {nb: shared(f"z{nb}", f"z{nb}", [P, T], F32) for nb in range(DIFF_BLOCKS, NB)}
-        x_raw = [shared(f"x_raw{db}", f"x_raw{db}", [P, T], F32) for db in range(DB)]
+        z = [[shared(f"z{nb}_{h}", f"z{nb}_{h}", [P, T // 2], F32) for h in range(2)] for nb in range(LAST_NB)]
+        z_last = keep.tile([P, T], F32)
+        neg_z = keep.tile([P, SLOTS, T // SLOTS], F32)
+        x_raw = [keep.tile([P, T], F32, name=f"x_raw{db}") for db in range(DB)]
         x_pairs = [keep.tile([P, 2, T // 2], BF16, name=f"x_pairs{db}") for db in range(DB)]
         x_turned = keep.tile([P, PASSES, D * SLOTS], BF16, align_bytes=64)
         x_scales = keep.tile([P, PASSES, D], U8, align_bytes=64)
@@ -99,9 +102,6 @@ def tile_attend_gvq_rw_w_kernel(tc, zT, cb, cb2, tw, xT, offs, offs2, out):
             cols = slice(half * T // 2, (half + 1) * T // 2)
             nc.sync.dma_start(out=z[nb][half][:], in_=zT[nb * P : (nb + 1) * P, cols])
 
-        def load_late_z(nb):
-            nc.sync.dma_start(out=z_late[nb][:], in_=zT[nb * P : (nb + 1) * P, :])
-
         def load_x(db, half):
             cols = slice(half * T // 2, (half + 1) * T // 2)
             nc.sync.dma_start(out=x_raw[db][:, cols], in_=xT[db * P : (db + 1) * P, cols])
@@ -119,14 +119,15 @@ def tile_attend_gvq_rw_w_kernel(tc, zT, cb, cb2, tw, xT, offs, offs2, out):
         load_book(1, 1)
         load_x(0, 1)
         load_x(1, 1)
-        load_late_z(3)
+        nc.sync.dma_start(out=z_last[:], in_=zT[LAST_NB * P :, :])
         load_z(1, 0)
         load_z(1, 1)
         load_book(0, 2)
         load_book(1, 2)
-        load_late_z(2)
         load_book(0, 3)
         load_book(1, 3)
+        load_z(2, 0)
+        load_z(2, 1)
 
         def turn_weights():
             nc.scalar.activation(
@@ -140,17 +141,15 @@ def tile_attend_gvq_rw_w_kernel(tc, zT, cb, cb2, tw, xT, offs, offs2, out):
                 nc.tensor.transpose(bank[:, j, :], tw_planes[:, j, :], ident[:])
             nc.scalar.copy(neg_w[:], bank[:, :, 0:PASSES].rearrange("p j k -> p k j"))
 
-        def negate_z(nb):
-            neg_z = shared(f"x_raw{nb % DB}", f"neg_z{nb}", [P, SLOTS, T // SLOTS], F32)
+        def negate_z():
             nc.gpsimd.tensor_scalar(
                 neg_z[:].rearrange("p j (m r) -> p j m r", r=RUN),
-                z_late[nb][:].rearrange("p (m j r) -> p j m r", j=SLOTS, r=RUN),
+                z_last[:].rearrange("p (m j r) -> p j m r", j=SLOTS, r=RUN),
                 -1.0,
                 0.0,
                 MULT,
                 ADD,
             )
-            return neg_z
 
         def minus_z(first, nb, half):
             cols = slice(half * T // 2, (half + 1) * T // 2)
@@ -237,40 +236,28 @@ def tile_attend_gvq_rw_w_kernel(tc, zT, cb, cb2, tw, xT, offs, offs2, out):
             if half == 0:
                 turn_weights()
 
-        neg_z = {}
-        for nb in range(DIFF_BLOCKS):
+        for nb in range(LAST_NB):
             first = shared("z0_0" if nb == 1 else "first", f"first{nb}", [P, T], F32)
             for k0, k1 in FIRST_PIECES[nb]:
                 gather_in_token_order(nb, k0, k1, first)
             second = shared("z0_1" if nb == 1 else "second", f"second{nb}", [P, SLOTS, T // SLOTS], F32)
-            gather_into_planes(1, nb, 0, PASSES, second[:])
+            for k0, k1 in SECOND_PIECES[nb]:
+                gather_into_planes(1, nb, k0, k1, second[:, :, k0 * P : k1 * P])
             for half in range(2):
                 diff = minus_z(first, nb, half)
                 for k in (2 * half, 2 * half + 1):
-                    bank = bank_tile(PASSES * nb + k, f"e{k}_{nb}", [P, SLOTS, P])
+                    bank = bank_tile(PASSES * (nb % 2) + k, f"e{k}_{nb}", [P, SLOTS, P])
                     turn(bank, diff, (k % 2) * P, True, False)
                     turn(bank, second, k * P, False, True)
                     weigh([bank[:, j, :] for j in range(SLOTS)], k, nb)
-            neg_z[LAST_NB - nb] = negate_z(LAST_NB - nb)
+            if nb == 0:
+                negate_z()
 
-        first = shared("first", "first2", [P, SLOTS, T // SLOTS], F32)
-        second = shared("second", "second2", [P, SLOTS, T // SLOTS], F32)
-        gather_into_planes(0, 2, 0, PASSES, first[:])
-        gather_into_planes(1, 2, 0, PASSES, second[:])
-        banks = [bank_tile(k, f"e{k}_2", [P, SLOTS, P]) for k in range(PASSES)]
-        for k in range(PASSES):
-            turn(banks[k], first, k * P, True, False)
-        for k in range(PASSES):
-            turn(banks[k], neg_z[2], k * P, False, False)
-        for k in range(PASSES):
-            turn(banks[k], second, k * P, False, True)
-            weigh([banks[k][:, j, :] for j in range(SLOTS)], k, 2)
-
-        both = shared("z2", "both_last", [P, 2, SLOTS, LAST_K * P], F32)
+        both = shared("z2_1", "both_last", [P, 2, SLOTS, LAST_K * P], F32)
         first, second = both[:, 0], both[:, 1]
         banks = [bank_tile(PASSES + k, f"e{k}_{LAST_NB}", [P, SLOTS, P]) for k in range(LAST_K)]
         for k in range(LAST_K):
-            turn(banks[k], neg_z[LAST_NB], k * P, True, False)
+            turn(banks[k], neg_z, k * P, True, False)
         for k0, k1 in ((0, 2), (2, LAST_K)):
             gather_into_planes(0, LAST_NB, k0, k1, first[:, :, k0 * P : k1 * P])
             gather_into_planes(1, LAST_NB, k0, k1, second[:, :, k0 * P : k1 * P])
@@ -336,7 +323,7 @@ def tile_attend_gvq_rw_w_kernel(tc, zT, cb, cb2, tw, xT, offs, offs2, out):
             for j in range(SLOTS):
                 nc.tensor.matmul(sums[j][:], planes[:, j, :], ident[:], start=start, stop=stop, is_transpose=True)
 
-        turn_last(neg_z[LAST_NB][:, :, LAST_K * P :], True, False)
+        turn_last(neg_z[:, :, LAST_K * P :], True, False)
 
         nc.gpsimd.memset(split_scales[:, DV // 2 : DV].bitcast(U32), 0)
         quantize_g(0, 0, 2, *early_part)

@@ -39,14 +39,14 @@ HALVES = [(0, 2), (2, PASSES)]
 FIRST_PIECES = [[(0, 1), (1, PASSES)], WHOLE, HALVES]
 SECOND_PIECES = [WHOLE, WHOLE, HALVES]
 SPLIT_WIDTH = DV + DV // 2
-AT_G_3 = 2 * K_PASS
-AT_X_LATE = AT_G_3 + 4 * DV
-AT_LAST_PLANES = AT_X_LATE + 4 * (2 * D + P)
+AT_CODES_3 = 2 * K_PASS
+AT_X_12 = AT_CODES_3 + 4 * (P + DV)
+AT_LAST_PLANES = AT_X_12 + 8 * D
 AT_LAST_FIRST = AT_LAST_PLANES + 4 * K_PASS
 AT_SPLIT_SCALES = AT_LAST_FIRST + 4 * K_PASS
 AT_X_0 = AT_SPLIT_SCALES + SPLIT_WIDTH
 LATE_END = AT_X_0 + 4 * D
-STAGING_SPAN = {(3, 2): LATE_END, (0, 3): AT_LAST_FIRST, (1, 3): AT_G_3, (2, 3): AT_X_LATE, (3, 3): AT_G_3}
+STAGING_SPAN = {(3, 2): LATE_END, (0, 3): AT_LAST_FIRST, (1, 3): AT_CODES_3, (2, 3): AT_X_12, (3, 3): AT_CODES_3}
 
 
 def tile_attend_gvq_rw_w_kernel(tc, zT, cb, cb2, tw, xT, offs, offs2, out):
@@ -269,18 +269,19 @@ def tile_attend_gvq_rw_w_kernel(tc, zT, cb, cb2, tw, xT, offs, offs2, out):
 
         split_scales = late.tile([P, SPLIT_WIDTH], U8, offset=AT_SPLIT_SCALES, align_bytes=64)
         x_codes_0 = late.tile([P, D], U32, offset=AT_X_0, align_bytes=64)
-        x_codes_late = late.tile([P, 2 * D + P], U32, offset=AT_X_LATE, align_bytes=64)
-        g_codes_3 = late.tile([P, DV], U32, offset=AT_G_3, align_bytes=64)
+        x_codes_12 = late.tile([P, 2 * D], U32, offset=AT_X_12, align_bytes=64)
+        codes_3 = late.tile([P, P + DV], U32, offset=AT_CODES_3, align_bytes=64)
         last_x_codes = late.tile([P, P], U32, offset=0, align_bytes=64)
         last_first = late.tile([P, SLOTS, P], F32, offset=AT_LAST_FIRST, align_bytes=64)
         last_planes = late.tile([P, SLOTS, P], F32, offset=AT_LAST_PLANES, align_bytes=64)
         g_codes_12 = keep.tile([P, 2, DV], U32, align_bytes=64)
         x_codes = [
             [x_codes_0[:, :P], x_codes_0[:, P:]],
-            [x_codes_late[:, :P], x_codes_late[:, P:D]],
-            [x_codes_late[:, D : D + P], x_codes_late[:, D + P : 2 * D]],
-            [x_codes_late[:, 2 * D :], last_x_codes[:]],
+            [x_codes_12[:, :P], x_codes_12[:, P:D]],
+            [x_codes_12[:, D : D + P], x_codes_12[:, D + P :]],
+            [codes_3[:, :P], last_x_codes[:]],
         ]
+        g_codes_3 = codes_3[:, P:]
 
         def quantize_x(k0, k1, codes):
             nc.vector.quantize_mx(
@@ -314,14 +315,16 @@ def tile_attend_gvq_rw_w_kernel(tc, zT, cb, cb2, tw, xT, offs, offs2, out):
 
         early_part = (split_codes[:, :DV], split_scales[:, :DV])
         late_part = (split_codes[:, SPLIT_WIDTH - DV :], split_scales[:, SPLIT_WIDTH - DV :])
-        acc = [bank_tile(db, f"acc{db}", [P, DV]) for db in range(DB)]
+        acc = [bank_tile(DB + db, f"acc{db}", [P, DV]) for db in range(DB)]
 
-        free_banks = (PASSES + LAST_K, DB, DB + 1, PASSES)
-        sums = [bank_tile(i, f"last{i}", [P, P]) for i in free_banks]
+        last_banks = [bank_tile(PASSES + LAST_K, "last0", [P, 1, P]), bank_tile(0, "last1", [P, 1, P]), bank_tile(1, "last23", [P, 2, P])]
+        sums = [last_banks[0][:, 0, :], last_banks[1][:, 0, :], last_banks[2][:, 0, :], last_banks[2][:, 1, :]]
 
         def turn_last(planes, start, stop):
             for j in range(SLOTS):
-                nc.tensor.matmul(sums[j][:], planes[:, j, :], ident[:], start=start, stop=stop, is_transpose=True)
+                nc.tensor.matmul(
+                    sums[j], planes[:, j, :], ident[:], start=(start and j != 3), stop=(stop and j != 2), is_transpose=True
+                )
 
         turn_last(neg_z[:, :, LAST_K * P :], True, False)
 
@@ -336,19 +339,19 @@ def tile_attend_gvq_rw_w_kernel(tc, zT, cb, cb2, tw, xT, offs, offs2, out):
         multiply(0, *late_part, False, False)
         gather_into_planes(1, LAST_NB, LAST_K, PASSES, last_planes[:])
         turn_last(last_planes, False, True)
-        weigh_in_pairs([slot_sum[:] for slot_sum in sums], LAST_K, LAST_NB)
+        weigh_in_pairs(sums, LAST_K, LAST_NB)
 
-        quantize_x(1, LAST_K, x_codes_late[:, : 2 * D])
-        quantize_last_x(0)
+        quantize_x(1, LAST_K, x_codes_12[:])
         for k in range(1, LAST_K):
             quantize_g(k, 0, NB, g_codes_12[:, k - 1, :], g_scales[:, k - 1, :])
             multiply(k, g_codes_12[:, k - 1, :], g_scales[:, k - 1, :], False, False)
         last_scales = g_scales[:, LAST_K - 1, :]
-        quantize_g(LAST_K, 0, 2, g_codes_3[:], last_scales)
-        quantize_g(LAST_K, 2, LAST_NB, g_codes_3[:], last_scales)
-        quantize_g(LAST_K, LAST_NB, NB, g_codes_3[:], last_scales)
+        quantize_last_x(0)
+        quantize_g(LAST_K, 0, 2, g_codes_3, last_scales)
+        quantize_g(LAST_K, 2, LAST_NB, g_codes_3, last_scales)
+        quantize_g(LAST_K, LAST_NB, NB, g_codes_3, last_scales)
         quantize_last_x(1)
-        multiply(LAST_K, g_codes_3[:], last_scales, False, True)
+        multiply(LAST_K, g_codes_3, last_scales, False, True)
 
         result = [keep.tile([P, DV], F32, name=f"result{db}") for db in range(DB)]
         for half in range(2):

@@ -39,14 +39,21 @@ HALVES = [(0, 2), (2, PASSES)]
 FIRST_PIECES = [[(0, 1), (1, PASSES)], WHOLE, HALVES]
 SECOND_PIECES = [WHOLE, WHOLE, HALVES]
 SPLIT_WIDTH = DV + DV // 2
-AT_CODES_3 = 2 * K_PASS
+STAGED = 2 * K_PASS
+AT_CODES_3 = 2 * STAGED
 AT_X_12 = AT_CODES_3 + 4 * (P + DV)
 AT_LAST_PLANES = AT_X_12 + 8 * D
 AT_LAST_FIRST = AT_LAST_PLANES + 4 * K_PASS
 AT_SPLIT_SCALES = AT_LAST_FIRST + 4 * K_PASS
 AT_X_0 = AT_SPLIT_SCALES + SPLIT_WIDTH
 LATE_END = AT_X_0 + 4 * D
-STAGING_SPAN = {(3, 2): LATE_END, (0, 3): AT_LAST_FIRST, (1, 3): AT_CODES_3, (2, 3): AT_X_12, (3, 3): AT_CODES_3}
+STAGING_SPAN = {
+    (3, 2): (STAGED, LATE_END),
+    (0, 3): (STAGED, AT_LAST_FIRST),
+    (1, 3): (0, STAGED),
+    (2, 3): (STAGED, AT_X_12),
+    (3, 3): (0, AT_CODES_3),
+}
 
 
 def tile_attend_gvq_rw_w_kernel(tc, zT, cb, cb2, tw, xT, offs, offs2, out):
@@ -191,7 +198,8 @@ def tile_attend_gvq_rw_w_kernel(tc, zT, cb, cb2, tw, xT, offs, offs2, out):
         def staging(k, nb):
             if (k, nb) not in STAGING_SPAN:
                 return ring.tile([P, K_PASS], BF16, tag="staged", name=f"staged{k}_{nb}")[:]
-            span = late.tile([P, STAGING_SPAN[k, nb] // 2], BF16, offset=0, align_bytes=64, name=f"staged{k}_{nb}")
+            start, end = STAGING_SPAN[k, nb]
+            span = late.tile([P, (end - start) // 2], BF16, offset=start, align_bytes=64, name=f"staged{k}_{nb}")
             return span[:, :K_PASS]
 
         def weigh(sums, k, nb):

@@ -335,20 +335,20 @@ def tile_attend_gvq_rw_w_kernel(tc, zT, cb, cb2, tw, xT, offs, offs2, out):
                 )
 
         turn_last(neg_z[:, :, LAST_K * P :], True, False)
-
-        nc.gpsimd.memset(split_scales[:, DV // 2 : DV].bitcast(U32), 0)
-        quantize_g(0, 0, 2, *early_part)
-        quantize_x(0, 1, x_codes_0[:])
-        multiply(0, *early_part, True, False)
-
         gather_into_planes(0, LAST_NB, LAST_K, PASSES, last_first[:])
         turn_last(last_first, False, False)
-        quantize_g(0, 2, NB, *late_part)
-        multiply(0, *late_part, False, False)
+
+        nc.gpsimd.memset(split_scales[:, DV // 2 : DV].bitcast(U32), 0)
+        quantize_x(0, 1, x_codes_0[:])
+        quantize_g(0, 0, 2, *early_part)
+        multiply(0, *early_part, True, False)
+
         gather_into_planes(1, LAST_NB, LAST_K, PASSES, last_planes[:])
         turn_last(last_planes, False, True)
         weigh_in_pairs(sums, LAST_K, LAST_NB)
 
+        quantize_g(0, 2, NB, *late_part)
+        multiply(0, *late_part, False, False)
         quantize_x(1, LAST_K, x_codes_12[:])
         for k in range(1, LAST_K):
             quantize_g(k, 0, NB, g_codes_12[:, k - 1, :], g_scales[:, k - 1, :])

@@ -28,345 +28,219 @@ PASSES = T // K_PASS
 NB = DV // P
 DB = D // P
 LIST_ROWS = 16
-LAST_NB = NB - 1
-LAST_K = PASSES - 1
-RING = 4
-
-WINDOW_BLOCKS = {1: 1, 2: 2, 3: 2, 4: 4}
-PADS = (2, 3)
-WHOLE = [(0, PASSES)]
-HALVES = [(0, 2), (2, PASSES)]
-FIRST_PIECES = [[(0, 1), (1, PASSES)], WHOLE, HALVES]
-SECOND_PIECES = [WHOLE, WHOLE, HALVES]
-SPLIT_WIDTH = DV + DV // 2
-STAGED = 2 * K_PASS
-AT_CODES_3 = 2 * STAGED
-AT_X_12 = AT_CODES_3 + 4 * (P + DV)
-AT_LAST_PLANES = AT_X_12 + 8 * D
-AT_LAST_FIRST = AT_LAST_PLANES + 4 * K_PASS
-AT_SPLIT_SCALES = AT_LAST_FIRST + 4 * K_PASS
-AT_X_0 = AT_SPLIT_SCALES + SPLIT_WIDTH
-LATE_END = AT_X_0 + 4 * D
-STAGING_SPAN = {
-    (3, 2): (STAGED, LATE_END),
-    (0, 3): (STAGED, AT_LAST_FIRST),
-    (1, 3): (0, STAGED),
-    (2, 3): (STAGED, AT_X_12),
-    (3, 3): (0, AT_CODES_3),
-}
+UNIT_BANKS = 7
+EVEN = ["SV", "SV", "VS", "VS"]
+MORE = ["SV", "SS", "VS", "VS"]
+WHO = [EVEN, MORE, MORE, MORE]
 
 
 def tile_attend_gvq_rw_w_kernel(tc, zT, cb, cb2, tw, xT, offs, offs2, out):
     nc = tc.nc
     with ExitStack() as ctx:
         keep = ctx.enter_context(tc.tile_pool(name="keep", bufs=1))
-        ring = ctx.enter_context(tc.tile_pool(name="ring", bufs=RING))
         late = ctx.enter_context(tc.tile_pool(name="late", bufs=1))
         psum = ctx.enter_context(tc.psum_pool(name="psum", bufs=1))
-
-        def shared(tag, name, shape, dtype):
-            return keep.tile(shape, dtype, tag=tag, name=name, align_bytes=64)
 
         def bank_tile(i, name, shape):
             return psum.tile(shape, F32, tag=f"bank{i}", name=name)
 
         lists = [keep.tile([P, T // LIST_ROWS], U16, name=f"list{b}") for b in range(2)]
-        books = [keep.tile([P, (NB + PADS[b]) * C], F32, name=f"book{b}") for b in range(2)]
-        z = [[shared(f"z{nb}_{h}", f"z{nb}_{h}", [P, T // 2], F32) for h in range(2)] for nb in range(LAST_NB)]
-        z_last = keep.tile([P, T], F32)
-        neg_z = keep.tile([P, SLOTS, T // SLOTS], F32)
-        x_raw = [keep.tile([P, T], F32, name=f"x_raw{db}") for db in range(DB)]
-        x_pairs = [keep.tile([P, 2, T // 2], BF16, name=f"x_pairs{db}") for db in range(DB)]
+        books = [[keep.tile([P, C], F32, name=f"book{b}_{nb}") for nb in range(NB)] for b in range(2)]
+        z = [[keep.tile([P, T // 2], F32, name=f"z{nb}_{h}")[:] for h in range(2) if (nb, h) != (NB - 1, 1)] for nb in range(NB)]
+        z_span = late.tile([P, 3 * T // 2], F32, offset=0, align_bytes=64)
+        z[NB - 1].append(z_span[:, : T // 2])
+        x_raw = [keep.tile([P, DB, K_PASS], F32, name=f"x_raw{k}") for k in range(PASSES)]
+        x_pairs = [keep.tile([P, 2, DB, 2 * P], BF16, name=f"x_pairs{k}") for k in range(PASSES)]
         x_turned = keep.tile([P, PASSES, D * SLOTS], BF16, align_bytes=64)
         x_scales = keep.tile([P, PASSES, D], U8, align_bytes=64)
-        g_scales = keep.tile([P, LAST_K, DV], U8, align_bytes=64)
-        g_turned = [keep.tile([P, NB * K_PASS], BF16, align_bytes=64, name=f"g_turned{k}") for k in range(PASSES)]
-        split_codes = keep.tile([P, SPLIT_WIDTH], U32, align_bytes=64)
+        g_01 = keep.tile([P, PASSES, 2 * K_PASS], BF16, align_bytes=64)
+        g_2 = keep.tile([P, PASSES, K_PASS], BF16, align_bytes=64)
+        g_3 = keep.tile([P, PASSES, K_PASS], BF16, align_bytes=64)
+        s_01 = keep.tile([P, PASSES, 2 * P], U8, align_bytes=64)
+        s_2 = keep.tile([P, PASSES, P], U8, align_bytes=64)
+        s_3 = keep.tile([P, PASSES, P], U8, align_bytes=64)
         ident = keep.tile([P, P], F32)
         tw_rows = keep.tile([P, K_PASS], F32)
         tw_planes = keep.tile([P, SLOTS, P], F32)
         neg_w = keep.tile([P, PASSES, SLOTS], F32)
 
-        def book_start(nb):
-            return (NB - 1 - nb) * C
-
-        def clear_pad(b, i):
-            nc.gpsimd.memset(books[b][:, (NB + i) * C : (NB + i + 1) * C], 0.0)
-
-        nc.vector.memset(books[0][:, NB * C : (NB + 1) * C], 0.0)
-        make_identity(nc, ident[:])
-        for i in range(PADS[1]):
-            clear_pad(1, i)
-        clear_pad(0, 1)
-        nc.gpsimd.memset(split_codes[:, DV // 2 : DV], 0)
         nc.vector.memset(tw_rows[:], 0.0)
+        make_identity(nc, ident[:])
 
         def load_book(b, nb):
-            src = (cb, cb2)[b]
-            nc.sync.dma_start(out=books[b][:, book_start(nb) : book_start(nb) + C], in_=src[nb * P : (nb + 1) * P, :])
+            nc.sync.dma_start(out=books[b][nb][:], in_=(cb, cb2)[b][nb * P : (nb + 1) * P, :])
 
         def load_z(nb, half):
-            cols = slice(half * T // 2, (half + 1) * T // 2)
-            nc.sync.dma_start(out=z[nb][half][:], in_=zT[nb * P : (nb + 1) * P, cols])
+            nc.sync.dma_start(out=z[nb][half], in_=zT[nb * P : (nb + 1) * P, half * T // 2 : (half + 1) * T // 2])
 
-        def load_x(db, half):
-            cols = slice(half * T // 2, (half + 1) * T // 2)
-            nc.sync.dma_start(out=x_raw[db][:, cols], in_=xT[db * P : (db + 1) * P, cols])
+        def load_x(k):
+            nc.sync.dma_start(out=x_raw[k][:], in_=xT[:, k * K_PASS : (k + 1) * K_PASS].rearrange("(b p) t -> p b t", p=P))
 
-        load_book(0, 0)
         nc.sync.dma_start(lists[0][:], offs)
-        load_book(1, 0)
-        nc.sync.dma_start(lists[1][:], offs2)
-        load_x(0, 0)
-        load_x(1, 0)
+        load_book(0, 0)
         load_z(0, 0)
+        nc.sync.dma_start(lists[1][:], offs2)
+        load_book(1, 0)
         nc.sync.dma_start(out=tw_rows[0:PASSES, :], in_=tw[0:1, :].rearrange("a (k t) -> (a k) t", k=PASSES))
-        load_book(0, 1)
         load_z(0, 1)
-        load_book(1, 1)
-        load_x(0, 1)
-        load_x(1, 1)
-        nc.sync.dma_start(out=z_last[:], in_=zT[LAST_NB * P :, :])
-        load_z(1, 0)
-        load_z(1, 1)
-        load_book(0, 2)
-        load_book(1, 2)
-        load_book(0, 3)
-        load_book(1, 3)
-        load_z(2, 0)
-        load_z(2, 1)
+        for nb in range(1, NB):
+            load_book(0, nb)
+            load_z(nb, 0)
+            load_book(1, nb)
+            load_z(nb, 1)
+        for k in range(PASSES):
+            load_x(k)
 
-        def turn_weights():
-            nc.scalar.activation(
-                tw_planes[:].rearrange("p j (q r) -> p j q r", r=RUN),
-                tw_rows[:].rearrange("p (q j r) -> p j q r", j=SLOTS, r=RUN),
-                COPY,
-                scale=-BETA,
-            )
-            bank = bank_tile(0, "w_bank", [P, SLOTS, P])
-            for j in range(SLOTS):
-                nc.tensor.transpose(bank[:, j, :], tw_planes[:, j, :], ident[:])
-            nc.scalar.copy(neg_w[:], bank[:, :, 0:PASSES].rearrange("p j k -> p k j"))
+        def planes_of(ap):
+            return ap.rearrange("p j (q r) -> p j q r", r=RUN)
 
-        def negate_z():
-            nc.gpsimd.tensor_scalar(
-                neg_z[:].rearrange("p j (m r) -> p j m r", r=RUN),
-                z_last[:].rearrange("p (m j r) -> p j m r", j=SLOTS, r=RUN),
-                -1.0,
-                0.0,
-                MULT,
-                ADD,
-            )
+        def tokens_of(ap):
+            return ap.rearrange("p (q j r) -> p j q r", j=SLOTS, r=RUN)
 
-        def minus_z(first, nb, half):
-            cols = slice(half * T // 2, (half + 1) * T // 2)
-            diff = ring.tile([P, SLOTS, 2 * P], F32, tag="diff", name=f"diff{half}_{nb}")
-            nc.gpsimd.tensor_tensor(
-                diff[:].rearrange("p j (m r) -> p j m r", r=RUN),
-                first[:, cols].rearrange("p (m j r) -> p j m r", j=SLOTS, r=RUN),
-                z[nb][half][:].rearrange("p (m j r) -> p j m r", j=SLOTS, r=RUN),
-                SUBTRACT,
-            )
-            return diff
+        nc.gpsimd.tensor_scalar(planes_of(tw_planes[:]), tokens_of(tw_rows[:]), -BETA, 0.0, MULT, ADD)
+        w_bank = bank_tile(7, "w_bank", [P, SLOTS, P])
+        for j in range(SLOTS):
+            nc.tensor.transpose(w_bank[:, j, :], tw_planes[:, j, :], ident[:])
+        nc.scalar.copy(neg_w[:], w_bank[:, :, 0:PASSES].rearrange("p j k -> p k j"))
 
-        def looked_up(b, nb, k0, k1):
-            columns = WINDOW_BLOCKS[k1 - k0] * C
-            window = books[b][:, book_start(nb) : book_start(nb) + columns].bitcast(U32)
-            return window.indirect(lists[b][:, k0 * K_PASS // LIST_ROWS : k1 * K_PASS // LIST_ROWS])
+        def offsets(b, k):
+            return lists[b][:, k * K_PASS // LIST_ROWS : (k + 1) * K_PASS // LIST_ROWS]
 
-        def gather_in_token_order(nb, k0, k1, first):
-            nc.vector.tensor_copy(first[:, k0 * K_PASS : k1 * K_PASS].bitcast(U32), looked_up(0, nb, k0, k1))
+        picked = {}
 
-        def gather_into_planes(b, nb, k0, k1, planes):
-            picked = planes.bitcast(U32).rearrange("p j (m r) -> p m j r", r=RUN)
-            nc.vector.tensor_copy(picked, looked_up(b, nb, k0, k1))
+        def gather(b, nb, k):
+            if WHO[nb][k][b] == "S":
+                tile = keep.tile([P, K_PASS], F32, name=f"c{b}_{nb}_{k}")
+                nc.scalar.activation(tile[:], books[b][nb][:].indirect(offsets(b, k)), COPY)
+            else:
+                tile = keep.tile([P, SLOTS, P], F32, name=f"c{b}_{nb}_{k}")
+                nc.vector.tensor_copy(
+                    tile[:].bitcast(U32).rearrange("p j (q r) -> p q j r", r=RUN),
+                    books[b][nb][:].bitcast(U32).indirect(offsets(b, k)),
+                )
+            picked[b, nb, k] = tile
 
-        def turn(bank, planes, col, start, stop):
+        def gather_block(nb):
+            for b in range(2):
+                for k in range(PASSES):
+                    gather(b, nb, k)
+
+        def turn(bank, planes, start, stop):
             for j in range(SLOTS):
                 nc.tensor.matmul(
-                    bank[:, j, :],
-                    planes[:, j, col : col + P],
-                    ident[:],
-                    start=(start and j == 0),
-                    stop=(stop and j == SLOTS - 1),
-                    is_transpose=True,
+                    bank[:, j, :], planes[:, j, :], ident[:], start=(start and j == 0), stop=(stop and j == SLOTS - 1), is_transpose=True
                 )
 
-        def g_words(k, nb0, nb1):
-            return g_turned[k][:, nb0 * K_PASS : nb1 * K_PASS]
+        def g_unit(nb, k):
+            if nb < 2:
+                return g_01[:, k, nb * K_PASS : (nb + 1) * K_PASS]
+            return (g_2, g_3)[nb - 2][:, k, :]
 
-        def staging(k, nb):
-            if (k, nb) not in STAGING_SPAN:
-                return ring.tile([P, K_PASS], BF16, tag="staged", name=f"staged{k}_{nb}")[:]
-            start, end = STAGING_SPAN[k, nb]
-            span = late.tile([P, (end - start) // 2], BF16, offset=start, align_bytes=64, name=f"staged{k}_{nb}")
-            return span[:, :K_PASS]
+        banks = {}
 
-        def weigh(sums, k, nb):
-            staged = staging(k, nb).rearrange("p (j n) -> p j n", j=SLOTS)
-            for j in range(SLOTS):
-                nc.scalar.activation(staged[:, j, :], sums[j], COPY, scale=neg_w[:, k, j : j + 1])
-            nc.scalar.copy(g_words(k, nb, nb + 1).rearrange("p (n j) -> p n j", j=SLOTS), staged.rearrange("p j n -> p n j"))
+        def add_up(nb, k):
+            who = WHO[nb][k]
+            first = who.index("S")
+            z_k = z[nb][k // 2][:, (k % 2) * K_PASS : (k % 2 + 1) * K_PASS]
+            diff = keep.tile([P, SLOTS, P], F32, name=f"diff{nb}_{k}")
+            nc.gpsimd.tensor_tensor(planes_of(diff[:]), tokens_of(picked[first, nb, k][:]), tokens_of(z_k), SUBTRACT)
+            other = picked[1 - first, nb, k]
+            if who[1 - first] == "S":
+                laid = keep.tile([P, SLOTS, P], F32, name=f"laid{nb}_{k}")
+                nc.gpsimd.tensor_scalar(planes_of(laid[:]), tokens_of(other[:]), 1.0, 0.0, MULT, ADD)
+                other = laid
+            bank = bank_tile((nb * PASSES + k) % UNIT_BANKS, f"e{nb}_{k}", [P, SLOTS, P])
+            turn(bank, diff, True, False)
+            turn(bank, other, False, True)
+            banks[nb, k] = bank
 
-        def weigh_in_pairs(sums, k, nb):
-            staged = staging(k, nb)
-            pairs = staged.rearrange("p (u n e) -> p u e n", u=2, e=2)
-            for j in range(SLOTS):
-                nc.scalar.activation(pairs[:, j // 2, j % 2, :], sums[j], COPY, scale=neg_w[:, k, j : j + 1])
-            nc.scalar.copy(
-                g_words(k, nb, nb + 1).bitcast(F32).rearrange("p (n u) -> p n u", u=2),
-                staged.bitcast(F32).rearrange("p (u n) -> p n u", u=2),
+        def weigh(nb, k):
+            nc.vector.tensor_tensor(
+                g_unit(nb, k).rearrange("p (n j) -> p n j", j=SLOTS),
+                banks[nb, k][:].rearrange("p j n -> p n j"),
+                neg_w[:, k, :].unsqueeze(1).to_broadcast([P, P, SLOTS]),
+                MULT,
             )
 
-        def cast_x(db, half):
-            cols = slice(half * T // 2, (half + 1) * T // 2)
-            src = x_raw[db][:, cols].rearrange("p (q u e r) -> p u q r e", u=2, e=2, r=RUN)
-            for u in range(2):
-                dst = x_pairs[db][:, u, half * T // 4 : (half + 1) * T // 4]
-                nc.scalar.copy(dst.rearrange("p (q r e) -> p q r e", r=RUN, e=2), src[:, u])
-
-        def turn_x(k):
-            bank = bank_tile(PASSES + k, f"x_bank{k}", [P, DB, 2, P])
+        def prepare_x(k):
+            nc.scalar.copy(
+                x_pairs[k][:].rearrange("p u b (q r e) -> p u (b q) r e", r=RUN, e=2),
+                x_raw[k][:].rearrange("p b (q u e r) -> p u (b q) r e", u=2, e=2, r=RUN),
+            )
+            bank = bank_tile((7, 4)[k % 2], f"x_bank{k}", [P, DB, 2, P])
             for db in range(DB):
                 for u in range(2):
-                    words = x_pairs[db][:, u, :].bitcast(F32)
-                    nc.tensor.transpose(bank[:, db, u, :], words[:, k * P : (k + 1) * P], ident[:])
+                    nc.tensor.transpose(bank[:, db, u, :], x_pairs[k][:, u, db, :].bitcast(F32), ident[:])
             nc.scalar.copy(
                 x_turned[:, k, :].bitcast(F32).rearrange("p (b d u) -> p b d u", b=DB, u=2),
                 bank[:].rearrange("p b u d -> p b d u"),
             )
 
-        for half in range(2):
-            for db in range(DB):
-                cast_x(db, half)
-            turn_x(2 * half)
-            turn_x(2 * half + 1)
-            if half == 0:
-                turn_weights()
+        gather_block(0)
+        for nb in range(NB):
+            for k in range(PASSES):
+                add_up(nb, k)
+            if nb + 1 < NB:
+                gather_block(nb + 1)
+            for k in range(PASSES):
+                weigh(nb, k)
+        for k in range(PASSES):
+            prepare_x(k)
 
-        for nb in range(LAST_NB):
-            first = shared("z0_0" if nb == 1 else "first", f"first{nb}", [P, T], F32)
-            for k0, k1 in FIRST_PIECES[nb]:
-                gather_in_token_order(nb, k0, k1, first)
-            second = shared("z0_1" if nb == 1 else "second", f"second{nb}", [P, SLOTS, T // SLOTS], F32)
-            for k0, k1 in SECOND_PIECES[nb]:
-                gather_into_planes(1, nb, k0, k1, second[:, :, k0 * P : k1 * P])
-            for half in range(2):
-                diff = minus_z(first, nb, half)
-                for k in (2 * half, 2 * half + 1):
-                    bank = bank_tile(PASSES * (nb % 2) + k, f"e{k}_{nb}", [P, SLOTS, P])
-                    turn(bank, diff, (k % 2) * P, True, False)
-                    turn(bank, second, k * P, False, True)
-                    weigh([bank[:, j, :] for j in range(SLOTS)], k, nb)
-            if nb == 0:
-                negate_z()
+        x_codes = late.tile([P, PASSES, D], U32, offset=0, align_bytes=64)
+        c_01 = late.tile([P, PASSES, 2 * P], U32, offset=4096, align_bytes=64)
+        c_2 = late.tile([P, PASSES, P], U32, offset=8192, align_bytes=64)
+        c_3 = late.tile([P, PASSES, P], U32, offset=8192 + 2048, align_bytes=64)
 
-        both = shared("z2_1", "both_last", [P, 2, SLOTS, LAST_K * P], F32)
-        first, second = both[:, 0], both[:, 1]
-        banks = [bank_tile(PASSES + k, f"e{k}_{LAST_NB}", [P, SLOTS, P]) for k in range(LAST_K)]
-        for k in range(LAST_K):
-            turn(banks[k], neg_z, k * P, True, False)
-        for k0, k1 in ((0, 2), (2, LAST_K)):
-            gather_into_planes(0, LAST_NB, k0, k1, first[:, :, k0 * P : k1 * P])
-            gather_into_planes(1, LAST_NB, k0, k1, second[:, :, k0 * P : k1 * P])
-            for k in range(k0, k1):
-                turn(banks[k], first, k * P, False, False)
-            for k in range(k0, k1):
-                turn(banks[k], second, k * P, False, True)
-                weigh([banks[k][:, j, :] for j in range(SLOTS)], k, LAST_NB)
-
-        split_scales = late.tile([P, SPLIT_WIDTH], U8, offset=AT_SPLIT_SCALES, align_bytes=64)
-        x_codes_0 = late.tile([P, D], U32, offset=AT_X_0, align_bytes=64)
-        x_codes_12 = late.tile([P, 2 * D], U32, offset=AT_X_12, align_bytes=64)
-        codes_3 = late.tile([P, P + DV], U32, offset=AT_CODES_3, align_bytes=64)
-        last_x_codes = late.tile([P, P], U32, offset=0, align_bytes=64)
-        last_first = late.tile([P, SLOTS, P], F32, offset=AT_LAST_FIRST, align_bytes=64)
-        last_planes = late.tile([P, SLOTS, P], F32, offset=AT_LAST_PLANES, align_bytes=64)
-        g_codes_12 = keep.tile([P, 2, DV], U32, align_bytes=64)
-        x_codes = [
-            [x_codes_0[:, :P], x_codes_0[:, P:]],
-            [x_codes_12[:, :P], x_codes_12[:, P:D]],
-            [x_codes_12[:, D : D + P], x_codes_12[:, D + P :]],
-            [codes_3[:, :P], last_x_codes[:]],
-        ]
-        g_codes_3 = codes_3[:, P:]
-
-        def quantize_x(k0, k1, codes):
+        def quantize(codes, scales, values, k0, k1, fmt):
             nc.vector.quantize_mx(
-                out=codes.bitcast(E4M3),
-                scales=x_scales[:, k0:k1, :].rearrange("p k d -> p (k d)"),
-                in_=x_turned[:, k0:k1, :].rearrange("p k c -> p (k c)"),
+                out=codes[:, k0:k1, :].rearrange("p k c -> p (k c)").bitcast(fmt),
+                scales=scales[:, k0:k1, :].rearrange("p k c -> p (k c)"),
+                in_=values[:, k0:k1, :].rearrange("p k c -> p (k c)"),
             )
 
-        def quantize_last_x(db):
-            nc.vector.quantize_mx(
-                out=x_codes[LAST_K][db].bitcast(E4M3),
-                scales=x_scales[:, LAST_K, db * P : (db + 1) * P],
-                in_=x_turned[:, LAST_K, db * K_PASS : (db + 1) * K_PASS],
+        def multiply(acc, db, k, codes, scales, start, stop):
+            nc.tensor.matmul_mx(
+                out=acc,
+                lhsT=x_codes[:, k, db * P : (db + 1) * P].bitcast(E4M3),
+                lhsT_scale=x_scales[:, k, db * P : (db + 1) * P],
+                rhs=codes[:, k, :].bitcast(E5M2),
+                rhs_scale=scales[:, k, :],
+                start=start,
+                stop=stop,
             )
 
-        def quantize_g(k, nb0, nb1, codes, scales):
-            cols = slice(nb0 * P, nb1 * P)
-            nc.vector.quantize_mx(out=codes[:, cols].bitcast(E5M2), scales=scales[:, cols], in_=g_words(k, nb0, nb1))
+        def out_cols(c0, c1):
+            return out[:, c0:c1].rearrange("(b p) n -> p b n", p=P)
 
-        def multiply(k, codes, scales, start, stop):
-            for db in range(DB):
-                nc.tensor.matmul_mx(
-                    out=acc[db][:],
-                    lhsT=x_codes[k][db].bitcast(E4M3),
-                    lhsT_scale=x_scales[:, k, db * P : (db + 1) * P],
-                    rhs=codes.bitcast(E5M2),
-                    rhs_scale=scales,
-                    start=start,
-                    stop=stop,
-                )
-
-        early_part = (split_codes[:, :DV], split_scales[:, :DV])
-        late_part = (split_codes[:, SPLIT_WIDTH - DV :], split_scales[:, SPLIT_WIDTH - DV :])
-        acc = [bank_tile(DB + db, f"acc{db}", [P, DV]) for db in range(DB)]
-
-        last_banks = [bank_tile(PASSES + LAST_K, "last0", [P, 1, P]), bank_tile(0, "last1", [P, 1, P]), bank_tile(1, "last23", [P, 2, P])]
-        sums = [last_banks[0][:, 0, :], last_banks[1][:, 0, :], last_banks[2][:, 0, :], last_banks[2][:, 1, :]]
-
-        def turn_last(planes, start, stop):
-            for j in range(SLOTS):
-                nc.tensor.matmul(
-                    sums[j], planes[:, j, :], ident[:], start=(start and j != 3), stop=(stop and j != 2), is_transpose=True
-                )
-
-        turn_last(neg_z[:, :, LAST_K * P :], True, False)
-        gather_into_planes(0, LAST_NB, LAST_K, PASSES, last_first[:])
-        turn_last(last_first, False, False)
-
-        nc.gpsimd.memset(split_scales[:, DV // 2 : DV].bitcast(U32), 0)
-        quantize_x(0, 1, x_codes_0[:])
-        quantize_g(0, 0, 2, *early_part)
-        multiply(0, *early_part, True, False)
-
-        gather_into_planes(1, LAST_NB, LAST_K, PASSES, last_planes[:])
-        turn_last(last_planes, False, True)
-        weigh_in_pairs(sums, LAST_K, LAST_NB)
-
-        quantize_g(0, 2, NB, *late_part)
-        multiply(0, *late_part, False, False)
-        quantize_x(1, LAST_K, x_codes_12[:])
-        for k in range(1, LAST_K):
-            quantize_g(k, 0, NB, g_codes_12[:, k - 1, :], g_scales[:, k - 1, :])
-            multiply(k, g_codes_12[:, k - 1, :], g_scales[:, k - 1, :], False, False)
-        last_scales = g_scales[:, LAST_K - 1, :]
-        quantize_last_x(0)
-        quantize_g(LAST_K, 0, 2, g_codes_3, last_scales)
-        quantize_g(LAST_K, 2, LAST_NB, g_codes_3, last_scales)
-        quantize_g(LAST_K, LAST_NB, NB, g_codes_3, last_scales)
-        quantize_last_x(1)
-        multiply(LAST_K, g_codes_3, last_scales, False, True)
-
-        result = [keep.tile([P, DV], F32, name=f"result{db}") for db in range(DB)]
+        acc_01 = bank_tile(5, "acc_01", [P, DB, 2 * P])
         for half in range(2):
-            cols = slice(half * DV // 2, (half + 1) * DV // 2)
-            nc.vector.tensor_copy(result[0][:, cols], acc[0][:, cols])
-            nc.sync.dma_start(out=out[0:P, cols], in_=result[0][:, cols])
-        for half, queue in enumerate((nc.sync, nc.scalar)):
-            cols = slice(half * DV // 2, (half + 1) * DV // 2)
-            nc.scalar.copy(result[1][:, cols], acc[1][:, cols])
-            queue.dma_start(out=out[P : 2 * P, cols], in_=result[1][:, cols])
+            quantize(x_codes, x_scales, x_turned, 2 * half, 2 * half + 2, E4M3)
+            quantize(c_01, s_01, g_01, 2 * half, 2 * half + 2, E5M2)
+            for k in (2 * half, 2 * half + 1):
+                for db in range(DB):
+                    multiply(acc_01[:, db, :], db, k, c_01, s_01, k == 0 and db == 0, k == PASSES - 1 and db == DB - 1)
+        r_01 = keep.tile([P, DB, 2 * P], F32)
+        nc.scalar.copy(r_01[:], acc_01[:])
+        nc.sync.dma_start(out=out_cols(0, 2 * P), in_=r_01[:])
+
+        acc_2 = bank_tile(6, "acc_2", [P, DB, P])
+        quantize(c_2, s_2, g_2, 0, PASSES, E5M2)
+        for k in range(PASSES):
+            for db in range(DB):
+                multiply(acc_2[:, db, :], db, k, c_2, s_2, k == 0 and db == 0, k == PASSES - 1 and db == DB - 1)
+        r_2 = keep.tile([P, DB, P], F32)
+        nc.scalar.copy(r_2[:], acc_2[:])
+        nc.sync.dma_start(out=out_cols(2 * P, 3 * P), in_=r_2[:])
+
+        acc_3 = [bank_tile(2 + db, f"acc_3_{db}", [P, P]) for db in range(DB)]
+        for k0, k1 in ((0, 2), (2, 3), (3, 4)):
+            quantize(c_3, s_3, g_3, k0, k1, E5M2)
+            for k in range(k0, k1):
+                for db in range(DB):
+                    multiply(acc_3[db][:], db, k, c_3, s_3, k == 0, k == PASSES - 1)
+        r_3 = [keep.tile([P, P], F32, name=f"r_3_{db}") for db in range(DB)]
+        nc.vector.tensor_copy(r_3[0][:], acc_3[0][:])
+        nc.sync.dma_start(out=out[0:P, 3 * P :], in_=r_3[0][:])
+        nc.scalar.copy(r_3[1][:], acc_3[1][:])
+        nc.scalar.dma_start(out=out[P:, 3 * P :], in_=r_3[1][:])

@@ -29,9 +29,11 @@ NB = DV // P
 DB = D // P
 LIST_ROWS = 16
 UNIT_BANKS = 7
-EVEN = ["SV", "SV", "VS", "VS"]
-MORE = ["SV", "SS", "VS", "VS"]
-WHO = [EVEN, MORE, MORE, MORE]
+PAD = 352
+EVEN = [(0, 0, 1), (0, 1, 2), (1, 2, 3), (1, 3, 4)]
+MORE = [(0, 0, 1), (0, 1, 2), (0, 3, 4), (1, 2, 3), (1, 3, 4)]
+SCALAR_PIECES = [EVEN, EVEN, MORE, MORE]
+VECTOR_PIECES = [[(0, 2, 4), (1, 0, 2)]] * 2 + [[(0, 2, 3), (1, 0, 2)]] * 2
 
 
 def tile_attend_gvq_rw_w_kernel(tc, zT, cb, cb2, tw, xT, offs, offs2, out):
@@ -45,30 +47,31 @@ def tile_attend_gvq_rw_w_kernel(tc, zT, cb, cb2, tw, xT, offs, offs2, out):
             return psum.tile(shape, F32, tag=f"bank{i}", name=name)
 
         lists = [keep.tile([P, T // LIST_ROWS], U16, name=f"list{b}") for b in range(2)]
-        books = [[keep.tile([P, C], F32, name=f"book{b}_{nb}") for nb in range(NB)] for b in range(2)]
-        z = [[keep.tile([P, T // 2], F32, name=f"z{nb}_{h}")[:] for h in range(2) if (nb, h) != (NB - 1, 1)] for nb in range(NB)]
-        z_span = late.tile([P, 3 * T // 2], F32, offset=0, align_bytes=64)
-        z[NB - 1].append(z_span[:, : T // 2])
+        books = [[keep.tile([P, C + PAD], F32, name=f"book{b}_{nb}") for nb in range(NB)] for b in range(2)]
+        z = [[keep.tile([P, T // 2], F32, name=f"z{nb}_{h}")[:] for h in range(2)] for nb in range(NB - 1)]
+        z_first = late.tile([P, T // 2 * 2], F32, offset=0, align_bytes=64)
+        z_span = late.tile([P, 3 * T // 2], F32, offset=8192, align_bytes=64)
+        z.append([z_first[:, : T // 2], z_span[:, : T // 2]])
         x_raw = [keep.tile([P, DB, K_PASS], F32, name=f"x_raw{k}") for k in range(PASSES)]
-        x_pairs = [keep.tile([P, 2, DB, 2 * P], BF16, name=f"x_pairs{k}") for k in range(PASSES)]
-        x_turned = keep.tile([P, PASSES, D * SLOTS], BF16, align_bytes=64)
+        x_turned = [keep.tile([P, D * SLOTS], BF16, align_bytes=64, name=f"x_turned{k}") for k in range(PASSES)]
         x_scales = keep.tile([P, PASSES, D], U8, align_bytes=64)
-        g_01 = keep.tile([P, PASSES, 2 * K_PASS], BF16, align_bytes=64)
-        g_2 = keep.tile([P, PASSES, K_PASS], BF16, align_bytes=64)
-        g_3 = keep.tile([P, PASSES, K_PASS], BF16, align_bytes=64)
-        s_01 = keep.tile([P, PASSES, 2 * P], U8, align_bytes=64)
-        s_2 = keep.tile([P, PASSES, P], U8, align_bytes=64)
-        s_3 = keep.tile([P, PASSES, P], U8, align_bytes=64)
+        g_turned = [keep.tile([P, NB * K_PASS], BF16, align_bytes=64, name=f"g_turned{k}") for k in range(PASSES)]
+        g_scales = keep.tile([P, PASSES, DV], U8, align_bytes=64)
         ident = keep.tile([P, P], F32)
         tw_rows = keep.tile([P, K_PASS], F32)
         tw_planes = keep.tile([P, SLOTS, P], F32)
         neg_w = keep.tile([P, PASSES, SLOTS], F32)
 
-        nc.vector.memset(tw_rows[:], 0.0)
+        nc.gpsimd.memset(tw_rows[:], 0.0)
+        for b in range(2):
+            nc.vector.memset(books[b][0][:, C:], 0.0)
         make_identity(nc, ident[:])
+        for nb in range(1, NB):
+            for b in range(2):
+                nc.gpsimd.memset(books[b][nb][:, C:], 0.0)
 
         def load_book(b, nb):
-            nc.sync.dma_start(out=books[b][nb][:], in_=(cb, cb2)[b][nb * P : (nb + 1) * P, :])
+            nc.sync.dma_start(out=books[b][nb][:, :C], in_=(cb, cb2)[b][nb * P : (nb + 1) * P, :])
 
         def load_z(nb, half):
             nc.sync.dma_start(out=z[nb][half], in_=zT[nb * P : (nb + 1) * P, half * T // 2 : (half + 1) * T // 2])
@@ -78,10 +81,10 @@ def tile_attend_gvq_rw_w_kernel(tc, zT, cb, cb2, tw, xT, offs, offs2, out):
 
         nc.sync.dma_start(lists[0][:], offs)
         load_book(0, 0)
+        nc.sync.dma_start(out=tw_rows[0:PASSES, :], in_=tw[0:1, :].rearrange("a (k t) -> (a k) t", k=PASSES))
         load_z(0, 0)
         nc.sync.dma_start(lists[1][:], offs2)
         load_book(1, 0)
-        nc.sync.dma_start(out=tw_rows[0:PASSES, :], in_=tw[0:1, :].rearrange("a (k t) -> (a k) t", k=PASSES))
         load_z(0, 1)
         for nb in range(1, NB):
             load_book(0, nb)
@@ -103,27 +106,38 @@ def tile_attend_gvq_rw_w_kernel(tc, zT, cb, cb2, tw, xT, offs, offs2, out):
             nc.tensor.transpose(w_bank[:, j, :], tw_planes[:, j, :], ident[:])
         nc.scalar.copy(neg_w[:], w_bank[:, :, 0:PASSES].rearrange("p j k -> p k j"))
 
-        def offsets(b, k):
-            return lists[b][:, k * K_PASS // LIST_ROWS : (k + 1) * K_PASS // LIST_ROWS]
+        def offsets(b, k0, k1):
+            return lists[b][:, k0 * K_PASS // LIST_ROWS : k1 * K_PASS // LIST_ROWS]
 
         picked = {}
-
-        def gather(b, nb, k):
-            if WHO[nb][k][b] == "S":
-                tile = keep.tile([P, K_PASS], F32, name=f"c{b}_{nb}_{k}")
-                nc.scalar.activation(tile[:], books[b][nb][:].indirect(offsets(b, k)), COPY)
-            else:
-                tile = keep.tile([P, SLOTS, P], F32, name=f"c{b}_{nb}_{k}")
-                nc.vector.tensor_copy(
-                    tile[:].bitcast(U32).rearrange("p j (q r) -> p q j r", r=RUN),
-                    books[b][nb][:].bitcast(U32).indirect(offsets(b, k)),
-                )
-            picked[b, nb, k] = tile
+        terms = {(nb, k): [] for nb in range(NB) for k in range(PASSES)}
 
         def gather_block(nb):
-            for b in range(2):
-                for k in range(PASSES):
-                    gather(b, nb, k)
+            for b, k0, k1 in SCALAR_PIECES[nb]:
+                tile = keep.tile([P, (k1 - k0) * K_PASS], F32, name=f"s{b}_{nb}_{k0}")
+                nc.scalar.activation(tile[:], books[b][nb][:].indirect(offsets(b, k0, k1)), COPY)
+                picked[b, nb, k0] = tile
+            for b, k0, k1 in VECTOR_PIECES[nb]:
+                tile = keep.tile([P, SLOTS, (k1 - k0) * P], F32, name=f"v{b}_{nb}_{k0}")
+                nc.vector.tensor_copy(
+                    tile[:].bitcast(U32).rearrange("p j (q r) -> p q j r", r=RUN),
+                    books[b][nb][:].bitcast(U32).indirect(offsets(b, k0, k1)),
+                )
+                picked[b, nb, k0] = tile
+
+        def lay_planes(nb):
+            for b, k0, k1 in SCALAR_PIECES[nb]:
+                laid = keep.tile([P, SLOTS, (k1 - k0) * P], F32, name=f"laid{b}_{nb}_{k0}")
+                if terms[nb, k0]:
+                    nc.gpsimd.tensor_scalar(planes_of(laid[:]), tokens_of(picked[b, nb, k0][:]), 1.0, 0.0, MULT, ADD)
+                else:
+                    z_k = z[nb][k0 // 2][:, (k0 % 2) * K_PASS : (k0 % 2 + k1 - k0) * K_PASS]
+                    nc.gpsimd.tensor_tensor(planes_of(laid[:]), tokens_of(picked[b, nb, k0][:]), tokens_of(z_k), SUBTRACT)
+                for k in range(k0, k1):
+                    terms[nb, k].append(laid[:, :, (k - k0) * P : (k - k0 + 1) * P])
+            for b, k0, k1 in VECTOR_PIECES[nb]:
+                for k in range(k0, k1):
+                    terms[nb, k].append(picked[b, nb, k0][:, :, (k - k0) * P : (k - k0 + 1) * P])
 
         def turn(bank, planes, start, stop):
             for j in range(SLOTS):
@@ -131,53 +145,40 @@ def tile_attend_gvq_rw_w_kernel(tc, zT, cb, cb2, tw, xT, offs, offs2, out):
                     bank[:, j, :], planes[:, j, :], ident[:], start=(start and j == 0), stop=(stop and j == SLOTS - 1), is_transpose=True
                 )
 
-        def g_unit(nb, k):
-            if nb < 2:
-                return g_01[:, k, nb * K_PASS : (nb + 1) * K_PASS]
-            return (g_2, g_3)[nb - 2][:, k, :]
-
         banks = {}
 
         def add_up(nb, k):
-            who = WHO[nb][k]
-            first = who.index("S")
-            z_k = z[nb][k // 2][:, (k % 2) * K_PASS : (k % 2 + 1) * K_PASS]
-            diff = keep.tile([P, SLOTS, P], F32, name=f"diff{nb}_{k}")
-            nc.gpsimd.tensor_tensor(planes_of(diff[:]), tokens_of(picked[first, nb, k][:]), tokens_of(z_k), SUBTRACT)
-            other = picked[1 - first, nb, k]
-            if who[1 - first] == "S":
-                laid = keep.tile([P, SLOTS, P], F32, name=f"laid{nb}_{k}")
-                nc.gpsimd.tensor_scalar(planes_of(laid[:]), tokens_of(other[:]), 1.0, 0.0, MULT, ADD)
-                other = laid
             bank = bank_tile((nb * PASSES + k) % UNIT_BANKS, f"e{nb}_{k}", [P, SLOTS, P])
-            turn(bank, diff, True, False)
-            turn(bank, other, False, True)
+            turn(bank, terms[nb, k][0], True, False)
+            turn(bank, terms[nb, k][1], False, True)
             banks[nb, k] = bank
 
         def weigh(nb, k):
             nc.vector.tensor_tensor(
-                g_unit(nb, k).rearrange("p (n j) -> p n j", j=SLOTS),
-                banks[nb, k][:].rearrange("p j n -> p n j"),
+                g_turned[k][:, nb * K_PASS : (nb + 1) * K_PASS].rearrange("p (n j) -> p n j", j=SLOTS),
                 neg_w[:, k, :].unsqueeze(1).to_broadcast([P, P, SLOTS]),
+                banks[nb, k][:].rearrange("p j n -> p n j"),
                 MULT,
             )
 
         def prepare_x(k):
+            pairs = late.tile([P, 2, DB, 2 * P], BF16, offset=2048 * k, align_bytes=64, name=f"x_pairs{k}")
             nc.scalar.copy(
-                x_pairs[k][:].rearrange("p u b (q r e) -> p u (b q) r e", r=RUN, e=2),
+                pairs[:].rearrange("p u b (q r e) -> p u (b q) r e", r=RUN, e=2),
                 x_raw[k][:].rearrange("p b (q u e r) -> p u (b q) r e", u=2, e=2, r=RUN),
             )
-            bank = bank_tile((7, 4)[k % 2], f"x_bank{k}", [P, DB, 2, P])
+            bank = bank_tile((7, 2)[k % 2], f"x_bank{k}", [P, DB, 2, P])
             for db in range(DB):
                 for u in range(2):
-                    nc.tensor.transpose(bank[:, db, u, :], x_pairs[k][:, u, db, :].bitcast(F32), ident[:])
+                    nc.tensor.transpose(bank[:, db, u, :], pairs[:, u, db, :].bitcast(F32), ident[:])
             nc.scalar.copy(
-                x_turned[:, k, :].bitcast(F32).rearrange("p (b d u) -> p b d u", b=DB, u=2),
+                x_turned[k][:].bitcast(F32).rearrange("p (b d u) -> p b d u", b=DB, u=2),
                 bank[:].rearrange("p b u d -> p b d u"),
             )
 
         gather_block(0)
         for nb in range(NB):
+            lay_planes(nb)
             for k in range(PASSES):
                 add_up(nb, k)
             if nb + 1 < NB:
@@ -187,60 +188,48 @@ def tile_attend_gvq_rw_w_kernel(tc, zT, cb, cb2, tw, xT, offs, offs2, out):
         for k in range(PASSES):
             prepare_x(k)
 
-        x_codes = late.tile([P, PASSES, D], U32, offset=0, align_bytes=64)
-        c_01 = late.tile([P, PASSES, 2 * P], U32, offset=4096, align_bytes=64)
-        c_2 = late.tile([P, PASSES, P], U32, offset=8192, align_bytes=64)
-        c_3 = late.tile([P, PASSES, P], U32, offset=8192 + 2048, align_bytes=64)
+        x_codes = late.tile([P, PASSES, D], U32, offset=8192, align_bytes=64)
+        g_codes = late.tile([P, PASSES, DV], U32, offset=8192 + 4096, align_bytes=64)
 
-        def quantize(codes, scales, values, k0, k1, fmt):
+        def quantize_g(k, nb0, nb1):
             nc.vector.quantize_mx(
-                out=codes[:, k0:k1, :].rearrange("p k c -> p (k c)").bitcast(fmt),
-                scales=scales[:, k0:k1, :].rearrange("p k c -> p (k c)"),
-                in_=values[:, k0:k1, :].rearrange("p k c -> p (k c)"),
+                out=g_codes[:, k, nb0 * P : nb1 * P].bitcast(E5M2),
+                scales=g_scales[:, k, nb0 * P : nb1 * P],
+                in_=g_turned[k][:, nb0 * K_PASS : nb1 * K_PASS],
             )
 
-        def multiply(acc, db, k, codes, scales, start, stop):
-            nc.tensor.matmul_mx(
-                out=acc,
-                lhsT=x_codes[:, k, db * P : (db + 1) * P].bitcast(E4M3),
-                lhsT_scale=x_scales[:, k, db * P : (db + 1) * P],
-                rhs=codes[:, k, :].bitcast(E5M2),
-                rhs_scale=scales[:, k, :],
-                start=start,
-                stop=stop,
+        def quantize_x(k, db0, db1):
+            nc.vector.quantize_mx(
+                out=x_codes[:, k, db0 * P : db1 * P].bitcast(E4M3),
+                scales=x_scales[:, k, db0 * P : db1 * P],
+                in_=x_turned[k][:, db0 * K_PASS : db1 * K_PASS],
             )
 
-        def out_cols(c0, c1):
-            return out[:, c0:c1].rearrange("(b p) n -> p b n", p=P)
+        acc = [bank_tile(3 + db, f"acc{db}", [P, DV]) for db in range(DB)]
 
-        acc_01 = bank_tile(5, "acc_01", [P, DB, 2 * P])
-        for half in range(2):
-            quantize(x_codes, x_scales, x_turned, 2 * half, 2 * half + 2, E4M3)
-            quantize(c_01, s_01, g_01, 2 * half, 2 * half + 2, E5M2)
-            for k in (2 * half, 2 * half + 1):
-                for db in range(DB):
-                    multiply(acc_01[:, db, :], db, k, c_01, s_01, k == 0 and db == 0, k == PASSES - 1 and db == DB - 1)
-        r_01 = keep.tile([P, DB, 2 * P], F32)
-        nc.scalar.copy(r_01[:], acc_01[:])
-        nc.sync.dma_start(out=out_cols(0, 2 * P), in_=r_01[:])
-
-        acc_2 = bank_tile(6, "acc_2", [P, DB, P])
-        quantize(c_2, s_2, g_2, 0, PASSES, E5M2)
-        for k in range(PASSES):
+        def multiply(k):
             for db in range(DB):
-                multiply(acc_2[:, db, :], db, k, c_2, s_2, k == 0 and db == 0, k == PASSES - 1 and db == DB - 1)
-        r_2 = keep.tile([P, DB, P], F32)
-        nc.scalar.copy(r_2[:], acc_2[:])
-        nc.sync.dma_start(out=out_cols(2 * P, 3 * P), in_=r_2[:])
+                nc.tensor.matmul_mx(
+                    out=acc[db][:],
+                    lhsT=x_codes[:, k, db * P : (db + 1) * P].bitcast(E4M3),
+                    lhsT_scale=x_scales[:, k, db * P : (db + 1) * P],
+                    rhs=g_codes[:, k, :].bitcast(E5M2),
+                    rhs_scale=g_scales[:, k, :],
+                    start=(k == 0),
+                    stop=(k == PASSES - 1),
+                )
 
-        acc_3 = [bank_tile(2 + db, f"acc_3_{db}", [P, P]) for db in range(DB)]
-        for k0, k1 in ((0, 2), (2, 3), (3, 4)):
-            quantize(c_3, s_3, g_3, k0, k1, E5M2)
-            for k in range(k0, k1):
-                for db in range(DB):
-                    multiply(acc_3[db][:], db, k, c_3, s_3, k == 0, k == PASSES - 1)
-        r_3 = [keep.tile([P, P], F32, name=f"r_3_{db}") for db in range(DB)]
-        nc.vector.tensor_copy(r_3[0][:], acc_3[0][:])
-        nc.sync.dma_start(out=out[0:P, 3 * P :], in_=r_3[0][:])
-        nc.scalar.copy(r_3[1][:], acc_3[1][:])
-        nc.scalar.dma_start(out=out[P:, 3 * P :], in_=r_3[1][:])
+        for k in range(PASSES):
+            quantize_x(k, 0, DB)
+            quantize_g(k, 0, NB)
+            multiply(k)
+
+        result = [keep.tile([P, DV], F32, name=f"result{db}") for db in range(DB)]
+        for half in range(2):
+            cols = slice(half * DV // 2, (half + 1) * DV // 2)
+            nc.vector.tensor_copy(result[0][:, cols], acc[0][:, cols])
+            nc.sync.dma_start(out=out[0:P, cols], in_=result[0][:, cols])
+        for half, queue in enumerate((nc.sync, nc.scalar)):
+            cols = slice(half * DV // 2, (half + 1) * DV // 2)
+            nc.scalar.copy(result[1][:, cols], acc[1][:, cols])
+            queue.dma_start(out=out[P : 2 * P, cols], in_=result[1][:, cols])

@@ -28,12 +28,13 @@ PASSES = T // K_PASS
 NB = DV // P
 DB = D // P
 LIST_ROWS = 16
-UNIT_BANKS = 7
-PAD = 352
-EVEN = [(0, 0, 1), (0, 1, 2), (1, 2, 3), (1, 3, 4)]
-MORE = [(0, 0, 1), (0, 1, 2), (0, 3, 4), (1, 2, 3), (1, 3, 4)]
-SCALAR_PIECES = [EVEN, EVEN, MORE, MORE]
-VECTOR_PIECES = [[(0, 2, 4), (1, 0, 2)]] * 2 + [[(0, 2, 3), (1, 0, 2)]] * 2
+UNIT_BANKS = 8
+CROSSED = [(0, 0), (0, 1), (1, 2), (1, 3)]
+STRAIGHT = [(0, 0), (0, 1), (0, 2), (0, 3)]
+SCALAR_PIECES = [CROSSED, CROSSED, STRAIGHT, STRAIGHT]
+VECTOR_PIECES = [[(0, 2), (0, 3), (1, 0), (1, 1)]] * 2 + [[(1, 0), (1, 1), (1, 2)]] * 2
+BOTH_ON_SCALAR = (2, 3)
+LEAD = 6
 
 
 def tile_attend_gvq_rw_w_kernel(tc, zT, cb, cb2, tw, xT, offs, offs2, out):
@@ -41,21 +42,17 @@ def tile_attend_gvq_rw_w_kernel(tc, zT, cb, cb2, tw, xT, offs, offs2, out):
     with ExitStack() as ctx:
         keep = ctx.enter_context(tc.tile_pool(name="keep", bufs=1))
         late = ctx.enter_context(tc.tile_pool(name="late", bufs=1))
+        ring = ctx.enter_context(tc.tile_pool(name="ring", bufs=LEAD))
         psum = ctx.enter_context(tc.psum_pool(name="psum", bufs=1))
 
         def bank_tile(i, name, shape):
             return psum.tile(shape, F32, tag=f"bank{i}", name=name)
 
         lists = [keep.tile([P, T // LIST_ROWS], U16, name=f"list{b}") for b in range(2)]
-        books = [[keep.tile([P, C + PAD], F32, name=f"book{b}_{nb}") for nb in range(NB)] for b in range(2)]
-        z = [[keep.tile([P, T // 2], F32, name=f"z{nb}_{h}")[:] for h in range(2)] for nb in range(NB - 1)]
-        z_first = late.tile([P, T // 2 * 2], F32, offset=0, align_bytes=64)
-        z_span = late.tile([P, 3 * T // 2], F32, offset=8192, align_bytes=64)
-        z.append([z_first[:, : T // 2], z_span[:, : T // 2]])
-        x_raw = [keep.tile([P, DB, K_PASS], F32, name=f"x_raw{k}") for k in range(PASSES)]
-        x_turned = [keep.tile([P, D * SLOTS], BF16, align_bytes=64, name=f"x_turned{k}") for k in range(PASSES)]
+        books = [[keep.tile([P, C], F32, tag=f"book{b}_{nb}", name=f"book{b}_{nb}") for nb in range(NB)] for b in range(2)]
+        z = [[keep.tile([P, T // 2], F32, tag=f"z{nb}_{h}", name=f"z{nb}_{h}")[:] for h in range(2)] for nb in range(NB)]
+        x_raw = [keep.tile([P, DB, K_PASS], F32, name=f"x_raw{k}")[:] for k in range(PASSES)]
         x_scales = keep.tile([P, PASSES, D], U8, align_bytes=64)
-        g_turned = [keep.tile([P, NB * K_PASS], BF16, align_bytes=64, name=f"g_turned{k}") for k in range(PASSES)]
         g_scales = keep.tile([P, PASSES, DV], U8, align_bytes=64)
         ident = keep.tile([P, P], F32)
         tw_rows = keep.tile([P, K_PASS], F32)
@@ -63,21 +60,16 @@ def tile_attend_gvq_rw_w_kernel(tc, zT, cb, cb2, tw, xT, offs, offs2, out):
         neg_w = keep.tile([P, PASSES, SLOTS], F32)
 
         nc.gpsimd.memset(tw_rows[:], 0.0)
-        for b in range(2):
-            nc.vector.memset(books[b][0][:, C:], 0.0)
         make_identity(nc, ident[:])
-        for nb in range(1, NB):
-            for b in range(2):
-                nc.gpsimd.memset(books[b][nb][:, C:], 0.0)
 
         def load_book(b, nb):
-            nc.sync.dma_start(out=books[b][nb][:, :C], in_=(cb, cb2)[b][nb * P : (nb + 1) * P, :])
+            nc.sync.dma_start(out=books[b][nb][:], in_=(cb, cb2)[b][nb * P : (nb + 1) * P, :])
 
         def load_z(nb, half):
             nc.sync.dma_start(out=z[nb][half], in_=zT[nb * P : (nb + 1) * P, half * T // 2 : (half + 1) * T // 2])
 
         def load_x(k):
-            nc.sync.dma_start(out=x_raw[k][:], in_=xT[:, k * K_PASS : (k + 1) * K_PASS].rearrange("(b p) t -> p b t", p=P))
+            nc.sync.dma_start(out=x_raw[k], in_=xT[:, k * K_PASS : (k + 1) * K_PASS].rearrange("(b p) t -> p b t", p=P))
 
         nc.sync.dma_start(lists[0][:], offs)
         load_book(0, 0)
@@ -87,12 +79,15 @@ def tile_attend_gvq_rw_w_kernel(tc, zT, cb, cb2, tw, xT, offs, offs2, out):
         load_book(1, 0)
         load_z(0, 1)
         for nb in range(1, NB):
+            if nb == NB - 1:
+                load_x(0)
+                load_x(1)
             load_book(0, nb)
             load_z(nb, 0)
             load_book(1, nb)
             load_z(nb, 1)
-        for k in range(PASSES):
-            load_x(k)
+        load_x(2)
+        load_x(3)
 
         def planes_of(ap):
             return ap.rearrange("p j (q r) -> p j q r", r=RUN)
@@ -109,35 +104,38 @@ def tile_attend_gvq_rw_w_kernel(tc, zT, cb, cb2, tw, xT, offs, offs2, out):
         def offsets(b, k0, k1):
             return lists[b][:, k0 * K_PASS // LIST_ROWS : k1 * K_PASS // LIST_ROWS]
 
-        picked = {}
-        terms = {(nb, k): [] for nb in range(NB) for k in range(PASSES)}
+        in_order = [[keep.tile([P, T // 2], F32, name=f"s{nb}_{h}")[:] for h in range(2)] for nb in range(NB)]
+        s_span = late.tile([P, 3 * T // 2], F32, offset=8192, align_bytes=64)
+        extra = {nb: keep.tile([P, K_PASS], F32, name=f"extra{nb}")[:] for nb in BOTH_ON_SCALAR[:-1]}
+        extra[NB - 1] = s_span[:, :K_PASS]
+        gathered = {}
+        laid = {}
+
+        def half_of(tiles, k0, k1):
+            return tiles[k0 // 2][:, (k0 % 2) * K_PASS : (k0 % 2 + k1 - k0) * K_PASS]
 
         def gather_block(nb):
-            for b, k0, k1 in SCALAR_PIECES[nb]:
-                tile = keep.tile([P, (k1 - k0) * K_PASS], F32, name=f"s{b}_{nb}_{k0}")
-                nc.scalar.activation(tile[:], books[b][nb][:].indirect(offsets(b, k0, k1)), COPY)
-                picked[b, nb, k0] = tile
-            for b, k0, k1 in VECTOR_PIECES[nb]:
-                tile = keep.tile([P, SLOTS, (k1 - k0) * P], F32, name=f"v{b}_{nb}_{k0}")
+            for b, k in SCALAR_PIECES[nb]:
+                nc.scalar.activation(half_of(in_order[nb], k, k + 1), books[b][nb][:].indirect(offsets(b, k, k + 1)), COPY)
+            if nb in extra:
+                nc.scalar.activation(extra[nb], books[1][nb][:].indirect(offsets(1, PASSES - 1, PASSES)), COPY)
+            for b, k in VECTOR_PIECES[nb]:
+                tile = ring.tile([P, SLOTS, P], F32, tag="planes", name=f"v{nb}_{k}")
                 nc.vector.tensor_copy(
                     tile[:].bitcast(U32).rearrange("p j (q r) -> p q j r", r=RUN),
-                    books[b][nb][:].bitcast(U32).indirect(offsets(b, k0, k1)),
+                    books[b][nb][:].bitcast(U32).indirect(offsets(b, k, k + 1)),
                 )
-                picked[b, nb, k0] = tile
+                gathered[nb, k] = tile[:]
 
         def lay_planes(nb):
-            for b, k0, k1 in SCALAR_PIECES[nb]:
-                laid = keep.tile([P, SLOTS, (k1 - k0) * P], F32, name=f"laid{b}_{nb}_{k0}")
-                if terms[nb, k0]:
-                    nc.gpsimd.tensor_scalar(planes_of(laid[:]), tokens_of(picked[b, nb, k0][:]), 1.0, 0.0, MULT, ADD)
-                else:
-                    z_k = z[nb][k0 // 2][:, (k0 % 2) * K_PASS : (k0 % 2 + k1 - k0) * K_PASS]
-                    nc.gpsimd.tensor_tensor(planes_of(laid[:]), tokens_of(picked[b, nb, k0][:]), tokens_of(z_k), SUBTRACT)
-                for k in range(k0, k1):
-                    terms[nb, k].append(laid[:, :, (k - k0) * P : (k - k0 + 1) * P])
-            for b, k0, k1 in VECTOR_PIECES[nb]:
-                for k in range(k0, k1):
-                    terms[nb, k].append(picked[b, nb, k0][:, :, (k - k0) * P : (k - k0 + 1) * P])
+            for k in range(PASSES):
+                tile = keep.tile([P, SLOTS, P], F32, name=f"laid{nb}_{k}")
+                nc.gpsimd.tensor_tensor(planes_of(tile[:]), tokens_of(half_of(in_order[nb], k, k + 1)), tokens_of(half_of(z[nb], k, k + 1)), SUBTRACT)
+                laid[nb, k] = tile[:]
+            if nb in extra:
+                tile = keep.tile([P, SLOTS, P], F32, tag=f"z{nb}_1", name=f"extra_laid{nb}")
+                nc.gpsimd.tensor_scalar(planes_of(tile[:]), tokens_of(extra[nb]), 1.0, 0.0, MULT, ADD)
+                gathered[nb, PASSES - 1] = tile[:]
 
         def turn(bank, planes, start, stop):
             for j in range(SLOTS):
@@ -149,8 +147,8 @@ def tile_attend_gvq_rw_w_kernel(tc, zT, cb, cb2, tw, xT, offs, offs2, out):
 
         def add_up(nb, k):
             bank = bank_tile((nb * PASSES + k) % UNIT_BANKS, f"e{nb}_{k}", [P, SLOTS, P])
-            turn(bank, terms[nb, k][0], True, False)
-            turn(bank, terms[nb, k][1], False, True)
+            turn(bank, laid[nb, k], True, False)
+            turn(bank, gathered[nb, k], False, True)
             banks[nb, k] = bank
 
         def weigh(nb, k):
@@ -161,32 +159,40 @@ def tile_attend_gvq_rw_w_kernel(tc, zT, cb, cb2, tw, xT, offs, offs2, out):
                 MULT,
             )
 
-        def prepare_x(k):
-            pairs = late.tile([P, 2, DB, 2 * P], BF16, offset=2048 * k, align_bytes=64, name=f"x_pairs{k}")
+        x_pairs = {}
+        x_turned = {}
+
+        def cast_x(k):
+            if k == 0:
+                x_pairs["first"] = keep.tile([P, 2, 2, DB, 2 * P], BF16, tag=f"book0_{NB - 1}", name="x_pairs_first")
+            x_pairs[k] = x_pairs["first"][:, k] if k < 2 else keep.tile([P, 2, DB, 2 * P], BF16, name=f"x_pairs{k}")[:]
             nc.scalar.copy(
-                pairs[:].rearrange("p u b (q r e) -> p u (b q) r e", r=RUN, e=2),
-                x_raw[k][:].rearrange("p b (q u e r) -> p u (b q) r e", u=2, e=2, r=RUN),
+                x_pairs[k].rearrange("p u b (q r e) -> p u (b q) r e", r=RUN, e=2),
+                x_raw[k].rearrange("p b (q u e r) -> p u (b q) r e", u=2, e=2, r=RUN),
             )
-            bank = bank_tile((7, 2)[k % 2], f"x_bank{k}", [P, DB, 2, P])
+
+        def turn_x(k):
+            bank = bank_tile(k, f"x_bank{k}", [P, DB, 2, P])
             for db in range(DB):
                 for u in range(2):
-                    nc.tensor.transpose(bank[:, db, u, :], pairs[:, u, db, :].bitcast(F32), ident[:])
+                    nc.tensor.transpose(bank[:, db, u, :], x_pairs[k][:, u, db, :].bitcast(F32), ident[:])
+            x_turned[k] = keep.tile([P, D * SLOTS], BF16, align_bytes=64, name=f"x_turned{k}")
             nc.scalar.copy(
                 x_turned[k][:].bitcast(F32).rearrange("p (b d u) -> p b d u", b=DB, u=2),
                 bank[:].rearrange("p b u d -> p b d u"),
             )
 
-        gather_block(0)
+        g_turned = [keep.tile([P, NB * K_PASS], BF16, align_bytes=64, name=f"g_turned{k}") for k in range(PASSES)]
+        for nb in range(NB):
+            gather_block(nb)
         for nb in range(NB):
             lay_planes(nb)
             for k in range(PASSES):
                 add_up(nb, k)
-            if nb + 1 < NB:
-                gather_block(nb + 1)
-            for k in range(PASSES):
                 weigh(nb, k)
         for k in range(PASSES):
-            prepare_x(k)
+            cast_x(k)
+            turn_x(k)
 
         x_codes = late.tile([P, PASSES, D], U32, offset=8192, align_bytes=64)
         g_codes = late.tile([P, PASSES, DV], U32, offset=8192 + 4096, align_bytes=64)
@@ -205,7 +211,7 @@ def tile_attend_gvq_rw_w_kernel(tc, zT, cb, cb2, tw, xT, offs, offs2, out):
                 in_=x_turned[k][:, db0 * K_PASS : db1 * K_PASS],
             )
 
-        acc = [bank_tile(3 + db, f"acc{db}", [P, DV]) for db in range(DB)]
+        acc = [bank_tile(4 + db, f"acc{db}", [P, DV]) for db in range(DB)]
 
         def multiply(k):
             for db in range(DB):
@@ -220,8 +226,13 @@ def tile_attend_gvq_rw_w_kernel(tc, zT, cb, cb2, tw, xT, offs, offs2, out):
                 )
 
         for k in range(PASSES):
+            if k < PASSES - 1:
+                quantize_g(k, 0, NB)
+            else:
+                quantize_g(k, 0, 2)
+                quantize_g(k, 2, 3)
+                quantize_g(k, 3, 4)
             quantize_x(k, 0, DB)
-            quantize_g(k, 0, NB)
             multiply(k)
 
         result = [keep.tile([P, DV], F32, name=f"result{db}") for db in range(DB)]

@@ -32,8 +32,8 @@ UNIT_BANKS = 8
 CROSSED = [(0, 0), (0, 1), (1, 2), (1, 3)]
 STRAIGHT = [(0, 0), (0, 1), (0, 2), (0, 3)]
 SCALAR_PIECES = [CROSSED, CROSSED, STRAIGHT, STRAIGHT]
-VECTOR_PIECES = [[(0, 2), (0, 3), (1, 0), (1, 1)]] * 2 + [[(1, 0), (1, 1), (1, 2)]] * 2
-BOTH_ON_SCALAR = (2, 3)
+VECTOR_PIECES = [[(0, 2), (0, 3), (1, 0), (1, 1)]] * 2 + [[(1, 0), (1, 1), (1, 2), (1, 3)], [(1, 0), (1, 1), (1, 2)]]
+BOTH_ON_SCALAR = (3,)
 LEAD = 6
 
 

@@ -53,7 +53,7 @@ def tile_attend_gvq_rw_w_kernel(tc, zT, cb, cb2, tw, xT, offs, offs2, out):
         z = [[keep.tile([P, T // 2], F32, tag=f"z{nb}_{h}", name=f"z{nb}_{h}")[:] for h in range(2)] for nb in range(NB)]
         x_raw = [keep.tile([P, DB, K_PASS], F32, name=f"x_raw{k}")[:] for k in range(PASSES)]
         x_scales = keep.tile([P, PASSES, D], U8, align_bytes=64)
-        g_scales = keep.tile([P, PASSES, DV], U8, align_bytes=64)
+        g_scales = keep.tile([P, NB, PASSES * P], U8, align_bytes=64)
         ident = keep.tile([P, P], F32)
         tw_rows = keep.tile([P, K_PASS], F32)
         tw_planes = keep.tile([P, SLOTS, P], F32)
@@ -78,14 +78,20 @@ def tile_attend_gvq_rw_w_kernel(tc, zT, cb, cb2, tw, xT, offs, offs2, out):
         nc.sync.dma_start(lists[1][:], offs2)
         load_book(1, 0)
         load_z(0, 1)
-        for nb in range(1, NB):
-            if nb == NB - 1:
-                load_x(0)
-                load_x(1)
-            load_book(0, nb)
-            load_z(nb, 0)
-            load_book(1, nb)
-            load_z(nb, 1)
+        load_book(0, 1)
+        load_book(1, 1)
+        load_z(1, 0)
+        load_book(1, 2)
+        load_z(1, 1)
+        load_book(0, 2)
+        load_book(1, 3)
+        load_z(2, 0)
+        load_z(2, 1)
+        load_book(0, 3)
+        load_x(0)
+        load_z(3, 0)
+        load_x(1)
+        load_z(3, 1)
         load_x(2)
         load_x(3)
 
@@ -153,7 +159,7 @@ def tile_attend_gvq_rw_w_kernel(tc, zT, cb, cb2, tw, xT, offs, offs2, out):
 
         def weigh(nb, k):
             nc.vector.tensor_tensor(
-                g_turned[k][:, nb * K_PASS : (nb + 1) * K_PASS].rearrange("p (n j) -> p n j", j=SLOTS),
+                g_turned[nb][:, k * K_PASS : (k + 1) * K_PASS].rearrange("p (n j) -> p n j", j=SLOTS),
                 neg_w[:, k, :].unsqueeze(1).to_broadcast([P, P, SLOTS]),
                 banks[nb, k][:].rearrange("p j n -> p n j"),
                 MULT,
@@ -172,7 +178,7 @@ def tile_attend_gvq_rw_w_kernel(tc, zT, cb, cb2, tw, xT, offs, offs2, out):
             )
 
         def turn_x(k):
-            bank = bank_tile(k, f"x_bank{k}", [P, DB, 2, P])
+            bank = bank_tile(k % 2, f"x_bank{k}", [P, DB, 2, P])
             for db in range(DB):
                 for u in range(2):
                     nc.tensor.transpose(bank[:, db, u, :], x_pairs[k][:, u, db, :].bitcast(F32), ident[:])
@@ -182,65 +188,89 @@ def tile_attend_gvq_rw_w_kernel(tc, zT, cb, cb2, tw, xT, offs, offs2, out):
                 bank[:].rearrange("p b u d -> p b d u"),
             )
 
-        g_turned = [keep.tile([P, NB * K_PASS], BF16, align_bytes=64, name=f"g_turned{k}") for k in range(PASSES)]
+        g_turned = [keep.tile([P, T], BF16, align_bytes=64, tag=f"g{nb}", name=f"g_turned{nb}") for nb in range(NB - 1)]
         for nb in range(NB):
             gather_block(nb)
         for nb in range(NB):
             lay_planes(nb)
             for k in range(PASSES):
                 add_up(nb, k)
-                weigh(nb, k)
+                if nb < NB - 1:
+                    weigh(nb, k)
         for k in range(PASSES):
             cast_x(k)
             turn_x(k)
 
         x_codes = late.tile([P, PASSES, D], U32, offset=8192, align_bytes=64)
-        g_codes = late.tile([P, PASSES, DV], U32, offset=8192 + 4096, align_bytes=64)
+        g_codes = late.tile([P, NB, PASSES * P], U32, offset=8192 + 4096, align_bytes=64)
 
-        def quantize_g(k, nb0, nb1):
+        def quantize_g(nb, k0, k1):
             nc.vector.quantize_mx(
-                out=g_codes[:, k, nb0 * P : nb1 * P].bitcast(E5M2),
-                scales=g_scales[:, k, nb0 * P : nb1 * P],
-                in_=g_turned[k][:, nb0 * K_PASS : nb1 * K_PASS],
+                out=g_codes[:, nb, k0 * P : k1 * P].bitcast(E5M2),
+                scales=g_scales[:, nb, k0 * P : k1 * P],
+                in_=g_turned[nb][:, k0 * K_PASS : k1 * K_PASS],
             )
 
-        def quantize_x(k, db0, db1):
-            nc.vector.quantize_mx(
-                out=x_codes[:, k, db0 * P : db1 * P].bitcast(E4M3),
-                scales=x_scales[:, k, db0 * P : db1 * P],
-                in_=x_turned[k][:, db0 * K_PASS : db1 * K_PASS],
+        def quantize_x(k):
+            nc.vector.quantize_mx(out=x_codes[:, k, :].bitcast(E4M3), scales=x_scales[:, k, :], in_=x_turned[k][:])
+
+        def multiply(acc, db, nb, k, start, stop):
+            nc.tensor.matmul_mx(
+                out=acc,
+                lhsT=x_codes[:, k, db * P : (db + 1) * P].bitcast(E4M3),
+                lhsT_scale=x_scales[:, k, db * P : (db + 1) * P],
+                rhs=g_codes[:, nb, k * P : (k + 1) * P].bitcast(E5M2),
+                rhs_scale=g_scales[:, nb, k * P : (k + 1) * P],
+                start=start,
+                stop=stop,
             )
 
-        acc = [bank_tile(4 + db, f"acc{db}", [P, DV]) for db in range(DB)]
-
-        def multiply(k):
+        last = NB - 1
+        acc = [bank_tile(2 + db, f"acc{db}", [P, last, P]) for db in range(DB)]
+        acc_last = [bank_tile(4 + db, f"acc_last{db}", [P, P]) for db in range(DB)]
+        def products(nb, k):
             for db in range(DB):
-                nc.tensor.matmul_mx(
-                    out=acc[db][:],
-                    lhsT=x_codes[:, k, db * P : (db + 1) * P].bitcast(E4M3),
-                    lhsT_scale=x_scales[:, k, db * P : (db + 1) * P],
-                    rhs=g_codes[:, k, :].bitcast(E5M2),
-                    rhs_scale=g_scales[:, k, :],
-                    start=(k == 0),
-                    stop=(k == PASSES - 1),
-                )
+                if nb < last:
+                    multiply(acc[db][:, nb, :], db, nb, k, (nb, k) == (0, 0), (nb, k) == (last - 1, last))
+                else:
+                    multiply(acc_last[db][:], db, nb, k, k == 0, k == last)
 
-        for k in range(PASSES):
-            if k < PASSES - 1:
-                quantize_g(k, 0, NB)
-            else:
-                quantize_g(k, 0, 2)
-                quantize_g(k, 2, 3)
-                quantize_g(k, 3, 4)
-            quantize_x(k, 0, DB)
-            multiply(k)
+        quantize_x(0)
+        quantize_g(0, 0, PASSES)
+        products(0, 0)
+        g_turned.append(keep.tile([P, T], BF16, align_bytes=64, tag="g0", name="g_turned3"))
+        quantize_g(1, 0, PASSES)
+        products(1, 0)
+        weigh(last, 0)
+        quantize_x(1)
+        products(0, 1)
+        products(1, 1)
+        quantize_g(2, 0, PASSES)
+        products(2, 0)
+        products(2, 1)
+        weigh(last, 1)
+        quantize_x(2)
+        for nb in range(last):
+            products(nb, 2)
+        weigh(last, 2)
+        quantize_g(last, 0, 2)
+        products(last, 0)
+        products(last, 1)
+        weigh(last, 3)
+        quantize_x(3)
+        for nb in range(last):
+            products(nb, 3)
+        for db in range(DB):
+            result = keep.tile([P, last * P], F32, name=f"result{db}")
+            nc.scalar.copy(result[:], acc[db][:].rearrange("p b n -> p (b n)"))
+            nc.sync.dma_start(out=out[db * P : (db + 1) * P, : last * P], in_=result[:])
+        quantize_g(last, 2, 3)
+        products(last, 2)
+        quantize_g(last, 3, 4)
+        products(last, 3)
 
-        result = [keep.tile([P, DV], F32, name=f"result{db}") for db in range(DB)]
-        for half in range(2):
-            cols = slice(half * DV // 2, (half + 1) * DV // 2)
-            nc.vector.tensor_copy(result[0][:, cols], acc[0][:, cols])
-            nc.sync.dma_start(out=out[0:P, cols], in_=result[0][:, cols])
-        for half, queue in enumerate((nc.sync, nc.scalar)):
-            cols = slice(half * DV // 2, (half + 1) * DV // 2)
-            nc.scalar.copy(result[1][:, cols], acc[1][:, cols])
-            queue.dma_start(out=out[P : 2 * P, cols], in_=result[1][:, cols])
+        tail = [keep.tile([P, P], F32, name=f"tail{db}") for db in range(DB)]
+        nc.vector.tensor_copy(tail[0][:], acc_last[0][:])
+        nc.sync.dma_start(out=out[0:P, last * P :], in_=tail[0][:])
+        nc.scalar.copy(tail[1][:], acc_last[1][:])
+        nc.scalar.dma_start(out=out[P:, last * P :], in_=tail[1][:])

@@ -79,13 +79,13 @@ def tile_attend_gvq_rw_w_kernel(tc, zT, cb, cb2, tw, xT, offs, offs2, out):
         load_book(1, 0)
         load_z(0, 1)
         load_book(0, 1)
-        load_book(1, 1)
         load_z(1, 0)
+        load_book(1, 1)
         load_book(1, 2)
         load_z(1, 1)
         load_book(0, 2)
-        load_book(1, 3)
         load_z(2, 0)
+        load_book(1, 3)
         load_z(2, 1)
         load_book(0, 3)
         load_x(0)
@@ -256,8 +256,8 @@ def tile_attend_gvq_rw_w_kernel(tc, zT, cb, cb2, tw, xT, offs, offs2, out):
         quantize_g(last, 0, 2)
         products(last, 0)
         products(last, 1)
-        weigh(last, 3)
         quantize_x(3)
+        weigh(last, 3)
         for nb in range(last):
             products(nb, 3)
         for db in range(DB):

@@ -53,7 +53,8 @@ def tile_attend_gvq_rw_w_kernel(tc, zT, cb, cb2, tw, xT, offs, offs2, out):
         z = [[keep.tile([P, T // 2], F32, tag=f"z{nb}_{h}", name=f"z{nb}_{h}")[:] for h in range(2)] for nb in range(NB)]
         x_raw = [keep.tile([P, DB, K_PASS], F32, name=f"x_raw{k}")[:] for k in range(PASSES)]
         x_scales = keep.tile([P, PASSES, D], U8, align_bytes=64)
-        g_scales = keep.tile([P, NB, PASSES * P], U8, align_bytes=64)
+        low_scales = keep.tile([P, PASSES, 2 * P], U8, align_bytes=64)
+        high_scales = keep.tile([P, 2, PASSES * P], U8, align_bytes=64)
         ident = keep.tile([P, P], F32)
         tw_rows = keep.tile([P, K_PASS], F32)
         tw_planes = keep.tile([P, SLOTS, P], F32)
@@ -157,9 +158,14 @@ def tile_attend_gvq_rw_w_kernel(tc, zT, cb, cb2, tw, xT, offs, offs2, out):
             turn(bank, gathered[nb, k], False, True)
             banks[nb, k] = bank
 
+        def g_unit(nb, k):
+            if nb < 2:
+                return g_low[k // 2][:, k % 2, nb * K_PASS : (nb + 1) * K_PASS]
+            return g_high[nb - 2][:, k * K_PASS : (k + 1) * K_PASS]
+
         def weigh(nb, k):
             nc.vector.tensor_tensor(
-                g_turned[nb][:, k * K_PASS : (k + 1) * K_PASS].rearrange("p (n j) -> p n j", j=SLOTS),
+                g_unit(nb, k).rearrange("p (n j) -> p n j", j=SLOTS),
                 neg_w[:, k, :].unsqueeze(1).to_broadcast([P, P, SLOTS]),
                 banks[nb, k][:].rearrange("p j n -> p n j"),
                 MULT,
@@ -188,7 +194,8 @@ def tile_attend_gvq_rw_w_kernel(tc, zT, cb, cb2, tw, xT, offs, offs2, out):
                 bank[:].rearrange("p b u d -> p b d u"),
             )
 
-        g_turned = [keep.tile([P, T], BF16, align_bytes=64, tag=f"g{nb}", name=f"g_turned{nb}") for nb in range(NB - 1)]
+        g_low = [keep.tile([P, 2, 2 * K_PASS], BF16, align_bytes=64, tag=f"g_low{h}", name=f"g_low{h}") for h in range(2)]
+        g_high = [keep.tile([P, T], BF16, align_bytes=64, name="g_high0")]
         for nb in range(NB):
             gather_block(nb)
         for nb in range(NB):
@@ -202,72 +209,82 @@ def tile_attend_gvq_rw_w_kernel(tc, zT, cb, cb2, tw, xT, offs, offs2, out):
             turn_x(k)
 
         x_codes = late.tile([P, PASSES, D], U32, offset=8192, align_bytes=64)
-        g_codes = late.tile([P, NB, PASSES * P], U32, offset=8192 + 4096, align_bytes=64)
+        low_codes = late.tile([P, PASSES, 2 * P], U32, offset=8192 + 4096, align_bytes=64)
+        high_codes = late.tile([P, 2, PASSES * P], U32, offset=8192 + 8192, align_bytes=64)
 
-        def quantize_g(nb, k0, k1):
+        def quantize_low(h):
             nc.vector.quantize_mx(
-                out=g_codes[:, nb, k0 * P : k1 * P].bitcast(E5M2),
-                scales=g_scales[:, nb, k0 * P : k1 * P],
-                in_=g_turned[nb][:, k0 * K_PASS : k1 * K_PASS],
+                out=low_codes[:, 2 * h : 2 * h + 2, :].rearrange("p k c -> p (k c)").bitcast(E5M2),
+                scales=low_scales[:, 2 * h : 2 * h + 2, :].rearrange("p k c -> p (k c)"),
+                in_=g_low[h][:].rearrange("p k c -> p (k c)"),
+            )
+
+        def quantize_high(i, k0, k1):
+            nc.vector.quantize_mx(
+                out=high_codes[:, i, k0 * P : k1 * P].bitcast(E5M2),
+                scales=high_scales[:, i, k0 * P : k1 * P],
+                in_=g_high[i][:, k0 * K_PASS : k1 * K_PASS],
             )
 
         def quantize_x(k):
             nc.vector.quantize_mx(out=x_codes[:, k, :].bitcast(E4M3), scales=x_scales[:, k, :], in_=x_turned[k][:])
 
-        def multiply(acc, db, nb, k, start, stop):
+        def multiply(sums, db, k, codes, scales, start, stop):
             nc.tensor.matmul_mx(
-                out=acc,
+                out=sums,
                 lhsT=x_codes[:, k, db * P : (db + 1) * P].bitcast(E4M3),
                 lhsT_scale=x_scales[:, k, db * P : (db + 1) * P],
-                rhs=g_codes[:, nb, k * P : (k + 1) * P].bitcast(E5M2),
-                rhs_scale=g_scales[:, nb, k * P : (k + 1) * P],
+                rhs=codes.bitcast(E5M2),
+                rhs_scale=scales,
                 start=start,
                 stop=stop,
             )
 
-        last = NB - 1
-        acc = [bank_tile(2 + db, f"acc{db}", [P, last, P]) for db in range(DB)]
+        last = PASSES - 1
+        acc = [bank_tile(2 + db, f"acc{db}", [P, 3 * P]) for db in range(DB)]
         acc_last = [bank_tile(4 + db, f"acc_last{db}", [P, P]) for db in range(DB)]
-        def products(nb, k):
-            for db in range(DB):
-                if nb < last:
-                    multiply(acc[db][:, nb, :], db, nb, k, (nb, k) == (0, 0), (nb, k) == (last - 1, last))
-                else:
-                    multiply(acc_last[db][:], db, nb, k, k == 0, k == last)
 
+        def low_products(k):
+            for db in range(DB):
+                multiply(acc[db][:, : 2 * P], db, k, low_codes[:, k, :], low_scales[:, k, :], k == 0, False)
+
+        def high_products(i, k):
+            cols = slice(k * P, (k + 1) * P)
+            for db in range(DB):
+                sums = acc[db][:, 2 * P :] if i == 0 else acc_last[db][:]
+                multiply(sums, db, k, high_codes[:, i, cols], high_scales[:, i, cols], i == 1 and k == 0, k == last)
+
+        quantize_low(0)
+        g_high.append(keep.tile([P, T], BF16, align_bytes=64, tag="g_low0", name="g_high1"))
         quantize_x(0)
-        quantize_g(0, 0, PASSES)
-        products(0, 0)
-        g_turned.append(keep.tile([P, T], BF16, align_bytes=64, tag="g0", name="g_turned3"))
-        quantize_g(1, 0, PASSES)
-        products(1, 0)
+        low_products(0)
+        quantize_high(0, 0, PASSES)
+        high_products(0, 0)
         weigh(last, 0)
         quantize_x(1)
-        products(0, 1)
-        products(1, 1)
-        quantize_g(2, 0, PASSES)
-        products(2, 0)
-        products(2, 1)
+        low_products(1)
+        high_products(0, 1)
+        quantize_low(1)
         weigh(last, 1)
         quantize_x(2)
-        for nb in range(last):
-            products(nb, 2)
+        low_products(2)
+        high_products(0, 2)
         weigh(last, 2)
-        quantize_g(last, 0, 2)
-        products(last, 0)
-        products(last, 1)
+        quantize_high(1, 0, 2)
+        high_products(1, 0)
+        high_products(1, 1)
         quantize_x(3)
         weigh(last, 3)
-        for nb in range(last):
-            products(nb, 3)
+        low_products(3)
+        high_products(0, 3)
         for db in range(DB):
-            result = keep.tile([P, last * P], F32, name=f"result{db}")
-            nc.scalar.copy(result[:], acc[db][:].rearrange("p b n -> p (b n)"))
-            nc.sync.dma_start(out=out[db * P : (db + 1) * P, : last * P], in_=result[:])
-        quantize_g(last, 2, 3)
-        products(last, 2)
-        quantize_g(last, 3, 4)
-        products(last, 3)
+            result = keep.tile([P, 3 * P], F32, name=f"result{db}")
+            nc.scalar.copy(result[:], acc[db][:])
+            nc.sync.dma_start(out=out[db * P : (db + 1) * P, : 3 * P], in_=result[:])
+        quantize_high(1, 2, 3)
+        high_products(1, 2)
+        quantize_high(1, 3, 4)
+        high_products(1, 3)
 
         tail = [keep.tile([P, P], F32, name=f"tail{db}") for db in range(DB)]
         nc.vector.tensor_copy(tail[0][:], acc_last[0][:])

@@ -32,9 +32,10 @@ UNIT_BANKS = 8
 CROSSED = [(0, 0), (0, 1), (1, 2), (1, 3)]
 STRAIGHT = [(0, 0), (0, 1), (0, 2), (0, 3)]
 SCALAR_PIECES = [CROSSED, CROSSED, STRAIGHT, STRAIGHT]
-VECTOR_PIECES = [[(0, 2), (0, 3), (1, 0), (1, 1)]] * 2 + [[(1, 0), (1, 1), (1, 2), (1, 3)], [(1, 0), (1, 1), (1, 2)]]
+VECTOR_PIECES = [[(0, 2, 4), (1, 0, 2)]] * 2 + [[(1, 0, 2), (1, 2, 4)], [(1, 0, 1), (1, 1, 2), (1, 2, 3)]]
+PAD = 352
 BOTH_ON_SCALAR = (3,)
-LEAD = 6
+LEAD = 8
 
 
 def tile_attend_gvq_rw_w_kernel(tc, zT, cb, cb2, tw, xT, offs, offs2, out):
@@ -42,14 +43,22 @@ def tile_attend_gvq_rw_w_kernel(tc, zT, cb, cb2, tw, xT, offs, offs2, out):
     with ExitStack() as ctx:
         keep = ctx.enter_context(tc.tile_pool(name="keep", bufs=1))
         late = ctx.enter_context(tc.tile_pool(name="late", bufs=1))
-        ring = ctx.enter_context(tc.tile_pool(name="ring", bufs=LEAD))
+        ring = ctx.enter_context(tc.tile_pool(name="ring", bufs=1))
         psum = ctx.enter_context(tc.psum_pool(name="psum", bufs=1))
 
         def bank_tile(i, name, shape):
             return psum.tile(shape, F32, tag=f"bank{i}", name=name)
 
         lists = [keep.tile([P, T // LIST_ROWS], U16, name=f"list{b}") for b in range(2)]
-        books = [[keep.tile([P, C], F32, tag=f"book{b}_{nb}", name=f"book{b}_{nb}") for nb in range(NB)] for b in range(2)]
+        books = [
+            [
+                late.tile([P, C + PAD], F32, offset=24576 + 2048, align_bytes=64, name="book0_1")
+                if (b, nb) == (0, 1)
+                else keep.tile([P, C + PAD * (nb < 2 or (b, nb) == (1, 2))], F32, tag=f"book{b}_{nb}", name=f"book{b}_{nb}")
+                for nb in range(NB)
+            ]
+            for b in range(2)
+        ]
         z = [[keep.tile([P, T // 2], F32, tag=f"z{nb}_{h}", name=f"z{nb}_{h}")[:] for h in range(2)] for nb in range(NB)]
         x_raw = [keep.tile([P, DB, K_PASS], F32, name=f"x_raw{k}")[:] for k in range(PASSES)]
         x_scales = keep.tile([P, PASSES, D], U8, align_bytes=64)
@@ -61,10 +70,12 @@ def tile_attend_gvq_rw_w_kernel(tc, zT, cb, cb2, tw, xT, offs, offs2, out):
         neg_w = keep.tile([P, PASSES, SLOTS], F32)
 
         nc.gpsimd.memset(tw_rows[:], 0.0)
+        for b, nb in ((0, 0), (1, 0), (0, 1), (1, 1), (1, 2)):
+            nc.vector.memset(books[b][nb][:, C:], 0.0)
         make_identity(nc, ident[:])
 
         def load_book(b, nb):
-            nc.sync.dma_start(out=books[b][nb][:], in_=(cb, cb2)[b][nb * P : (nb + 1) * P, :])
+            nc.sync.dma_start(out=books[b][nb][:, :C], in_=(cb, cb2)[b][nb * P : (nb + 1) * P, :])
 
         def load_z(nb, half):
             nc.sync.dma_start(out=z[nb][half], in_=zT[nb * P : (nb + 1) * P, half * T // 2 : (half + 1) * T // 2])
@@ -80,13 +91,13 @@ def tile_attend_gvq_rw_w_kernel(tc, zT, cb, cb2, tw, xT, offs, offs2, out):
         load_book(1, 0)
         load_z(0, 1)
         load_book(0, 1)
-        load_z(1, 0)
         load_book(1, 1)
+        load_z(1, 0)
         load_book(1, 2)
         load_z(1, 1)
         load_book(0, 2)
-        load_z(2, 0)
         load_book(1, 3)
+        load_z(2, 0)
         load_z(2, 1)
         load_book(0, 3)
         load_x(0)
@@ -115,6 +126,7 @@ def tile_attend_gvq_rw_w_kernel(tc, zT, cb, cb2, tw, xT, offs, offs2, out):
         s_span = late.tile([P, 3 * T // 2], F32, offset=8192, align_bytes=64)
         extra = {nb: keep.tile([P, K_PASS], F32, name=f"extra{nb}")[:] for nb in BOTH_ON_SCALAR[:-1]}
         extra[NB - 1] = s_span[:, :K_PASS]
+        gathered_by_vector = []
         gathered = {}
         laid = {}
 
@@ -126,13 +138,16 @@ def tile_attend_gvq_rw_w_kernel(tc, zT, cb, cb2, tw, xT, offs, offs2, out):
                 nc.scalar.activation(half_of(in_order[nb], k, k + 1), books[b][nb][:].indirect(offsets(b, k, k + 1)), COPY)
             if nb in extra:
                 nc.scalar.activation(extra[nb], books[1][nb][:].indirect(offsets(1, PASSES - 1, PASSES)), COPY)
-            for b, k in VECTOR_PIECES[nb]:
-                tile = ring.tile([P, SLOTS, P], F32, tag="planes", name=f"v{nb}_{k}")
+            for b, k0, k1 in VECTOR_PIECES[nb]:
+                slot = len(gathered_by_vector) % LEAD
+                tile = ring.tile([P, SLOTS, (k1 - k0) * P], F32, offset=slot * 4 * K_PASS, name=f"v{nb}_{k0}")
+                gathered_by_vector.extend(range(k0, k1))
                 nc.vector.tensor_copy(
                     tile[:].bitcast(U32).rearrange("p j (q r) -> p q j r", r=RUN),
-                    books[b][nb][:].bitcast(U32).indirect(offsets(b, k, k + 1)),
+                    books[b][nb][:].bitcast(U32).indirect(offsets(b, k0, k1)),
                 )
-                gathered[nb, k] = tile[:]
+                for k in range(k0, k1):
+                    gathered[nb, k] = tile[:, :, (k - k0) * P : (k - k0 + 1) * P]
 
         def lay_planes(nb):
             for k in range(PASSES):
@@ -154,8 +169,11 @@ def tile_attend_gvq_rw_w_kernel(tc, zT, cb, cb2, tw, xT, offs, offs2, out):
 
         def add_up(nb, k):
             bank = bank_tile((nb * PASSES + k) % UNIT_BANKS, f"e{nb}_{k}", [P, SLOTS, P])
-            turn(bank, laid[nb, k], True, False)
-            turn(bank, gathered[nb, k], False, True)
+            terms = [laid[nb, k], gathered[nb, k]]
+            if nb == 0 and k >= 2:
+                terms.reverse()
+            turn(bank, terms[0], True, False)
+            turn(bank, terms[1], False, True)
             banks[nb, k] = bank
 
         def g_unit(nb, k):
@@ -194,10 +212,10 @@ def tile_attend_gvq_rw_w_kernel(tc, zT, cb, cb2, tw, xT, offs, offs2, out):
                 bank[:].rearrange("p b u d -> p b d u"),
             )
 
-        g_low = [keep.tile([P, 2, 2 * K_PASS], BF16, align_bytes=64, tag=f"g_low{h}", name=f"g_low{h}") for h in range(2)]
         g_high = [keep.tile([P, T], BF16, align_bytes=64, name="g_high0")]
         for nb in range(NB):
             gather_block(nb)
+        g_low = [late.tile([P, 2, 2 * K_PASS], BF16, offset=24576 + 4096 * h, align_bytes=64, name=f"g_low{h}") for h in range(2)]
         for nb in range(NB):
             lay_planes(nb)
             for k in range(PASSES):
@@ -255,7 +273,7 @@ def tile_attend_gvq_rw_w_kernel(tc, zT, cb, cb2, tw, xT, offs, offs2, out):
                 multiply(sums, db, k, high_codes[:, i, cols], high_scales[:, i, cols], i == 1 and k == 0, k == last)
 
         quantize_low(0)
-        g_high.append(keep.tile([P, T], BF16, align_bytes=64, tag="g_low0", name="g_high1"))
+        g_high.append(late.tile([P, T], BF16, offset=24576, align_bytes=64, name="g_high1"))
         quantize_x(0)
         low_products(0)
         quantize_high(0, 0, PASSES)

@@ -71,7 +71,7 @@ def tile_attend_gvq_rw_w_kernel(tc, zT, cb, cb2, tw, xT, offs, offs2, out):
 
         nc.gpsimd.memset(tw_rows[:], 0.0)
         for b, nb in ((0, 0), (1, 0), (0, 1), (1, 1), (1, 2)):
-            nc.vector.memset(books[b][nb][:, C:], 0.0)
+            nc.vector.memset(books[b][nb][:, C:].bitcast(U32), 0)
         make_identity(nc, ident[:])
 
         def load_book(b, nb):
@@ -179,7 +179,11 @@ def tile_attend_gvq_rw_w_kernel(tc, zT, cb, cb2, tw, xT, offs, offs2, out):
         def g_unit(nb, k):
             if nb < 2:
                 return g_low[k // 2][:, k % 2, nb * K_PASS : (nb + 1) * K_PASS]
-            return g_high[nb - 2][:, k * K_PASS : (k + 1) * K_PASS]
+            if nb == 2:
+                return g_mid[:, k * K_PASS : (k + 1) * K_PASS]
+            if k in (1, 2):
+                return g_end[1][:, (k - 1) * K_PASS : k * K_PASS]
+            return g_end[k][:]
 
         def weigh(nb, k):
             nc.vector.tensor_tensor(
@@ -212,7 +216,8 @@ def tile_attend_gvq_rw_w_kernel(tc, zT, cb, cb2, tw, xT, offs, offs2, out):
                 bank[:].rearrange("p b u d -> p b d u"),
             )
 
-        g_high = [keep.tile([P, T], BF16, align_bytes=64, name="g_high0")]
+        g_mid = keep.tile([P, T], BF16, align_bytes=64)
+        g_end = {k: keep.tile([P, K_PASS], BF16, align_bytes=64, name=f"g_end{k}") for k in (0, 3)}
         for nb in range(NB):
             gather_block(nb)
         g_low = [late.tile([P, 2, 2 * K_PASS], BF16, offset=24576 + 4096 * h, align_bytes=64, name=f"g_low{h}") for h in range(2)]
@@ -241,7 +246,7 @@ def tile_attend_gvq_rw_w_kernel(tc, zT, cb, cb2, tw, xT, offs, offs2, out):
             nc.vector.quantize_mx(
                 out=high_codes[:, i, k0 * P : k1 * P].bitcast(E5M2),
                 scales=high_scales[:, i, k0 * P : k1 * P],
-                in_=g_high[i][:, k0 * K_PASS : k1 * K_PASS],
+                in_=g_end[k0][:] if i else g_mid[:],
             )
 
         def quantize_x(k):
@@ -272,37 +277,37 @@ def tile_attend_gvq_rw_w_kernel(tc, zT, cb, cb2, tw, xT, offs, offs2, out):
                 sums = acc[db][:, 2 * P :] if i == 0 else acc_last[db][:]
                 multiply(sums, db, k, high_codes[:, i, cols], high_scales[:, i, cols], i == 1 and k == 0, k == last)
 
+        weigh(last, 0)
         quantize_low(0)
-        g_high.append(late.tile([P, T], BF16, offset=24576, align_bytes=64, name="g_high1"))
+        g_end[1] = late.tile([P, 2 * K_PASS], BF16, offset=24576, align_bytes=64, name="g_end1")
         quantize_x(0)
         low_products(0)
         quantize_high(0, 0, PASSES)
         high_products(0, 0)
-        weigh(last, 0)
+        quantize_high(1, 0, 1)
+        high_products(1, 0)
+        weigh(last, 1)
         quantize_x(1)
         low_products(1)
         high_products(0, 1)
         quantize_low(1)
-        weigh(last, 1)
+        weigh(last, 2)
         quantize_x(2)
         low_products(2)
         high_products(0, 2)
-        weigh(last, 2)
-        quantize_high(1, 0, 2)
-        high_products(1, 0)
-        high_products(1, 1)
-        quantize_x(3)
         weigh(last, 3)
+        quantize_x(3)
         low_products(3)
         high_products(0, 3)
-        for db in range(DB):
-            result = keep.tile([P, 3 * P], F32, name=f"result{db}")
-            nc.scalar.copy(result[:], acc[db][:])
-            nc.sync.dma_start(out=out[db * P : (db + 1) * P, : 3 * P], in_=result[:])
-        quantize_high(1, 2, 3)
+        quantize_high(1, 1, 3)
+        high_products(1, 1)
         high_products(1, 2)
         quantize_high(1, 3, 4)
         high_products(1, 3)
+        for db in range(DB):
+            result = keep.tile([P, 3 * P], F32, name=f"result{db}")
+            (nc.vector.tensor_copy, nc.scalar.copy)[db](result[:], acc[db][:])
+            nc.sync.dma_start(out=out[db * P : (db + 1) * P, : 3 * P], in_=result[:])
 
         tail = [keep.tile([P, P], F32, name=f"tail{db}") for db in range(DB)]
         nc.vector.tensor_copy(tail[0][:], acc_last[0][:])

@@ -60,7 +60,7 @@ def tile_attend_gvq_rw_w_kernel(tc, zT, cb, cb2, tw, xT, offs, offs2, out):
             for b in range(2)
         ]
         z = [[keep.tile([P, T // 2], F32, tag=f"z{nb}_{h}", name=f"z{nb}_{h}")[:] for h in range(2)] for nb in range(NB)]
-        x_raw = [keep.tile([P, DB, K_PASS], F32, name=f"x_raw{k}")[:] for k in range(PASSES)]
+        x_raw = [keep.tile([P, DB, K_PASS], F32, tag=f"x_raw{k}", name=f"x_raw{k}", align_bytes=64)[:] for k in range(PASSES)]
         x_scales = keep.tile([P, PASSES, D], U8, align_bytes=64)
         low_scales = keep.tile([P, PASSES, 2 * P], U8, align_bytes=64)
         high_scales = keep.tile([P, 2, PASSES * P], U8, align_bytes=64)
@@ -210,7 +210,7 @@ def tile_attend_gvq_rw_w_kernel(tc, zT, cb, cb2, tw, xT, offs, offs2, out):
             for db in range(DB):
                 for u in range(2):
                     nc.tensor.transpose(bank[:, db, u, :], x_pairs[k][:, u, db, :].bitcast(F32), ident[:])
-            x_turned[k] = keep.tile([P, D * SLOTS], BF16, align_bytes=64, name=f"x_turned{k}")
+            x_turned[k] = keep.tile([P, D * SLOTS], BF16, align_bytes=64, tag="x_raw3" if k == 1 else f"x_turned{k}", name=f"x_turned{k}")
             nc.scalar.copy(
                 x_turned[k][:].bitcast(F32).rearrange("p (b d u) -> p b d u", b=DB, u=2),
                 bank[:].rearrange("p b u d -> p b d u"),
@@ -229,6 +229,7 @@ def tile_attend_gvq_rw_w_kernel(tc, zT, cb, cb2, tw, xT, offs, offs2, out):
                     weigh(nb, k)
         for k in range(PASSES):
             cast_x(k)
+        for k in range(PASSES):
             turn_x(k)
 
         x_codes = late.tile([P, PASSES, D], U32, offset=8192, align_bytes=64)
@@ -287,18 +288,18 @@ def tile_attend_gvq_rw_w_kernel(tc, zT, cb, cb2, tw, xT, offs, offs2, out):
         quantize_high(1, 0, 1)
         high_products(1, 0)
         weigh(last, 1)
+        quantize_low(1)
         quantize_x(1)
         low_products(1)
         high_products(0, 1)
-        quantize_low(1)
         weigh(last, 2)
         quantize_x(2)
         low_products(2)
         high_products(0, 2)
-        weigh(last, 3)
         quantize_x(3)
         low_products(3)
         high_products(0, 3)
+        weigh(last, 3)
         quantize_high(1, 1, 3)
         high_products(1, 1)
         high_products(1, 2)

@@ -28,60 +28,56 @@ PASSES = T // K_PASS
 NB = DV // P
 DB = D // P
 LIST_ROWS = 16
-UNIT_BANKS = 8
-CROSSED = [(0, 0), (0, 1), (1, 2), (1, 3)]
-STRAIGHT = [(0, 0), (0, 1), (0, 2), (0, 3)]
-SCALAR_PIECES = [CROSSED, CROSSED, STRAIGHT, STRAIGHT]
-VECTOR_PIECES = [[(0, 2, 4), (1, 0, 2)]] * 2 + [[(1, 0, 2), (1, 2, 4)], [(1, 0, 1), (1, 1, 2), (1, 2, 3)]]
 PAD = 352
-BOTH_ON_SCALAR = (3,)
-LEAD = 8
+KIB = 1024
 
 
 def tile_attend_gvq_rw_w_kernel(tc, zT, cb, cb2, tw, xT, offs, offs2, out):
     nc = tc.nc
     with ExitStack() as ctx:
         keep = ctx.enter_context(tc.tile_pool(name="keep", bufs=1))
-        late = ctx.enter_context(tc.tile_pool(name="late", bufs=1))
-        ring = ctx.enter_context(tc.tile_pool(name="ring", bufs=1))
+        placed = ctx.enter_context(tc.tile_pool(name="placed", bufs=1))
         psum = ctx.enter_context(tc.psum_pool(name="psum", bufs=1))
+
+        def held(name, shape, dtype, on=None):
+            return keep.tile(shape, dtype, name=name, tag=on or name, align_bytes=64)
+
+        def at(kib, name, shape, dtype):
+            return placed.tile(shape, dtype, name=name, offset=kib * KIB, align_bytes=64)
 
         def bank_tile(i, name, shape):
             return psum.tile(shape, F32, tag=f"bank{i}", name=name)
 
         lists = [keep.tile([P, T // LIST_ROWS], U16, name=f"list{b}") for b in range(2)]
-        books = [
-            [
-                late.tile([P, C + PAD], F32, offset=24576 + 2048, align_bytes=64, name="book0_1")
-                if (b, nb) == (0, 1)
-                else keep.tile([P, C + PAD * (nb < 2 or (b, nb) == (1, 2))], F32, tag=f"book{b}_{nb}", name=f"book{b}_{nb}")
-                for nb in range(NB)
-            ]
-            for b in range(2)
-        ]
-        z = [[keep.tile([P, T // 2], F32, tag=f"z{nb}_{h}", name=f"z{nb}_{h}")[:] for h in range(2)] for nb in range(NB)]
-        x_raw = [keep.tile([P, DB, K_PASS], F32, tag=f"x_raw{k}", name=f"x_raw{k}", align_bytes=64)[:] for k in range(PASSES)]
-        x_scales = keep.tile([P, PASSES, D], U8, align_bytes=64)
-        low_scales = keep.tile([P, PASSES, 2 * P], U8, align_bytes=64)
-        high_scales = keep.tile([P, 2, PASSES * P], U8, align_bytes=64)
-        ident = keep.tile([P, P], F32)
-        tw_rows = keep.tile([P, K_PASS], F32)
-        tw_planes = keep.tile([P, SLOTS, P], F32)
-        neg_w = keep.tile([P, PASSES, SLOTS], F32)
+        padded = [(0, 0), (1, 1), (1, 2), (1, 3)]
+        books = {}
+        for b in range(2):
+            for nb in range(NB):
+                shape = [P, C + PAD * ((b, nb) in padded)]
+                books[b, nb] = at(32, "book1_1", shape, F32) if (b, nb) == (1, 1) else held(f"book{b}_{nb}", shape, F32)
+        z = [[held(f"z{nb}_{h}", [P, T // 2], F32) for h in range(2)] for nb in range(NB)]
+        x_raw = [held(f"x_raw{k}", [P, DB, K_PASS], F32) for k in range(PASSES)]
+        ident = held("ident", [P, P], F32)
+        tw_rows = held("tw_rows", [P, K_PASS], F32)
+        tw_planes = held("tw_planes", [P, SLOTS, P], F32)
+        neg_w = held("neg_w", [P, PASSES, SLOTS], F32)
 
-        nc.gpsimd.memset(tw_rows[:], 0.0)
-        for b, nb in ((0, 0), (1, 0), (0, 1), (1, 1), (1, 2)):
-            nc.vector.memset(books[b][nb][:, C:].bitcast(U32), 0)
+        warm = held("warm", [P, 16], F32)
+        nc.vector.memset(warm[:, :8], 0.0)
+        nc.scalar.activation(warm[:, 8:], warm[:, :8], COPY)
+        nc.vector.memset(tw_rows[:], 0.0)
+        for key in padded:
+            nc.vector.memset(books[key][:, C:].bitcast(U32), 0)
         make_identity(nc, ident[:])
 
         def load_book(b, nb):
-            nc.sync.dma_start(out=books[b][nb][:, :C], in_=(cb, cb2)[b][nb * P : (nb + 1) * P, :])
+            nc.sync.dma_start(out=books[b, nb][:, :C], in_=(cb, cb2)[b][nb * P : (nb + 1) * P, :])
 
         def load_z(nb, half):
-            nc.sync.dma_start(out=z[nb][half], in_=zT[nb * P : (nb + 1) * P, half * T // 2 : (half + 1) * T // 2])
+            nc.sync.dma_start(out=z[nb][half][:], in_=zT[nb * P : (nb + 1) * P, half * T // 2 : (half + 1) * T // 2])
 
         def load_x(k):
-            nc.sync.dma_start(out=x_raw[k], in_=xT[:, k * K_PASS : (k + 1) * K_PASS].rearrange("(b p) t -> p b t", p=P))
+            nc.sync.dma_start(out=x_raw[k][:], in_=xT[:, k * K_PASS : (k + 1) * K_PASS].rearrange("(b p) t -> p b t", p=P))
 
         nc.sync.dma_start(lists[0][:], offs)
         load_book(0, 0)
@@ -93,19 +89,19 @@ def tile_attend_gvq_rw_w_kernel(tc, zT, cb, cb2, tw, xT, offs, offs2, out):
         load_book(0, 1)
         load_book(1, 1)
         load_z(1, 0)
-        load_book(1, 2)
         load_z(1, 1)
+        load_x(0)
+        load_x(1)
         load_book(0, 2)
-        load_book(1, 3)
+        load_book(1, 2)
         load_z(2, 0)
         load_z(2, 1)
-        load_book(0, 3)
-        load_x(0)
-        load_z(3, 0)
-        load_x(1)
-        load_z(3, 1)
         load_x(2)
         load_x(3)
+        load_book(1, 3)
+        load_book(0, 3)
+        load_z(3, 0)
+        load_z(3, 1)
 
         def planes_of(ap):
             return ap.rearrange("p j (q r) -> p j q r", r=RUN)
@@ -114,7 +110,7 @@ def tile_attend_gvq_rw_w_kernel(tc, zT, cb, cb2, tw, xT, offs, offs2, out):
             return ap.rearrange("p (q j r) -> p j q r", j=SLOTS, r=RUN)
 
         nc.gpsimd.tensor_scalar(planes_of(tw_planes[:]), tokens_of(tw_rows[:]), -BETA, 0.0, MULT, ADD)
-        w_bank = bank_tile(7, "w_bank", [P, SLOTS, P])
+        w_bank = bank_tile(2, "w_bank", [P, SLOTS, P])
         for j in range(SLOTS):
             nc.tensor.transpose(w_bank[:, j, :], tw_planes[:, j, :], ident[:])
         nc.scalar.copy(neg_w[:], w_bank[:, :, 0:PASSES].rearrange("p j k -> p k j"))
@@ -122,196 +118,223 @@ def tile_attend_gvq_rw_w_kernel(tc, zT, cb, cb2, tw, xT, offs, offs2, out):
         def offsets(b, k0, k1):
             return lists[b][:, k0 * K_PASS // LIST_ROWS : k1 * K_PASS // LIST_ROWS]
 
-        in_order = [[keep.tile([P, T // 2], F32, name=f"s{nb}_{h}")[:] for h in range(2)] for nb in range(NB)]
-        s_span = late.tile([P, 3 * T // 2], F32, offset=8192, align_bytes=64)
-        extra = {nb: keep.tile([P, K_PASS], F32, name=f"extra{nb}")[:] for nb in BOTH_ON_SCALAR[:-1]}
-        extra[NB - 1] = s_span[:, :K_PASS]
-        gathered_by_vector = []
-        gathered = {}
+        listed = {}
+        planes = {}
         laid = {}
-
-        def half_of(tiles, k0, k1):
-            return tiles[k0 // 2][:, (k0 % 2) * K_PASS : (k0 % 2 + k1 - k0) * K_PASS]
-
-        def gather_block(nb):
-            for b, k in SCALAR_PIECES[nb]:
-                nc.scalar.activation(half_of(in_order[nb], k, k + 1), books[b][nb][:].indirect(offsets(b, k, k + 1)), COPY)
-            if nb in extra:
-                nc.scalar.activation(extra[nb], books[1][nb][:].indirect(offsets(1, PASSES - 1, PASSES)), COPY)
-            for b, k0, k1 in VECTOR_PIECES[nb]:
-                slot = len(gathered_by_vector) % LEAD
-                tile = ring.tile([P, SLOTS, (k1 - k0) * P], F32, offset=slot * 4 * K_PASS, name=f"v{nb}_{k0}")
-                gathered_by_vector.extend(range(k0, k1))
-                nc.vector.tensor_copy(
-                    tile[:].bitcast(U32).rearrange("p j (q r) -> p q j r", r=RUN),
-                    books[b][nb][:].bitcast(U32).indirect(offsets(b, k0, k1)),
-                )
-                for k in range(k0, k1):
-                    gathered[nb, k] = tile[:, :, (k - k0) * P : (k - k0 + 1) * P]
-
-        def lay_planes(nb):
-            for k in range(PASSES):
-                tile = keep.tile([P, SLOTS, P], F32, name=f"laid{nb}_{k}")
-                nc.gpsimd.tensor_tensor(planes_of(tile[:]), tokens_of(half_of(in_order[nb], k, k + 1)), tokens_of(half_of(z[nb], k, k + 1)), SUBTRACT)
-                laid[nb, k] = tile[:]
-            if nb in extra:
-                tile = keep.tile([P, SLOTS, P], F32, tag=f"z{nb}_1", name=f"extra_laid{nb}")
-                nc.gpsimd.tensor_scalar(planes_of(tile[:]), tokens_of(extra[nb]), 1.0, 0.0, MULT, ADD)
-                gathered[nb, PASSES - 1] = tile[:]
-
-        def turn(bank, planes, start, stop):
-            for j in range(SLOTS):
-                nc.tensor.matmul(
-                    bank[:, j, :], planes[:, j, :], ident[:], start=(start and j == 0), stop=(stop and j == SLOTS - 1), is_transpose=True
-                )
-
         banks = {}
+        g = {}
 
-        def add_up(nb, k):
-            bank = bank_tile((nb * PASSES + k) % UNIT_BANKS, f"e{nb}_{k}", [P, SLOTS, P])
-            terms = [laid[nb, k], gathered[nb, k]]
-            if nb == 0 and k >= 2:
-                terms.reverse()
-            turn(bank, terms[0], True, False)
-            turn(bank, terms[1], False, True)
-            banks[nb, k] = bank
+        def scalar_gather(dest, b, nb, k):
+            nc.scalar.activation(dest, books[b, nb][:].indirect(offsets(b, k, k + 1)), COPY)
+            listed[nb, k] = dest
 
-        def g_unit(nb, k):
-            if nb < 2:
-                return g_low[k // 2][:, k % 2, nb * K_PASS : (nb + 1) * K_PASS]
-            if nb == 2:
-                return g_mid[:, k * K_PASS : (k + 1) * K_PASS]
-            if k in (1, 2):
-                return g_end[1][:, (k - 1) * K_PASS : k * K_PASS]
-            return g_end[k][:]
+        def vector_gather(tile, b, nb, k0, k1):
+            nc.vector.tensor_copy(
+                tile[:].bitcast(U32).rearrange("p j (q r) -> p q j r", r=RUN),
+                books[b, nb][:].bitcast(U32).indirect(offsets(b, k0, k1)),
+            )
+            for k in range(k0, k1):
+                planes[nb, k] = tile[:, :, (k - k0) * P : (k - k0 + 1) * P]
+
+        def subtract_z(tile, nb):
+            for k in range(PASSES):
+                laid[nb, k] = tile[:, k * K_PASS : (k + 1) * K_PASS].rearrange("p (j n) -> p j n", j=SLOTS)
+                z_pass = z[nb][k // 2][:, (k % 2) * K_PASS : (k % 2 + 1) * K_PASS]
+                nc.gpsimd.tensor_tensor(planes_of(laid[nb, k]), tokens_of(listed[nb, k]), tokens_of(z_pass), SUBTRACT)
+
+        def add_up(i, nb, k, first, second):
+            banks[nb, k] = bank_tile(i, f"e{nb}_{k}", [P, SLOTS, P])
+            for term, terms in enumerate((first, second)):
+                for j in range(SLOTS):
+                    nc.tensor.matmul(
+                        banks[nb, k][:, j, :],
+                        terms[nb, k][:, j, :],
+                        ident[:],
+                        start=(term == 0 and j == 0),
+                        stop=(term == 1 and j == SLOTS - 1),
+                        is_transpose=True,
+                    )
 
         def weigh(nb, k):
             nc.vector.tensor_tensor(
-                g_unit(nb, k).rearrange("p (n j) -> p n j", j=SLOTS),
+                g[nb, k].rearrange("p (n j) -> p n j", j=SLOTS),
                 neg_w[:, k, :].unsqueeze(1).to_broadcast([P, P, SLOTS]),
                 banks[nb, k][:].rearrange("p j n -> p n j"),
                 MULT,
             )
 
-        x_pairs = {}
-        x_turned = {}
+        def units_in(tile, col, units):
+            for i, unit in enumerate(units):
+                g[unit] = tile[:, col + i * K_PASS : col + (i + 1) * K_PASS]
 
-        def cast_x(k):
-            if k == 0:
-                x_pairs["first"] = keep.tile([P, 2, 2, DB, 2 * P], BF16, tag=f"book0_{NB - 1}", name="x_pairs_first")
-            x_pairs[k] = x_pairs["first"][:, k] if k < 2 else keep.tile([P, 2, DB, 2 * P], BF16, name=f"x_pairs{k}")[:]
-            nc.scalar.copy(
-                x_pairs[k].rearrange("p u b (q r e) -> p u (b q) r e", r=RUN, e=2),
-                x_raw[k].rearrange("p b (q u e r) -> p u (b q) r e", u=2, e=2, r=RUN),
-            )
+        x_banks = {}
 
-        def turn_x(k):
-            bank = bank_tile(k % 2, f"x_bank{k}", [P, DB, 2, P])
+        def cast_and_turn_x(half, first_bank):
+            pairs = [held(f"x_pairs{2 * half + i}", [P, 2, DB, 2 * P], BF16) for i in range(2)]
+            for i in range(2):
+                nc.scalar.copy(
+                    pairs[i][:].rearrange("p u b (q r e) -> p u (b q) r e", r=RUN, e=2),
+                    x_raw[2 * half + i][:].rearrange("p b (q u e r) -> p u (b q) r e", u=2, e=2, r=RUN),
+                )
+            for i in range(2):
+                bank = bank_tile(first_bank + i, f"x_bank{2 * half + i}", [P, DB, 2, P])
+                for db in range(DB):
+                    for u in range(2):
+                        nc.tensor.transpose(bank[:, db, u, :], pairs[i][:, u, db, :].bitcast(F32), ident[:])
+                x_banks[2 * half + i] = bank
+
+        def copy_x(half, turned):
+            for i in range(2):
+                nc.scalar.copy(
+                    turned[:, i * D * SLOTS : (i + 1) * D * SLOTS].bitcast(F32).rearrange("p (b d u) -> p b d u", b=DB, u=2),
+                    x_banks[2 * half + i][:].rearrange("p b u d -> p b d u"),
+                )
+
+        x_codes = held("x_codes", [P, PASSES * D], U32)
+        x_scales = held("x_scales", [P, PASSES * D], U8)
+        g_scales = held("g_scales", [P, NB * PASSES * P], U8)
+        quantised = {}
+        used = []
+
+        def quantize_x(half, turned):
+            cols = slice(2 * half * D, 2 * (half + 1) * D)
+            nc.vector.quantize_mx(out=x_codes[:, cols].bitcast(E4M3), scales=x_scales[:, cols], in_=turned)
+
+        def quantize_g(values, codes, units):
+            first = len(used) * P
+            nc.vector.quantize_mx(out=codes.bitcast(E5M2), scales=g_scales[:, first : first + len(units) * P], in_=values)
+            for i, unit in enumerate(units):
+                quantised[unit] = (codes, i * P, first + i * P)
+            used.extend(units)
+
+        def multiply(sums, nb, k, blocks, start, stop):
+            codes, col, scale_col = quantised[nb, k]
             for db in range(DB):
-                for u in range(2):
-                    nc.tensor.transpose(bank[:, db, u, :], x_pairs[k][:, u, db, :].bitcast(F32), ident[:])
-            x_turned[k] = keep.tile([P, D * SLOTS], BF16, align_bytes=64, tag="x_raw3" if k == 1 else f"x_turned{k}", name=f"x_turned{k}")
-            nc.scalar.copy(
-                x_turned[k][:].bitcast(F32).rearrange("p (b d u) -> p b d u", b=DB, u=2),
-                bank[:].rearrange("p b u d -> p b d u"),
-            )
+                cols = slice(k * D + db * P, k * D + (db + 1) * P)
+                nc.tensor.matmul_mx(
+                    out=sums[db],
+                    lhsT=x_codes[:, cols].bitcast(E4M3),
+                    lhsT_scale=x_scales[:, cols],
+                    rhs=codes[:, col : col + blocks * P].bitcast(E5M2),
+                    rhs_scale=g_scales[:, scale_col : scale_col + blocks * P],
+                    start=start,
+                    stop=stop,
+                )
 
-        g_mid = keep.tile([P, T], BF16, align_bytes=64)
-        g_end = {k: keep.tile([P, K_PASS], BF16, align_bytes=64, name=f"g_end{k}") for k in (0, 3)}
-        for nb in range(NB):
-            gather_block(nb)
-        g_low = [late.tile([P, 2, 2 * K_PASS], BF16, offset=24576 + 4096 * h, align_bytes=64, name=f"g_low{h}") for h in range(2)]
-        for nb in range(NB):
-            lay_planes(nb)
-            for k in range(PASSES):
-                add_up(nb, k)
-                if nb < NB - 1:
-                    weigh(nb, k)
+        s0 = held("listed0", [P, T], F32)
+        for k in range(2):
+            scalar_gather(s0[:, k * K_PASS : (k + 1) * K_PASS], 0, 0, k)
+        vector_gather(held("planes0_23", [P, SLOTS, 2 * P], F32), 0, 0, 2, 4)
+        for k in range(2, 4):
+            scalar_gather(s0[:, k * K_PASS : (k + 1) * K_PASS], 1, 0, k)
+        for k in range(2):
+            vector_gather(held(f"planes0_{k}", [P, SLOTS, P], F32), 1, 0, k, k + 1)
+        subtract_z(held("laid0", [P, T], F32), 0)
         for k in range(PASSES):
-            cast_x(k)
+            add_up(k, 0, k, *((planes, laid) if k == 2 else (laid, planes)))
+        stage_a = at(7, "stage_a", [P, 2 * T], BF16)
+        early = [(0, 0), (1, 0), (0, 1), (1, 1)]
+        units_in(stage_a, 0, early)
+        weigh(0, 0)
+        weigh(0, 1)
+
+        s1 = held("listed1", [P, T], F32)
         for k in range(PASSES):
-            turn_x(k)
+            scalar_gather(s1[:, k * K_PASS : (k + 1) * K_PASS], 0, 1, k)
+        for h in range(2):
+            vector_gather(held(f"planes1_{h}", [P, SLOTS, 2 * P], F32), 1, 1, 2 * h, 2 * h + 2)
+        subtract_z(held("laid1", [P, T], F32), 1)
+        for k in range(2):
+            add_up(4 + k, 1, k, planes, laid)
+        stage_b = at(25, "stage_b", [P, 2 * T], BF16)
+        middle = [(0, 2), (0, 3), (2, 0), (2, 1)]
+        units_in(stage_b, 0, middle)
+        weigh(0, 2)
+        weigh(0, 3)
+        weigh(1, 0)
+        weigh(1, 1)
 
-        x_codes = late.tile([P, PASSES, D], U32, offset=8192, align_bytes=64)
-        low_codes = late.tile([P, PASSES, 2 * P], U32, offset=8192 + 4096, align_bytes=64)
-        high_codes = late.tile([P, 2, PASSES * P], U32, offset=8192 + 8192, align_bytes=64)
+        cast_and_turn_x(0, 0)
+        copy_x(0, stage_a[:, T:])
+        quantize_g(stage_a[:, :T], held("codes_a", [P, 4 * P], U32, on="z1_1")[:], early)
+        quantize_x(0, stage_a[:, T:])
+        for k in range(2, 4):
+            add_up(k - 2, 1, k, laid, planes)
+        acc = [bank_tile(6 + db, f"acc{db}", [P, 3 * P]) for db in range(DB)]
+        low = [acc[db][:, : 2 * P] for db in range(DB)]
+        columns = [[acc[db][:, nb * P : (nb + 1) * P] for db in range(DB)] for nb in range(3)]
+        for k in range(2):
+            multiply(low, 0, k, 2, k == 0, False)
 
-        def quantize_low(h):
-            nc.vector.quantize_mx(
-                out=low_codes[:, 2 * h : 2 * h + 2, :].rearrange("p k c -> p (k c)").bitcast(E5M2),
-                scales=low_scales[:, 2 * h : 2 * h + 2, :].rearrange("p k c -> p (k c)"),
-                in_=g_low[h][:].rearrange("p k c -> p (k c)"),
-            )
+        s2 = held("listed2", [P, T], F32, on="x_pairs1")
+        for k in range(PASSES):
+            scalar_gather(s2[:, k * K_PASS : (k + 1) * K_PASS], 0, 2, k)
+        vector_gather(at(8, "planes2_01", [P, SLOTS, 2 * P], F32), 1, 2, 0, 2)
+        stage_e = at(12, "stage_e", [P, 2 * K_PASS], BF16)
+        units_in(stage_e, 0, [(1, 2), (1, 3)])
+        weigh(1, 2)
+        weigh(1, 3)
+        vector_gather(held("planes2_23", [P, SLOTS, 2 * P], F32, on="planes1_1"), 1, 2, 2, 4)
+        subtract_z(at(0, "laid2", [P, T], F32), 2)
+        for k in range(2):
+            add_up(4 + k, 2, k, laid, planes)
+        weigh(2, 0)
+        weigh(2, 1)
 
-        def quantize_high(i, k0, k1):
-            nc.vector.quantize_mx(
-                out=high_codes[:, i, k0 * P : k1 * P].bitcast(E5M2),
-                scales=high_scales[:, i, k0 * P : k1 * P],
-                in_=g_end[k0][:] if i else g_mid[:],
-            )
+        cast_and_turn_x(1, 2)
+        copy_x(1, stage_b[:, T:])
+        codes_b = held("codes_b", [P, 6 * P], U32, on="z2_1")
+        quantize_g(stage_e[:], codes_b[:, 4 * P :], [(1, 2), (1, 3)])
+        quantize_g(stage_b[:, :T], codes_b[:, : 4 * P], middle)
+        quantize_x(1, stage_b[:, T:])
+        for k in range(2, 4):
+            add_up(k, 2, k, laid, planes)
+        for k in range(2, 4):
+            for nb in range(2):
+                multiply(columns[nb], nb, k, 1, False, False)
+        for k in range(2):
+            multiply(columns[2], 2, k, 1, False, False)
 
-        def quantize_x(k):
-            nc.vector.quantize_mx(out=x_codes[:, k, :].bitcast(E4M3), scales=x_scales[:, k, :], in_=x_turned[k][:])
+        s3 = held("listed3", [P, T], F32, on="x_pairs3")
+        for k in range(PASSES):
+            scalar_gather(s3[:, k * K_PASS : (k + 1) * K_PASS], 0, 3, k)
+        vector_gather(at(26, "planes3_01", [P, SLOTS, 2 * P], F32), 1, 3, 0, 2)
+        stage_c = at(32, "stage_c", [P, T], BF16)
+        late = [(2, 2), (2, 3), (3, 0), (3, 1)]
+        units_in(stage_c, 0, late)
+        weigh(2, 2)
+        weigh(2, 3)
+        vector_gather(at(30, "planes3_2", [P, SLOTS, P], F32), 1, 3, 2, 3)
+        subtract_z(at(18, "laid3", [P, T], F32), 3)
+        extra = held("extra", [P, K_PASS], F32, on="book0_3")
+        nc.scalar.activation(extra[:], books[1, 3][:].indirect(offsets(1, 3, 4)), COPY)
+        extra_laid = held("extra_laid", [P, SLOTS, P], F32, on="z3_1")
+        nc.gpsimd.tensor_scalar(planes_of(extra_laid[:]), tokens_of(extra[:]), 1.0, 0.0, MULT, ADD)
+        planes[3, 3] = extra_laid[:]
+        for k in range(PASSES):
+            add_up((0, 1, 4, 5)[k], 3, k, laid, planes)
+        stage_d = held("stage_d", [P, 2 * K_PASS], BF16)
+        units_in(stage_d, 0, [(3, 2), (3, 3)])
+        for k in range(3):
+            weigh(3, k)
 
-        def multiply(sums, db, k, codes, scales, start, stop):
-            nc.tensor.matmul_mx(
-                out=sums,
-                lhsT=x_codes[:, k, db * P : (db + 1) * P].bitcast(E4M3),
-                lhsT_scale=x_scales[:, k, db * P : (db + 1) * P],
-                rhs=codes.bitcast(E5M2),
-                rhs_scale=scales,
-                start=start,
-                stop=stop,
-            )
-
-        last = PASSES - 1
-        acc = [bank_tile(2 + db, f"acc{db}", [P, 3 * P]) for db in range(DB)]
-        acc_last = [bank_tile(4 + db, f"acc_last{db}", [P, P]) for db in range(DB)]
-
-        def low_products(k):
-            for db in range(DB):
-                multiply(acc[db][:, : 2 * P], db, k, low_codes[:, k, :], low_scales[:, k, :], k == 0, False)
-
-        def high_products(i, k):
-            cols = slice(k * P, (k + 1) * P)
-            for db in range(DB):
-                sums = acc[db][:, 2 * P :] if i == 0 else acc_last[db][:]
-                multiply(sums, db, k, high_codes[:, i, cols], high_scales[:, i, cols], i == 1 and k == 0, k == last)
-
-        weigh(last, 0)
-        quantize_low(0)
-        g_end[1] = late.tile([P, 2 * K_PASS], BF16, offset=24576, align_bytes=64, name="g_end1")
-        quantize_x(0)
-        low_products(0)
-        quantize_high(0, 0, PASSES)
-        high_products(0, 0)
-        quantize_high(1, 0, 1)
-        high_products(1, 0)
-        weigh(last, 1)
-        quantize_low(1)
-        quantize_x(1)
-        low_products(1)
-        high_products(0, 1)
-        weigh(last, 2)
-        quantize_x(2)
-        low_products(2)
-        high_products(0, 2)
-        quantize_x(3)
-        low_products(3)
-        high_products(0, 3)
-        weigh(last, 3)
-        quantize_high(1, 1, 3)
-        high_products(1, 1)
-        high_products(1, 2)
-        quantize_high(1, 3, 4)
-        high_products(1, 3)
+        codes_c = held("codes_c", [P, 6 * P], U32, on="book0_3")
+        quantize_g(stage_c[:], codes_c[:, : 4 * P], late)
+        for k in range(2, 4):
+            multiply(columns[2], 2, k, 1, False, k == 3)
+        last = [bank_tile(2 + db, f"last{db}", [P, P])[:] for db in range(DB)]
+        for k in range(2):
+            multiply(last, 3, k, 1, k == 0, False)
         for db in range(DB):
-            result = keep.tile([P, 3 * P], F32, name=f"result{db}")
-            (nc.vector.tensor_copy, nc.scalar.copy)[db](result[:], acc[db][:])
+            result = held(f"result{db}", [P, 3 * P], F32)
+            nc.scalar.copy(result[:], acc[db][:])
             nc.sync.dma_start(out=out[db * P : (db + 1) * P, : 3 * P], in_=result[:])
-
-        tail = [keep.tile([P, P], F32, name=f"tail{db}") for db in range(DB)]
-        nc.vector.tensor_copy(tail[0][:], acc_last[0][:])
-        nc.sync.dma_start(out=out[0:P, last * P :], in_=tail[0][:])
-        nc.scalar.copy(tail[1][:], acc_last[1][:])
-        nc.scalar.dma_start(out=out[P:, last * P :], in_=tail[1][:])
+        weigh(3, 3)
+        for k in range(2, 4):
+            quantize_g(g[3, k], codes_c[:, (2 + k) * P : (3 + k) * P], [(3, k)])
+            multiply(last, 3, k, 1, False, k == 3)
+        tail = [held(f"tail{db}", [P, P], F32) for db in range(DB)]
+        nc.vector.tensor_copy(tail[0][:], last[0])
+        nc.sync.dma_start(out=out[0:P, 3 * P :], in_=tail[0][:])
+        nc.scalar.copy(tail[1][:], last[1])
+        nc.scalar.dma_start(out=out[P:, 3 * P :], in_=tail[1][:])

@@ -29,32 +29,23 @@ NB = DV // P
 DB = D // P
 LIST_ROWS = 16
 PAD = 352
-KIB = 1024
 
 
 def tile_attend_gvq_rw_w_kernel(tc, zT, cb, cb2, tw, xT, offs, offs2, out):
     nc = tc.nc
     with ExitStack() as ctx:
         keep = ctx.enter_context(tc.tile_pool(name="keep", bufs=1))
-        placed = ctx.enter_context(tc.tile_pool(name="placed", bufs=1))
         psum = ctx.enter_context(tc.psum_pool(name="psum", bufs=1))
 
         def held(name, shape, dtype, on=None):
             return keep.tile(shape, dtype, name=name, tag=on or name, align_bytes=64)
 
-        def at(kib, name, shape, dtype):
-            return placed.tile(shape, dtype, name=name, offset=kib * KIB, align_bytes=64)
-
         def bank_tile(i, name, shape):
             return psum.tile(shape, F32, tag=f"bank{i}", name=name)
 
         lists = [keep.tile([P, T // LIST_ROWS], U16, name=f"list{b}") for b in range(2)]
-        padded = [(0, 0), (1, 1), (1, 2), (1, 3)]
-        books = {}
-        for b in range(2):
-            for nb in range(NB):
-                shape = [P, C + PAD * ((b, nb) in padded)]
-                books[b, nb] = at(32, "book1_1", shape, F32) if (b, nb) == (1, 1) else held(f"book{b}_{nb}", shape, F32)
+        padded = {(0, 0): PAD, (1, 1): PAD, (1, 2): PAD, (1, 3): PAD, (0, 1): 32, (0, 2): 32}
+        books = {(b, nb): held(f"book{b}_{nb}", [P, C + padded.get((b, nb), 0)], F32) for b in range(2) for nb in range(NB)}
         z = [[held(f"z{nb}_{h}", [P, T // 2], F32) for h in range(2)] for nb in range(NB)]
         x_raw = [held(f"x_raw{k}", [P, DB, K_PASS], F32) for k in range(PASSES)]
         ident = held("ident", [P, P], F32)
@@ -62,10 +53,14 @@ def tile_attend_gvq_rw_w_kernel(tc, zT, cb, cb2, tw, xT, offs, offs2, out):
         tw_planes = held("tw_planes", [P, SLOTS, P], F32)
         neg_w = held("neg_w", [P, PASSES, SLOTS], F32)
 
-        warm = held("warm", [P, 16], F32)
-        nc.vector.memset(warm[:, :8], 0.0)
-        nc.scalar.activation(warm[:, 8:], warm[:, :8], COPY)
-        nc.vector.memset(tw_rows[:], 0.0)
+        zeros = held("zeros", [P, RUN], F32)
+        nc.vector.memset(zeros[:], 0.0)
+        nc.vector.memset(tw_rows[: P // 2, :], 0.0)
+        nc.scalar.activation(
+            tw_rows[P // 2 :, :].rearrange("p (n r) -> p n r", r=RUN),
+            zeros[P // 2 :, :].unsqueeze(1).to_broadcast([P // 2, K_PASS // RUN, RUN]),
+            COPY,
+        )
         for key in padded:
             nc.vector.memset(books[key][:, C:].bitcast(U32), 0)
         make_identity(nc, ident[:])
@@ -90,18 +85,18 @@ def tile_attend_gvq_rw_w_kernel(tc, zT, cb, cb2, tw, xT, offs, offs2, out):
         load_book(1, 1)
         load_z(1, 0)
         load_z(1, 1)
-        load_x(0)
-        load_x(1)
         load_book(0, 2)
         load_book(1, 2)
         load_z(2, 0)
-        load_z(2, 1)
-        load_x(2)
-        load_x(3)
         load_book(1, 3)
+        load_z(2, 1)
         load_book(0, 3)
         load_z(3, 0)
+        load_x(0)
+        load_x(1)
         load_z(3, 1)
+        load_x(2)
+        load_x(3)
 
         def planes_of(ap):
             return ap.rearrange("p j (q r) -> p j q r", r=RUN)
@@ -118,17 +113,18 @@ def tile_attend_gvq_rw_w_kernel(tc, zT, cb, cb2, tw, xT, offs, offs2, out):
         def offsets(b, k0, k1):
             return lists[b][:, k0 * K_PASS // LIST_ROWS : k1 * K_PASS // LIST_ROWS]
 
-        listed = {}
         planes = {}
         laid = {}
         banks = {}
         g = {}
 
-        def scalar_gather(dest, b, nb, k):
-            nc.scalar.activation(dest, books[b, nb][:].indirect(offsets(b, k, k + 1)), COPY)
-            listed[nb, k] = dest
+        def scalar_gather(name, b, nb, k0, k1):
+            tile = held(name, [P, (k1 - k0) * K_PASS], F32)
+            nc.scalar.activation(tile[:], books[b, nb][:].indirect(offsets(b, k0, k1)), COPY)
+            return tile
 
-        def vector_gather(tile, b, nb, k0, k1):
+        def vector_gather(b, nb, k0, k1):
+            tile = held(f"planes{nb}_{k0}", [P, SLOTS, (k1 - k0) * P], F32)
             nc.vector.tensor_copy(
                 tile[:].bitcast(U32).rearrange("p j (q r) -> p q j r", r=RUN),
                 books[b, nb][:].bitcast(U32).indirect(offsets(b, k0, k1)),
@@ -136,14 +132,16 @@ def tile_attend_gvq_rw_w_kernel(tc, zT, cb, cb2, tw, xT, offs, offs2, out):
             for k in range(k0, k1):
                 planes[nb, k] = tile[:, :, (k - k0) * P : (k - k0 + 1) * P]
 
-        def subtract_z(tile, nb):
-            for k in range(PASSES):
-                laid[nb, k] = tile[:, k * K_PASS : (k + 1) * K_PASS].rearrange("p (j n) -> p j n", j=SLOTS)
-                z_pass = z[nb][k // 2][:, (k % 2) * K_PASS : (k % 2 + 1) * K_PASS]
-                nc.gpsimd.tensor_tensor(planes_of(laid[nb, k]), tokens_of(listed[nb, k]), tokens_of(z_pass), SUBTRACT)
+        def gather_less_z(b, nb, k0, k1):
+            listed = scalar_gather(f"listed{nb}_{k0}", b, nb, k0, k1)
+            tile = held(f"laid{nb}_{k0}", [P, SLOTS, (k1 - k0) * P], F32)
+            z_part = z[nb][k0 // 2][:, (k0 % 2) * K_PASS : (k0 % 2 + k1 - k0) * K_PASS]
+            nc.gpsimd.tensor_tensor(planes_of(tile[:]), tokens_of(listed[:]), tokens_of(z_part), SUBTRACT)
+            for k in range(k0, k1):
+                laid[nb, k] = tile[:, :, (k - k0) * P : (k - k0 + 1) * P]
 
-        def add_up(i, nb, k, first, second):
-            banks[nb, k] = bank_tile(i, f"e{nb}_{k}", [P, SLOTS, P])
+        def add_up(nb, k, first, second):
+            banks[nb, k] = bank_tile((nb * PASSES + k) % 8, f"e{nb}_{k}", [P, SLOTS, P])
             for term, terms in enumerate((first, second)):
                 for j in range(SLOTS):
                     nc.tensor.matmul(
@@ -163,176 +161,142 @@ def tile_attend_gvq_rw_w_kernel(tc, zT, cb, cb2, tw, xT, offs, offs2, out):
                 MULT,
             )
 
-        def units_in(tile, col, units):
+        def staging(name, units, on=None):
+            tile = held(name, [P, len(units) * K_PASS], BF16, on=on)
             for i, unit in enumerate(units):
-                g[unit] = tile[:, col + i * K_PASS : col + (i + 1) * K_PASS]
+                g[unit] = tile[:, i * K_PASS : (i + 1) * K_PASS]
+            return tile[:], units
 
         x_banks = {}
+        x_turned = {}
 
-        def cast_and_turn_x(half, first_bank):
-            pairs = [held(f"x_pairs{2 * half + i}", [P, 2, DB, 2 * P], BF16) for i in range(2)]
-            for i in range(2):
-                nc.scalar.copy(
-                    pairs[i][:].rearrange("p u b (q r e) -> p u (b q) r e", r=RUN, e=2),
-                    x_raw[2 * half + i][:].rearrange("p b (q u e r) -> p u (b q) r e", u=2, e=2, r=RUN),
-                )
-            for i in range(2):
-                bank = bank_tile(first_bank + i, f"x_bank{2 * half + i}", [P, DB, 2, P])
-                for db in range(DB):
-                    for u in range(2):
-                        nc.tensor.transpose(bank[:, db, u, :], pairs[i][:, u, db, :].bitcast(F32), ident[:])
-                x_banks[2 * half + i] = bank
+        def cast_and_turn_x(k):
+            pairs = held(f"x_pairs{k}", [P, 2, DB, 2 * P], BF16)
+            nc.scalar.copy(
+                pairs[:].rearrange("p u b (q r e) -> p u (b q) r e", r=RUN, e=2),
+                x_raw[k][:].rearrange("p b (q u e r) -> p u (b q) r e", u=2, e=2, r=RUN),
+            )
+            x_banks[k] = bank_tile(k % 2, f"x_bank{k}", [P, DB, 2, P])
+            for db in range(DB):
+                for u in range(2):
+                    nc.tensor.transpose(x_banks[k][:, db, u, :], pairs[:, u, db, :].bitcast(F32), ident[:])
 
-        def copy_x(half, turned):
-            for i in range(2):
-                nc.scalar.copy(
-                    turned[:, i * D * SLOTS : (i + 1) * D * SLOTS].bitcast(F32).rearrange("p (b d u) -> p b d u", b=DB, u=2),
-                    x_banks[2 * half + i][:].rearrange("p b u d -> p b d u"),
-                )
+        def copy_x(k):
+            x_turned[k] = held(f"x_turned{k}", [P, D * SLOTS], BF16)
+            nc.scalar.copy(
+                x_turned[k][:].bitcast(F32).rearrange("p (b d u) -> p b d u", b=DB, u=2),
+                x_banks[k][:].rearrange("p b u d -> p b d u"),
+            )
 
-        x_codes = held("x_codes", [P, PASSES * D], U32)
         x_scales = held("x_scales", [P, PASSES * D], U8)
         g_scales = held("g_scales", [P, NB * PASSES * P], U8)
         quantised = {}
-        used = []
 
-        def quantize_x(half, turned):
-            cols = slice(2 * half * D, 2 * (half + 1) * D)
-            nc.vector.quantize_mx(out=x_codes[:, cols].bitcast(E4M3), scales=x_scales[:, cols], in_=turned)
+        def quantize_x(k):
+            cols = slice(k * D, (k + 1) * D)
+            nc.vector.quantize_mx(out=x_codes[:, cols].bitcast(E4M3), scales=x_scales[:, cols], in_=x_turned[k][:])
 
-        def quantize_g(values, codes, units):
-            first = len(used) * P
-            nc.vector.quantize_mx(out=codes.bitcast(E5M2), scales=g_scales[:, first : first + len(units) * P], in_=values)
-            for i, unit in enumerate(units):
-                quantised[unit] = (codes, i * P, first + i * P)
-            used.extend(units)
+        def quantize_g(values, units):
+            cols = slice(len(quantised) * P, (len(quantised) + len(units)) * P)
+            nc.vector.quantize_mx(out=g_codes[:, cols].bitcast(E5M2), scales=g_scales[:, cols], in_=values)
+            for unit in units:
+                quantised[unit] = len(quantised) * P
 
         def multiply(sums, nb, k, blocks, start, stop):
-            codes, col, scale_col = quantised[nb, k]
+            g_cols = slice(quantised[nb, k], quantised[nb, k] + blocks * P)
             for db in range(DB):
                 cols = slice(k * D + db * P, k * D + (db + 1) * P)
                 nc.tensor.matmul_mx(
                     out=sums[db],
                     lhsT=x_codes[:, cols].bitcast(E4M3),
                     lhsT_scale=x_scales[:, cols],
-                    rhs=codes[:, col : col + blocks * P].bitcast(E5M2),
-                    rhs_scale=g_scales[:, scale_col : scale_col + blocks * P],
+                    rhs=g_codes[:, g_cols].bitcast(E5M2),
+                    rhs_scale=g_scales[:, g_cols],
                     start=start,
                     stop=stop,
                 )
 
-        s0 = held("listed0", [P, T], F32)
         for k in range(2):
-            scalar_gather(s0[:, k * K_PASS : (k + 1) * K_PASS], 0, 0, k)
-        vector_gather(held("planes0_23", [P, SLOTS, 2 * P], F32), 0, 0, 2, 4)
+            gather_less_z(0, 0, k, k + 1)
+        vector_gather(0, 0, 2, 4)
         for k in range(2, 4):
-            scalar_gather(s0[:, k * K_PASS : (k + 1) * K_PASS], 1, 0, k)
+            gather_less_z(1, 0, k, k + 1)
         for k in range(2):
-            vector_gather(held(f"planes0_{k}", [P, SLOTS, P], F32), 1, 0, k, k + 1)
-        subtract_z(held("laid0", [P, T], F32), 0)
+            vector_gather(1, 0, k, k + 1)
         for k in range(PASSES):
-            add_up(k, 0, k, *((planes, laid) if k == 2 else (laid, planes)))
-        stage_a = at(7, "stage_a", [P, 2 * T], BF16)
-        early = [(0, 0), (1, 0), (0, 1), (1, 1)]
-        units_in(stage_a, 0, early)
+            add_up(0, k, *((planes, laid) if k == 2 else (laid, planes)))
+        low = staging("g_low", [(0, 0), (1, 0), (0, 1), (1, 1)])
+        high = staging("g_high", [(2, 0), (2, 1), (3, 0), (3, 1)])
+        late = {}
         weigh(0, 0)
         weigh(0, 1)
 
-        s1 = held("listed1", [P, T], F32)
-        for k in range(PASSES):
-            scalar_gather(s1[:, k * K_PASS : (k + 1) * K_PASS], 0, 1, k)
-        for h in range(2):
-            vector_gather(held(f"planes1_{h}", [P, SLOTS, 2 * P], F32), 1, 1, 2 * h, 2 * h + 2)
-        subtract_z(held("laid1", [P, T], F32), 1)
-        for k in range(2):
-            add_up(4 + k, 1, k, planes, laid)
-        stage_b = at(25, "stage_b", [P, 2 * T], BF16)
-        middle = [(0, 2), (0, 3), (2, 0), (2, 1)]
-        units_in(stage_b, 0, middle)
-        weigh(0, 2)
-        weigh(0, 3)
-        weigh(1, 0)
-        weigh(1, 1)
+        for nb in range(1, NB):
+            if nb < NB - 1:
+                for h in range(2):
+                    gather_less_z(0, nb, 2 * h, 2 * h + 2)
+                    vector_gather(1, nb, 2 * h, 2 * h + 2)
+            else:
+                extra = scalar_gather("extra", 1, nb, 2, 4)
+                extra_laid = held("extra_laid", [P, SLOTS, 2 * P], F32, on="z2_1")
+                nc.gpsimd.tensor_scalar(planes_of(extra_laid[:]), tokens_of(extra[:]), 1.0, 0.0, MULT, ADD)
+                for k in range(2, 4):
+                    planes[nb, k] = extra_laid[:, :, (k - 2) * P : (k - 1) * P]
+                for k in range(PASSES):
+                    gather_less_z(0, nb, k, k + 1)
+                vector_gather(1, nb, 0, 2)
+            late[nb - 1] = staging(f"g_late{nb - 1}", [(nb - 1, 2), (nb - 1, 3)], on=f"book1_{nb}")
+            weigh(nb - 1, 2)
+            weigh(nb - 1, 3)
+            for k in range(PASSES):
+                planes_first = (nb == 1 and k < 2) or (nb == NB - 1 and k >= 2)
+                add_up(nb, k, *((planes, laid) if planes_first else (laid, planes)))
+            weigh(nb, 0)
+            weigh(nb, 1)
 
-        cast_and_turn_x(0, 0)
-        copy_x(0, stage_a[:, T:])
-        quantize_g(stage_a[:, :T], held("codes_a", [P, 4 * P], U32, on="z1_1")[:], early)
-        quantize_x(0, stage_a[:, T:])
-        for k in range(2, 4):
-            add_up(k - 2, 1, k, laid, planes)
-        acc = [bank_tile(6 + db, f"acc{db}", [P, 3 * P]) for db in range(DB)]
-        low = [acc[db][:, : 2 * P] for db in range(DB)]
-        columns = [[acc[db][:, nb * P : (nb + 1) * P] for db in range(DB)] for nb in range(3)]
-        for k in range(2):
-            multiply(low, 0, k, 2, k == 0, False)
+        for half in range(2):
+            cast_and_turn_x(2 * half)
+            cast_and_turn_x(2 * half + 1)
+            copy_x(2 * half)
+            copy_x(2 * half + 1)
 
-        s2 = held("listed2", [P, T], F32, on="x_pairs1")
-        for k in range(PASSES):
-            scalar_gather(s2[:, k * K_PASS : (k + 1) * K_PASS], 0, 2, k)
-        vector_gather(at(8, "planes2_01", [P, SLOTS, 2 * P], F32), 1, 2, 0, 2)
-        stage_e = at(12, "stage_e", [P, 2 * K_PASS], BF16)
-        units_in(stage_e, 0, [(1, 2), (1, 3)])
-        weigh(1, 2)
-        weigh(1, 3)
-        vector_gather(held("planes2_23", [P, SLOTS, 2 * P], F32, on="planes1_1"), 1, 2, 2, 4)
-        subtract_z(at(0, "laid2", [P, T], F32), 2)
-        for k in range(2):
-            add_up(4 + k, 2, k, laid, planes)
-        weigh(2, 0)
-        weigh(2, 1)
+        codes = held("codes", [P, NB * PASSES * P + PASSES * D], U32, on="z3_1")
+        g_codes, x_codes = codes[:, : NB * PASSES * P], codes[:, NB * PASSES * P :]
+        acc = [bank_tile(2 + db, f"acc{db}", [P, 3 * P]) for db in range(DB)]
+        last = [bank_tile(4 + db, f"last{db}", [P, P])[:] for db in range(DB)]
+        sums = [[acc[db][:, nb * P : (nb + 1) * P] for db in range(DB)] for nb in range(3)] + [last]
+        pair = [acc[db][:, : 2 * P] for db in range(DB)]
 
-        cast_and_turn_x(1, 2)
-        copy_x(1, stage_b[:, T:])
-        codes_b = held("codes_b", [P, 6 * P], U32, on="z2_1")
-        quantize_g(stage_e[:], codes_b[:, 4 * P :], [(1, 2), (1, 3)])
-        quantize_g(stage_b[:, :T], codes_b[:, : 4 * P], middle)
-        quantize_x(1, stage_b[:, T:])
-        for k in range(2, 4):
-            add_up(k, 2, k, laid, planes)
-        for k in range(2, 4):
-            for nb in range(2):
-                multiply(columns[nb], nb, k, 1, False, False)
-        for k in range(2):
-            multiply(columns[2], 2, k, 1, False, False)
-
-        s3 = held("listed3", [P, T], F32, on="x_pairs3")
-        for k in range(PASSES):
-            scalar_gather(s3[:, k * K_PASS : (k + 1) * K_PASS], 0, 3, k)
-        vector_gather(at(26, "planes3_01", [P, SLOTS, 2 * P], F32), 1, 3, 0, 2)
-        stage_c = at(32, "stage_c", [P, T], BF16)
-        late = [(2, 2), (2, 3), (3, 0), (3, 1)]
-        units_in(stage_c, 0, late)
-        weigh(2, 2)
-        weigh(2, 3)
-        vector_gather(at(30, "planes3_2", [P, SLOTS, P], F32), 1, 3, 2, 3)
-        subtract_z(at(18, "laid3", [P, T], F32), 3)
-        extra = held("extra", [P, K_PASS], F32, on="book0_3")
-        nc.scalar.activation(extra[:], books[1, 3][:].indirect(offsets(1, 3, 4)), COPY)
-        extra_laid = held("extra_laid", [P, SLOTS, P], F32, on="z3_1")
-        nc.gpsimd.tensor_scalar(planes_of(extra_laid[:]), tokens_of(extra[:]), 1.0, 0.0, MULT, ADD)
-        planes[3, 3] = extra_laid[:]
-        for k in range(PASSES):
-            add_up((0, 1, 4, 5)[k], 3, k, laid, planes)
-        stage_d = held("stage_d", [P, 2 * K_PASS], BF16)
-        units_in(stage_d, 0, [(3, 2), (3, 3)])
-        for k in range(3):
-            weigh(3, k)
-
-        codes_c = held("codes_c", [P, 6 * P], U32, on="book0_3")
-        quantize_g(stage_c[:], codes_c[:, : 4 * P], late)
-        for k in range(2, 4):
-            multiply(columns[2], 2, k, 1, False, k == 3)
-        last = [bank_tile(2 + db, f"last{db}", [P, P])[:] for db in range(DB)]
-        for k in range(2):
-            multiply(last, 3, k, 1, k == 0, False)
-        for db in range(DB):
-            result = held(f"result{db}", [P, 3 * P], F32)
-            nc.scalar.copy(result[:], acc[db][:])
-            nc.sync.dma_start(out=out[db * P : (db + 1) * P, : 3 * P], in_=result[:])
+        quantize_g(*low)
+        quantize_x(0)
+        multiply(pair, 0, 0, 2, True, False)
+        quantize_g(*high)
+        multiply(sums[2], 2, 0, 1, False, False)
+        multiply(last, 3, 0, 1, True, False)
+        quantize_x(1)
+        multiply(pair, 0, 1, 2, False, False)
+        multiply(sums[2], 2, 1, 1, False, False)
+        multiply(last, 3, 1, 1, False, False)
+        staging("g3_2", [(3, 2)])
+        weigh(3, 2)
+        quantize_g(*late[0])
+        quantize_g(*late[1])
+        quantize_x(2)
+        quantize_g(*late[2])
+        for nb in range(3):
+            multiply(sums[nb], nb, 2, 1, False, False)
+        quantize_x(3)
+        for nb in range(3):
+            multiply(sums[nb], nb, 3, 1, False, nb == 2)
+        staging("g3_3", [(3, 3)], on="x_turned3")
         weigh(3, 3)
         for k in range(2, 4):
-            quantize_g(g[3, k], codes_c[:, (2 + k) * P : (3 + k) * P], [(3, k)])
+            quantize_g(g[3, k], [(3, k)])
             multiply(last, 3, k, 1, False, k == 3)
+        for db in range(DB):
+            result = held(f"result{db}", [P, 3 * P], F32)
+            (nc.vector.tensor_copy, nc.scalar.copy)[db](result[:], acc[db][:])
+            nc.sync.dma_start(out=out[db * P : (db + 1) * P, : 3 * P], in_=result[:])
         tail = [held(f"tail{db}", [P, P], F32) for db in range(DB)]
         nc.vector.tensor_copy(tail[0][:], last[0])
         nc.sync.dma_start(out=out[0:P, 3 * P :], in_=tail[0][:])

@@ -44,10 +44,10 @@ def tile_attend_gvq_rw_w_kernel(tc, zT, cb, cb2, tw, xT, offs, offs2, out):
             return psum.tile(shape, F32, tag=f"bank{i}", name=name)
 
         lists = [keep.tile([P, T // LIST_ROWS], U16, name=f"list{b}") for b in range(2)]
-        padded = {(0, 0): PAD, (1, 1): PAD, (1, 2): PAD, (1, 3): PAD, (0, 1): 32, (0, 2): 32}
+        padded = {(0, 0): PAD, (1, 1): PAD, (1, 2): PAD, (1, 3): PAD, (0, 1): 32, (0, 2): 32, (0, 3): 32}
         books = {(b, nb): held(f"book{b}_{nb}", [P, C + padded.get((b, nb), 0)], F32) for b in range(2) for nb in range(NB)}
         z = [[held(f"z{nb}_{h}", [P, T // 2], F32) for h in range(2)] for nb in range(NB)]
-        x_raw = [held(f"x_raw{k}", [P, DB, K_PASS], F32) for k in range(PASSES)]
+        x_raw = [held(f"x_raw{h}", [P, DB, T // 2], F32) for h in range(2)]
         ident = held("ident", [P, P], F32)
         tw_rows = held("tw_rows", [P, K_PASS], F32)
         tw_planes = held("tw_planes", [P, SLOTS, P], F32)
@@ -71,8 +71,8 @@ def tile_attend_gvq_rw_w_kernel(tc, zT, cb, cb2, tw, xT, offs, offs2, out):
         def load_z(nb, half):
             nc.sync.dma_start(out=z[nb][half][:], in_=zT[nb * P : (nb + 1) * P, half * T // 2 : (half + 1) * T // 2])
 
-        def load_x(k):
-            nc.sync.dma_start(out=x_raw[k][:], in_=xT[:, k * K_PASS : (k + 1) * K_PASS].rearrange("(b p) t -> p b t", p=P))
+        def load_x(half):
+            nc.sync.dma_start(out=x_raw[half][:], in_=xT[:, half * T // 2 : (half + 1) * T // 2].rearrange("(b p) t -> p b t", p=P))
 
         nc.sync.dma_start(lists[0][:], offs)
         load_book(0, 0)
@@ -88,15 +88,13 @@ def tile_attend_gvq_rw_w_kernel(tc, zT, cb, cb2, tw, xT, offs, offs2, out):
         load_book(0, 2)
         load_book(1, 2)
         load_z(2, 0)
+        load_book(0, 3)
         load_book(1, 3)
         load_z(2, 1)
-        load_book(0, 3)
         load_z(3, 0)
         load_x(0)
-        load_x(1)
         load_z(3, 1)
-        load_x(2)
-        load_x(3)
+        load_x(1)
 
         def planes_of(ap):
             return ap.rearrange("p j (q r) -> p j q r", r=RUN)
@@ -110,33 +108,33 @@ def tile_attend_gvq_rw_w_kernel(tc, zT, cb, cb2, tw, xT, offs, offs2, out):
             nc.tensor.transpose(w_bank[:, j, :], tw_planes[:, j, :], ident[:])
         nc.scalar.copy(neg_w[:], w_bank[:, :, 0:PASSES].rearrange("p j k -> p k j"))
 
-        def offsets(b, k0, k1):
-            return lists[b][:, k0 * K_PASS // LIST_ROWS : k1 * K_PASS // LIST_ROWS]
+        def offsets(b, t0, t1):
+            return lists[b][:, t0 // LIST_ROWS : t1 // LIST_ROWS]
 
         planes = {}
         laid = {}
         banks = {}
         g = {}
 
-        def scalar_gather(name, b, nb, k0, k1):
-            tile = held(name, [P, (k1 - k0) * K_PASS], F32)
-            nc.scalar.activation(tile[:], books[b, nb][:].indirect(offsets(b, k0, k1)), COPY)
-            return tile
+        def scalar_gather(dest, b, nb, t0, t1):
+            nc.scalar.activation(dest, books[b, nb][:].indirect(offsets(b, t0, t1)), COPY)
 
         def vector_gather(b, nb, k0, k1):
             tile = held(f"planes{nb}_{k0}", [P, SLOTS, (k1 - k0) * P], F32)
             nc.vector.tensor_copy(
                 tile[:].bitcast(U32).rearrange("p j (q r) -> p q j r", r=RUN),
-                books[b, nb][:].bitcast(U32).indirect(offsets(b, k0, k1)),
+                books[b, nb][:].bitcast(U32).indirect(offsets(b, k0 * K_PASS, k1 * K_PASS)),
             )
             for k in range(k0, k1):
                 planes[nb, k] = tile[:, :, (k - k0) * P : (k - k0 + 1) * P]
 
-        def gather_less_z(b, nb, k0, k1):
-            listed = scalar_gather(f"listed{nb}_{k0}", b, nb, k0, k1)
+        def gather_less_z(b, nb, k0, k1, listed=None):
+            if listed is None:
+                listed = held(f"listed{nb}_{k0}", [P, (k1 - k0) * K_PASS], F32)[:]
+            scalar_gather(listed, b, nb, k0 * K_PASS, k1 * K_PASS)
             tile = held(f"laid{nb}_{k0}", [P, SLOTS, (k1 - k0) * P], F32)
             z_part = z[nb][k0 // 2][:, (k0 % 2) * K_PASS : (k0 % 2 + k1 - k0) * K_PASS]
-            nc.gpsimd.tensor_tensor(planes_of(tile[:]), tokens_of(listed[:]), tokens_of(z_part), SUBTRACT)
+            nc.gpsimd.tensor_tensor(planes_of(tile[:]), tokens_of(listed), tokens_of(z_part), SUBTRACT)
             for k in range(k0, k1):
                 laid[nb, k] = tile[:, :, (k - k0) * P : (k - k0 + 1) * P]
 
@@ -170,31 +168,43 @@ def tile_attend_gvq_rw_w_kernel(tc, zT, cb, cb2, tw, xT, offs, offs2, out):
         x_banks = {}
         x_turned = {}
 
-        def cast_and_turn_x(k):
-            pairs = held(f"x_pairs{k}", [P, 2, DB, 2 * P], BF16)
-            nc.scalar.copy(
-                pairs[:].rearrange("p u b (q r e) -> p u (b q) r e", r=RUN, e=2),
-                x_raw[k][:].rearrange("p b (q u e r) -> p u (b q) r e", u=2, e=2, r=RUN),
-            )
-            x_banks[k] = bank_tile(k % 2, f"x_bank{k}", [P, DB, 2, P])
-            for db in range(DB):
-                for u in range(2):
-                    nc.tensor.transpose(x_banks[k][:, db, u, :], pairs[:, u, db, :].bitcast(F32), ident[:])
+        def turn_x(half, db, u, words):
+            if (half, db) not in x_banks:
+                x_banks[half, db] = bank_tile(db, f"x_bank{half}_{db}", [P, 2, 2, P])
+            for k in range(2):
+                nc.tensor.transpose(x_banks[half, db][:, k, u, :], words[:, k * 2 * P : (k + 1) * 2 * P].bitcast(F32), ident[:])
 
-        def copy_x(k):
-            x_turned[k] = held(f"x_turned{k}", [P, D * SLOTS], BF16)
+        def x_tokens(half, db):
+            return x_raw[half][:, db, :].rearrange("p (q u e r) -> p u q r e", u=2, e=2, r=RUN)
+
+        def cast_and_turn_x(half, db):
+            if (half, db) != (1, 1):
+                pairs = held(f"x_pairs{half}_{db}", [P, 2, K_PASS], BF16)
+                nc.scalar.copy(pairs[:].rearrange("p u (q r e) -> p u q r e", r=RUN, e=2), x_tokens(half, db))
+                for u in range(2):
+                    turn_x(half, db, u, pairs[:, u, :])
+                return
+            halves = [held(f"x_pairs{half}_{db}_{u}", [P, K_PASS], BF16) for u in range(2)]
+            views = [tile[:].rearrange("p (q r e) -> p q r e", r=RUN, e=2) for tile in halves]
+            nc.gpsimd.tensor_scalar(views[1], x_tokens(half, db)[:, 1], 1.0, 0.0, MULT, ADD)
+            nc.scalar.copy(views[0], x_tokens(half, db)[:, 0])
+            for u in (1, 0):
+                turn_x(half, db, u, halves[u][:])
+
+        def copy_x(half, db):
+            x_turned[half, db] = held(f"x_turned{half}_{db}", [P, 2 * K_PASS], BF16)
             nc.scalar.copy(
-                x_turned[k][:].bitcast(F32).rearrange("p (b d u) -> p b d u", b=DB, u=2),
-                x_banks[k][:].rearrange("p b u d -> p b d u"),
+                x_turned[half, db][:].bitcast(F32).rearrange("p (k d u) -> p k d u", k=2, u=2),
+                x_banks[half, db][:].rearrange("p k u d -> p k d u"),
             )
 
         x_scales = held("x_scales", [P, PASSES * D], U8)
         g_scales = held("g_scales", [P, NB * PASSES * P], U8)
         quantised = {}
 
-        def quantize_x(k):
-            cols = slice(k * D, (k + 1) * D)
-            nc.vector.quantize_mx(out=x_codes[:, cols].bitcast(E4M3), scales=x_scales[:, cols], in_=x_turned[k][:])
+        def quantize_x(half, db):
+            cols = slice((db * PASSES + 2 * half) * P, (db * PASSES + 2 * half + 2) * P)
+            nc.vector.quantize_mx(out=x_codes[:, cols].bitcast(E4M3), scales=x_scales[:, cols], in_=x_turned[half, db][:])
 
         def quantize_g(values, units):
             cols = slice(len(quantised) * P, (len(quantised) + len(units)) * P)
@@ -202,19 +212,18 @@ def tile_attend_gvq_rw_w_kernel(tc, zT, cb, cb2, tw, xT, offs, offs2, out):
             for unit in units:
                 quantised[unit] = len(quantised) * P
 
-        def multiply(sums, nb, k, blocks, start, stop):
+        def multiply(sums, db, nb, k, blocks, start, stop):
             g_cols = slice(quantised[nb, k], quantised[nb, k] + blocks * P)
-            for db in range(DB):
-                cols = slice(k * D + db * P, k * D + (db + 1) * P)
-                nc.tensor.matmul_mx(
-                    out=sums[db],
-                    lhsT=x_codes[:, cols].bitcast(E4M3),
-                    lhsT_scale=x_scales[:, cols],
-                    rhs=g_codes[:, g_cols].bitcast(E5M2),
-                    rhs_scale=g_scales[:, g_cols],
-                    start=start,
-                    stop=stop,
-                )
+            x_cols = slice((db * PASSES + k) * P, (db * PASSES + k + 1) * P)
+            nc.tensor.matmul_mx(
+                out=sums,
+                lhsT=x_codes[:, x_cols].bitcast(E4M3),
+                lhsT_scale=x_scales[:, x_cols],
+                rhs=g_codes[:, g_cols].bitcast(E5M2),
+                rhs_scale=g_scales[:, g_cols],
+                start=start,
+                stop=stop,
+            )
 
         for k in range(2):
             gather_less_z(0, 0, k, k + 1)
@@ -226,77 +235,93 @@ def tile_attend_gvq_rw_w_kernel(tc, zT, cb, cb2, tw, xT, offs, offs2, out):
         for k in range(PASSES):
             add_up(0, k, *((planes, laid) if k == 2 else (laid, planes)))
         low = staging("g_low", [(0, 0), (1, 0), (0, 1), (1, 1)])
-        high = staging("g_high", [(2, 0), (2, 1), (3, 0), (3, 1)])
-        late = {}
         weigh(0, 0)
         weigh(0, 1)
 
-        for nb in range(1, NB):
-            if nb < NB - 1:
-                for h in range(2):
-                    gather_less_z(0, nb, 2 * h, 2 * h + 2)
-                    vector_gather(1, nb, 2 * h, 2 * h + 2)
-            else:
-                extra = scalar_gather("extra", 1, nb, 2, 4)
-                extra_laid = held("extra_laid", [P, SLOTS, 2 * P], F32, on="z2_1")
-                nc.gpsimd.tensor_scalar(planes_of(extra_laid[:]), tokens_of(extra[:]), 1.0, 0.0, MULT, ADD)
-                for k in range(2, 4):
-                    planes[nb, k] = extra_laid[:, :, (k - 2) * P : (k - 1) * P]
-                for k in range(PASSES):
-                    gather_less_z(0, nb, k, k + 1)
-                vector_gather(1, nb, 0, 2)
-            late[nb - 1] = staging(f"g_late{nb - 1}", [(nb - 1, 2), (nb - 1, 3)], on=f"book1_{nb}")
-            weigh(nb - 1, 2)
-            weigh(nb - 1, 3)
-            for k in range(PASSES):
-                planes_first = (nb == 1 and k < 2) or (nb == NB - 1 and k >= 2)
-                add_up(nb, k, *((planes, laid) if planes_first else (laid, planes)))
-            weigh(nb, 0)
-            weigh(nb, 1)
+        for h in range(2):
+            gather_less_z(0, 1, 2 * h, 2 * h + 2)
+            vector_gather(1, 1, 2 * h, 2 * h + 2)
+        late = staging("g_late", [(0, 2), (0, 3), (2, 2), (2, 3)], on="book1_1")
+        weigh(0, 2)
+        weigh(0, 3)
+        for k in range(PASSES):
+            add_up(1, k, *((planes, laid) if k < 2 else (laid, planes)))
+        weigh(1, 0)
+        weigh(1, 1)
+
+        for h in range(2):
+            gather_less_z(0, 2, 2 * h, 2 * h + 2)
+            vector_gather(1, 2, 2 * h, 2 * h + 2)
+        for k in range(PASSES):
+            add_up(2, k, laid, planes)
+        gather_less_z(0, 3, 0, 2)
+        extra = held("extra", [P, 2 * K_PASS], F32)
+        scalar_gather(extra[:], 1, 3, 2 * K_PASS, T)
+        extra_laid = held("extra_laid", [P, SLOTS, 2 * P], F32, on="z3_0")
+        nc.gpsimd.tensor_scalar(planes_of(extra_laid[:]), tokens_of(extra[:]), 1.0, 0.0, MULT, ADD)
+        rest = held("listed3_2", [P, 2 * K_PASS], F32, on="z2_1")
+        for k in range(2, 4):
+            planes[3, k] = extra_laid[:, :, (k - 2) * P : (k - 1) * P]
+            gather_less_z(0, 3, k, k + 1, rest[:, (k - 2) * K_PASS : (k - 1) * K_PASS])
+        vector_gather(1, 3, 0, 2)
+        middle = staging("g_middle", [(1, 2), (1, 3), (2, 0), (2, 1)], on="book1_3")
+        weigh(1, 2)
+        weigh(1, 3)
+        for k in range(PASSES):
+            add_up(3, k, *((laid, planes) if k < 2 else (planes, laid)))
+        for k in range(PASSES):
+            weigh(2, k)
+        high = staging("g_high", [(3, 0), (3, 1)])
+        weigh(3, 0)
+        weigh(3, 1)
 
         for half in range(2):
-            cast_and_turn_x(2 * half)
-            cast_and_turn_x(2 * half + 1)
-            copy_x(2 * half)
-            copy_x(2 * half + 1)
+            for db in range(DB):
+                cast_and_turn_x(half, db)
+            for db in range(DB):
+                copy_x(half, db)
 
         codes = held("codes", [P, NB * PASSES * P + PASSES * D], U32, on="z3_1")
         g_codes, x_codes = codes[:, : NB * PASSES * P], codes[:, NB * PASSES * P :]
         acc = [bank_tile(2 + db, f"acc{db}", [P, 3 * P]) for db in range(DB)]
         last = [bank_tile(4 + db, f"last{db}", [P, P])[:] for db in range(DB)]
-        sums = [[acc[db][:, nb * P : (nb + 1) * P] for db in range(DB)] for nb in range(3)] + [last]
-        pair = [acc[db][:, : 2 * P] for db in range(DB)]
+
+        def second_half(db):
+            for nb in range(3):
+                for k in range(2, 4):
+                    multiply(acc[db][:, nb * P : (nb + 1) * P], db, nb, k, 1, False, nb == 2 and k == 3)
+            result = held(f"result{db}", [P, 3 * P], F32)
+            nc.scalar.copy(result[:], acc[db][:])
+            nc.sync.dma_start(out=out[db * P : (db + 1) * P, : 3 * P], in_=result[:])
 
         quantize_g(*low)
-        quantize_x(0)
-        multiply(pair, 0, 0, 2, True, False)
+        quantize_x(0, 0)
+        for k in range(2):
+            multiply(acc[0][:, : 2 * P], 0, 0, k, 2, k == 0, False)
+        quantize_g(*middle)
+        for k in range(2):
+            multiply(acc[0][:, 2 * P :], 0, 2, k, 1, False, False)
+        quantize_x(0, 1)
+        for k in range(2):
+            multiply(acc[1][:, : 2 * P], 1, 0, k, 2, k == 0, False)
+            multiply(acc[1][:, 2 * P :], 1, 2, k, 1, False, False)
         quantize_g(*high)
-        multiply(sums[2], 2, 0, 1, False, False)
-        multiply(last, 3, 0, 1, True, False)
-        quantize_x(1)
-        multiply(pair, 0, 1, 2, False, False)
-        multiply(sums[2], 2, 1, 1, False, False)
-        multiply(last, 3, 1, 1, False, False)
-        staging("g3_2", [(3, 2)])
+        for k in range(2):
+            for db in range(DB):
+                multiply(last[db], db, 3, k, 1, k == 0, False)
+        quantize_g(*late)
+        quantize_x(1, 0)
+        second_half(0)
+        staging("g3_2", [(3, 2)], on="x_turned1_0")
         weigh(3, 2)
-        quantize_g(*late[0])
-        quantize_g(*late[1])
-        quantize_x(2)
-        quantize_g(*late[2])
-        for nb in range(3):
-            multiply(sums[nb], nb, 2, 1, False, False)
-        quantize_x(3)
-        for nb in range(3):
-            multiply(sums[nb], nb, 3, 1, False, nb == 2)
-        staging("g3_3", [(3, 3)], on="x_turned3")
+        quantize_x(1, 1)
+        second_half(1)
+        staging("g3_3", [(3, 3)], on="x_turned1_1")
         weigh(3, 3)
         for k in range(2, 4):
             quantize_g(g[3, k], [(3, k)])
-            multiply(last, 3, k, 1, False, k == 3)
-        for db in range(DB):
-            result = held(f"result{db}", [P, 3 * P], F32)
-            (nc.vector.tensor_copy, nc.scalar.copy)[db](result[:], acc[db][:])
-            nc.sync.dma_start(out=out[db * P : (db + 1) * P, : 3 * P], in_=result[:])
+            for db in range(DB):
+                multiply(last[db], db, 3, k, 1, False, k == 3)
         tail = [held(f"tail{db}", [P, P], F32) for db in range(DB)]
         nc.vector.tensor_copy(tail[0][:], last[0])
         nc.sync.dma_start(out=out[0:P, 3 * P :], in_=tail[0][:])

@@ -206,21 +206,21 @@ def tile_attend_gvq_rw_w_kernel(tc, zT, cb, cb2, tw, xT, offs, offs2, out):
             cols = slice((db * PASSES + 2 * half) * P, (db * PASSES + 2 * half + 2) * P)
             nc.vector.quantize_mx(out=x_codes[:, cols].bitcast(E4M3), scales=x_scales[:, cols], in_=x_turned[half, db][:])
 
-        def quantize_g(values, units):
-            cols = slice(len(quantised) * P, (len(quantised) + len(units)) * P)
-            nc.vector.quantize_mx(out=g_codes[:, cols].bitcast(E5M2), scales=g_scales[:, cols], in_=values)
-            for unit in units:
-                quantised[unit] = len(quantised) * P
+        def quantize_g(values, units, codes, col):
+            first, width = len(quantised) * P, len(units) * P
+            nc.vector.quantize_mx(out=codes[:, col : col + width].bitcast(E5M2), scales=g_scales[:, first : first + width], in_=values)
+            for i, unit in enumerate(units):
+                quantised[unit] = (codes, col + i * P, first + i * P)
 
         def multiply(sums, db, nb, k, blocks, start, stop):
-            g_cols = slice(quantised[nb, k], quantised[nb, k] + blocks * P)
+            codes, col, scale_col = quantised[nb, k]
             x_cols = slice((db * PASSES + k) * P, (db * PASSES + k + 1) * P)
             nc.tensor.matmul_mx(
                 out=sums,
                 lhsT=x_codes[:, x_cols].bitcast(E4M3),
                 lhsT_scale=x_scales[:, x_cols],
-                rhs=g_codes[:, g_cols].bitcast(E5M2),
-                rhs_scale=g_scales[:, g_cols],
+                rhs=codes[:, col : col + blocks * P].bitcast(E5M2),
+                rhs_scale=g_scales[:, scale_col : scale_col + blocks * P],
                 start=start,
                 stop=stop,
             )
@@ -241,7 +241,7 @@ def tile_attend_gvq_rw_w_kernel(tc, zT, cb, cb2, tw, xT, offs, offs2, out):
         for h in range(2):
             gather_less_z(0, 1, 2 * h, 2 * h + 2)
             vector_gather(1, 1, 2 * h, 2 * h + 2)
-        late = staging("g_late", [(0, 2), (0, 3), (2, 2), (2, 3)], on="book1_1")
+        late = staging("g_late", [(0, 2), (0, 3)], on="book1_1")
         weigh(0, 2)
         weigh(0, 3)
         for k in range(PASSES):
@@ -252,8 +252,14 @@ def tile_attend_gvq_rw_w_kernel(tc, zT, cb, cb2, tw, xT, offs, offs2, out):
         for h in range(2):
             gather_less_z(0, 2, 2 * h, 2 * h + 2)
             vector_gather(1, 2, 2 * h, 2 * h + 2)
+        middle = staging("g_middle", [(1, 2), (1, 3), (2, 0), (2, 1)], on="book1_2")
+        weigh(1, 2)
+        weigh(1, 3)
         for k in range(PASSES):
             add_up(2, k, laid, planes)
+        weigh(2, 0)
+        weigh(2, 1)
+
         gather_less_z(0, 3, 0, 2)
         extra = held("extra", [P, 2 * K_PASS], F32)
         scalar_gather(extra[:], 1, 3, 2 * K_PASS, T)
@@ -264,14 +270,11 @@ def tile_attend_gvq_rw_w_kernel(tc, zT, cb, cb2, tw, xT, offs, offs2, out):
             planes[3, k] = extra_laid[:, :, (k - 2) * P : (k - 1) * P]
             gather_less_z(0, 3, k, k + 1, rest[:, (k - 2) * K_PASS : (k - 1) * K_PASS])
         vector_gather(1, 3, 0, 2)
-        middle = staging("g_middle", [(1, 2), (1, 3), (2, 0), (2, 1)], on="book1_3")
-        weigh(1, 2)
-        weigh(1, 3)
+        high = staging("g_high", [(2, 2), (2, 3), (3, 0), (3, 1)], on="book1_3")
+        weigh(2, 2)
+        weigh(2, 3)
         for k in range(PASSES):
             add_up(3, k, *((laid, planes) if k < 2 else (planes, laid)))
-        for k in range(PASSES):
-            weigh(2, k)
-        high = staging("g_high", [(3, 0), (3, 1)])
         weigh(3, 0)
         weigh(3, 1)
 
@@ -281,35 +284,34 @@ def tile_attend_gvq_rw_w_kernel(tc, zT, cb, cb2, tw, xT, offs, offs2, out):
             for db in range(DB):
                 copy_x(half, db)
 
-        codes = held("codes", [P, NB * PASSES * P + PASSES * D], U32, on="z3_1")
-        g_codes, x_codes = codes[:, : NB * PASSES * P], codes[:, NB * PASSES * P :]
+        first_codes = held("first_codes", [P, 10 * P + PASSES * D], U32, on="z3_1")
+        x_codes = first_codes[:, 10 * P :]
         acc = [bank_tile(2 + db, f"acc{db}", [P, 3 * P]) for db in range(DB)]
         last = [bank_tile(4 + db, f"last{db}", [P, P])[:] for db in range(DB)]
 
         def second_half(db):
-            for nb in range(3):
-                for k in range(2, 4):
-                    multiply(acc[db][:, nb * P : (nb + 1) * P], db, nb, k, 1, False, nb == 2 and k == 3)
+            rest_of_db = [(nb, k) for nb in range(3) for k in range(2, 4)] + [(2, 0), (2, 1)] * (db == 0)
+            for nb, k in rest_of_db:
+                multiply(acc[db][:, nb * P : (nb + 1) * P], db, nb, k, 1, False, (nb, k) == rest_of_db[-1])
             result = held(f"result{db}", [P, 3 * P], F32)
             nc.scalar.copy(result[:], acc[db][:])
             nc.sync.dma_start(out=out[db * P : (db + 1) * P, : 3 * P], in_=result[:])
 
-        quantize_g(*low)
+        quantize_g(*low, first_codes, 0)
+        quantize_g(*middle, first_codes, 4 * P)
+        quantize_g(*late, first_codes, 8 * P)
         quantize_x(0, 0)
         for k in range(2):
             multiply(acc[0][:, : 2 * P], 0, 0, k, 2, k == 0, False)
-        quantize_g(*middle)
-        for k in range(2):
-            multiply(acc[0][:, 2 * P :], 0, 2, k, 1, False, False)
+        more_codes = held("more_codes", [P, 6 * P], U32, on="x_turned0_0")
+        quantize_g(*high, more_codes, 0)
         quantize_x(0, 1)
         for k in range(2):
             multiply(acc[1][:, : 2 * P], 1, 0, k, 2, k == 0, False)
             multiply(acc[1][:, 2 * P :], 1, 2, k, 1, False, False)
-        quantize_g(*high)
         for k in range(2):
-            for db in range(DB):
+            for db in (1, 0):
                 multiply(last[db], db, 3, k, 1, k == 0, False)
-        quantize_g(*late)
         quantize_x(1, 0)
         second_half(0)
         staging("g3_2", [(3, 2)], on="x_turned1_0")
@@ -319,7 +321,7 @@ def tile_attend_gvq_rw_w_kernel(tc, zT, cb, cb2, tw, xT, offs, offs2, out):
         staging("g3_3", [(3, 3)], on="x_turned1_1")
         weigh(3, 3)
         for k in range(2, 4):
-            quantize_g(g[3, k], [(3, k)])
+            quantize_g(g[3, k], [(3, k)], more_codes, (2 + k) * P)
             for db in range(DB):
                 multiply(last[db], db, 3, k, 1, False, k == 3)
         tail = [held(f"tail{db}", [P, P], F32) for db in range(DB)]

@@ -170,7 +170,7 @@ def tile_attend_gvq_rw_w_kernel(tc, zT, cb, cb2, tw, xT, offs, offs2, out):
 
         def turn_x(half, db, u, words):
             if (half, db) not in x_banks:
-                x_banks[half, db] = bank_tile(db, f"x_bank{half}_{db}", [P, 2, 2, P])
+                x_banks[half, db] = bank_tile(4 * half + db, f"x_bank{half}_{db}", [P, 2, 2, P])
             for k in range(2):
                 nc.tensor.transpose(x_banks[half, db][:, k, u, :], words[:, k * 2 * P : (k + 1) * 2 * P].bitcast(F32), ident[:])
 
@@ -287,12 +287,12 @@ def tile_attend_gvq_rw_w_kernel(tc, zT, cb, cb2, tw, xT, offs, offs2, out):
         first_codes = held("first_codes", [P, 10 * P + PASSES * D], U32, on="z3_1")
         x_codes = first_codes[:, 10 * P :]
         acc = [bank_tile(2 + db, f"acc{db}", [P, 3 * P]) for db in range(DB)]
-        last = [bank_tile(4 + db, f"last{db}", [P, P])[:] for db in range(DB)]
+        last = [bank_tile(db, f"last{db}", [P, P])[:] for db in range(DB)]
 
         def second_half(db):
-            rest_of_db = [(nb, k) for nb in range(3) for k in range(2, 4)] + [(2, 0), (2, 1)] * (db == 0)
-            for nb, k in rest_of_db:
-                multiply(acc[db][:, nb * P : (nb + 1) * P], db, nb, k, 1, False, (nb, k) == rest_of_db[-1])
+            for nb in range(3):
+                for k in range(2, 4):
+                    multiply(acc[db][:, nb * P : (nb + 1) * P], db, nb, k, 1, False, nb == 2 and k == 3)
             result = held(f"result{db}", [P, 3 * P], F32)
             nc.scalar.copy(result[:], acc[db][:])
             nc.sync.dma_start(out=out[db * P : (db + 1) * P, : 3 * P], in_=result[:])
@@ -303,6 +303,7 @@ def tile_attend_gvq_rw_w_kernel(tc, zT, cb, cb2, tw, xT, offs, offs2, out):
         quantize_x(0, 0)
         for k in range(2):
             multiply(acc[0][:, : 2 * P], 0, 0, k, 2, k == 0, False)
+            multiply(acc[0][:, 2 * P :], 0, 2, k, 1, False, False)
         more_codes = held("more_codes", [P, 6 * P], U32, on="x_turned0_0")
         quantize_g(*high, more_codes, 0)
         quantize_x(0, 1)
@@ -310,7 +311,7 @@ def tile_attend_gvq_rw_w_kernel(tc, zT, cb, cb2, tw, xT, offs, offs2, out):
             multiply(acc[1][:, : 2 * P], 1, 0, k, 2, k == 0, False)
             multiply(acc[1][:, 2 * P :], 1, 2, k, 1, False, False)
         for k in range(2):
-            for db in (1, 0):
+            for db in range(DB):
                 multiply(last[db], db, 3, k, 1, k == 0, False)
         quantize_x(1, 0)
         second_half(0)

@@ -92,8 +92,8 @@ def tile_attend_gvq_rw_w_kernel(tc, zT, cb, cb2, tw, xT, offs, offs2, out):
         load_book(1, 3)
         load_z(2, 1)
         load_z(3, 0)
-        load_x(0)
         load_z(3, 1)
+        load_x(0)
         load_x(1)
 
         def planes_of(ap):
@@ -128,9 +128,8 @@ def tile_attend_gvq_rw_w_kernel(tc, zT, cb, cb2, tw, xT, offs, offs2, out):
             for k in range(k0, k1):
                 planes[nb, k] = tile[:, :, (k - k0) * P : (k - k0 + 1) * P]
 
-        def gather_less_z(b, nb, k0, k1, listed=None):
-            if listed is None:
-                listed = held(f"listed{nb}_{k0}", [P, (k1 - k0) * K_PASS], F32)[:]
+        def gather_less_z(b, nb, k0, k1):
+            listed = held(f"listed{nb}_{k0}", [P, (k1 - k0) * K_PASS], F32)[:]
             scalar_gather(listed, b, nb, k0 * K_PASS, k1 * K_PASS)
             tile = held(f"laid{nb}_{k0}", [P, SLOTS, (k1 - k0) * P], F32)
             z_part = z[nb][k0 // 2][:, (k0 % 2) * K_PASS : (k0 % 2 + k1 - k0) * K_PASS]
@@ -260,21 +259,20 @@ def tile_attend_gvq_rw_w_kernel(tc, zT, cb, cb2, tw, xT, offs, offs2, out):
         weigh(2, 0)
         weigh(2, 1)
 
-        gather_less_z(0, 3, 0, 2)
+        for h in range(2):
+            gather_less_z(0, 3, 2 * h, 2 * h + 2)
         extra = held("extra", [P, 2 * K_PASS], F32)
         scalar_gather(extra[:], 1, 3, 2 * K_PASS, T)
-        extra_laid = held("extra_laid", [P, SLOTS, 2 * P], F32, on="z3_0")
+        extra_laid = held("extra_laid", [P, SLOTS, 2 * P], F32, on="z3_1")
         nc.gpsimd.tensor_scalar(planes_of(extra_laid[:]), tokens_of(extra[:]), 1.0, 0.0, MULT, ADD)
-        rest = held("listed3_2", [P, 2 * K_PASS], F32, on="z2_1")
         for k in range(2, 4):
             planes[3, k] = extra_laid[:, :, (k - 2) * P : (k - 1) * P]
-            gather_less_z(0, 3, k, k + 1, rest[:, (k - 2) * K_PASS : (k - 1) * K_PASS])
         vector_gather(1, 3, 0, 2)
         high = staging("g_high", [(2, 2), (2, 3), (3, 0), (3, 1)], on="book1_3")
         weigh(2, 2)
         weigh(2, 3)
         for k in range(PASSES):
-            add_up(3, k, *((laid, planes) if k < 2 else (planes, laid)))
+            add_up(3, k, laid, planes)
         weigh(3, 0)
         weigh(3, 1)
 
@@ -284,7 +282,7 @@ def tile_attend_gvq_rw_w_kernel(tc, zT, cb, cb2, tw, xT, offs, offs2, out):
             for db in range(DB):
                 copy_x(half, db)
 
-        first_codes = held("first_codes", [P, 10 * P + PASSES * D], U32, on="z3_1")
+        first_codes = held("first_codes", [P, 10 * P + PASSES * D], U32, on="extra")
         x_codes = first_codes[:, 10 * P :]
         acc = [bank_tile(2 + db, f"acc{db}", [P, 3 * P]) for db in range(DB)]
         last = [bank_tile(db, f"last{db}", [P, P])[:] for db in range(DB)]

from contextlib import ExitStack

import concourse.mybir as mybir
from concourse.masks import make_identity

T, C, D, DV = 2048, 1024, 256, 512
BETA = 0.25
FLOPS = 2 * T * D * DV
BYTES = 4 * (DV * T + 2 * DV * C + T + D * T + D * DV) + 2 * 2 * 128 * (T // 16)

F32 = mybir.dt.float32
BF16 = mybir.dt.bfloat16
U32 = mybir.dt.uint32
U16 = mybir.dt.uint16
U8 = mybir.dt.uint8
E4M3 = mybir.dt.float8_e4m3fn_x4
E5M2 = mybir.dt.float8_e5m2_x4
COPY = mybir.ActivationFunctionType.Copy
MULT = mybir.AluOpType.mult
ADD = mybir.AluOpType.add
SUBTRACT = mybir.AluOpType.subtract

P = 128
SLOTS = 4
RUN = 8
K_PASS = P * SLOTS
PASSES = T // K_PASS
NB = DV // P
DB = D // P
LIST_ROWS = 16
PAD = 352


def tile_attend_gvq_rw_w_kernel(tc, zT, cb, cb2, tw, xT, offs, offs2, out):
    nc = tc.nc
    with ExitStack() as ctx:
        keep = ctx.enter_context(tc.tile_pool(name="keep", bufs=1))
        psum = ctx.enter_context(tc.psum_pool(name="psum", bufs=1))

        def held(name, shape, dtype, on=None):
            return keep.tile(shape, dtype, name=name, tag=on or name, align_bytes=64)

        def bank_tile(i, name, shape):
            return psum.tile(shape, F32, tag=f"bank{i}", name=name)

        lists = [keep.tile([P, T // LIST_ROWS], U16, name=f"list{b}") for b in range(2)]
        padded = {(0, 0): PAD, (1, 1): PAD, (1, 2): PAD, (1, 3): PAD, (0, 1): 32, (0, 2): 32, (0, 3): 32}
        books = {(b, nb): held(f"book{b}_{nb}", [P, C + padded.get((b, nb), 0)], F32) for b in range(2) for nb in range(NB)}
        z = [[held(f"z{nb}_{h}", [P, T // 2], F32) for h in range(2)] for nb in range(NB)]
        x_raw = [held(f"x_raw{h}", [P, DB, T // 2], F32) for h in range(2)]
        ident = held("ident", [P, P], F32)
        tw_rows = held("tw_rows", [P, K_PASS], F32)
        tw_planes = held("tw_planes", [P, SLOTS, P], F32)
        neg_w = held("neg_w", [P, PASSES, SLOTS], F32)

        zeros = held("zeros", [P, RUN], F32)
        nc.vector.memset(zeros[:], 0.0)
        nc.vector.memset(tw_rows[: P // 2, :], 0.0)
        nc.scalar.activation(
            tw_rows[P // 2 :, :].rearrange("p (n r) -> p n r", r=RUN),
            zeros[P // 2 :, :].unsqueeze(1).to_broadcast([P // 2, K_PASS // RUN, RUN]),
            COPY,
        )
        for key in padded:
            nc.vector.memset(books[key][:, C:].bitcast(U32), 0)
        make_identity(nc, ident[:])

        def load_book(b, nb):
            nc.sync.dma_start(out=books[b, nb][:, :C], in_=(cb, cb2)[b][nb * P : (nb + 1) * P, :])

        def load_z(nb, half):
            nc.sync.dma_start(out=z[nb][half][:], in_=zT[nb * P : (nb + 1) * P, half * T // 2 : (half + 1) * T // 2])

        def load_x(half):
            nc.sync.dma_start(out=x_raw[half][:], in_=xT[:, half * T // 2 : (half + 1) * T // 2].rearrange("(b p) t -> p b t", p=P))

        nc.sync.dma_start(lists[0][:], offs)
        load_book(0, 0)
        nc.sync.dma_start(out=tw_rows[0:PASSES, :], in_=tw[0:1, :].rearrange("a (k t) -> (a k) t", k=PASSES))
        load_z(0, 0)
        nc.sync.dma_start(lists[1][:], offs2)
        load_book(1, 0)
        load_z(0, 1)
        load_book(0, 1)
        load_book(1, 1)
        load_z(1, 0)
        load_z(1, 1)
        load_book(0, 2)
        load_book(1, 2)
        load_z(2, 0)
        load_book(0, 3)
        load_book(1, 3)
        load_z(2, 1)
        load_z(3, 0)
        load_z(3, 1)
        load_x(0)
        load_x(1)

        def planes_of(ap):
            return ap.rearrange("p j (q r) -> p j q r", r=RUN)

        def tokens_of(ap):
            return ap.rearrange("p (q j r) -> p j q r", j=SLOTS, r=RUN)

        nc.gpsimd.tensor_scalar(planes_of(tw_planes[:]), tokens_of(tw_rows[:]), -BETA, 0.0, MULT, ADD)
        w_bank = bank_tile(2, "w_bank", [P, SLOTS, P])
        for j in range(SLOTS):
            nc.tensor.transpose(w_bank[:, j, :], tw_planes[:, j, :], ident[:])
        nc.scalar.copy(neg_w[:], w_bank[:, :, 0:PASSES].rearrange("p j k -> p k j"))

        def offsets(b, t0, t1):
            return lists[b][:, t0 // LIST_ROWS : t1 // LIST_ROWS]

        planes = {}
        laid = {}
        banks = {}
        g = {}

        def scalar_gather(dest, b, nb, t0, t1):
            nc.scalar.activation(dest, books[b, nb][:].indirect(offsets(b, t0, t1)), COPY)

        def vector_gather(b, nb, k0, k1):
            tile = held(f"planes{nb}_{k0}", [P, SLOTS, (k1 - k0) * P], F32)
            nc.vector.tensor_copy(
                tile[:].bitcast(U32).rearrange("p j (q r) -> p q j r", r=RUN),
                books[b, nb][:].bitcast(U32).indirect(offsets(b, k0 * K_PASS, k1 * K_PASS)),
            )
            for k in range(k0, k1):
                planes[nb, k] = tile[:, :, (k - k0) * P : (k - k0 + 1) * P]

        def gather_less_z(b, nb, k0, k1):
            listed = held(f"listed{nb}_{k0}", [P, (k1 - k0) * K_PASS], F32)[:]
            scalar_gather(listed, b, nb, k0 * K_PASS, k1 * K_PASS)
            tile = held(f"laid{nb}_{k0}", [P, SLOTS, (k1 - k0) * P], F32)
            z_part = z[nb][k0 // 2][:, (k0 % 2) * K_PASS : (k0 % 2 + k1 - k0) * K_PASS]
            nc.gpsimd.tensor_tensor(planes_of(tile[:]), tokens_of(listed), tokens_of(z_part), SUBTRACT)
            for k in range(k0, k1):
                laid[nb, k] = tile[:, :, (k - k0) * P : (k - k0 + 1) * P]

        def add_up(nb, k, first, second):
            banks[nb, k] = bank_tile((nb * PASSES + k) % 8, f"e{nb}_{k}", [P, SLOTS, P])
            for term, terms in enumerate((first, second)):
                for j in range(SLOTS):
                    nc.tensor.matmul(
                        banks[nb, k][:, j, :],
                        terms[nb, k][:, j, :],
                        ident[:],
                        start=(term == 0 and j == 0),
                        stop=(term == 1 and j == SLOTS - 1),
                        is_transpose=True,
                    )

        def weigh(nb, k):
            nc.vector.tensor_tensor(
                g[nb, k].rearrange("p (n j) -> p n j", j=SLOTS),
                neg_w[:, k, :].unsqueeze(1).to_broadcast([P, P, SLOTS]),
                banks[nb, k][:].rearrange("p j n -> p n j"),
                MULT,
            )

        def staging(name, units, on=None):
            tile = held(name, [P, len(units) * K_PASS], BF16, on=on)
            for i, unit in enumerate(units):
                g[unit] = tile[:, i * K_PASS : (i + 1) * K_PASS]
            return tile[:], units

        x_banks = {}
        x_turned = {}

        def turn_x(half, db, u, words):
            if (half, db) not in x_banks:
                x_banks[half, db] = bank_tile(4 * half + db, f"x_bank{half}_{db}", [P, 2, 2, P])
            for k in range(2):
                nc.tensor.transpose(x_banks[half, db][:, k, u, :], words[:, k * 2 * P : (k + 1) * 2 * P].bitcast(F32), ident[:])

        def x_tokens(half, db):
            return x_raw[half][:, db, :].rearrange("p (q u e r) -> p u q r e", u=2, e=2, r=RUN)

        def cast_and_turn_x(half, db):
            if (half, db) != (1, 1):
                pairs = held(f"x_pairs{half}_{db}", [P, 2, K_PASS], BF16)
                nc.scalar.copy(pairs[:].rearrange("p u (q r e) -> p u q r e", r=RUN, e=2), x_tokens(half, db))
                for u in range(2):
                    turn_x(half, db, u, pairs[:, u, :])
                return
            halves = [held(f"x_pairs{half}_{db}_{u}", [P, K_PASS], BF16) for u in range(2)]
            views = [tile[:].rearrange("p (q r e) -> p q r e", r=RUN, e=2) for tile in halves]
            nc.gpsimd.tensor_scalar(views[1], x_tokens(half, db)[:, 1], 1.0, 0.0, MULT, ADD)
            nc.scalar.copy(views[0], x_tokens(half, db)[:, 0])
            for u in (1, 0):
                turn_x(half, db, u, halves[u][:])

        def copy_x(half, db):
            x_turned[half, db] = held(f"x_turned{half}_{db}", [P, 2 * K_PASS], BF16)
            nc.scalar.copy(
                x_turned[half, db][:].bitcast(F32).rearrange("p (k d u) -> p k d u", k=2, u=2),
                x_banks[half, db][:].rearrange("p k u d -> p k d u"),
            )

        x_scales = held("x_scales", [P, PASSES * D], U8)
        g_scales = held("g_scales", [P, NB * PASSES * P], U8)
        quantised = {}

        def quantize_x(half, db):
            cols = slice((db * PASSES + 2 * half) * P, (db * PASSES + 2 * half + 2) * P)
            nc.vector.quantize_mx(out=x_codes[:, cols].bitcast(E4M3), scales=x_scales[:, cols], in_=x_turned[half, db][:])

        def quantize_g(values, units, codes, col):
            first, width = len(quantised) * P, len(units) * P
            nc.vector.quantize_mx(out=codes[:, col : col + width].bitcast(E5M2), scales=g_scales[:, first : first + width], in_=values)
            for i, unit in enumerate(units):
                quantised[unit] = (codes, col + i * P, first + i * P)

        def multiply(sums, db, nb, k, blocks, start, stop):
            codes, col, scale_col = quantised[nb, k]
            x_cols = slice((db * PASSES + k) * P, (db * PASSES + k + 1) * P)
            nc.tensor.matmul_mx(
                out=sums,
                lhsT=x_codes[:, x_cols].bitcast(E4M3),
                lhsT_scale=x_scales[:, x_cols],
                rhs=codes[:, col : col + blocks * P].bitcast(E5M2),
                rhs_scale=g_scales[:, scale_col : scale_col + blocks * P],
                start=start,
                stop=stop,
            )

        for k in range(2):
            gather_less_z(0, 0, k, k + 1)
        vector_gather(0, 0, 2, 4)
        for k in range(2, 4):
            gather_less_z(1, 0, k, k + 1)
        for k in range(2):
            vector_gather(1, 0, k, k + 1)
        for k in range(PASSES):
            add_up(0, k, *((planes, laid) if k == 2 else (laid, planes)))
        low = staging("g_low", [(0, 0), (1, 0), (0, 1), (1, 1)])
        weigh(0, 0)
        weigh(0, 1)

        for h in range(2):
            gather_less_z(0, 1, 2 * h, 2 * h + 2)
            vector_gather(1, 1, 2 * h, 2 * h + 2)
        late = staging("g_late", [(0, 2), (0, 3)], on="book1_1")
        weigh(0, 2)
        weigh(0, 3)
        for k in range(PASSES):
            add_up(1, k, *((planes, laid) if k < 2 else (laid, planes)))
        weigh(1, 0)
        weigh(1, 1)

        for h in range(2):
            gather_less_z(0, 2, 2 * h, 2 * h + 2)
            vector_gather(1, 2, 2 * h, 2 * h + 2)
        middle = staging("g_middle", [(1, 2), (1, 3), (2, 0), (2, 1)], on="book1_2")
        weigh(1, 2)
        weigh(1, 3)
        for k in range(PASSES):
            add_up(2, k, laid, planes)
        weigh(2, 0)
        weigh(2, 1)

        for h in range(2):
            gather_less_z(0, 3, 2 * h, 2 * h + 2)
        extra = held("extra", [P, 2 * K_PASS], F32)
        scalar_gather(extra[:], 1, 3, 2 * K_PASS, T)
        extra_laid = held("extra_laid", [P, SLOTS, 2 * P], F32, on="z3_1")
        nc.gpsimd.tensor_scalar(planes_of(extra_laid[:]), tokens_of(extra[:]), 1.0, 0.0, MULT, ADD)
        for k in range(2, 4):
            planes[3, k] = extra_laid[:, :, (k - 2) * P : (k - 1) * P]
        vector_gather(1, 3, 0, 2)
        high = staging("g_high", [(2, 2), (2, 3), (3, 0), (3, 1)], on="book1_3")
        weigh(2, 2)
        weigh(2, 3)
        for k in range(PASSES):
            add_up(3, k, laid, planes)
        weigh(3, 0)
        weigh(3, 1)

        for half in range(2):
            for db in range(DB):
                cast_and_turn_x(half, db)
            for db in range(DB):
                copy_x(half, db)

        first_codes = held("first_codes", [P, 10 * P + PASSES * D], U32, on="extra")
        x_codes = first_codes[:, 10 * P :]
        acc = [bank_tile(2 + db, f"acc{db}", [P, 3 * P]) for db in range(DB)]
        last = [bank_tile(db, f"last{db}", [P, P])[:] for db in range(DB)]

        def second_half(db):
            for nb in range(3):
                for k in range(2, 4):
                    multiply(acc[db][:, nb * P : (nb + 1) * P], db, nb, k, 1, False, nb == 2 and k == 3)
            result = held(f"result{db}", [P, 3 * P], F32)
            nc.scalar.copy(result[:], acc[db][:])
            nc.sync.dma_start(out=out[db * P : (db + 1) * P, : 3 * P], in_=result[:])

        quantize_g(*low, first_codes, 0)
        quantize_g(*middle, first_codes, 4 * P)
        quantize_g(*late, first_codes, 8 * P)
        quantize_x(0, 0)
        for k in range(2):
            multiply(acc[0][:, : 2 * P], 0, 0, k, 2, k == 0, False)
            multiply(acc[0][:, 2 * P :], 0, 2, k, 1, False, False)
        more_codes = held("more_codes", [P, 6 * P], U32, on="x_turned0_0")
        quantize_g(*high, more_codes, 0)
        quantize_x(0, 1)
        for k in range(2):
            multiply(acc[1][:, : 2 * P], 1, 0, k, 2, k == 0, False)
            multiply(acc[1][:, 2 * P :], 1, 2, k, 1, False, False)
        for k in range(2):
            for db in range(DB):
                multiply(last[db], db, 3, k, 1, k == 0, False)
        quantize_x(1, 0)
        second_half(0)
        staging("g3_2", [(3, 2)], on="x_turned1_0")
        weigh(3, 2)
        quantize_x(1, 1)
        second_half(1)
        staging("g3_3", [(3, 3)], on="x_turned1_1")
        weigh(3, 3)
        for k in range(2, 4):
            quantize_g(g[3, k], [(3, k)], more_codes, (2 + k) * P)
            for db in range(DB):
                multiply(last[db], db, 3, k, 1, False, k == 3)
        tail = [held(f"tail{db}", [P, P], F32) for db in range(DB)]
        nc.vector.tensor_copy(tail[0][:], last[0])
        nc.sync.dma_start(out=out[0:P, 3 * P :], in_=tail[0][:])
        nc.scalar.copy(tail[1][:], last[1])
        nc.scalar.dma_start(out=out[P:, 3 * P :], in_=tail[1][:])
